import numpy as np, ml_dtypes
CORES = [16,18,20,22]
N = 4
import mx_ref
BF = ml_dtypes.bfloat16
def tile(rs):
    return np.stack(rs, axis=2).reshape(128, -1).astype(BF)
def pick(q, e):
    c = np.concatenate([q[0].reshape(128, -1, 4), np.zeros((128, 1, 4), np.uint8)], axis=1); s = np.concatenate([q[1], np.ones((16, 1), np.uint8)], axis=1)
    return (np.ascontiguousarray(c[:, e].reshape(128, -1)), np.ascontiguousarray(s[:, e]))
def join(*qs):
    return (np.concatenate([q[0] for q in qs], axis=1), np.concatenate([q[1] for q in qs], axis=1))
def put(q, e, v):
    c, s = q[0].reshape(128, -1, 4).copy(), q[1].copy(); c[:, e] = v[0].reshape(128, -1, 4); s[:, e] = v[1]
    return (c.reshape(128, -1), s)
def pk(c, s):
    return (np.ascontiguousarray(c), mx_ref.live(s))
def emit(q):
    return q[0], q[1]
def packed(v, rng):
    q = [mx_ref.quantize(np.ascontiguousarray(v[r])) for r in range(N)]
    return np.stack([a for a, b in q]), np.stack([mx_ref.plane(b, rng) for a, b in q])
def values_of_codes():
    e, c = np.zeros((128, 128, 4), np.float32), np.zeros((128, 2, 4), np.uint8)
    e[np.arange(128), np.arange(128), 0] = 1
    c[:127, :, 0] = np.arange(256).reshape(2, 128).T[:127]
    return mx_ref.matmul(mx_ref.quantize(e.reshape(128, 512).astype(BF)), (c.reshape(128, 8), np.full((16, 2), 127, np.uint8))).T.reshape(-1).astype(np.float64)
CODE_VALUE, SCALE_VALUE = values_of_codes(), 2.0 ** (np.arange(256) - 127.0)
def decode(q):
    return (CODE_VALUE[q[0]].reshape(16, 8, -1, 4) * SCALE_VALUE[q[1]][:, None, :, None] + 0.0).reshape(128, -1).astype(np.float32)
def f(rng, *shape):
    return mx_ref.flush((rng.standard_normal(shape, dtype=np.float32) * np.exp2(rng.integers(-2, 3, shape[:-1] + (1,)))).astype(BF))
def wide(rng, *shape, cols=0):
    v = rng.standard_normal(shape, dtype=np.float32) * np.exp2(rng.integers(-12, 13, shape)).astype(np.float32)
    if cols: v *= np.repeat(np.exp2(rng.integers(-cols, cols + 1, shape[:-2] + (1, shape[-1] // 4))) * (rng.random(shape[:-2] + (1, shape[-1] // 4)) > 0.0625), 4, axis=-1).astype(np.float32)
    return mx_ref.flush(v.astype(BF))
C, F, STEP, R = 448, 192, 56, 3
def big(v):
    v = v.astype(np.float32)
    v[np.abs(v) < np.float32(2.0 ** -16)] = 0
    return v.astype(BF)
def numbers_of(rng):
    return {"x": big(f(rng, N, 128, 4 * C)), "u": np.array(f(rng, N, 128, 512)), "v": np.array(f(rng, N, 128, 512))}
def layers(rng):
    return big(f(rng, N, 128, 2048)).reshape(N, 8, 16, 4, 8, 16, 4)
def weights(rng, w):
    c, p = packed(np.ascontiguousarray(w).reshape(N, 128, 2048), rng)
    return {"wc": c, "ws": p}
def setup_inputs(rng):
    return {**numbers_of(rng), **weights(rng, layers(rng))}
def setup_inputs_ties(rng):
    d = numbers_of(rng)
    x = d["x"].reshape(N, 8, 16, C, 4)
    x[:, :, 0] = 0
    x[:, :, 0, :, :2] = rng.integers(1, 4, (N, 8, C, 2)).astype(np.float32).astype(BF)
    for r in range(N): x[r, 0, 0, :, 1] = (rng.permutation(C) % 3 + 1).astype(np.float32).astype(BF)
    u = d["u"].reshape(N, 128, 128, 4)
    u[:, :, ::16] = 0
    u[:, :, 1] = 0
    o = rng.permutation(N)
    for r in range(N):
        k = 0.0 if o[r] == 0 else -1.0 if o[r] % 2 == 1 else 1.0
        for h in range(0, 128, 16): u[r, h, h, 0] = k
        u[r, 0, 1, 1] = k
    w = layers(rng)
    w[:, :, :, :, :, 0] = 0
    return {"x": x.reshape(N, 128, 4 * C), "u": u.reshape(N, 128, 512), "v": d["v"], **weights(rng, w)}
def setup_inputs_near(rng):
    d = numbers_of(rng)
    x = d["x"].astype(np.float32).reshape(N, 8, 16, C, 4)
    x[:, :, 0] = 0
    x[:, :, 8:] = 0
    z = (N, 8, 7, C, 4)
    x[:, :, 1:8] = (1.0 + (2 * rng.integers(0, 64, z) + 1) / 128.0) * np.exp2(10.0 - rng.integers(11, 15, z)) * rng.choice([-1.0, 1.0], z)
    x[:, :, 1, :, 0] = 1.96875 * 2.0 ** 10
    n = rng.integers(0, 16, (N, 8, 2, C))
    x[:, :, 8:10] = ((n[..., None] >> np.arange(4)) & 1) * np.exp2(np.arange(4) - 23.0)
    x[:, :, 0, :, 0] = 1
    x[:, :, 11, :, 0] = 2.0 ** -10
    u = d["u"].reshape(N, 128, 128, 4)
    u[:, :, ::16] = 0
    u[:, :, 1] = 0
    o = rng.permutation(N) % 4
    for r in range(N):
        a = 16 * int(rng.integers(8))
        k = 1.0 if o[r] == 0 else -1.0 if o[r] == 1 else 2.0 ** -30
        if o[r] == 2: k *= float(rng.choice([-1.0, 1.0]))
        u[r, a, 1, 0] = k
        if o[r] == 3:
            x[r, :, 0] = 0
            x[r, :, 8:] = 0
            x[r, :, 10, :, :2] = rng.choice([1.0, 1.125], (8, C, 2)) * 2.0 ** -27
            m = rng.permutation(8) % 2 * 2.0 - 1.0
            for g in range(8): u[r, 16 * g + 10, 16 * g, 0] = k * float(m[g])
            u[r, a + 10, 1, 1] = k
        else:
            for h in range(0, 128, 16):
                u[r, h, h, 0] = k
                u[r, h + 8, h] = k
                u[r, h + 11, h, 0] = k
            u[r, a + 9, 1] = k
            u[r, a + 11, 1, 0] = k
        x[r, a // 16, 0, rng.integers(C), 0] = 2.0 ** 29
    w = layers(rng)
    for i in [0] + [8 + j for j in range(8)]:
        w[:, :, i] = 0
        w[:, :, :, :, :, i] = 0
    w[:, :, 1, :, :, :, 0] = 0
    return {"x": x.reshape(N, 128, 4 * C).astype(BF), "u": u.reshape(N, 128, 512), "v": d["v"], **weights(rng, w)}
def setup_inputs_huge(rng):
    d = numbers_of(rng)
    o = rng.permutation(N)
    x = 0.6 + 0.09 * rng.random((N, 8, 16, C, 4))
    x[o == 0] = 0.8 + 0.2 * rng.random((8, 16, C, 4))
    a = 2.0 ** 29 * (1.0 - 0.1 * rng.random((N, 8, 16, 9, 4)))
    for g in range(8): a[:, g, :, g] *= 2.0
    a[:, :, :, 8] *= 2.0
    for r in range(N):
        m = np.ones(C)
        m[rng.permutation(C)[:C // 4 if o[r] % 2 == 0 else 3 * C // 4]] = -1
        x[r] *= m[:, None]
        if o[r] == 0:
            a[r] = 2.0 ** 30
            for g in range(8): a[r, 0, :7 - g, g] *= 0.5
        if o[r] < N // 2: a[r, :, :, :8] *= (rng.permutation(8) % 2 * 2.0 - 1.0)[:, None]
    a = a.reshape(N, 128, 9, 4).astype(np.float32).astype(BF)
    u = d["u"].reshape(N, 128, 128, 4)
    u[:, :, ::16] = a[:, :, :8]
    u[:, :, 1] = a[:, :, 8]
    w = np.zeros((N, 128, 4, 128, 4), np.float32)
    i = np.arange(128)
    for b in range(4): w[:, i, b, i, b] = -1
    return {"x": (2.0 ** 30 * x).astype(np.float32).reshape(N, 128, 4 * C).astype(BF), "u": u.reshape(N, 128, 512), "v": d["v"], **weights(rng, w.astype(BF))}
def setup_inputs_crowd(rng):
    d = numbers_of(rng)
    x = d["x"].reshape(N, 8, 16, C, 4)
    u = d["u"].reshape(N, 128, 128, 4)
    u[:, :, ::16] = 0
    u[:, :, 1] = 0
    for h in range(0, 128, 16): u[:, h, h, 0] = 1
    u[:, 0, 1, 1] = 1
    rest = rng.permutation(np.r_[0, 1, 4:N]) if N > 4 else np.arange(2)
    o = np.roll(np.concatenate([[2, 3], rest]), int(rng.integers(N)))
    g = int(rng.integers(8))
    i = np.arange(C)
    for r in range(N):
        c = (8 * rng.permutation(C // 8)[:F // 8, None] + np.arange(8)).reshape(-1)
        l = i % 8
        if o[r] == 0:
            c = np.arange(C - F, C)
            l = rng.integers(0, 8, C)
        if o[r] == 1: c = np.arange(F)
        l = np.where(l == g, (g + 1) % 8, l)
        h = np.full(C, g)
        if o[r] == 2:
            c = np.arange(C - F, C)
            l = np.zeros(C, int)
            h = 4 + i // STEP % 4
        if o[r] == 3:
            c = np.arange(F)
            l = np.full(C, 7)
            h = (i - 7) // STEP % 4
        a = rng.integers(-1, 2, (8, C)).astype(np.float32)
        a[h, i] = 2
        a[l, i] = -2
        b = np.ones((8, C), np.float32)
        b[0, c] = -1
        x[r, :, 0] = 0
        x[r, :, 0, :, 0] = a.astype(BF)
        x[r, :, 0, :, 1] = b.astype(BF)
    return {"x": x.reshape(N, 128, 4 * C), "u": u.reshape(N, 128, 512), "v": d["v"], **weights(rng, layers(rng))}
def setup_inputs_spread(rng):
    d = setup_inputs(rng)
    x = big(wide(rng, N, 128, 4 * C, cols=6)).reshape(N, 16, 8, C, 4)
    for r in range(N):
        z = (16, 8, C // 4, 4)
        m = (1.0 + (2 * rng.integers(0, 64, z) + 1) / 128.0) * np.exp2(-1.0 * rng.integers(8, 15, z)) * rng.choice([-1.0, 1.0], z)
        m[:, 0, :, 0] = 1.96875
        x[r][:, :, rng.permutation(C)[:C // 4]] = m.astype(np.float32).astype(BF)
    d["x"] = x.reshape(N, 128, 4 * C)
    return d
def check_inputs(d):
    b = []
    for k in ("x", "u", "v"):
        a = np.abs(d[k].astype(np.float32))
        if not (np.isfinite(a).all() and ((a == 0) | (a >= 2.0 ** -30) & (a <= 2.0 ** 30)).all()): b.append("a value of " + k)
    none, least, most = [emit(mx_ref.quantize(np.full((128, 16), k, np.float32).astype(BF)))[1][0, 0] for k in (0.0, 2.0 ** -30, 2.0 ** 30)]
    for r in range(N):
        if ((d["wc"][r] == 0x7F) | (d["wc"][r] == 0xFF)).any(): b.append("wc: a code that is no number")
        s = mx_ref.live(d["ws"][r])
        if ((s != none) & ((s < least) | (s > most))).any(): b.append("ws: a scale out of range")
    return b
def reference(x, u, v, wc, ws):
    qu = [mx_ref.quantize(u[r]) for r in range(N)]
    lay = [pk(wc[r], ws[r]) for r in range(N)]
    now = [x[r] for r in range(N)]
    for t in range(R):
        own, fall, group, lag = [], [], [], []
        for r in range(N):
            q = mx_ref.quantize(now[r])
            own.append(decode(q))
            s = mx_ref.matmul(qu[r], q) + np.float32(0.0)
            fall.append(np.argsort(s[1], kind="stable")[:F])
            group.append(np.argmax(s[::16], axis=0))
            lag.append(np.argmin(s[::16], axis=0))
        made = []
        for r in range(N):
            e = (r - 1) % N
            first = np.full((8, C), 16 * C)
            for a, b in ((r, 0), (e, 1)):
                c = fall[a][:, None]
                j = c + STEP * np.arange(1, 9) - lag[a][c] - b * C
                h = group[a][c] + 0 * j
                here = (j >= 0) & (j < C)
                np.minimum.at(first, (h[here], j[here]), (8 * (b * C + c) + np.arange(8))[here])
            g, j = np.nonzero(first < 16 * C)
            n, k = first[g, j] // 8, first[g, j] % 8
            both = np.concatenate([own[r].reshape(8, 16, C, 4), own[e].reshape(8, 16, C, 4)], axis=2)
            z = own[r].reshape(8, 16, C, 4).copy()
            z[g, :, j] = (z[g, :, j] + both[k, :, n]) * np.float32(0.5)
            y = z.reshape(128, 4 * C).astype(BF)
            q = mx_ref.quantize(y)
            made.append(tile([mx_ref.matmul(pick(lay[r], np.arange(128 * b, 128 * b + 128)), q) * np.float32(0.03125) + y[:, b::4].astype(np.float32) for b in range(4)]))
        now = made
    out = np.zeros((N, 128, C), np.float32)
    oc, osc = np.zeros((N, 128, 4 * C), np.uint8), np.zeros((N, 16, C), np.uint8)
    for r in range(N):
        q = mx_ref.quantize(now[r])
        out[r] = mx_ref.matmul(mx_ref.quantize(v[r]), q)
        oc[r], osc[r] = emit(q)
    return {"y": out, "oc": oc, "osc": osc}

@@ -1,0 +1,515 @@
+from concourse.mybir import dt, AluOpType as A, ActivationFunctionType as AF
+
+C, NF, R = 448, 192, 3
+BIG = 8192.0
+CUTS = (0, 256, 448)
+Q4, U8, BF, F32, I32, U16 = "float8_e4m3fn_x4", "uint8", "bfloat16", "float32", "int32", "uint16"
+SCRATCH = {}
+
+
+def _sb(name, n, d):
+    SCRATCH[name] = ("sbuf", [128, n], d)
+
+
+def _q(name, n):
+    _sb(name + "c", n, Q4)
+    _sb(name + "s", n, U8)
+
+
+for _r in range(R + 1):
+    _q("t%d" % _r, 512)
+for _r in range(R):
+    _q("slot%d" % _r, NF)
+    _q("land%d" % _r, NF)
+    _sb("pk%d" % _r, 16, U16)
+    _sb("lst%d" % _r, 16, U16)
+for _n, _w in (("qu", 128), ("qup", 128), ("qu1", 128), ("qv", 128), ("qw", 512), ("ef", 512), ("eb", 1024), ("ka", 512),
+               ("kb", 512), ("m", 512), ("fl", 256), ("cm", 384), ("so", 256), ("qy", C)):
+    _q(_n, _w)
+for _n, _w in (("xin", 2048), ("xs", 2048), ("x32", 4 * C), ("ut", 512), ("vt", 512), ("eft", 2048), ("th", 128),
+               ("kat", 2048), ("kbt", 2048), ("mt", 2048), ("flt", 1024), ("cmt", 1536), ("sot", 1024), ("dd", 1152), ("ctri", 128),
+               ("ios", 384), ("ioh", 128), ("kv", 128), ("win", 4864), ("yt", 4 * C), ("fh", 4 * C), ("yy", 4 * C), ("y32", 4 * C), ("nar", 384)):
+    _sb(_n, _w, BF)
+for _n, _w in (("sc", 80), ("cmx", 80), ("cm2", 80), ("rr", 80), ("hs", 80), ("cde", 16), ("k72", 160), ("thr", 256), ("ebi", 64), ("kd", 64),
+               ("eq", 32), ("wv", 32), ("lrow", 384), ("ln", 128), ("nb", 128), ("cand", 128), ("sm", 128), ("kmin", 160),
+               ("pkf", 32), ("ko", 32), ("kos", 32), ("own", 32), ("kn", 32), ("kns", 32), ("res", 32), ("rep", 128), ("kst", 64), ("idc", 32),
+               ("cb", 16), ("w1", 96), ("w2", 80), ("pv", 8), ("yo", C), ("tj", 128), ("lc", 4), ("pn", 4)):
+    _sb(_n, _w, F32)
+for _n, _w in (("lev", 128), ("ai", 16), ("a2", 32), ("pi", 8), ("wi", 16)):
+    _sb(_n, _w, I32)
+for _n, _w in (("ul", 8), ("u1l", 8), ("pl", 12), ("rev", 2), ("ordr", 8), ("off", 112), ("ebl", 64)):
+    _sb(_n, _w, U16)
+SCRATCH["ps"] = ("psum", [128, 4096], F32)
+SEMAPHORES = ["V", "S", "P", "G", "dx0", "dx1", "du", "dv", "dwc", "dws", "outs", "sent"] + \
+             ["%s%d" % (k, r) for k in ("ac", "al") for r in range(R)]
+CY, OV, LAT, PE = 0.001, 0.03, 0.07, 0.0008
+EARLY = {'ctri': 2.0, 'k72d': -1.0, 'm': -0.5, 'yy300': -1.0, 'pl': 4.0, 'xs31': -2.0, 'fb3': 4.0, 'idc': 1.0, 'w21': 0.5, 'wo4': -0.5, 'so01': 4.0,
+         'm3d': 0.5, 'ft1': -2.5, 'cm': -1.0, 'kmin0': -2.0, 'yy210': -1.5, 'm1d': 0.5, 'yy001': -2.0, 'qu1c': 0.5, 'xin1': -2.5, 'yt01': 1.0,
+         'cm1': 4.0, 'yy121': -1.0, 'yy021': -2.0, 'yy230': -0.5, 'yy220': -1.0, 'kat0': 12.5, 'flz': 9, 'ka0': 9, 'rid': 10, 'c4': 12, 'cb1': 10,
+         'thr0': 8, 'kb1': 2, 'eb1s': 6, 'cde': 1.0, 'pi3': -1.0, 'yy120': -2.0, 'lrow': -2.0, 'rev': 0.2, 'ft0': 4.0, 'off': -0.5, 'yy111': -0.5,
+         'mi2': 0.2, 'lc1': 4.0, 'wo0': 0.5, 'r16b': -0.2, 'yo0': -0.5, 'fa3': 1.0, 'eb0c': 2.0, 'slotc': 1.0, 'slots': 1.0, 'ft3': 2.0,
+         'rho': -1.0, 'eft0': -0.5, 'yy320': 1.0, 'qws': 0.2, 'wa1': 1.0, 'qy0': 0.2, 'qu1s': 0.2, 'mtp': 4.0}
+SPARE = {'thr1': 0.3, 'y3231': 1.0, 'yy131': 0.6, 'y3221': 1.0, 'y3211': 0.3, 'kat20': 0.3, 'thr0': 1.0, 'c4': 0.3, 'sc3': 1.0, 'c': 0.3,
+         'sc2': 1.0, 'kat31': -0.3, 'fh0': 2, 'fh1': 2, 'fh2': 2, 'fh3': 2}
+SPAN = [0.0]
+
+
+def name(k):
+    return k[0] + k[2:] if k[0] == "t" and k[2:3] == "_" else k[:4] + k[5:] if k[:4] in ("slot", "land") else k[:2] if k[:2] in ("pk", "ls") else k
+
+
+def schedule(ops):
+    n = len(ops)
+    succ = [[] for _ in range(n)]
+    for i, o in enumerate(ops):
+        for d in o["deps"]:
+            succ[d].append(i)
+    rank = [0.0] * n
+    for i in range(n - 1, -1, -1):
+        c = min(a[1] + a[2] for a in ops[i]["alts"].values())
+        rank[i] = c + LAT + max([rank[j] for j in succ[i]] + [0.0])
+    pri = [rank[i] + EARLY.get(ops[i]["key"], 0.0) for i in range(n)]
+    for i in range(n - 1, -1, -1):
+        pri[i] = max([pri[i]] + [pri[j] + 1e-3 for j in succ[i]])
+    busy = {}
+    done, eng, start = [0.0] * n, [None] * n, [0.0] * n
+    for i in sorted(range(n), key=lambda k: -pri[k]):
+        best = None
+        for e, (fn, hold, tail) in ops[i]["alts"].items():
+            t = 0.0
+            for d, raw in ops[i]["deps"].items():
+                t = max(t, done[d] + LAT if raw or eng[d] != e else start[d] + 1e-6)
+            for a, b in busy.get(e, []):
+                if t + hold <= a:
+                    break
+                t = max(t, b)
+            val = t + hold + tail + (SPARE.get(ops[i]["key"], 0.0) if e == "V" else 0.0)
+            if best is None or val < best[4]:
+                best = (t + hold + tail, t, e, hold, val)
+        done[i], start[i], eng[i] = best[0], best[1], best[2]
+        busy.setdefault(best[2], []).append((best[1], best[1] + best[3]))
+        busy[best[2]].sort()
+    SPAN[0] = max(done)
+    return sorted((start[i], i, eng[i]) for i in range(n))
+
+
+def rank_program(g, core, T, topo):
+    rank = T.rank_of(core)
+    if rank is None:
+        return
+    nxt = T.cores[(rank + 1) % len(T.cores)]
+    rid, pid, _ = topo.addr(nxt)
+    mask = topo.mask(core, nxt)
+    neng = len(topo.engines(core, nxt))
+    V, S = g.vector, g.scalar
+    ops, lastw, readers = [], {}, {}
+
+    def add(alts, rd, wr, sem=None, arrive=None):
+        deps = {}
+        for k in wr:
+            for d in ([lastw[k]] if k in lastw else []) + readers.get(k, []):
+                deps[d] = k[0] != "#"
+        for k in rd:
+            if k[0] == "#":
+                for d in readers.get(k, [])[-1:]:
+                    deps.setdefault(d, False)
+        for k in rd:
+            if k in lastw:
+                deps[lastw[k]] = True
+        for k in rd:
+            readers.setdefault(k, []).append(len(ops))
+        for k in wr:
+            lastw[k] = len(ops)
+            readers[k] = []
+        ops.append({"alts": alts, "deps": deps, "sem": sem, "arrive": arrive, "key": name(wr[0] if wr[:1] and wr[0][0] != "#" else rd[0])})
+
+    def w(ap):
+        return ap.shape[1]
+
+    def vc(n, f=1.0):
+        return max(64, n * f) * CY + OV
+
+    def ts(out, in0, s1, o0, rd, wr, s2=None, o1=None, f=1.0):
+        if o1 is None:
+            add({"V": (lambda: V.tensor_scalar(out, in0, s1, None, o0), vc(w(out), f), 0)}, rd, wr)
+        else:
+            add({"V": (lambda: V.tensor_scalar(out, in0, s1, s2, o0, o1), vc(w(out), f), 0)}, rd, wr)
+
+    def tt(out, a, b, o, rd, wr, f=2.0):
+        add({"V": (lambda: V.tensor_tensor(out, a, b, o), vc(w(out), f), 0)}, rd, wr)
+
+    def cp(out, a, rd, wr, f=1.0):
+        add({"V": (lambda: V.tensor_copy(out, a), vc(w(out), f), 0)}, rd, wr)
+
+    def mv(out, a, rd, wr, scale=None, f=1.0, on="VS"):
+        n, alts = w(out), {}
+        if "V" in on:
+            alts["V"] = ((lambda: V.tensor_copy(out, a)) if scale is None else (lambda: V.tensor_scalar(out, a, scale, None, A.mult)), vc(n, f), 0)
+        if "S" in on:
+            alts["S"] = ((lambda: S.activation(out, a, AF.Copy)) if scale is None else (lambda: S.activation(out, a, AF.Copy, scale=scale)), vc(n), 0)
+        if "G" in on:
+            alts["G"] = (lambda: g.affine_select(out, a, [[0, n]], A.is_ge, 0.0, 0, 0), 0.24 + 2 * n * CY + OV, 0)
+        add(alts, rd, wr)
+
+    def lin(out, a, k, c, rd, wr):
+        add({"V": (lambda: V.tensor_scalar(out, a, k, c, A.mult, A.add), vc(w(out)), 0),
+             "S": (lambda: S.activation(out, a, AF.Identity, bias=c, scale=k), vc(w(out)), 0)}, rd, wr)
+
+    def ms(ap, v, wr, f=1.0, s=True):
+        alts = {"V": (lambda: V.memset(ap, v), vc(w(ap), f), 0)}
+        if s and w(ap) <= 128:
+            alts["S"] = (lambda: S.activation(ap, T.tj[:, 0:w(ap)], AF.Identity, bias=float(v), scale=0.0), vc(w(ap)), 0)
+        add(alts, ["tj"] if len(alts) > 1 else [], wr)
+
+    def scan(out, d0, d1, init, o0, o1, rd, wr):
+        add({"V": (lambda: V.tensor_tensor_scan(out, d0, d1, init, o0, o1), vc(w(out)), 0)}, rd, wr)
+
+    def act(out, a, rd, wr, fn, extra=0.0, **kw):
+        add({"S": (lambda: S.activation(out, a, fn, **kw), vc(w(out)) + extra, 0)}, rd, wr)
+
+    def iota(out, pat, base, ch, wr, flag=True):
+        fn = (lambda: g.iota(out, pat, base, ch, allow_small_or_imprecise_dtypes=True)) if flag else (lambda: g.iota(out, pat, base, ch))
+        add({"G": (fn, 0.13 + 2 * w(out) * CY + OV, 0)}, [], wr)
+
+    def asel(out, a, pat, cmp, fill, base, ch, rd, wr):
+        add({"G": (lambda: g.affine_select(out, a, pat, cmp, fill, base, ch), 0.17 + 2 * w(out) * CY + OV, 0)}, rd, wr)
+
+    def quant(nm, a, b, tile, rd, wr):
+        add({"V": (lambda: V.quantize_mx(T[nm + "c"][:, a:b], T[nm + "s"][:, a:b], tile[:, 4 * a:4 * b]), 0.012 + 0.001 * (b - a) + OV, 0)}, rd, wr)
+
+    def mm(bank, st, sa, mo, ma, n, rd, start=True, stop=True):
+        add({"P": (lambda: g.tensor.matmul_mx(T.ps[:, 512 * bank:512 * bank + n], T[st + "c"][:, sa:sa + 128], T[st + "s"][:, sa:sa + 128],
+                                              T[mo + "c"][:, ma:ma + n], T[mo + "s"][:, ma:ma + n], start, stop), (n + 16) * PE, 0)}, rd, ["#%d" % bank])
+
+    def ps(bank, a, b, p=128):
+        return T.ps[0:p, 512 * bank + a:512 * bank + b]
+
+    def pick(dst, src, n, wd, off, rd, a=0, key=None):
+        add({"V": (lambda: V.tensor_copy(T[dst + "c"][:, a:a + n].bitcast(dt.uint32), T[src + "c"][:, 0:wd].bitcast(dt.uint32).indirect(off)),
+                   0.08 + 1.56 * n * CY, 0)}, rd, [(key or dst) + "c"])
+        add({"S": (lambda: S.activation(T[dst + "s"][:, a:a + n], T[src + "s"][:, 0:wd].indirect(off), AF.Copy), 0.09 + 1.56 * n * CY, 0)},
+            rd, [(key or dst) + "s"])
+
+    def dma(on, sem, out, in_, rd, wr, t=2.2):
+        qs = {"Y": g.sync, "S": S}
+        add({e: (lambda e=e: qs[e].dma_start(out, in_), 0.08, t) for e in on}, rd, wr, sem)
+
+    def send(out, in_, sem, n, rd, wr, t):
+        add({"G": (lambda: g.remote_dma(out, in_, T.sem[sem], T.sem.sent, pid, rid, mask), 0.4, t)}, rd, wr, None, (sem, n * neng))
+
+    dma("Y", "du", T.ut[:], T.u[:], [], ["ut"], 1.8)
+    dma("Y", "dx0", T.xin[:, 0:1024], T.x[:, 0:1024], [], ["xin0"], 2.4)
+    dma("S", "dx1", T.xin[:, 1024:1792], T.x[:, 1024:1792], [], ["xin1"], 2.4)
+    dma("Y", "dwc", T.qwc[:].bitcast(dt.uint8), T.wc[:], ["xin0"], ["qwc"])
+    dma("Y", "dws", T.qws[:], T.ws[:], ["xin0"], ["qws"])
+    dma("Y", "dv", T.vt[:], T.v[:], ["xin0"], ["vt"])
+
+    iota(T.pi[:, 0:1], [[0, 1]], 0, 1, ["pi0"], False)
+    iota(T.tj[:], [[1, 128]], 0, -1, ["tj"])
+    iota(T.k72[:, 0:36], [[0, 4], [16, 9]], 0, 0, ["k72a"])
+    iota(T.k72[:, 36:72], [[0, 4], [1, 9]], 0, 0, ["k72b"])
+    iota(T.kd[:, 0:32], [[0, 4], [-1, 8]], -1, 0, ["kd"])
+    iota(T.th[:, 0:64], [[1, 4], [7, 8], [1, 2]], -7, 0, ["tha"])
+    iota(T.th[:, 64:128], [[1, 4], [-7, 8], [1, 2]], 49, 0, ["thb"])
+    iota(T.kv[:, 0:64], [[16, 4], [1, 8], [128, 2]], -1, 0, ["kva"])
+    iota(T.kv[:, 64:128], [[16, 4], [-1, 8], [128, 2]], 7, 0, ["kvb"])
+    iota(T.ios[:], [[16, 12], [0, 2], [1, 16]], 0, 0, ["ios"])
+    for k in range(4):
+        iota(T.ioh[:, 32 * k:32 * k + 32], [[16, 2], [1, 8], [32, 2]], 64 * k, 0, ["ioh%d" % k])
+    iota(T.w1[:, 0:8], [[-1, 2], [16, 4]], 0, 0, ["w1a"])
+    iota(T.w1[:, 8:16], [[16, 8]], 0, 0, ["w1b"])
+    iota(T.idc[:], [[16, 4], [-112, 8]], 784 + 1536 - int(BIG), 0, ["idc"])
+    IOH = ["ioh%d" % k for k in range(4)]
+    ms(T.xin[:, 1792:2048], 0.0, ["xinp"], 0.5)
+    ms(T.xs[:, 1792:2048], 0.0, ["xsp"], 0.5)
+    ms(T.u1l[:], 1, ["u1l"], s=False)
+    ms(T.ul[:], 1, ["ul"], s=False)
+    ts(T.pi[:, 1:2], T.pi[:, 0:1], 15, A.bitwise_and, ["pi0"], ["pi1"])
+    ts(T.pi[:, 2:3], T.pi[:, 0:1], 7, A.bitwise_and, ["pi0"], ["pi2"])
+    ts(T.pi[:, 3:4], T.pi[:, 0:1], 3, A.arith_shift_right, ["pi0"], ["pi3"])
+    ts(T.pi[:, 4:5], T.pi[:, 0:1], 5, A.arith_shift_right, ["pi0"], ["pi4"], 1, A.bitwise_and)
+    ts(T.pi[:, 5:6], T.pi[:, 0:1], 6, A.arith_shift_right, ["pi0"], ["pi5"])
+    cp(T.pv[:, 0:5], T.pi[:, 1:6], ["pi1", "pi2", "pi3", "pi4", "pi5"], ["pv"])
+    ts(T.w2[:, 0:1], T.pv[:, 0:1], 8.0, A.is_lt, ["pv"], ["w20"], T.pv[:, 0:1], A.mult)
+    ts(T.w2[:, 1:2], T.pv[:, 0:1], 8.0, A.is_ge, ["pv"], ["w21"])
+    ts(T.ul[:, 0:1], T.w2[:, 0:1], 16.0, A.mult, ["w20", "w21"], ["ul"], T.w2[:, 1:2], A.add)
+    quant("qu", 0, 128, T.ut, ["ut"], ["qu"])
+    pick("qup", "qu", 128, 128, T.ul[:, 0:8], ["qu", "ul"])
+    pick("qu1", "qu", 128, 128, T.u1l[:, 0:8], ["qu", "u1l"])
+    quant("qv", 0, 128, T.vt, ["vt"], ["qv"])
+    ms(T.mt[64:128, 3:1792:4], 0.0, ["mtp"], 0.5)
+    ms(T.mt[:, 1792:2048], 0.0, ["mtp2"], 0.5)
+    ts(T.ctri[:], T.tj[:], 0.0, A.is_gt, ["tj"], ["ctri"], 2.0 ** -100, A.mult)
+    ms(T.kat[:, 0:512], 1.0, ["kat0"], 0.5)
+    quant("ka", 0, 128, T.kat, ["kat0"], ["ka0"])
+    one = T.kat[:, 0:128]
+    asel(T.nar[:, 0:128], one, [[1, 128]], A.is_ge, 0.0, 0, -1, ["kat0"], ["tri"])
+    asel(T.nar[:, 128:256], T.nar[:, 0:128], [[-8, 16], [0, 8]], A.is_ge, 0.0, 0, 1, ["tri"], ["blk"])
+    asel(T.nar[:, 256:384], T.nar[:, 128:256], [[1, 128]], A.not_equal, -8.0, 0, -1, ["blk"], ["del"])
+    for t in range(4):
+        mv(T.kat[:, 512 + t:1024:4], T.nar[:, 0:128], ["tri"], ["kat1%d" % t], f=0.5)
+        mv(T.kat[:, 1024 + t:1536:4], T.nar[:, 256:384], ["del"], ["kat2%d" % t], f=0.5)
+        ms(T.kat[:, 1536 + t:2048:4], 1.0 if t < 2 else 0.5, ["kat3%d" % t], 0.5)
+    quant("ka", 128, 512, T.kat, ["kat%d%d" % (a, t) for a in (1, 2, 3) for t in range(4)], ["ka1"])
+    ms(T.flt[:], 0.0, ["flz", "fa3", "fb3"], 0.5)
+    ms(T.thr[:], -1.0, ["thr%d" % t for t in range(4)] + ["thc%d" % t for t in range(4)])
+    for t in range(4):
+        ms(T.thr[:, 72 * t:72 * t + 8], float(NF), ["thr%d" % t])
+        if t < 3:
+            ms(T.thr[:, 72 * t + 40:64 * t + 64], float(NF), ["thc%d" % t])
+    ms(T.k72[:, 80:152], 0.0, ["k72d"])
+    ms(T.k72[:, 80:152:9], -1e29, ["k72d"])
+    ms(T.hs[:], 1.0, ["hs"])
+    ms(T.hs[:, 0:72:9], 0.0, ["hs"])
+    ms(T.cmx[:, 0:1], 0.0, ["cmx0"])
+    ms(T.kd[:, 32:64], 0.25, ["kdr"])
+    ms(T.kd[:, 32:64:8], 0.0, ["kdr"])
+    ms(T.lc[:, 0:1], 0.25, ["lc0"], s=False)
+    act(T.lc[:, 1:2], T.lc[:, 0:1], ["lc0"], ["lc1"], AF.Ln, 1.3)
+    add({"V": (lambda: V.reciprocal(T.lc[:, 2:3], T.lc[:, 1:2]), 0.22, 0)}, ["lc1"], ["lc"])
+    for b in range(4):
+        asel(T.eft[:, 512 * b:512 * b + 512], T.kat[:, 0:512], [[-256, 4], [-1, 32], [256, 4]], A.is_equal, 0.0, -32 * b, 1, ["kat0"], ["eft%d" % b])
+        quant("ef", 128 * b, 128 * b + 128, T.eft, ["eft%d" % b], ["ef%d" % b])
+    for e in range(2):
+        iota(T.ebi[:, e:64:2], [[128, 4], [16, 2], [32, 4]], 0, 0, ["ebi%d" % e])
+    ts(T.ebl[:], T.ebi[:], T.pv[:, 0:1], A.add, ["ebi0", "ebi1", "pv"], ["ebl"])
+    for b in range(4):
+        pick("eb", "ef", 256, 512, T.ebl[:, 16 * b:16 * b + 16], ["ef%d" % j for j in range(4)] + ["ebl"], 256 * b, "eb%d" % b)
+    lin(T.w2[:, 8:16], T.w1[:, 0:8], 1.0, T.pv[:, 2:3], ["w1a", "pv"], ["c"])
+    lin(T.w2[:, 16:24], T.w2[:, 8:16], 1.0 / 7.0, -3.0 / 7.0, ["c"], ["mf"])
+    lin(T.w2[:, 72:76], T.w2[:, 8:12], 1.0, -4.0, ["c"], ["c4"])
+    cp(T.wi[:, 0:8], T.w2[:, 16:24], ["mf"], ["mi"])
+    ts(T.w2[:, 56:64], T.wi[:, 0:8], -7.0, A.mult, ["mi"], ["m7"])
+    tt(T.w2[:, 24:32], T.w2[:, 56:64], T.w2[:, 8:16], A.add, ["m7", "c"], ["rho"])
+    ts(T.w2[:, 32:40], T.w2[:, 24:32], 4.0, A.is_ge, ["rho"], ["y128"], 128.0, A.mult)
+    lin(T.cb[:, 0:4], T.w2[:, 32:36], 1.0, T.pv[:, 1:2], ["y128", "pv"], ["cb0"])
+    ts(T.cb[:, 4:8], T.w2[:, 36:40], T.pv[:, 1:2], A.add, ["y128", "pv"], ["cb1"], 8.0, A.add)
+    lin(T.w2[:, 40:44], T.w2[:, 24:28], 16.0, 0.0, ["rho"], ["r16a"])
+    lin(T.w2[:, 44:48], T.w2[:, 28:32], 16.0, 128.0, ["rho"], ["r16b"])
+    ts(T.w2[:, 48:56], T.w2[:, 24:32], 4.0, A.is_ge, ["rho"], ["y64"], -64.0, A.mult)
+    tt(T.w2[:, 64:72], T.w2[:, 40:48], T.wi[:, 0:8], A.add, ["r16a", "r16b", "mi"], ["r17"])
+    tt(T.cb[:, 8:16], T.w2[:, 64:72], T.w2[:, 48:56], A.add, ["r17", "y64"], ["rid"])
+    for a in range(2):
+        for t in range(4):
+            ts(T.kbt[:, 512 * a + t:512 * a + 512:4], T.kv[:], T.cb[:, 8 + 4 * a + t:9 + 4 * a + t], A.is_equal,
+               ["kva", "kvb", "rid"], ["kb%d%d" % (a, t)], f=0.5)
+            ts(T.kbt[:, 1024 + 512 * a + t:1536 + 512 * a:4], T.th[:], T.w2[:, (72 if a else 8) + t:(73 if a else 9) + t], A.is_gt,
+               ["tha", "thb", "c", "c4"], ["kb%d%d" % (2 + a, t)], f=0.5)
+    quant("kb", 0, 256, T.kbt, ["kb%d%d" % (a, t) for a in (0, 1) for t in range(4)], ["kb0"])
+    quant("kb", 256, 512, T.kbt, ["kb%d%d" % (a, t) for a in (2, 3) for t in range(4)], ["kb1"])
+    ms(T.kmin[:, 0:128:2], 255.0, ["kmin0"])
+    ms(T.kmin[:, 1:128:2], -1.0, ["kmin1"])
+    ms(T.kmin[:, 128:160:2], 0.0, ["kpk0"])
+    ms(T.kmin[:, 129:160:2], 256.0, ["kpk1"])
+    ms(T.kst[:, 0:32], -float(NF), ["kst0"])
+    ms(T.kst[:, 32:64], float(NF), ["kst1"])
+    ms(T.kst[:, 0:64:8], 2 * BIG, ["kst0", "kst1"])
+    lin(T.w2[:, 2:3], T.pv[:, 3:4], 896.0, T.pv[:, 0:1], ["pv"], ["w22"])
+    lin(T.w2[:, 3:4], T.pv[:, 4:5], 64.0, T.w2[:, 2:3], ["pv", "w22"], ["w23"])
+    lin(T.idc[:], T.idc[:], 1.0, T.w2[:, 3:4], ["idc", "w23"], ["idc"])
+    n_ = T.w1[:, 16:24]
+    lin(n_, T.w1[:, 8:16], 1.0, T.pv[:, 0:1], ["w1b", "pv"], ["n"])
+    lin(T.w2[:, 4:5], T.pv[:, 1:2], -2.0, 7.0, ["pv"], ["w24"])
+    ts(T.rev[:], T.w1[:, 16:18], T.w2[:, 4:5], A.add, ["n", "w24"], ["rev"])
+    lin(T.w1[:, 40:48], n_, 1.0 / 7.0, -3.0 / 7.0, ["n"], ["mf2"])
+    cp(T.wi[:, 8:16], T.w1[:, 40:48], ["mf2"], ["mi2"])
+    ts(T.w1[:, 64:72], T.wi[:, 8:16], -57.0, A.mult, ["mi2"], ["m72"])
+    lin(T.w1[:, 72:80], n_, 8.0, 7.0, ["n"], ["r8"])
+    ts(T.w1[:, 80:88], n_, 56.0, A.is_ge, ["n"], ["b32"], 72.0, A.mult)
+    tt(T.w1[:, 72:80], T.w1[:, 72:80], T.w1[:, 64:72], A.add, ["r8", "m72"], ["r8"])
+    tt(T.w1[:, 88:96], T.w1[:, 72:80], T.w1[:, 80:88], A.add, ["r8", "b32"], ["o2"])
+    cp(T.ordr[:], T.w1[:, 88:96], ["o2"], ["ordr"])
+
+    H = len(CUTS) - 1
+
+    def quant_x(r, tile, h, rd):
+        last = h == H - 1 and r < R
+        quant("t%d" % r, CUTS[h], 512 if last else CUTS[h + 1], tile, rd, ["t%d_%d" % (r, h)])
+
+    for h in range(H):
+        quant_x(0, T.xin, h, ["xin0", "xinp"] + (["xin1"] if CUTS[h + 1] > 256 else []))
+
+    for r in range(R):
+        t_ = "t%d" % r
+        TA = ["%s_%d" % (t_, h) for h in range(H)]
+
+        def tk(a, b):
+            return ["%s_%d" % (t_, h) for h in range(H) if CUTS[h] < b and a < CUTS[h + 1]]
+        for t, bk in enumerate((0, 1, 4, 5)):
+            mm(bk, t_, 128 * t, "qup", 0, 128, tk(128 * t, 128 * t + 128) + ["qupc", "qups"])
+            mv(T.sc[:, 9 * t:9 * t + 9], ps(bk, 0, 9), ["#%d" % bk], ["sc%d" % t])
+        for bk, a, z in ((2, 0, 256), (3, 0, 256), (6, 256, C), (7, 256, C)):
+            mm(bk, "qu1", 0, t_, a, z - a, tk(a, z) + ["qu1c", "qu1s"])
+
+        def si(t, p=128):
+            return T.sc[0:p, 9 * t + 8:9 * t + 9]
+
+        def mt(t, a, b, p=128):
+            return T.mt[0:p, 4 * a + t:4 * b:4]
+        act(T.dd[:, 896:1024], ps(3, 0, 128), ["#3", "sc0"], ["d0"], AF.Identity, bias=si(0), scale=-1.0)
+        act(T.dd[:, 1024:1152], ps(3, 128, 256), ["#3", "sc1"], ["d1"], AF.Identity, bias=si(1), scale=-1.0)
+        act(T.dd[:, 256:448], ps(7, 0, 192), ["#7", "sc2"], ["d2"], AF.Identity, bias=si(2), scale=-1.0)
+        act(T.dd[0:64, 704:896], ps(7, 0, 192, 64), ["#7", "sc3"], ["d3"], AF.Identity, bias=si(3, 64), scale=-1.0)
+        act(T.dd[:, 0:256], ps(3, 0, 256), ["#3", "sc2"], ["d2a"], AF.Identity, bias=si(2), scale=-1.0)
+        act(T.dd[0:64, 448:704], ps(3, 0, 256, 64), ["#3", "sc3"], ["d3a"], AF.Identity, bias=si(3, 64), scale=-1.0)
+        ts(mt(0, 128, 256), ps(2, 128, 256), si(0), A.is_ge, ["#2", "sc0"], ["m0q"])
+        ts(mt(1, 0, 128), ps(2, 0, 128), si(1), A.is_gt, ["#2", "sc1"], ["m1l"])
+        ts(mt(0, 256, C), ps(6, 0, 192), si(0), A.is_ge, ["#6", "sc0"], ["m0r"])
+        ts(mt(1, 256, C), ps(6, 0, 192), si(1), A.is_ge, ["#6", "sc1"], ["m1r"])
+        tt(mt(0, 0, 128), T.dd[:, 896:1024], T.ctri[:], A.is_lt, ["d0", "ctri"], ["m0d"])
+        tt(mt(1, 128, 256), T.dd[:, 1024:1152], T.ctri[:], A.is_lt, ["d1", "ctri"], ["m1d"])
+        ts(mt(2, 0, 256), T.dd[:, 0:256], 0.0, A.is_lt, ["d2a"], ["m2l"], f=0.5)
+        ts(mt(2, 384, C), T.dd[:, 384:448], 0.0, A.is_le, ["d2"], ["m2r"], f=0.5)
+        tt(mt(2, 256, 384), T.dd[:, 256:384], T.ctri[:], A.is_lt, ["d2", "ctri"], ["m2d"])
+        ts(mt(3, 0, 384, 64), T.dd[0:64, 448:832], 0.0, A.is_lt, ["d3", "d3a"], ["m3l"], f=0.5)
+        tt(mt(3, 384, C, 64), T.dd[0:64, 832:896], T.ctri[0:64, 0:64], A.is_lt, ["d3", "ctri"], ["m3d"])
+        SC = ["sc0", "sc1", "sc2", "sc3"]
+        mv(T.sc[:, 36:72], T.sc[:, 0:36], SC, ["scn"], -1.0)
+        quant("m", 0, 512 if r == 0 else C, T.mt, ["m0q", "m0r", "m1l", "m1r", "m2l", "m2r", "m2d", "m0d", "m1d", "m3l", "m3d", "mtp", "mtp2"], ["m"])
+        for t in range(4):
+            mm(t, "m", 128 * t, "ka", 0, 128, ["m", "ka0"])
+        scan(T.cmx[:, 1:73], T.k72[:, 80:152], T.sc[:, 0:72], -1e29, A.add, A.max, SC + ["scn", "k72d"], ["cmx"])
+        tt(T.rr[:, 0:72], T.sc[:, 0:72], T.cmx[:, 0:72], A.is_gt, SC + ["scn", "cmx", "cmx0"], ["rr"])
+        tt(T.rr[:, 0:72], T.rr[:, 0:72], T.k72[:, 0:72], A.mult, ["rr", "k72a", "k72b"], ["rr"])
+        scan(T.cm2[:, 0:72], T.hs[:, 0:72], T.rr[:, 0:72], 0.0, A.mult, A.max, ["rr", "hs"], ["cm2"])
+        tt(T.cde[:, 0:4], T.cm2[:, 7:36:9], T.cm2[:, 43:72:9], A.subtract, ["cm2"], ["cde"])
+        tt(T.cde[:, 8:12], T.cde[:, 0:4], T.cb[:, 0:4], A.add, ["cde", "cb0"], ["cd0"])
+        tt(T.cde[:, 12:16], T.cde[:, 0:4], T.cb[:, 4:8], A.add, ["cde", "cb1"], ["cd1"])
+        for b in range(4):
+            mm(6 + b % 2, "ef", 128 * b, t_, 0, C, ["ef%d" % b] + TA)
+            o = 3072 + 896 * (b // 2) + b % 2
+            mv(T.win[:, o:3072 + 896 * (b // 2 + 1):2], ps(6 + b % 2, 0, C), ["#%d" % (6 + b % 2)], ["ft%d" % b], 0.5, on="S")
+        for k in range(4):
+            mv(T.fh[:, C * k:C * k + C], T.win[:, 3072 + C * k:3072 + C * k + C], ["ft%d" % (k & 2), "ft%d" % (k | 1)], ["fh%d" % k], f=0.5, on="VSG")
+        for t in range(4):
+            p = 128 if t < 3 else 64
+            tt(T.flt[0:p, t:256:4], ps(t, 0, 64, p), T.thr[0:p, 64 * t:64 * t + 64], A.is_lt, ["#%d" % t, "flz", "thr%d" % t, "thc%d" % t], ["fa%d" % t], 1.0)
+            act(T.flt[0:p, 512 + t:768:4], T.tj[0:p, 0:64], ["fa%d" % t, "tj"], ["fb%d" % t], AF.Identity, bias=T.flt[0:p, 33 * t:33 * t + 1], scale=0.0)
+        quant("fl", 0, 128, T.flt, ["fa%d" % t for t in range(4)], ["fl0"])
+        quant("fl", 128, 256, T.flt, ["fb%d" % t for t in range(4)], ["fl1"])
+        mm(5, "ka", 128, "fl", 0, 128, ["fl0", "ka1"], True, False)
+        mm(5, "ka", 0, "fl", 32, 128, ["fl0", "fl1"] if r == 0 else ["fl0"], False, True)
+        mm(4, "ka", 256, "fl", 0, 128, ["fl0", "ka1"])
+        act(T.pn[:, 0:2], T.ps[:, 2560 + 16:2560 + 32:8], ["#5"], ["pn"], AF.Identity, bias=0.5, scale=-1.0)
+        for t in (0, 1):
+            ts(T.cmt[:, t:1536:4], T.ios[:], ps(5, 8 * t, 8 * t + 1), A.is_ge, ["#5", "ios"], ["cm%d" % t], f=0.5)
+        for t in (2, 3):
+            act(T.cmt[:, t:1536:4], T.ios[:], ["pn", "ios"], ["cm%d" % t], AF.Sign, bias=T.pn[:, t - 2:t - 1])
+        quant("cm", 0, 384, T.cmt, ["cm%d" % t for t in range(4)], ["cm"])
+        mm(1, "ka", 384, "cm", 0, 384, ["cm", "ka1"])
+        mm(0, "fl", 128, "kb", 256, 128, ["fl1", "kb1"], True, False)
+        mm(0, "fl", 64, "kb", 384, 128, ["fl0", "fl1", "kb1"], False, True)
+        tt(T.eq[:], ps(4, 0, 32), T.kd[:, 0:32], A.is_equal, ["#4", "kd"], ["eq"], 1.0)
+        scan(T.wv[:], T.kd[:, 32:64], T.eq[:], 0.0, A.mult, A.add, ["eq", "kdr"], ["wv"])
+        add({"V": (lambda: V.transpose(T.lrow[:], ps(1, 0, 384)), vc(384), 0)}, ["#1"], ["lrow"])
+        ts(T.pl[:], T.lrow[:, 0:384:32], 128.0, A.add, ["lrow"], ["pl"])
+        sl, ld = "slot%d" % r, "land%d" % r
+        pick(sl, t_, NF, 512, T.pl[:, 0:12], TA + ["pl"])
+        send(T[ld + "c"][:].bitcast(dt.uint8), T[sl + "c"][:].bitcast(dt.uint8), "ac%d" % r, 2, [sl + "c"], [ld + "c"], 2.2)
+        send(T[ld + "s"][:], T[sl + "s"][:], "ac%d" % r, 2, [sl + "s"], [ld + "s"], 1.8)
+        for bor in range(2):
+            for t in range(4):
+                ts(T.sot[:, 512 * bor + t:512 * bor + 512:4], T.ioh[:], T.cde[:, 8 + 4 * bor + t:9 + 4 * bor + t], A.is_equal,
+                   IOH + ["cd%d" % bor, "wv"], ["so%d%d" % (bor, t)], T.wv[:, 8 * t + 7:8 * t + 8], A.mult, 0.5)
+        quant("so", 0, 256, T.sot, ["so%d%d" % (b, t) for b in range(2) for t in range(4)], ["so"])
+        mm(2, "so", 0, "kb", 0, 128, ["so", "kb0"], True, False)
+        mm(2, "so", 128, "kb", 128, 128, ["so", "kb0"], False, True)
+        act(T.ln[:], ps(2, 0, 128), ["#2", "lc1"], ["ln"], AF.Ln, bias=2.0 ** -62)
+        ts(T.lev[:], T.ln[:], T.lc[:, 2:3], A.mult, ["ln", "lc"], ["lev"], 0.3, A.add)
+        act(T.nb[:], T.ln[:], ["ln"], ["nb"], AF.Relu, bias=-2000.0, scale=-100.0)
+        tt(T.cand[:], ps(0, 0, 128), T.lev[:], A.add, ["#0", "lev"], ["cand"], 1.0)
+        tt(T.cand[:], T.cand[:], T.nb[:], A.add, ["cand", "nb"], ["cand"])
+        scan(T.sm[:], T.kmin[:, 0:128], T.cand[:], 0.0, A.max, A.min, ["cand", "kmin0", "kmin1"], ["sm"])
+        scan(T.pkf[:], T.kmin[:, 128:160], T.sm[:, 65:128:2], 0.0, A.mult, A.add, ["sm", "kpk0", "kpk1"], ["pkf"])
+        cp(T["pk%d" % r][:], T.pkf[:, 1:32:2], ["pkf"], ["pk%d" % r])
+        send(T["lst%d" % r][:], T["pk%d" % r][:], "al%d" % r, 1, ["pk%d" % r], ["lst%d" % r], 1.6)
+
+        def unpack(src, base, key, banks, on):
+            for k in range(8):
+                bk = banks[k % len(banks)]
+                mm(bk, "eb", 128 * k, src, 0, NF, [src + "c", src + "s", "eb%dc" % (k // 2), "eb%ds" % (k // 2)])
+                o = base + NF * (7 - k)
+                mv(T.win[:, o:o + NF], ps(bk, 0, NF), ["#%d" % bk], ["%s%d" % (key, k)], 0.5, on=on)
+        unpack(sl, 0, "wo", (3, 4, 5), "S")
+        ts(T.ko[:], T.sm[:, 1:64:2], float(NF), A.is_lt, ["sm"], ["ko"], -(BIG + NF), A.mult)
+        tt(T.ko[:], T.ko[:], T.sm[:, 1:64:2], A.add, ["ko", "sm"], ["ko"])
+        scan(T.kos[:], T.kst[:, 0:32], T.ko[:], 0.0, A.add, A.min, ["ko", "kst0"], ["kos"])
+        tt(T.own[:], T.kos[:, 0:32].indirect(T.rev[:, 0:2]), T.idc[:], A.min, ["kos", "rev", "idc"], ["own"], 3.0)
+        unpack(ld, 1536, "wa", (6, 7, 1, 2, 0), "SV")
+        cp(T.ai[:], T["lst%d" % r][:], ["lst%d" % r], ["ai"])
+        ts(T.a2[:, 0:32:2], T.ai[:], 8, A.arith_shift_right, ["ai"], ["a2h"])
+        ts(T.a2[:, 1:32:2], T.ai[:], 255, A.bitwise_and, ["ai"], ["a2l"])
+        ts(T.kn[:], T.a2[:], float(NF), A.is_lt, ["a2h", "a2l"], ["kn"], -BIG, A.mult)
+        tt(T.kn[:], T.kn[:], T.a2[:], A.add, ["kn", "a2h", "a2l"], ["kn"])
+        scan(T.kns[:], T.kst[:, 32:64], T.kn[:], 0.0, A.add, A.min, ["kn", "kst1"], ["kns"])
+        tt(T.res[:], T.kns[:], T.own[:], A.min, ["kns", "own"], ["res"])
+        for k in range(4):
+            o = 64 * (k % 2) + 32 * (k // 2)
+            mv(T.rep[0:32, o:o + 32], T.res[32 * k:32 * k + 32, :], ["res"], ["rep%d" % k])
+        for k in range(1, 4):
+            mv(T.rep[32 * k:32 * k + 32, :], T.rep[0:32, :], ["rep%d" % j for j in range(4)], ["rp%d" % k])
+        ts(T.off[:], T.rep[:, 0:128].indirect(T.ordr[:, 0:7]), 1536.0 + BIG, A.add,
+           ["rp1", "rp2", "rp3", "ordr"] + ["rep%d" % j for j in range(4)], ["off"], f=2.0)
+        WIN = ["ft%d" % b for b in range(4)] + ["%s%d" % (a, k) for a in ("wo", "wa") for k in range(8)]
+        for h in range(H):
+            a, z = CUTS[h], CUTS[h + 1]
+            for b1 in range(2):
+                lo, hi = 896 * b1 + 2 * a, 896 * b1 + 2 * z
+                tt(T.yt[:, lo:hi], T.win[:, 0:4864].indirect(T.off[:, lo // 16:hi // 16]), T.fh[:, lo:hi],
+                   A.add, WIN + ["off", "fh%d" % (2 * b1), "fh%d" % (2 * b1 + 1)], ["yt%d%d" % (b1, h)], 1.8)
+            for be in range(4):
+                for b in range(4):
+                    o = 896 * (be // 2)
+                    mv(T.yy[32 * be:32 * be + 32, 4 * a + b:4 * z:4], T.yt[32 * b:32 * b + 32, o + 2 * a + be % 2:o + 2 * z:2],
+                       ["yt%d%d" % (be // 2, h)], ["yy%d%d%d" % (be, b, h)], f=0.5, on="VSG")
+            quant("qy", a, z, T.yy, ["yy%d%d%d" % (i, b, h) for i in range(4) for b in range(4)], ["qy%d" % h])
+            for b in range(4):
+                bk = (4 * h + b) % 8
+                pl = slice(C * b + a, C * b + z)
+                mm(bk, "qw", 128 * b, "qy", a, z - a, ["qy%d" % h, "qwc", "qws"])
+                mv(T.y32[:, pl], T.yy[:, 4 * a + b:4 * z:4], ["yy%d%d%d" % (i, b, h) for i in range(4)], ["y32%d%d" % (b, h)], 32.0, 0.5)
+                tt(T.x32[:, pl], ps(bk, 0, z - a), T.y32[:, pl], A.add, ["#%d" % bk, "y32%d%d" % (b, h)], ["x32%d%d" % (b, h)], 1.0)
+                mv(T.xs[:, 4 * a + b:4 * z:4], T.x32[:, pl], ["x32%d%d" % (b, h)], ["xs%d%d" % (b, h)], 0.03125, 0.5)
+            quant_x(r + 1, T.xs, h, ["xs%d%d" % (b, h) for b in range(4)] + ["xsp"])
+
+    t_ = "t%d" % R
+    for h in range(H):
+        a, z = CUTS[h], CUTS[h + 1]
+        k_ = ["%s_%d" % (t_, h)]
+        mm(h, "qv", 0, t_, a, z - a, ["qv"] + k_)
+        dma("Y", "outs", T.oc[:, 4 * a:4 * z], T[t_ + "c"][:, a:z].bitcast(dt.uint8), k_, [])
+        mv(T.yo[:, a:z], ps(h, 0, z - a), ["#%d" % h], ["yo%d" % h])
+        dma("Y", "outs", T.y[:, a:z], T.yo[:, a:z], ["yo%d" % h], [])
+    for k in range(4):
+        dma("YS", "outs", T.osc[4 * k:4 * k + 4, :], T[t_ + "s"][32 * k:32 * k + 4, 0:C], ["%s_%d" % (t_, h) for h in range(H)], [], 1.8)
+
+    Q = {"V": V, "S": S, "P": g.tensor, "G": g, "Y": g.sync}
+    cnt, seen, tok, eng, knew, sent = {}, {e: {} for e in Q}, {}, {}, {}, 0
+    for _, i, e in schedule(ops):
+        o = ops[i]
+        for d, raw in sorted(o["deps"].items(), reverse=True):
+            if raw or eng[d] != e or ops[d]["sem"] or ops[d]["arrive"]:
+                s, v = tok[d]
+                if seen[e].get(s, 0) < v:
+                    Q[e].wait_ge(T.sem[s], v)
+                    seen[e][s] = v
+                    if not ops[d]["arrive"]:
+                        for s2, v2 in knew[d].items():
+                            seen[e][s2] = max(seen[e].get(s2, 0), v2)
+        if e == "G" and not o["arrive"] and len(o["alts"]) > 1 and seen[e].get(e, 0) < cnt.get(e, 0):
+            g.wait_ge(T.sem.G, cnt[e])
+            seen[e][e] = cnt[e]
+        ins = o["alts"][e][0]()
+        eng[i] = e
+        knew[i] = dict(seen[e])
+        if o["arrive"]:
+            tok[i] = o["arrive"]
+            sent += neng
+        else:
+            s, n = (o["sem"], 16) if o["sem"] else (e, 1)
+            cnt[s] = cnt.get(s, 0) + n
+            ins.then_inc(T.sem[s], n)
+            tok[i] = (s, cnt[s])
+    for s in cnt:
+        g.sync.wait_ge(T.sem[s], cnt[s])
+    g.wait_ge(T.sem.sent, sent)

@@ -2,7 +2,7 @@ from concourse.mybir import dt, AluOpType as A, ActivationFunctionType as AF
 
 C, NF, R = 448, 192, 3
 BIG = 8192.0
-CUTS = (0, 256, 448)
+CUTS = (0, 320, 448)
 Q4, U8, BF, F32, I32, U16 = "float8_e4m3fn_x4", "uint8", "bfloat16", "float32", "int32", "uint16"
 SCRATCH = {}
 
@@ -28,11 +28,12 @@ for _n, _w in (("qu", 128), ("qup", 128), ("qu1", 128), ("qv", 128), ("qw", 512)
     _q(_n, _w)
 for _n, _w in (("xin", 2048), ("xs", 2048), ("x32", 4 * C), ("ut", 512), ("vt", 512), ("eft", 2048), ("th", 128),
                ("kat", 2048), ("kbt", 2048), ("mt", 2048), ("flt", 1024), ("cmt", 1536), ("sot", 1024), ("dd", 1152), ("ctri", 128),
-               ("ios", 384), ("ioh", 128), ("kv", 128), ("win", 4864), ("yt", 4 * C), ("fh", 4 * C), ("yy", 4 * C), ("y32", 4 * C), ("nar", 384)):
+               ("ios", 384), ("ioh", 128), ("io4", 1024), ("kv", 128), ("win", 4864), ("yt", 4 * C), ("fh", 4 * C), ("yy", 4 * C),
+               ("y32", 4 * C), ("nar", 384)):
     _sb(_n, _w, BF)
 for _n, _w in (("sc", 80), ("cmx", 80), ("cm2", 80), ("rr", 80), ("hs", 80), ("cde", 16), ("k72", 160), ("thr", 256), ("ebi", 64), ("kd", 64),
                ("eq", 32), ("wv", 32), ("lrow", 384), ("ln", 128), ("nb", 128), ("cand", 128), ("sm", 128), ("kmin", 160),
-               ("pkf", 32), ("ko", 32), ("kos", 32), ("own", 32), ("kn", 32), ("kns", 32), ("res", 32), ("rep", 128), ("kst", 64), ("idc", 32),
+               ("pkf", 32), ("ko", 32), ("kos", 32), ("own", 32), ("kn", 32), ("kns", 32), ("rep", 128), ("kst", 64), ("idc", 32),
                ("cb", 16), ("w1", 96), ("w2", 80), ("pv", 8), ("yo", C), ("tj", 128), ("lc", 4), ("pn", 4)):
     _sb(_n, _w, F32)
 for _n, _w in (("lev", 128), ("ai", 16), ("a2", 32), ("pi", 8), ("wi", 16)):
@@ -40,17 +41,27 @@ for _n, _w in (("lev", 128), ("ai", 16), ("a2", 32), ("pi", 8), ("wi", 16)):
 for _n, _w in (("ul", 8), ("u1l", 8), ("pl", 12), ("rev", 2), ("ordr", 8), ("off", 112), ("ebl", 64)):
     _sb(_n, _w, U16)
 SCRATCH["ps"] = ("psum", [128, 4096], F32)
-SEMAPHORES = ["V", "S", "P", "G", "dx0", "dx1", "du", "dv", "dwc", "dws", "outs", "sent"] + \
+SEMAPHORES = ["V", "S", "P", "G", "dx0", "dx1", "du", "dv", "dwc", "dws", "outs", "sent", "dfh0", "dfh1"] + \
              ["%s%d" % (k, r) for k in ("ac", "al") for r in range(R)]
-CY, OV, LAT, PE = 0.001, 0.03, 0.07, 0.0008
-EARLY = {'ctri': 2.0, 'k72d': -1.0, 'm': -0.5, 'yy300': -1.0, 'pl': 4.0, 'xs31': -2.0, 'fb3': 4.0, 'idc': 1.0, 'w21': 0.5, 'wo4': -0.5, 'so01': 4.0,
-         'm3d': 0.5, 'ft1': -2.5, 'cm': -1.0, 'kmin0': -2.0, 'yy210': -1.5, 'm1d': 0.5, 'yy001': -2.0, 'qu1c': 0.5, 'xin1': -2.5, 'yt01': 1.0,
-         'cm1': 4.0, 'yy121': -1.0, 'yy021': -2.0, 'yy230': -0.5, 'yy220': -1.0, 'kat0': 12.5, 'flz': 9, 'ka0': 9, 'rid': 10, 'c4': 12, 'cb1': 10,
-         'thr0': 8, 'kb1': 2, 'eb1s': 6, 'cde': 1.0, 'pi3': -1.0, 'yy120': -2.0, 'lrow': -2.0, 'rev': 0.2, 'ft0': 4.0, 'off': -0.5, 'yy111': -0.5,
-         'mi2': 0.2, 'lc1': 4.0, 'wo0': 0.5, 'r16b': -0.2, 'yo0': -0.5, 'fa3': 1.0, 'eb0c': 2.0, 'slotc': 1.0, 'slots': 1.0, 'ft3': 2.0,
-         'rho': -1.0, 'eft0': -0.5, 'yy320': 1.0, 'qws': 0.2, 'wa1': 1.0, 'qy0': 0.2, 'qu1s': 0.2, 'mtp': 4.0}
-SPARE = {'thr1': 0.3, 'y3231': 1.0, 'yy131': 0.6, 'y3221': 1.0, 'y3211': 0.3, 'kat20': 0.3, 'thr0': 1.0, 'c4': 0.3, 'sc3': 1.0, 'c': 0.3,
-         'sc2': 1.0, 'kat31': -0.3, 'fh0': 2, 'fh1': 2, 'fh2': 2, 'fh3': 2}
+CY, OV, LAT, PE = 0.00087, 0.05, 0.12, 0.0008
+EARLY = {'ctri': 2.5, 'k72d': -1.0, 'm': -0.5, 'yy300': -1.0, 'pl': 8.0, 'xs31': -2.0, 'fb3': 4.0, 'idc': 1.0, 'w21': 0.5, 'wo4': -0.5, 'm3d': 0.5,
+         'ft1': -2.3, 'cm': -1.0, 'kmin0': -2.0, 'yy210': -1.5, 'm1d': 0.5, 'yy001': -2.0, 'qu1c': 2.5, 'xin1': -2.5, 'cm1': 4.0, 'yy121': -1.0,
+         'yy021': -2.0, 'yy230': -0.5, 'yy220': -1.0, 'kat0': 12.5, 'flz': 9.5, 'ka0': 9, 'rid': 9, 'c4': 12, 'cb1': 10, 'thr0': 7.8, 'kb1': 2,
+         'eb1s': 5, 'cde': 1.0, 'pi3': -1.0, 'yy120': -0.5, 'lrow': -3.0, 'rev': 0.2, 'ft0': 4.0, 'off': -0.5, 'yy111': -0.5, 'mi2': 0.2,
+         'lc1': 4.0, 'wo0': 0.5, 'r16b': -2.2, 'yo0': -0.3, 'fa3': 1.5, 'eb0c': 2.0, 'slotc': 1.5, 'slots': 0.8, 'rho': -1.0, 'eft0': -1.5,
+         'yy320': -1.0, 'qws': 0.2, 'wa1': 0.8, 'qy0': 0.2, 'qu1s': 0.2, 'mtp': 4.0, 'a2l': -1.0, 'yy201': -1.8, 'y3200': -0.2, 'so0': 0.5,
+         'cmx': 0.2, 'm72': -2.0, 'y3231': -1.0, 'x3221': 0.5, 'kat23': 4.0, 'thc0': -1.0, 'ul': -0.2, 'yy331': -0.5, 'kat30': -2.0, 'so2': 5.5,
+         'io03': 1.0, 'a2h': 4.0, 'kst1': -0.2, 'fa0': -1.0, 'hs': -1.0, 'wo2': 4.0, 'yy321': -2.0, 'kat12': -1.0, 'eft3': 0.5, 'wa6': 1.0,
+         'kat32': 0.5, 'mi': 0.5, 'pk': -2.0, 'kat33': -0.5, 'w24': 1.0, 'tj': -2.0, 'yy131': -0.2, 'm2l': 5.0, 'lands': 5.0, 'wo6': -1.0,
+         'xs21': 0.2, 'fly': 6, 'xinp': 4, 'mtp2': 8, 'ln': 2.0, 'io10': 1.0, 'tha': 0.5, 'ef1': 4.0, 'm2d': 2.0, 'kb30': 0.2, 'tri': -0.2,
+         'w1b': -0.5, 'x3230': 4.0, 'm2r': 0.5, 'kb32': 1.0, 'eft2': -0.5, 'so1': 2.0, 'b32': 4.0, 'rep3': 0.5, 'y3230': 2.0, 'wa3': -1.0,
+         'cm2': -0.2, 'kb03': -1.0, 'lc': 2.0, 'xs30': 0.5, 'fb1': -0.2, 'ebi0': -0.5, 'x3210': 4.0, 'kns': -1.0, 'yt10': -0.5, 'x3200': 0.5,
+         't_0': -2.0, 'yt01': 4.0, 'w23': 4.0}
+SPARE = {'y3231': 1.3, 'yy131': 0.6, 'y3221': 1.0, 'y3211': 0.3, 'kat20': 0.3, 'thr0': 3, 'c4': 3, 'sc3': 1.0, 'c': 0.3, 'sc2': 0.7, 'kat31': -0.3,
+         'kat13': -0.3, 'yy320': 0.3, 'wa6': 0.3, 'xs30': 1.0, 'yy031': -1.0, 'yy300': -0.3, 'rp2': -0.3, 'wa2': 1, 'kst0': -0.3, 'r16b': 0.3,
+         'wa4': 1.0, 'sc0': 1.0, 'y3230': 1.0, 'scn': 0.7, 'io12': 0.3, 'wa3': 0.3, 'yy201': -0.6, 'yy020': -0.3, 'wa1': 0.3, 'rp3': 0.3,
+         'yo1': 2.0, 'flz': 3.3, 'fly': 3, 'xinp': 3, 'xsp': 3, 'mtp': 3, 'mtp2': 3, 'c0': 3, 'sc1': 1.0, 'kat23': 1.0, 'thr2': 0.3, 'wa0': -1.0,
+         'xs10': -1.0, 'xs00': 1.0, 'xs11': 0.3, 'kdr': -1.0, 'yy231': 1.0, 'yy331': 0.3}
 SPAN = [0.0]
 
 
@@ -159,7 +170,9 @@ def rank_program(g, core, T, topo):
         alts = {"V": (lambda: V.memset(ap, v), vc(w(ap), f), 0)}
         if s and w(ap) <= 128:
             alts["S"] = (lambda: S.activation(ap, T.tj[:, 0:w(ap)], AF.Identity, bias=float(v), scale=0.0), vc(w(ap)), 0)
-        add(alts, ["tj"] if len(alts) > 1 else [], wr)
+        elif s:
+            alts["S"] = (lambda: S.activation(ap, T.kat[0:ap.shape[0], 0:w(ap)], AF.Identity, bias=float(v), scale=0.0), vc(w(ap)), 0)
+        add(alts, [] if len(alts) == 1 else ["tj"] if w(ap) <= 128 else ["kat0"], wr)
 
     def scan(out, d0, d1, init, o0, o1, rd, wr):
         add({"V": (lambda: V.tensor_tensor_scan(out, d0, d1, init, o0, o1), vc(w(out)), 0)}, rd, wr)
@@ -220,6 +233,7 @@ def rank_program(g, core, T, topo):
     iota(T.w1[:, 8:16], [[16, 8]], 0, 0, ["w1b"])
     iota(T.idc[:], [[16, 4], [-112, 8]], 784 + 1536 - int(BIG), 0, ["idc"])
     IOH = ["ioh%d" % k for k in range(4)]
+    ms(T.kat[:, 0:512], 1.0, ["kat0"], 0.5, False)
     ms(T.xin[:, 1792:2048], 0.0, ["xinp"], 0.5)
     ms(T.xs[:, 1792:2048], 0.0, ["xsp"], 0.5)
     ms(T.u1l[:], 1, ["u1l"], s=False)
@@ -240,7 +254,6 @@ def rank_program(g, core, T, topo):
     ms(T.mt[64:128, 3:1792:4], 0.0, ["mtp"], 0.5)
     ms(T.mt[:, 1792:2048], 0.0, ["mtp2"], 0.5)
     ts(T.ctri[:], T.tj[:], 0.0, A.is_gt, ["tj"], ["ctri"], 2.0 ** -100, A.mult)
-    ms(T.kat[:, 0:512], 1.0, ["kat0"], 0.5)
     quant("ka", 0, 128, T.kat, ["kat0"], ["ka0"])
     one = T.kat[:, 0:128]
     asel(T.nar[:, 0:128], one, [[1, 128]], A.is_ge, 0.0, 0, -1, ["kat0"], ["tri"])
@@ -251,7 +264,8 @@ def rank_program(g, core, T, topo):
         mv(T.kat[:, 1024 + t:1536:4], T.nar[:, 256:384], ["del"], ["kat2%d" % t], f=0.5)
         ms(T.kat[:, 1536 + t:2048:4], 1.0 if t < 2 else 0.5, ["kat3%d" % t], 0.5)
     quant("ka", 128, 512, T.kat, ["kat%d%d" % (a, t) for a in (1, 2, 3) for t in range(4)], ["ka1"])
-    ms(T.flt[:], 0.0, ["flz", "fa3", "fb3"], 0.5)
+    ms(T.flt[:, 0:512], 0.0, ["flz", "fa3"], 0.5)
+    ms(T.flt[:, 512:1024], 0.0, ["fly", "fb3"], 0.5)
     ms(T.thr[:], -1.0, ["thr%d" % t for t in range(4)] + ["thc%d" % t for t in range(4)])
     for t in range(4):
         ms(T.thr[:, 72 * t:72 * t + 8], float(NF), ["thr%d" % t])
@@ -277,13 +291,17 @@ def rank_program(g, core, T, topo):
         pick("eb", "ef", 256, 512, T.ebl[:, 16 * b:16 * b + 16], ["ef%d" % j for j in range(4)] + ["ebl"], 256 * b, "eb%d" % b)
     lin(T.w2[:, 8:16], T.w1[:, 0:8], 1.0, T.pv[:, 2:3], ["w1a", "pv"], ["c"])
     lin(T.w2[:, 16:24], T.w2[:, 8:16], 1.0 / 7.0, -3.0 / 7.0, ["c"], ["mf"])
-    lin(T.w2[:, 72:76], T.w2[:, 8:12], 1.0, -4.0, ["c"], ["c4"])
+    lin(T.w2[:, 72:76], T.w2[:, 8:12], -1.0, 0.0, ["c"], ["c0"])
+    lin(T.w2[:, 76:80], T.w2[:, 8:12], -1.0, 4.0, ["c", "c0"], ["c4"])
     cp(T.wi[:, 0:8], T.w2[:, 16:24], ["mf"], ["mi"])
     ts(T.w2[:, 56:64], T.wi[:, 0:8], -7.0, A.mult, ["mi"], ["m7"])
     tt(T.w2[:, 24:32], T.w2[:, 56:64], T.w2[:, 8:16], A.add, ["m7", "c"], ["rho"])
-    ts(T.w2[:, 32:40], T.w2[:, 24:32], 4.0, A.is_ge, ["rho"], ["y128"], 128.0, A.mult)
-    lin(T.cb[:, 0:4], T.w2[:, 32:36], 1.0, T.pv[:, 1:2], ["y128", "pv"], ["cb0"])
-    ts(T.cb[:, 4:8], T.w2[:, 36:40], T.pv[:, 1:2], A.add, ["y128", "pv"], ["cb1"], 8.0, A.add)
+    ts(T.w2[:, 32:40], T.w2[:, 24:32], 4.0, A.is_ge, ["rho"], ["y128"], -128.0, A.mult)
+    ts(T.cb[:, 0:4], T.w2[:, 32:36], T.pv[:, 1:2], A.subtract, ["y128", "pv"], ["cb0"])
+    ts(T.cb[:, 4:8], T.w2[:, 36:40], T.pv[:, 1:2], A.subtract, ["y128", "pv"], ["cb1"], -8.0, A.add)
+    for a in range(2):
+        for t in range(4):
+            lin(T.io4[:, 256 * t + 128 * a:256 * t + 128 * a + 128], T.ioh[:], 1.0, T.cb[:, 4 * a + t:4 * a + t + 1], IOH + ["cb%d" % a], ["io%d%d" % (a, t)])
     lin(T.w2[:, 40:44], T.w2[:, 24:28], 16.0, 0.0, ["rho"], ["r16a"])
     lin(T.w2[:, 44:48], T.w2[:, 28:32], 16.0, 128.0, ["rho"], ["r16b"])
     ts(T.w2[:, 48:56], T.w2[:, 24:32], 4.0, A.is_ge, ["rho"], ["y64"], -64.0, A.mult)
@@ -293,8 +311,9 @@ def rank_program(g, core, T, topo):
         for t in range(4):
             ts(T.kbt[:, 512 * a + t:512 * a + 512:4], T.kv[:], T.cb[:, 8 + 4 * a + t:9 + 4 * a + t], A.is_equal,
                ["kva", "kvb", "rid"], ["kb%d%d" % (a, t)], f=0.5)
-            ts(T.kbt[:, 1024 + 512 * a + t:1536 + 512 * a:4], T.th[:], T.w2[:, (72 if a else 8) + t:(73 if a else 9) + t], A.is_gt,
-               ["tha", "thb", "c", "c4"], ["kb%d%d" % (2 + a, t)], f=0.5)
+            o = T.kbt[:, 1024 + 512 * a + t:1536 + 512 * a:4]
+            act(o, T.th[:], ["tha", "thb", "c4"], ["kb%d%d" % (2 + a, t)], AF.Relu, bias=T.w2[:, 72 + 4 * a + t:73 + 4 * a + t])
+            act(o, o, ["kb%d%d" % (2 + a, t)], ["kb%d%d" % (2 + a, t)], AF.Sign)
     quant("kb", 0, 256, T.kbt, ["kb%d%d" % (a, t) for a in (0, 1) for t in range(4)], ["kb0"])
     quant("kb", 256, 512, T.kbt, ["kb%d%d" % (a, t) for a in (2, 3) for t in range(4)], ["kb1"])
     ms(T.kmin[:, 0:128:2], 255.0, ["kmin0"])
@@ -373,18 +392,16 @@ def rank_program(g, core, T, topo):
         tt(T.rr[:, 0:72], T.rr[:, 0:72], T.k72[:, 0:72], A.mult, ["rr", "k72a", "k72b"], ["rr"])
         scan(T.cm2[:, 0:72], T.hs[:, 0:72], T.rr[:, 0:72], 0.0, A.mult, A.max, ["rr", "hs"], ["cm2"])
         tt(T.cde[:, 0:4], T.cm2[:, 7:36:9], T.cm2[:, 43:72:9], A.subtract, ["cm2"], ["cde"])
-        tt(T.cde[:, 8:12], T.cde[:, 0:4], T.cb[:, 0:4], A.add, ["cde", "cb0"], ["cd0"])
-        tt(T.cde[:, 12:16], T.cde[:, 0:4], T.cb[:, 4:8], A.add, ["cde", "cb1"], ["cd1"])
         for b in range(4):
             mm(6 + b % 2, "ef", 128 * b, t_, 0, C, ["ef%d" % b] + TA)
             o = 3072 + 896 * (b // 2) + b % 2
             mv(T.win[:, o:3072 + 896 * (b // 2 + 1):2], ps(6 + b % 2, 0, C), ["#%d" % (6 + b % 2)], ["ft%d" % b], 0.5, on="S")
-        for k in range(4):
-            mv(T.fh[:, C * k:C * k + C], T.win[:, 3072 + C * k:3072 + C * k + C], ["ft%d" % (k & 2), "ft%d" % (k | 1)], ["fh%d" % k], f=0.5, on="VSG")
+        for k in range(2):
+            dma("Y", "dfh%d" % k, T.fh[:, 896 * k:896 * k + 896], T.win[:, 3072 + 896 * k:3968 + 896 * k], ["ft%d" % (2 * k), "ft%d" % (2 * k + 1)], ["fh%d" % k], 2.5)
         for t in range(4):
             p = 128 if t < 3 else 64
             tt(T.flt[0:p, t:256:4], ps(t, 0, 64, p), T.thr[0:p, 64 * t:64 * t + 64], A.is_lt, ["#%d" % t, "flz", "thr%d" % t, "thc%d" % t], ["fa%d" % t], 1.0)
-            act(T.flt[0:p, 512 + t:768:4], T.tj[0:p, 0:64], ["fa%d" % t, "tj"], ["fb%d" % t], AF.Identity, bias=T.flt[0:p, 33 * t:33 * t + 1], scale=0.0)
+            act(T.flt[0:p, 512 + t:768:4], T.tj[0:p, 0:64], ["fa%d" % t, "tj", "fly"], ["fb%d" % t], AF.Identity, bias=T.flt[0:p, 33 * t:33 * t + 1], scale=0.0)
         quant("fl", 0, 128, T.flt, ["fa%d" % t for t in range(4)], ["fl0"])
         quant("fl", 128, 256, T.flt, ["fb%d" % t for t in range(4)], ["fl1"])
         mm(5, "ka", 128, "fl", 0, 128, ["fl0", "ka1"], True, False)
@@ -407,11 +424,10 @@ def rank_program(g, core, T, topo):
         pick(sl, t_, NF, 512, T.pl[:, 0:12], TA + ["pl"])
         send(T[ld + "c"][:].bitcast(dt.uint8), T[sl + "c"][:].bitcast(dt.uint8), "ac%d" % r, 2, [sl + "c"], [ld + "c"], 2.2)
         send(T[ld + "s"][:], T[sl + "s"][:], "ac%d" % r, 2, [sl + "s"], [ld + "s"], 1.8)
-        for bor in range(2):
-            for t in range(4):
-                ts(T.sot[:, 512 * bor + t:512 * bor + 512:4], T.ioh[:], T.cde[:, 8 + 4 * bor + t:9 + 4 * bor + t], A.is_equal,
-                   IOH + ["cd%d" % bor, "wv"], ["so%d%d" % (bor, t)], T.wv[:, 8 * t + 7:8 * t + 8], A.mult, 0.5)
-        quant("so", 0, 256, T.sot, ["so%d%d" % (b, t) for b in range(2) for t in range(4)], ["so"])
+        for t in range(4):
+            ts(T.sot[:, t:1024:4], T.io4[:, 256 * t:256 * t + 256], T.cde[:, t:t + 1], A.is_equal,
+               ["io0%d" % t, "io1%d" % t, "cde", "wv"], ["so%d" % t], T.wv[:, 8 * t + 7:8 * t + 8], A.mult, 0.5)
+        quant("so", 0, 256, T.sot, ["so%d" % t for t in range(4)], ["so"])
         mm(2, "so", 0, "kb", 0, 128, ["so", "kb0"], True, False)
         mm(2, "so", 128, "kb", 128, 128, ["so", "kb0"], False, True)
         act(T.ln[:], ps(2, 0, 128), ["#2", "lc1"], ["ln"], AF.Ln, bias=2.0 ** -62)
@@ -429,7 +445,8 @@ def rank_program(g, core, T, topo):
                 bk = banks[k % len(banks)]
                 mm(bk, "eb", 128 * k, src, 0, NF, [src + "c", src + "s", "eb%dc" % (k // 2), "eb%ds" % (k // 2)])
                 o = base + NF * (7 - k)
-                mv(T.win[:, o:o + NF], ps(bk, 0, NF), ["#%d" % bk], ["%s%d" % (key, k)], 0.5, on=on)
+                a, z = (0, NF) if r == 0 else (max(0, 136 - 56 * k), NF) if base else (0, min(NF, 399 - 56 * k))
+                mv(T.win[:, o + a:o + z], ps(bk, a, z), ["#%d" % bk], ["%s%d" % (key, k)], 0.5, on=on)
         unpack(sl, 0, "wo", (3, 4, 5), "S")
         ts(T.ko[:], T.sm[:, 1:64:2], float(NF), A.is_lt, ["sm"], ["ko"], -(BIG + NF), A.mult)
         tt(T.ko[:], T.ko[:], T.sm[:, 1:64:2], A.add, ["ko", "sm"], ["ko"])
@@ -442,10 +459,9 @@ def rank_program(g, core, T, topo):
         ts(T.kn[:], T.a2[:], float(NF), A.is_lt, ["a2h", "a2l"], ["kn"], -BIG, A.mult)
         tt(T.kn[:], T.kn[:], T.a2[:], A.add, ["kn", "a2h", "a2l"], ["kn"])
         scan(T.kns[:], T.kst[:, 32:64], T.kn[:], 0.0, A.add, A.min, ["kn", "kst1"], ["kns"])
-        tt(T.res[:], T.kns[:], T.own[:], A.min, ["kns", "own"], ["res"])
         for k in range(4):
             o = 64 * (k % 2) + 32 * (k // 2)
-            mv(T.rep[0:32, o:o + 32], T.res[32 * k:32 * k + 32, :], ["res"], ["rep%d" % k])
+            tt(T.rep[0:32, o:o + 32], T.kns[32 * k:32 * k + 32, :], T.own[32 * k:32 * k + 32, :], A.min, ["kns", "own"], ["rep%d" % k])
         for k in range(1, 4):
             mv(T.rep[32 * k:32 * k + 32, :], T.rep[0:32, :], ["rep%d" % j for j in range(4)], ["rp%d" % k])
         ts(T.off[:], T.rep[:, 0:128].indirect(T.ordr[:, 0:7]), 1536.0 + BIG, A.add,
@@ -456,7 +472,7 @@ def rank_program(g, core, T, topo):
             for b1 in range(2):
                 lo, hi = 896 * b1 + 2 * a, 896 * b1 + 2 * z
                 tt(T.yt[:, lo:hi], T.win[:, 0:4864].indirect(T.off[:, lo // 16:hi // 16]), T.fh[:, lo:hi],
-                   A.add, WIN + ["off", "fh%d" % (2 * b1), "fh%d" % (2 * b1 + 1)], ["yt%d%d" % (b1, h)], 1.8)
+                   A.add, WIN + ["off", "fh%d" % b1], ["yt%d%d" % (b1, h)], 1.8)
             for be in range(4):
                 for b in range(4):
                     o = 896 * (be // 2)

@@ -1,8 +1,9 @@
+import math
 from concourse.mybir import dt, AluOpType as A, ActivationFunctionType as AF
 
 C, NF, R = 448, 192, 3
 BIG = 8192.0
-CUTS = (0, 320, 448)
+CUTS = (0, 256, 448)
 Q4, U8, BF, F32, I32, U16 = "float8_e4m3fn_x4", "uint8", "bfloat16", "float32", "int32", "uint16"
 SCRATCH = {}
 
@@ -24,17 +25,17 @@ for _r in range(R):
     _sb("pk%d" % _r, 16, U16)
     _sb("lst%d" % _r, 16, U16)
 for _n, _w in (("qu", 128), ("qup", 128), ("qu1", 128), ("qv", 128), ("qw", 512), ("ef", 512), ("eb", 1024), ("ka", 512),
-               ("kb", 512), ("m", 512), ("fl", 256), ("cm", 384), ("so", 256), ("qy", C)):
+               ("kb", 512), ("m", 512), ("fl", 288), ("cm", 384), ("so", 256), ("qy", C)):
     _q(_n, _w)
-for _n, _w in (("xin", 2048), ("xs", 2048), ("x32", 4 * C), ("ut", 512), ("vt", 512), ("eft", 2048), ("th", 128),
-               ("kat", 2048), ("kbt", 2048), ("mt", 2048), ("flt", 1024), ("cmt", 1536), ("sot", 1024), ("dd", 1152), ("ctri", 128),
+for _n, _w in (("xin", 2048), ("xs", 2048), ("ut", 512), ("vt", 512), ("eft", 2048), ("th", 128),
+               ("kat", 2048), ("kbt", 2048), ("mt", 2048), ("flt", 1152), ("cmt", 1536), ("sot", 1024), ("dd", 1152), ("ctri", 128),
                ("ios", 384), ("ioh", 128), ("io4", 1024), ("kv", 128), ("win", 4864), ("yt", 4 * C), ("fh", 4 * C), ("yy", 4 * C),
-               ("y32", 4 * C), ("nar", 384)):
+               ("y1", 4 * C), ("nar", 384)):
     _sb(_n, _w, BF)
-for _n, _w in (("sc", 80), ("cmx", 80), ("cm2", 80), ("rr", 80), ("hs", 80), ("cde", 16), ("k72", 160), ("thr", 256), ("ebi", 64), ("kd", 64),
+for _n, _w in (("sc", 80), ("cmx", 80), ("cm2", 80), ("rr", 80), ("cde", 16), ("k72", 160), ("thr", 256), ("th2", 192), ("ebi", 64), ("kd", 64),
                ("eq", 32), ("wv", 32), ("lrow", 384), ("ln", 128), ("nb", 128), ("cand", 128), ("sm", 128), ("kmin", 160),
-               ("pkf", 32), ("ko", 32), ("kos", 32), ("own", 32), ("kn", 32), ("kns", 32), ("rep", 128), ("kst", 64), ("idc", 32),
-               ("cb", 16), ("w1", 96), ("w2", 80), ("pv", 8), ("yo", C), ("tj", 128), ("lc", 4), ("pn", 4)):
+               ("pkf", 32), ("kos", 32), ("own", 32), ("kn", 32), ("kns", 32), ("rep", 128), ("kst", 64), ("idc", 32),
+               ("cb", 16), ("w1", 96), ("w2", 80), ("pv", 8), ("yo", C), ("tj", 128), ("acc", 4), ("pn", 4)):
     _sb(_n, _w, F32)
 for _n, _w in (("lev", 128), ("ai", 16), ("a2", 32), ("pi", 8), ("wi", 16)):
     _sb(_n, _w, I32)
@@ -44,32 +45,53 @@ SCRATCH["ps"] = ("psum", [128, 4096], F32)
 SEMAPHORES = ["V", "S", "P", "G", "dx0", "dx1", "du", "dv", "dwc", "dws", "outs", "sent", "dfh0", "dfh1"] + \
              ["%s%d" % (k, r) for k in ("ac", "al") for r in range(R)]
 CY, OV, LAT, PE = 0.00087, 0.05, 0.12, 0.0008
-EARLY = {'ctri': 2.5, 'k72d': -1.0, 'm': -0.5, 'yy300': -1.0, 'pl': 8.0, 'xs31': -2.0, 'fb3': 4.0, 'idc': 1.0, 'w21': 0.5, 'wo4': -0.5, 'm3d': 0.5,
-         'ft1': -2.3, 'cm': -1.0, 'kmin0': -2.0, 'yy210': -1.5, 'm1d': 0.5, 'yy001': -2.0, 'qu1c': 2.5, 'xin1': -2.5, 'cm1': 4.0, 'yy121': -1.0,
-         'yy021': -2.0, 'yy230': -0.5, 'yy220': -1.0, 'kat0': 12.5, 'flz': 9.5, 'ka0': 9, 'rid': 9, 'c4': 12, 'cb1': 10, 'thr0': 7.8, 'kb1': 2,
-         'eb1s': 5, 'cde': 1.0, 'pi3': -1.0, 'yy120': -0.5, 'lrow': -3.0, 'rev': 0.2, 'ft0': 4.0, 'off': -0.5, 'yy111': -0.5, 'mi2': 0.2,
-         'lc1': 4.0, 'wo0': 0.5, 'r16b': -2.2, 'yo0': -0.3, 'fa3': 1.5, 'eb0c': 2.0, 'slotc': 1.5, 'slots': 0.8, 'rho': -1.0, 'eft0': -1.5,
-         'yy320': -1.0, 'qws': 0.2, 'wa1': 0.8, 'qy0': 0.2, 'qu1s': 0.2, 'mtp': 4.0, 'a2l': -1.0, 'yy201': -1.8, 'y3200': -0.2, 'so0': 0.5,
-         'cmx': 0.2, 'm72': -2.0, 'y3231': -1.0, 'x3221': 0.5, 'kat23': 4.0, 'thc0': -1.0, 'ul': -0.2, 'yy331': -0.5, 'kat30': -2.0, 'so2': 5.5,
-         'io03': 1.0, 'a2h': 4.0, 'kst1': -0.2, 'fa0': -1.0, 'hs': -1.0, 'wo2': 4.0, 'yy321': -2.0, 'kat12': -1.0, 'eft3': 0.5, 'wa6': 1.0,
-         'kat32': 0.5, 'mi': 0.5, 'pk': -2.0, 'kat33': -0.5, 'w24': 1.0, 'tj': -2.0, 'yy131': -0.2, 'm2l': 5.0, 'lands': 5.0, 'wo6': -1.0,
-         'xs21': 0.2, 'fly': 6, 'xinp': 4, 'mtp2': 8, 'ln': 2.0, 'io10': 1.0, 'tha': 0.5, 'ef1': 4.0, 'm2d': 2.0, 'kb30': 0.2, 'tri': -0.2,
-         'w1b': -0.5, 'x3230': 4.0, 'm2r': 0.5, 'kb32': 1.0, 'eft2': -0.5, 'so1': 2.0, 'b32': 4.0, 'rep3': 0.5, 'y3230': 2.0, 'wa3': -1.0,
-         'cm2': -0.2, 'kb03': -1.0, 'lc': 2.0, 'xs30': 0.5, 'fb1': -0.2, 'ebi0': -0.5, 'x3210': 4.0, 'kns': -1.0, 'yt10': -0.5, 'x3200': 0.5,
-         't_0': -2.0, 'yt01': 4.0, 'w23': 4.0}
-SPARE = {'y3231': 1.3, 'yy131': 0.6, 'y3221': 1.0, 'y3211': 0.3, 'kat20': 0.3, 'thr0': 3, 'c4': 3, 'sc3': 1.0, 'c': 0.3, 'sc2': 0.7, 'kat31': -0.3,
-         'kat13': -0.3, 'yy320': 0.3, 'wa6': 0.3, 'xs30': 1.0, 'yy031': -1.0, 'yy300': -0.3, 'rp2': -0.3, 'wa2': 1, 'kst0': -0.3, 'r16b': 0.3,
-         'wa4': 1.0, 'sc0': 1.0, 'y3230': 1.0, 'scn': 0.7, 'io12': 0.3, 'wa3': 0.3, 'yy201': -0.6, 'yy020': -0.3, 'wa1': 0.3, 'rp3': 0.3,
-         'yo1': 2.0, 'flz': 3.3, 'fly': 3, 'xinp': 3, 'xsp': 3, 'mtp': 3, 'mtp2': 3, 'c0': 3, 'sc1': 1.0, 'kat23': 1.0, 'thr2': 0.3, 'wa0': -1.0,
-         'xs10': -1.0, 'xs00': 1.0, 'xs11': 0.3, 'kdr': -1.0, 'yy231': 1.0, 'yy331': 0.3}
-SPAN = [0.0]
+TRIES = 3000
+SPAN, PLAN = [0.0], []
 
 
 def name(k):
     return k[0] + k[2:] if k[0] == "t" and k[2:3] == "_" else k[:4] + k[5:] if k[:4] in ("slot", "land") else k[:2] if k[:2] in ("pk", "ls") else k
 
 
+def deal(ops, succ, rank, early, spare):
+    n = len(ops)
+    pri = [rank[i] + early.get(ops[i]["key"], 0.0) for i in range(n)]
+    for i in range(n - 1, -1, -1):
+        for j in succ[i]:
+            if pri[j] + 1e-3 > pri[i]:
+                pri[i] = pri[j] + 1e-3
+    busy = {}
+    done, eng, start = [0.0] * n, [None] * n, [0.0] * n
+    for i in sorted(range(n), key=lambda k: -pri[k]):
+        best = None
+        for e, (fn, hold, tail) in ops[i]["alts"].items():
+            t = 0.0
+            for d, raw in ops[i]["deps"].items():
+                u = done[d] + LAT if raw or eng[d] != e else start[d] + 1e-6
+                if u > t:
+                    t = u
+            line = busy.setdefault(e, [])
+            lo, hi = 0, len(line)
+            while lo < hi:
+                mid = (lo + hi) // 2
+                if line[mid][1] <= t:
+                    lo = mid + 1
+                else:
+                    hi = mid
+            while lo < len(line) and t + hold > line[lo][0]:
+                t = max(t, line[lo][1])
+                lo += 1
+            val = t + hold + tail + (spare.get(ops[i]["key"], 0.0) if e == "V" else 0.0)
+            if best is None or val < best[4]:
+                best = (t + hold + tail, t, e, hold, val, lo)
+        done[i], start[i], eng[i] = best[0], best[1], best[2]
+        busy[best[2]].insert(best[5], (best[1], best[1] + best[3]))
+    return max(done), sorted((start[i], i, eng[i]) for i in range(n))
+
+
 def schedule(ops):
+    if PLAN:
+        return PLAN[0]
     n = len(ops)
     succ = [[] for _ in range(n)]
     for i, o in enumerate(ops):
@@ -79,29 +101,28 @@ def schedule(ops):
     for i in range(n - 1, -1, -1):
         c = min(a[1] + a[2] for a in ops[i]["alts"].values())
         rank[i] = c + LAT + max([rank[j] for j in succ[i]] + [0.0])
-    pri = [rank[i] + EARLY.get(ops[i]["key"], 0.0) for i in range(n)]
-    for i in range(n - 1, -1, -1):
-        pri[i] = max([pri[i]] + [pri[j] + 1e-3 for j in succ[i]])
-    busy = {}
-    done, eng, start = [0.0] * n, [None] * n, [0.0] * n
-    for i in sorted(range(n), key=lambda k: -pri[k]):
-        best = None
-        for e, (fn, hold, tail) in ops[i]["alts"].items():
-            t = 0.0
-            for d, raw in ops[i]["deps"].items():
-                t = max(t, done[d] + LAT if raw or eng[d] != e else start[d] + 1e-6)
-            for a, b in busy.get(e, []):
-                if t + hold <= a:
-                    break
-                t = max(t, b)
-            val = t + hold + tail + (SPARE.get(ops[i]["key"], 0.0) if e == "V" else 0.0)
-            if best is None or val < best[4]:
-                best = (t + hold + tail, t, e, hold, val)
-        done[i], start[i], eng[i] = best[0], best[1], best[2]
-        busy.setdefault(best[2], []).append((best[1], best[1] + best[3]))
-        busy[best[2]].sort()
-    SPAN[0] = max(done)
-    return sorted((start[i], i, eng[i]) for i in range(n))
+    keys = sorted(set(o["key"] for o in ops))
+    both = sorted(set(o["key"] for o in ops if len(o["alts"]) > 1 and "V" in o["alts"]))
+    early, spare = {}, {k: 0.3 for k in both}
+    best = deal(ops, succ, rank, early, spare)
+    z = 12345
+    for _ in range(TRIES):
+        e2, s2 = dict(early), dict(spare)
+        for _k in range(3):
+            z = (z * 1103515245 + 12345) % 2147483648
+            step = (-2.0, -1.0, -0.5, -0.2, 0.2, 0.5, 1.0, 2.0)[(z >> 8) % 8]
+            if (z >> 12) % 3 == 0:
+                k = both[(z >> 14) % len(both)]
+                s2[k] = s2.get(k, 0.0) + step / 2
+            else:
+                k = keys[(z >> 14) % len(keys)]
+                e2[k] = e2.get(k, 0.0) + step
+        got = deal(ops, succ, rank, e2, s2)
+        if got[0] <= best[0]:
+            best, early, spare = got, e2, s2
+    SPAN[0] = best[0]
+    PLAN.append(best[1])
+    return best[1]
 
 
 def rank_program(g, core, T, topo):
@@ -162,8 +183,8 @@ def rank_program(g, core, T, topo):
             alts["G"] = (lambda: g.affine_select(out, a, [[0, n]], A.is_ge, 0.0, 0, 0), 0.24 + 2 * n * CY + OV, 0)
         add(alts, rd, wr)
 
-    def lin(out, a, k, c, rd, wr):
-        add({"V": (lambda: V.tensor_scalar(out, a, k, c, A.mult, A.add), vc(w(out)), 0),
+    def lin(out, a, k, c, rd, wr, f=1.0):
+        add({"V": (lambda: V.tensor_scalar(out, a, k, c, A.mult, A.add), vc(w(out), f), 0),
              "S": (lambda: S.activation(out, a, AF.Identity, bias=c, scale=k), vc(w(out)), 0)}, rd, wr)
 
     def ms(ap, v, wr, f=1.0, s=True):
@@ -188,7 +209,7 @@ def rank_program(g, core, T, topo):
         add({"G": (lambda: g.affine_select(out, a, pat, cmp, fill, base, ch), 0.17 + 2 * w(out) * CY + OV, 0)}, rd, wr)
 
     def quant(nm, a, b, tile, rd, wr):
-        add({"V": (lambda: V.quantize_mx(T[nm + "c"][:, a:b], T[nm + "s"][:, a:b], tile[:, 4 * a:4 * b]), 0.012 + 0.001 * (b - a) + OV, 0)}, rd, wr)
+        add({"V": (lambda: V.quantize_mx(T[nm + "c"][:, a:b], T[nm + "s"][:, a:b], tile[:, 4 * a:4 * b]), 0.012 + 0.00092 * (b - a) + OV, 0)}, rd, wr)
 
     def mm(bank, st, sa, mo, ma, n, rd, start=True, stop=True):
         add({"P": (lambda: g.tensor.matmul_mx(T.ps[:, 512 * bank:512 * bank + n], T[st + "c"][:, sa:sa + 128], T[st + "s"][:, sa:sa + 128],
@@ -210,17 +231,16 @@ def rank_program(g, core, T, topo):
     def send(out, in_, sem, n, rd, wr, t):
         add({"G": (lambda: g.remote_dma(out, in_, T.sem[sem], T.sem.sent, pid, rid, mask), 0.4, t)}, rd, wr, None, (sem, n * neng))
 
-    dma("Y", "du", T.ut[:], T.u[:], [], ["ut"], 1.8)
-    dma("Y", "dx0", T.xin[:, 0:1024], T.x[:, 0:1024], [], ["xin0"], 2.4)
-    dma("S", "dx1", T.xin[:, 1024:1792], T.x[:, 1024:1792], [], ["xin1"], 2.4)
-    dma("Y", "dwc", T.qwc[:].bitcast(dt.uint8), T.wc[:], ["xin0"], ["qwc"])
+    dma("Y", "du", T.ut[:], T.u[:], [], ["ut"], 2.5)
+    dma("Y", "dx0", T.xin[:, 0:1024], T.x[:, 0:1024], [], ["xin0"], 3.0)
+    dma("S", "dx1", T.xin[:, 1024:1792], T.x[:, 1024:1792], [], ["xin1"], 2.8)
+    dma("Y", "dwc", T.qwc[:].bitcast(dt.uint8), T.wc[:], ["xin0"], ["qwc"], 3.0)
     dma("Y", "dws", T.qws[:], T.ws[:], ["xin0"], ["qws"])
     dma("Y", "dv", T.vt[:], T.v[:], ["xin0"], ["vt"])
 
     iota(T.pi[:, 0:1], [[0, 1]], 0, 1, ["pi0"], False)
     iota(T.tj[:], [[1, 128]], 0, -1, ["tj"])
-    iota(T.k72[:, 0:36], [[0, 4], [16, 9]], 0, 0, ["k72a"])
-    iota(T.k72[:, 36:72], [[0, 4], [1, 9]], 0, 0, ["k72b"])
+    iota(T.k72[:, 0:72], [[-15, 2], [0, 36]], 16, 0, ["k72a"])
     iota(T.kd[:, 0:32], [[0, 4], [-1, 8]], -1, 0, ["kd"])
     iota(T.th[:, 0:64], [[1, 4], [7, 8], [1, 2]], -7, 0, ["tha"])
     iota(T.th[:, 64:128], [[1, 4], [-7, 8], [1, 2]], 49, 0, ["thb"])
@@ -228,12 +248,13 @@ def rank_program(g, core, T, topo):
     iota(T.kv[:, 64:128], [[16, 4], [-1, 8], [128, 2]], 7, 0, ["kvb"])
     iota(T.ios[:], [[16, 12], [0, 2], [1, 16]], 0, 0, ["ios"])
     for k in range(4):
-        iota(T.ioh[:, 32 * k:32 * k + 32], [[16, 2], [1, 8], [32, 2]], 64 * k, 0, ["ioh%d" % k])
+        iota(T.ioh[:, 32 * k:32 * k + 32], [[16, 2], [1, 8], [32, 2]], 64 * k - 105, 0, ["ioh%d" % k])
     iota(T.w1[:, 0:8], [[-1, 2], [16, 4]], 0, 0, ["w1a"])
     iota(T.w1[:, 8:16], [[16, 8]], 0, 0, ["w1b"])
-    iota(T.idc[:], [[16, 4], [-112, 8]], 784 + 1536 - int(BIG), 0, ["idc"])
+    iota(T.idc[:], [[16, 4], [-112, 8]], 784 + 1536, 0, ["idc"])
     IOH = ["ioh%d" % k for k in range(4)]
     ms(T.kat[:, 0:512], 1.0, ["kat0"], 0.5, False)
+    ms(T.mt[:], 0.0, ["mtp"], 0.5, False)
     ms(T.xin[:, 1792:2048], 0.0, ["xinp"], 0.5)
     ms(T.xs[:, 1792:2048], 0.0, ["xsp"], 0.5)
     ms(T.u1l[:], 1, ["u1l"], s=False)
@@ -251,8 +272,6 @@ def rank_program(g, core, T, topo):
     pick("qup", "qu", 128, 128, T.ul[:, 0:8], ["qu", "ul"])
     pick("qu1", "qu", 128, 128, T.u1l[:, 0:8], ["qu", "u1l"])
     quant("qv", 0, 128, T.vt, ["vt"], ["qv"])
-    ms(T.mt[64:128, 3:1792:4], 0.0, ["mtp"], 0.5)
-    ms(T.mt[:, 1792:2048], 0.0, ["mtp2"], 0.5)
     ts(T.ctri[:], T.tj[:], 0.0, A.is_gt, ["tj"], ["ctri"], 2.0 ** -100, A.mult)
     quant("ka", 0, 128, T.kat, ["kat0"], ["ka0"])
     one = T.kat[:, 0:128]
@@ -265,22 +284,18 @@ def rank_program(g, core, T, topo):
         ms(T.kat[:, 1536 + t:2048:4], 1.0 if t < 2 else 0.5, ["kat3%d" % t], 0.5)
     quant("ka", 128, 512, T.kat, ["kat%d%d" % (a, t) for a in (1, 2, 3) for t in range(4)], ["ka1"])
     ms(T.flt[:, 0:512], 0.0, ["flz", "fa3"], 0.5)
-    ms(T.flt[:, 512:1024], 0.0, ["fly", "fb3"], 0.5)
+    ms(T.flt[:, 512:1152], 0.0, ["fly", "fb3"], 0.5, False)
+    quant("fl", 128, 256, T.flt, ["fly"], ["flw", "fl1"])
     ms(T.thr[:], -1.0, ["thr%d" % t for t in range(4)] + ["thc%d" % t for t in range(4)])
     for t in range(4):
         ms(T.thr[:, 72 * t:72 * t + 8], float(NF), ["thr%d" % t])
         if t < 3:
             ms(T.thr[:, 72 * t + 40:64 * t + 64], float(NF), ["thc%d" % t])
     ms(T.k72[:, 80:152], 0.0, ["k72d"])
-    ms(T.k72[:, 80:152:9], -1e29, ["k72d"])
-    ms(T.hs[:], 1.0, ["hs"])
-    ms(T.hs[:, 0:72:9], 0.0, ["hs"])
-    ms(T.cmx[:, 0:1], 0.0, ["cmx0"])
-    ms(T.kd[:, 32:64], 0.25, ["kdr"])
-    ms(T.kd[:, 32:64:8], 0.0, ["kdr"])
-    ms(T.lc[:, 0:1], 0.25, ["lc0"], s=False)
-    act(T.lc[:, 1:2], T.lc[:, 0:1], ["lc0"], ["lc1"], AF.Ln, 1.3)
-    add({"V": (lambda: V.reciprocal(T.lc[:, 2:3], T.lc[:, 1:2]), 0.22, 0)}, ["lc1"], ["lc"])
+    ms(T.k72[:, 88:152:9], -1e29, ["k72d"])
+    ms(T.cmx[:, 0:1], -1e29, ["cmx0"])
+    ms(T.kd[:, 32:64], math.exp(-1.0), ["kdr"])
+    act(T.kd[:, 32:64:8], T.kat[:, 0:4], ["kat0"], ["kdr"], AF.Ln, 1.3)
     for b in range(4):
         asel(T.eft[:, 512 * b:512 * b + 512], T.kat[:, 0:512], [[-256, 4], [-1, 32], [256, 4]], A.is_equal, 0.0, -32 * b, 1, ["kat0"], ["eft%d" % b])
         quant("ef", 128 * b, 128 * b + 128, T.eft, ["eft%d" % b], ["ef%d" % b])
@@ -291,8 +306,8 @@ def rank_program(g, core, T, topo):
         pick("eb", "ef", 256, 512, T.ebl[:, 16 * b:16 * b + 16], ["ef%d" % j for j in range(4)] + ["ebl"], 256 * b, "eb%d" % b)
     lin(T.w2[:, 8:16], T.w1[:, 0:8], 1.0, T.pv[:, 2:3], ["w1a", "pv"], ["c"])
     lin(T.w2[:, 16:24], T.w2[:, 8:16], 1.0 / 7.0, -3.0 / 7.0, ["c"], ["mf"])
-    lin(T.w2[:, 72:76], T.w2[:, 8:12], -1.0, 0.0, ["c"], ["c0"])
-    lin(T.w2[:, 76:80], T.w2[:, 8:12], -1.0, 4.0, ["c", "c0"], ["c4"])
+    lin(T.w2[:, 72:76], T.w2[:, 8:12], -1.0, -0.5, ["c"], ["c0"])
+    lin(T.w2[:, 76:80], T.w2[:, 8:12], -1.0, 3.5, ["c"], ["c4"])
     cp(T.wi[:, 0:8], T.w2[:, 16:24], ["mf"], ["mi"])
     ts(T.w2[:, 56:64], T.wi[:, 0:8], -7.0, A.mult, ["mi"], ["m7"])
     tt(T.w2[:, 24:32], T.w2[:, 56:64], T.w2[:, 8:16], A.add, ["m7", "c"], ["rho"])
@@ -301,7 +316,7 @@ def rank_program(g, core, T, topo):
     ts(T.cb[:, 4:8], T.w2[:, 36:40], T.pv[:, 1:2], A.subtract, ["y128", "pv"], ["cb1"], -8.0, A.add)
     for a in range(2):
         for t in range(4):
-            lin(T.io4[:, 256 * t + 128 * a:256 * t + 128 * a + 128], T.ioh[:], 1.0, T.cb[:, 4 * a + t:4 * a + t + 1], IOH + ["cb%d" % a], ["io%d%d" % (a, t)])
+            lin(T.io4[:, 256 * t + 128 * a:256 * t + 128 * a + 128], T.ioh[:], 1.0, T.cb[:, 4 * a + t:4 * a + t + 1], IOH + ["cb%d" % a], ["io%d%d" % (a, t)], 0.5)
     lin(T.w2[:, 40:44], T.w2[:, 24:28], 16.0, 0.0, ["rho"], ["r16a"])
     lin(T.w2[:, 44:48], T.w2[:, 28:32], 16.0, 128.0, ["rho"], ["r16b"])
     ts(T.w2[:, 48:56], T.w2[:, 24:32], 4.0, A.is_ge, ["rho"], ["y64"], -64.0, A.mult)
@@ -311,13 +326,15 @@ def rank_program(g, core, T, topo):
         for t in range(4):
             ts(T.kbt[:, 512 * a + t:512 * a + 512:4], T.kv[:], T.cb[:, 8 + 4 * a + t:9 + 4 * a + t], A.is_equal,
                ["kva", "kvb", "rid"], ["kb%d%d" % (a, t)], f=0.5)
-            o = T.kbt[:, 1024 + 512 * a + t:1536 + 512 * a:4]
-            act(o, T.th[:], ["tha", "thb", "c4"], ["kb%d%d" % (2 + a, t)], AF.Relu, bias=T.w2[:, 72 + 4 * a + t:73 + 4 * a + t])
-            act(o, o, ["kb%d%d" % (2 + a, t)], ["kb%d%d" % (2 + a, t)], AF.Sign)
+            act(T.kbt[:, 1024 + 512 * a + t:1536 + 512 * a:4], T.th[:], ["tha", "thb", "c0", "c4"], ["kb%d%d" % (2 + a, t)], AF.Sign,
+                bias=T.w2[:, 72 + 4 * a + t:73 + 4 * a + t])
+        for z in range(2):
+            o = T.kbt[:, 1024 + 512 * a + 256 * z:1280 + 512 * a + 256 * z]
+            lin(o, o, 0.5, z - 0.5, ["kb%d%d" % (2 + a, t) for t in range(4)], ["kc%d%d" % (a, z)], 0.5)
     quant("kb", 0, 256, T.kbt, ["kb%d%d" % (a, t) for a in (0, 1) for t in range(4)], ["kb0"])
-    quant("kb", 256, 512, T.kbt, ["kb%d%d" % (a, t) for a in (2, 3) for t in range(4)], ["kb1"])
-    ms(T.kmin[:, 0:128:2], 255.0, ["kmin0"])
-    ms(T.kmin[:, 1:128:2], -1.0, ["kmin1"])
+    quant("kb", 256, 512, T.kbt, ["kc00", "kc01", "kc10", "kc11"], ["kb1"])
+    ms(T.kmin[:, 0:128:2], 2 * BIG, ["kmin0"])
+    ms(T.kmin[:, 1:128:2], -BIG, ["kmin1"])
     ms(T.kmin[:, 128:160:2], 0.0, ["kpk0"])
     ms(T.kmin[:, 129:160:2], 256.0, ["kpk1"])
     ms(T.kst[:, 0:32], -float(NF), ["kst0"])
@@ -333,13 +350,16 @@ def rank_program(g, core, T, topo):
     lin(T.w1[:, 40:48], n_, 1.0 / 7.0, -3.0 / 7.0, ["n"], ["mf2"])
     cp(T.wi[:, 8:16], T.w1[:, 40:48], ["mf2"], ["mi2"])
     ts(T.w1[:, 64:72], T.wi[:, 8:16], -57.0, A.mult, ["mi2"], ["m72"])
-    lin(T.w1[:, 72:80], n_, 8.0, 7.0, ["n"], ["r8"])
-    ts(T.w1[:, 80:88], n_, 56.0, A.is_ge, ["n"], ["b32"], 72.0, A.mult)
+    lin(T.w2[:, 5:6], T.pv[:, 3:4], 64.0, 7.0, ["pv"], ["w25"])
+    lin(T.w2[:, 6:7], T.pv[:, 3:4], -128.0, 72.0, ["pv"], ["w26"])
+    lin(T.w1[:, 72:80], n_, 8.0, T.w2[:, 5:6], ["n", "w25"], ["r8"])
+    ts(T.w1[:, 80:88], n_, 56.0, A.is_ge, ["n", "w26"], ["b32"], T.w2[:, 6:7], A.mult)
     tt(T.w1[:, 72:80], T.w1[:, 72:80], T.w1[:, 64:72], A.add, ["r8", "m72"], ["r8"])
     tt(T.w1[:, 88:96], T.w1[:, 72:80], T.w1[:, 80:88], A.add, ["r8", "b32"], ["o2"])
     cp(T.ordr[:], T.w1[:, 88:96], ["o2"], ["ordr"])
 
     H = len(CUTS) - 1
+    SC64 = 1.0 / 64
 
     def quant_x(r, tile, h, rd):
         last = h == H - 1 and r < R
@@ -357,7 +377,7 @@ def rank_program(g, core, T, topo):
         for t, bk in enumerate((0, 1, 4, 5)):
             mm(bk, t_, 128 * t, "qup", 0, 128, tk(128 * t, 128 * t + 128) + ["qupc", "qups"])
             mv(T.sc[:, 9 * t:9 * t + 9], ps(bk, 0, 9), ["#%d" % bk], ["sc%d" % t])
-        for bk, a, z in ((2, 0, 256), (3, 0, 256), (6, 256, C), (7, 256, C)):
+        for bk, a, z in ((3, 0, 256), (2, 128, C), (7, 256, C)):
             mm(bk, "qu1", 0, t_, a, z - a, tk(a, z) + ["qu1c", "qu1s"])
 
         def si(t, p=128):
@@ -365,48 +385,61 @@ def rank_program(g, core, T, topo):
 
         def mt(t, a, b, p=128):
             return T.mt[0:p, 4 * a + t:4 * b:4]
-        act(T.dd[:, 896:1024], ps(3, 0, 128), ["#3", "sc0"], ["d0"], AF.Identity, bias=si(0), scale=-1.0)
-        act(T.dd[:, 1024:1152], ps(3, 128, 256), ["#3", "sc1"], ["d1"], AF.Identity, bias=si(1), scale=-1.0)
-        act(T.dd[:, 256:448], ps(7, 0, 192), ["#7", "sc2"], ["d2"], AF.Identity, bias=si(2), scale=-1.0)
-        act(T.dd[0:64, 704:896], ps(7, 0, 192, 64), ["#7", "sc3"], ["d3"], AF.Identity, bias=si(3, 64), scale=-1.0)
-        act(T.dd[:, 0:256], ps(3, 0, 256), ["#3", "sc2"], ["d2a"], AF.Identity, bias=si(2), scale=-1.0)
-        act(T.dd[0:64, 448:704], ps(3, 0, 256, 64), ["#3", "sc3"], ["d3a"], AF.Identity, bias=si(3, 64), scale=-1.0)
-        ts(mt(0, 128, 256), ps(2, 128, 256), si(0), A.is_ge, ["#2", "sc0"], ["m0q"])
-        ts(mt(1, 0, 128), ps(2, 0, 128), si(1), A.is_gt, ["#2", "sc1"], ["m1l"])
-        ts(mt(0, 256, C), ps(6, 0, 192), si(0), A.is_ge, ["#6", "sc0"], ["m0r"])
-        ts(mt(1, 256, C), ps(6, 0, 192), si(1), A.is_ge, ["#6", "sc1"], ["m1r"])
-        tt(mt(0, 0, 128), T.dd[:, 896:1024], T.ctri[:], A.is_lt, ["d0", "ctri"], ["m0d"])
-        tt(mt(1, 128, 256), T.dd[:, 1024:1152], T.ctri[:], A.is_lt, ["d1", "ctri"], ["m1d"])
-        ts(mt(2, 0, 256), T.dd[:, 0:256], 0.0, A.is_lt, ["d2a"], ["m2l"], f=0.5)
-        ts(mt(2, 384, C), T.dd[:, 384:448], 0.0, A.is_le, ["d2"], ["m2r"], f=0.5)
-        tt(mt(2, 256, 384), T.dd[:, 256:384], T.ctri[:], A.is_lt, ["d2", "ctri"], ["m2d"])
-        ts(mt(3, 0, 384, 64), T.dd[0:64, 448:832], 0.0, A.is_lt, ["d3", "d3a"], ["m3l"], f=0.5)
-        tt(mt(3, 384, C, 64), T.dd[0:64, 832:896], T.ctri[0:64, 0:64], A.is_lt, ["d3", "ctri"], ["m3d"])
+        for t in range(4):
+            p, a = (128 if t < 3 else 64), 128 * t
+            act(T.dd[0:p, a:a + p], ps(3 if t < 2 else 7, a % 256, a % 256 + p, p), ["#%d" % (3 if t < 2 else 7), "sc%d" % t], ["d%d" % t],
+                AF.Identity, bias=si(t, p), scale=-1.0)
+            tt(mt(t, a, a + p, p), T.dd[0:p, a:a + p], T.ctri[0:p, 0:p], A.is_lt, ["d%d" % t, "ctri", "mtp"], ["md%d" % t])
+            if t < 3:
+                ts(mt(t, a + 128, C), ps(2, a, C - 128), si(t), A.is_ge, ["#2", "sc%d" % t, "mtp"], ["mu%d" % t])
+                act(T.dd[:, 512:512 + C - 128 - a], mt(t, a + 128, C), ["mu%d" % t], ["acc%d" % t, "junk"], AF.Identity, 0.02,
+                    bias=-1.0, accum_out=T.acc[:, t:t + 1])
+                act(T.th2[:, 64 * t:64 * t + 64], T.thr[:, 64 * t:64 * t + 64], ["acc%d" % t, "thr%d" % t, "thc%d" % t], ["th2%d" % t], AF.Identity,
+                    bias=T.acc[:, t:t + 1])
         SC = ["sc0", "sc1", "sc2", "sc3"]
         mv(T.sc[:, 36:72], T.sc[:, 0:36], SC, ["scn"], -1.0)
-        quant("m", 0, 512 if r == 0 else C, T.mt, ["m0q", "m0r", "m1l", "m1r", "m2l", "m2r", "m2d", "m0d", "m1d", "m3l", "m3d", "mtp", "mtp2"], ["m"])
+        quant("m", 0, 512 if r == 0 else C, T.mt, ["md0", "md1", "md2", "md3", "mu0", "mu1", "mu2", "mtp"], ["m"])
         for t in range(4):
             mm(t, "m", 128 * t, "ka", 0, 128, ["m", "ka0"])
-        scan(T.cmx[:, 1:73], T.k72[:, 80:152], T.sc[:, 0:72], -1e29, A.add, A.max, SC + ["scn", "k72d"], ["cmx"])
-        tt(T.rr[:, 0:72], T.sc[:, 0:72], T.cmx[:, 0:72], A.is_gt, SC + ["scn", "cmx", "cmx0"], ["rr"])
-        tt(T.rr[:, 0:72], T.rr[:, 0:72], T.k72[:, 0:72], A.mult, ["rr", "k72a", "k72b"], ["rr"])
-        scan(T.cm2[:, 0:72], T.hs[:, 0:72], T.rr[:, 0:72], 0.0, A.mult, A.max, ["rr", "hs"], ["cm2"])
-        tt(T.cde[:, 0:4], T.cm2[:, 7:36:9], T.cm2[:, 43:72:9], A.subtract, ["cm2"], ["cde"])
+        scan(T.cmx[:, 1:73], T.sc[:, 0:72], T.k72[:, 80:152], -1e29, A.max, A.add, SC + ["scn", "k72d"], ["cmx"])
+        tt(T.rr[:, 0:72], T.sc[:, 0:72], T.cmx[:, 0:72], A.is_le, SC + ["scn", "cmx", "cmx0"], ["rr"])
+        scan(T.cm2[:, 0:72], T.k72[:, 0:72], T.rr[:, 0:72], 0.0, A.add, A.mult, ["rr", "k72a"], ["cm2"])
+        tt(T.cde[:, 0:4], T.cm2[:, 43:72:9], T.cm2[:, 7:36:9], A.subtract, ["cm2"], ["cde"])
         for b in range(4):
             mm(6 + b % 2, "ef", 128 * b, t_, 0, C, ["ef%d" % b] + TA)
             o = 3072 + 896 * (b // 2) + b % 2
-            mv(T.win[:, o:3072 + 896 * (b // 2 + 1):2], ps(6 + b % 2, 0, C), ["#%d" % (6 + b % 2)], ["ft%d" % b], 0.5, on="S")
+            mv(T.win[:, o:3072 + 896 * (b // 2 + 1):2], ps(6 + b % 2, 0, C), ["#%d" % (6 + b % 2)], ["ft%d" % b], SC64, on="S")
         for k in range(2):
-            dma("Y", "dfh%d" % k, T.fh[:, 896 * k:896 * k + 896], T.win[:, 3072 + 896 * k:3968 + 896 * k], ["ft%d" % (2 * k), "ft%d" % (2 * k + 1)], ["fh%d" % k], 2.5)
+            dma("Y", "dfh%d" % k, T.fh[:, 896 * k:896 * k + 896], T.win[:, 3072 + 896 * k:3968 + 896 * k], ["ft%d" % (2 * k), "ft%d" % (2 * k + 1)], ["fh%d" % k], 2.9)
         for t in range(4):
             p = 128 if t < 3 else 64
-            tt(T.flt[0:p, t:256:4], ps(t, 0, 64, p), T.thr[0:p, 64 * t:64 * t + 64], A.is_lt, ["#%d" % t, "flz", "thr%d" % t, "thc%d" % t], ["fa%d" % t], 1.0)
-            act(T.flt[0:p, 512 + t:768:4], T.tj[0:p, 0:64], ["fa%d" % t, "tj", "fly"], ["fb%d" % t], AF.Identity, bias=T.flt[0:p, 33 * t:33 * t + 1], scale=0.0)
+            th_ = (T.th2 if t < 3 else T.thr)[0:p, 64 * t:64 * t + 64]
+            tt(T.flt[0:p, t:256:4], ps(t, 0, 64, p), th_, A.is_lt, ["#%d" % t, "flz", "th2%d" % t if t < 3 else "thr3"], ["fa%d" % t], 1.0)
+            act(T.flt[0:p, 640 + t:896:4], T.tj[0:p, 0:64], ["fa%d" % t, "tj", "flw"], ["fb%d" % t], AF.Identity, bias=T.flt[0:p, 33 * t:33 * t + 1], scale=0.0)
         quant("fl", 0, 128, T.flt, ["fa%d" % t for t in range(4)], ["fl0"])
-        quant("fl", 128, 256, T.flt, ["fb%d" % t for t in range(4)], ["fl1"])
+        quant("fl", 160, 288, T.flt, ["fb%d" % t for t in range(4)], ["fl1"])
         mm(5, "ka", 128, "fl", 0, 128, ["fl0", "ka1"], True, False)
-        mm(5, "ka", 0, "fl", 32, 128, ["fl0", "fl1"] if r == 0 else ["fl0"], False, True)
+        mm(5, "ka", 0, "fl", 32, 128, ["fl0", "flw"], False, True)
         mm(4, "ka", 256, "fl", 0, 128, ["fl0", "ka1"])
+        tt(T.eq[:], ps(4, 0, 32), T.kd[:, 0:32], A.is_equal, ["#4", "kd"], ["eq"], 1.0)
+        scan(T.wv[:], T.kd[:, 32:64], T.eq[:], 0.0, A.mult, A.add, ["eq", "kdr"], ["wv"])
+        for t in range(4):
+            ts(T.sot[:, t:1024:4], T.io4[:, 256 * t:256 * t + 256], T.cde[:, t:t + 1], A.is_equal,
+               ["io0%d" % t, "io1%d" % t, "cde", "wv"], ["so%d" % t], T.wv[:, 8 * t + 7:8 * t + 8], A.mult, 0.5)
+        quant("so", 0, 256, T.sot, ["so%d" % t for t in range(4)], ["so"])
+        mm(0, "fl", 160, "kb", 256, 128, ["fl1", "kb1"], True, False)
+        mm(0, "fl", 96, "kb", 384, 128, ["fl0", "fl1", "flw", "kb1"], False, True)
+        mm(2, "so", 0, "kb", 0, 128, ["so", "kb0"], True, False)
+        mm(2, "so", 128, "kb", 128, 128, ["so", "kb0"], False, True)
+        act(T.ln[:], ps(2, 0, 128), ["#2", "kdr"], ["ln"], AF.Ln, bias=2.0 ** -62, scale=math.exp(-0.2))
+        act(T.nb[:, 64:128], ps(2, 64, 128), ["#2"], ["nb1"], AF.Identity, bias=255.0, scale=-2.0 ** 30)
+        act(T.nb[:, 0:64], ps(2, 0, 64), ["#2"], ["nb0"], AF.Identity, bias=BIG, scale=-2.0 ** 30)
+        tt(T.lev[:], ps(0, 0, 128), T.ln[:], A.subtract, ["#0", "ln"], ["lev"], 1.0)
+        tt(T.cand[:], T.lev[:], T.nb[:], A.max, ["lev", "nb0", "nb1"], ["cand"])
+        scan(T.sm[:], T.kmin[:, 0:128], T.cand[:], 0.0, A.max, A.min, ["cand", "kmin0", "kmin1"], ["sm"])
+        scan(T.pkf[:], T.kmin[:, 128:160], T.sm[:, 65:128:2], 0.0, A.mult, A.add, ["sm", "kpk0", "kpk1"], ["pkf"])
+        cp(T["pk%d" % r][:], T.pkf[:, 1:32:2], ["pkf"], ["pk%d" % r])
+        send(T["lst%d" % r][:], T["pk%d" % r][:], "al%d" % r, 1, ["pk%d" % r], ["lst%d" % r], 2.0)
         act(T.pn[:, 0:2], T.ps[:, 2560 + 16:2560 + 32:8], ["#5"], ["pn"], AF.Identity, bias=0.5, scale=-1.0)
         for t in (0, 1):
             ts(T.cmt[:, t:1536:4], T.ios[:], ps(5, 8 * t, 8 * t + 1), A.is_ge, ["#5", "ios"], ["cm%d" % t], f=0.5)
@@ -414,31 +447,12 @@ def rank_program(g, core, T, topo):
             act(T.cmt[:, t:1536:4], T.ios[:], ["pn", "ios"], ["cm%d" % t], AF.Sign, bias=T.pn[:, t - 2:t - 1])
         quant("cm", 0, 384, T.cmt, ["cm%d" % t for t in range(4)], ["cm"])
         mm(1, "ka", 384, "cm", 0, 384, ["cm", "ka1"])
-        mm(0, "fl", 128, "kb", 256, 128, ["fl1", "kb1"], True, False)
-        mm(0, "fl", 64, "kb", 384, 128, ["fl0", "fl1", "kb1"], False, True)
-        tt(T.eq[:], ps(4, 0, 32), T.kd[:, 0:32], A.is_equal, ["#4", "kd"], ["eq"], 1.0)
-        scan(T.wv[:], T.kd[:, 32:64], T.eq[:], 0.0, A.mult, A.add, ["eq", "kdr"], ["wv"])
         add({"V": (lambda: V.transpose(T.lrow[:], ps(1, 0, 384)), vc(384), 0)}, ["#1"], ["lrow"])
         ts(T.pl[:], T.lrow[:, 0:384:32], 128.0, A.add, ["lrow"], ["pl"])
         sl, ld = "slot%d" % r, "land%d" % r
         pick(sl, t_, NF, 512, T.pl[:, 0:12], TA + ["pl"])
-        send(T[ld + "c"][:].bitcast(dt.uint8), T[sl + "c"][:].bitcast(dt.uint8), "ac%d" % r, 2, [sl + "c"], [ld + "c"], 2.2)
-        send(T[ld + "s"][:], T[sl + "s"][:], "ac%d" % r, 2, [sl + "s"], [ld + "s"], 1.8)
-        for t in range(4):
-            ts(T.sot[:, t:1024:4], T.io4[:, 256 * t:256 * t + 256], T.cde[:, t:t + 1], A.is_equal,
-               ["io0%d" % t, "io1%d" % t, "cde", "wv"], ["so%d" % t], T.wv[:, 8 * t + 7:8 * t + 8], A.mult, 0.5)
-        quant("so", 0, 256, T.sot, ["so%d" % t for t in range(4)], ["so"])
-        mm(2, "so", 0, "kb", 0, 128, ["so", "kb0"], True, False)
-        mm(2, "so", 128, "kb", 128, 128, ["so", "kb0"], False, True)
-        act(T.ln[:], ps(2, 0, 128), ["#2", "lc1"], ["ln"], AF.Ln, bias=2.0 ** -62)
-        ts(T.lev[:], T.ln[:], T.lc[:, 2:3], A.mult, ["ln", "lc"], ["lev"], 0.3, A.add)
-        act(T.nb[:], T.ln[:], ["ln"], ["nb"], AF.Relu, bias=-2000.0, scale=-100.0)
-        tt(T.cand[:], ps(0, 0, 128), T.lev[:], A.add, ["#0", "lev"], ["cand"], 1.0)
-        tt(T.cand[:], T.cand[:], T.nb[:], A.add, ["cand", "nb"], ["cand"])
-        scan(T.sm[:], T.kmin[:, 0:128], T.cand[:], 0.0, A.max, A.min, ["cand", "kmin0", "kmin1"], ["sm"])
-        scan(T.pkf[:], T.kmin[:, 128:160], T.sm[:, 65:128:2], 0.0, A.mult, A.add, ["sm", "kpk0", "kpk1"], ["pkf"])
-        cp(T["pk%d" % r][:], T.pkf[:, 1:32:2], ["pkf"], ["pk%d" % r])
-        send(T["lst%d" % r][:], T["pk%d" % r][:], "al%d" % r, 1, ["pk%d" % r], ["lst%d" % r], 1.6)
+        send(T[ld + "c"][:].bitcast(dt.uint8), T[sl + "c"][:].bitcast(dt.uint8), "ac%d" % r, 2, [sl + "c"], [ld + "c"], 2.3)
+        send(T[ld + "s"][:], T[sl + "s"][:], "ac%d" % r, 2, [sl + "s"], [ld + "s"], 2.1)
 
         def unpack(src, base, key, banks, on):
             for k in range(8):
@@ -446,33 +460,30 @@ def rank_program(g, core, T, topo):
                 mm(bk, "eb", 128 * k, src, 0, NF, [src + "c", src + "s", "eb%dc" % (k // 2), "eb%ds" % (k // 2)])
                 o = base + NF * (7 - k)
                 a, z = (0, NF) if r == 0 else (max(0, 136 - 56 * k), NF) if base else (0, min(NF, 399 - 56 * k))
-                mv(T.win[:, o + a:o + z], ps(bk, a, z), ["#%d" % bk], ["%s%d" % (key, k)], 0.5, on=on)
+                mv(T.win[:, o + a:o + z], ps(bk, a, z), ["#%d" % bk], ["%s%d" % (key, k)], SC64, on=on)
         unpack(sl, 0, "wo", (3, 4, 5), "S")
-        ts(T.ko[:], T.sm[:, 1:64:2], float(NF), A.is_lt, ["sm"], ["ko"], -(BIG + NF), A.mult)
-        tt(T.ko[:], T.ko[:], T.sm[:, 1:64:2], A.add, ["ko", "sm"], ["ko"])
-        scan(T.kos[:], T.kst[:, 0:32], T.ko[:], 0.0, A.add, A.min, ["ko", "kst0"], ["kos"])
+        scan(T.kos[:], T.kst[:, 0:32], T.sm[:, 1:64:2], 0.0, A.add, A.min, ["sm", "kst0"], ["kos"])
         tt(T.own[:], T.kos[:, 0:32].indirect(T.rev[:, 0:2]), T.idc[:], A.min, ["kos", "rev", "idc"], ["own"], 3.0)
         unpack(ld, 1536, "wa", (6, 7, 1, 2, 0), "SV")
         cp(T.ai[:], T["lst%d" % r][:], ["lst%d" % r], ["ai"])
         ts(T.a2[:, 0:32:2], T.ai[:], 8, A.arith_shift_right, ["ai"], ["a2h"])
         ts(T.a2[:, 1:32:2], T.ai[:], 255, A.bitwise_and, ["ai"], ["a2l"])
-        ts(T.kn[:], T.a2[:], float(NF), A.is_lt, ["a2h", "a2l"], ["kn"], -BIG, A.mult)
+        ts(T.kn[:], T.a2[:], float(NF), A.is_ge, ["a2h", "a2l"], ["kn"], BIG, A.mult)
         tt(T.kn[:], T.kn[:], T.a2[:], A.add, ["kn", "a2h", "a2l"], ["kn"])
         scan(T.kns[:], T.kst[:, 32:64], T.kn[:], 0.0, A.add, A.min, ["kn", "kst1"], ["kns"])
-        for k in range(4):
-            o = 64 * (k % 2) + 32 * (k // 2)
-            tt(T.rep[0:32, o:o + 32], T.kns[32 * k:32 * k + 32, :], T.own[32 * k:32 * k + 32, :], A.min, ["kns", "own"], ["rep%d" % k])
-        for k in range(1, 4):
-            mv(T.rep[32 * k:32 * k + 32, :], T.rep[0:32, :], ["rep%d" % j for j in range(4)], ["rp%d" % k])
-        ts(T.off[:], T.rep[:, 0:128].indirect(T.ordr[:, 0:7]), 1536.0 + BIG, A.add,
-           ["rp1", "rp2", "rp3", "ordr"] + ["rep%d" % j for j in range(4)], ["off"], f=2.0)
+        for k in range(2):
+            tt(T.rep[0:64, 32 * k:32 * k + 32], T.kns[64 * k:64 * k + 64, :], T.own[64 * k:64 * k + 64, :], A.min, ["kns", "own"], ["rep%d" % k])
+        for k in range(2):
+            mv(T.rep[32 * k:32 * k + 32, 64:128], T.rep[32 - 32 * k:64 - 32 * k, 0:64], ["rep0", "rep1"], ["rp%d" % k])
+        mv(T.rep[64:128, :], T.rep[0:64, :], ["rep0", "rep1", "rp0", "rp1"], ["rp2"])
+        ts(T.off[:], T.rep[:, 0:128].indirect(T.ordr[:, 0:7]), 1536.0, A.add, ["rep0", "rep1", "rp0", "rp1", "rp2", "ordr"], ["off"], f=2.0)
         WIN = ["ft%d" % b for b in range(4)] + ["%s%d" % (a, k) for a in ("wo", "wa") for k in range(8)]
         for h in range(H):
             a, z = CUTS[h], CUTS[h + 1]
             for b1 in range(2):
                 lo, hi = 896 * b1 + 2 * a, 896 * b1 + 2 * z
                 tt(T.yt[:, lo:hi], T.win[:, 0:4864].indirect(T.off[:, lo // 16:hi // 16]), T.fh[:, lo:hi],
-                   A.add, WIN + ["off", "fh%d" % b1], ["yt%d%d" % (b1, h)], 1.8)
+                   A.add, WIN + ["off", "fh%d" % b1], ["yt%d%d" % (b1, h)], 1.6)
             for be in range(4):
                 for b in range(4):
                     o = 896 * (be // 2)
@@ -483,9 +494,8 @@ def rank_program(g, core, T, topo):
                 bk = (4 * h + b) % 8
                 pl = slice(C * b + a, C * b + z)
                 mm(bk, "qw", 128 * b, "qy", a, z - a, ["qy%d" % h, "qwc", "qws"])
-                mv(T.y32[:, pl], T.yy[:, 4 * a + b:4 * z:4], ["yy%d%d%d" % (i, b, h) for i in range(4)], ["y32%d%d" % (b, h)], 32.0, 0.5)
-                tt(T.x32[:, pl], ps(bk, 0, z - a), T.y32[:, pl], A.add, ["#%d" % bk, "y32%d%d" % (b, h)], ["x32%d%d" % (b, h)], 1.0)
-                mv(T.xs[:, 4 * a + b:4 * z:4], T.x32[:, pl], ["x32%d%d" % (b, h)], ["xs%d%d" % (b, h)], 0.03125, 0.5)
+                mv(T.y1[:, pl], T.yy[:, 4 * a + b:4 * z:4], ["yy%d%d%d" % (i, b, h) for i in range(4)], ["y1%d%d" % (b, h)], 32.0, 0.5)
+                tt(T.xs[:, 4 * a + b:4 * z:4], ps(bk, 0, z - a), T.y1[:, pl], A.add, ["#%d" % bk, "y1%d%d" % (b, h)], ["xs%d%d" % (b, h)], 1.0)
             quant_x(r + 1, T.xs, h, ["xs%d%d" % (b, h) for b in range(4)] + ["xsp"])
 
     t_ = "t%d" % R
@@ -493,11 +503,11 @@ def rank_program(g, core, T, topo):
         a, z = CUTS[h], CUTS[h + 1]
         k_ = ["%s_%d" % (t_, h)]
         mm(h, "qv", 0, t_, a, z - a, ["qv"] + k_)
-        dma("Y", "outs", T.oc[:, 4 * a:4 * z], T[t_ + "c"][:, a:z].bitcast(dt.uint8), k_, [])
+        dma("Y", "outs", T.oc[:, 4 * a:4 * z], T[t_ + "c"][:, a:z].bitcast(dt.uint8), k_, [], 2.5)
         mv(T.yo[:, a:z], ps(h, 0, z - a), ["#%d" % h], ["yo%d" % h])
-        dma("Y", "outs", T.y[:, a:z], T.yo[:, a:z], ["yo%d" % h], [])
+        dma("Y", "outs", T.y[:, a:z], T.yo[:, a:z], ["yo%d" % h], [], 2.5)
     for k in range(4):
-        dma("YS", "outs", T.osc[4 * k:4 * k + 4, :], T[t_ + "s"][32 * k:32 * k + 4, 0:C], ["%s_%d" % (t_, h) for h in range(H)], [], 1.8)
+        dma("YS", "outs", T.osc[4 * k:4 * k + 4, :], T[t_ + "s"][32 * k:32 * k + 4, 0:C], ["%s_%d" % (t_, h) for h in range(H)], [], 2.0)
 
     Q = {"V": V, "S": S, "P": g.tensor, "G": g, "Y": g.sync}
     cnt, seen, tok, eng, knew, sent = {}, {e: {} for e in Q}, {}, {}, {}, 0

@@ -3,7 +3,12 @@ from concourse.mybir import dt, AluOpType as A, ActivationFunctionType as AF
 
 C, NF, R = 448, 192, 3
 BIG = 8192.0
-CUTS = (0, 256, 448)
+CUTS = (0, 320, 448)
+B0 = (0, 128, 192, 320)
+B1 = (0, 128, 256, 320, 448)
+CMS = (1, 2, 3)
+GM = False
+GC = "VS"
 Q4, U8, BF, F32, I32, U16 = "float8_e4m3fn_x4", "uint8", "bfloat16", "float32", "int32", "uint16"
 SCRATCH = {}
 
@@ -18,34 +23,33 @@ def _q(name, n):
 
 
 for _r in range(R + 1):
-    _q("t%d" % _r, 512)
+    _q("t%d" % _r, C)
 for _r in range(R):
     _q("slot%d" % _r, NF)
     _q("land%d" % _r, NF)
     _sb("pk%d" % _r, 16, U16)
     _sb("lst%d" % _r, 16, U16)
-for _n, _w in (("qu", 128), ("qup", 128), ("qu1", 128), ("qv", 128), ("qw", 512), ("ef", 512), ("eb", 1024), ("ka", 512),
-               ("kb", 512), ("m", 512), ("fl", 288), ("cm", 384), ("so", 256), ("qy", C)):
+for _n, _w in (("qu", 128), ("qup", 144), ("qv", 128), ("qw", 512), ("ef", 512), ("eb", 1024), ("ka", 384),
+               ("kb", 256), ("kr", 152), ("m", C), ("fl", 288), ("cm", 384), ("so", 128), ("qy", C)):
     _q(_n, _w)
-for _n, _w in (("xin", 2048), ("xs", 2048), ("ut", 512), ("vt", 512), ("eft", 2048), ("th", 128),
-               ("kat", 2048), ("kbt", 2048), ("mt", 2048), ("flt", 1152), ("cmt", 1536), ("sot", 1024), ("dd", 1152), ("ctri", 128),
-               ("ios", 384), ("ioh", 128), ("io4", 1024), ("kv", 128), ("win", 4864), ("yt", 4 * C), ("fh", 4 * C), ("yy", 4 * C),
-               ("y1", 4 * C), ("nar", 384)):
+for _n, _w in (("xin", 4 * C), ("xs", 4 * C), ("ut", 512), ("vt", 512), ("eft", 2048), ("kat", 1536), ("kbt", 1024), ("mt", 4 * C),
+               ("flt", 1152), ("cmt", 1536), ("sot", 512), ("krt", 608), ("ios", 384), ("ioh", 128), ("kv", 128), ("win", 4864),
+               ("yt", 4 * C), ("fh", 4 * C), ("yy", 4 * C), ("y1", 4 * C), ("nar", 384), ("df", C), ("ctri", 128)):
     _sb(_n, _w, BF)
-for _n, _w in (("sc", 80), ("cmx", 80), ("cm2", 80), ("rr", 80), ("cde", 16), ("k72", 160), ("thr", 256), ("th2", 192), ("ebi", 64), ("kd", 64),
-               ("eq", 32), ("wv", 32), ("lrow", 384), ("ln", 128), ("nb", 128), ("cand", 128), ("sm", 128), ("kmin", 160),
+for _n, _w in (("sc", 80), ("cmx", 80), ("cm2", 80), ("rr", 80), ("cde", 16), ("k72", 160), ("thr", 4), ("th2", 4), ("dd", C), ("ebi", 64), ("kd", 64),
+               ("eq", 32), ("wv", 32), ("lrow", 384), ("ln", 128), ("nb", 128), ("cand", 128), ("sm", 64), ("kpk", 32),
                ("pkf", 32), ("kos", 32), ("own", 32), ("kn", 32), ("kns", 32), ("rep", 128), ("kst", 64), ("idc", 32),
-               ("cb", 16), ("w1", 96), ("w2", 80), ("pv", 8), ("yo", C), ("tj", 128), ("acc", 4), ("pn", 4)):
+               ("w1", 32), ("w2", 16), ("pv", 8), ("yo", C), ("tj", 128), ("acc", 8), ("pn", 4)):
     _sb(_n, _w, F32)
-for _n, _w in (("lev", 128), ("ai", 16), ("a2", 32), ("pi", 8), ("wi", 16)):
+for _n, _w in (("lev", 128), ("ai", 16), ("a2", 32), ("pi", 8), ("wi", 8)):
     _sb(_n, _w, I32)
-for _n, _w in (("ul", 8), ("u1l", 8), ("pl", 12), ("rev", 2), ("ordr", 8), ("off", 112), ("ebl", 64)):
+for _n, _w in (("ul", 10), ("pl", 12), ("ordr", 8), ("off", 128), ("ebl", 64)):
     _sb(_n, _w, U16)
 SCRATCH["ps"] = ("psum", [128, 4096], F32)
 SEMAPHORES = ["V", "S", "P", "G", "dx0", "dx1", "du", "dv", "dwc", "dws", "outs", "sent", "dfh0", "dfh1"] + \
              ["%s%d" % (k, r) for k in ("ac", "al") for r in range(R)]
 CY, OV, LAT, PE = 0.00087, 0.05, 0.12, 0.0008
-TRIES = 3000
+TRIES = 6000
 SPAN, PLAN = [0.0], []
 
 
@@ -53,23 +57,20 @@ def name(k):
     return k[0] + k[2:] if k[0] == "t" and k[2:3] == "_" else k[:4] + k[5:] if k[:4] in ("slot", "land") else k[:2] if k[:2] in ("pk", "ls") else k
 
 
-def deal(ops, succ, rank, early, spare):
+def deal(ops, order, spare, back=None):
     n = len(ops)
-    pri = [rank[i] + early.get(ops[i]["key"], 0.0) for i in range(n)]
-    for i in range(n - 1, -1, -1):
-        for j in succ[i]:
-            if pri[j] + 1e-3 > pri[i]:
-                pri[i] = pri[j] + 1e-3
     busy = {}
     done, eng, start = [0.0] * n, [None] * n, [0.0] * n
-    for i in sorted(range(n), key=lambda k: -pri[k]):
+    for i in order:
         best = None
         for e, (fn, hold, tail) in ops[i]["alts"].items():
             t = 0.0
-            for d, raw in ops[i]["deps"].items():
-                u = done[d] + LAT if raw or eng[d] != e else start[d] + 1e-6
+            for d, raw in (back[i] if back else ops[i]["deps"]).items():
+                u = done[d] + LAT if raw or eng[d] != e else (done[d] if back else start[d] + 1e-6)
                 if u > t:
                     t = u
+            if back:
+                t, tail = t + tail, 0.0
             line = busy.setdefault(e, [])
             lo, hi = 0, len(line)
             while lo < hi:
@@ -86,43 +87,59 @@ def deal(ops, succ, rank, early, spare):
                 best = (t + hold + tail, t, e, hold, val, lo)
         done[i], start[i], eng[i] = best[0], best[1], best[2]
         busy[best[2]].insert(best[5], (best[1], best[1] + best[3]))
-    return max(done), sorted((start[i], i, eng[i]) for i in range(n))
+    return max(done), start, done, eng
 
 
 def schedule(ops):
     if PLAN:
         return PLAN[0]
     n = len(ops)
-    succ = [[] for _ in range(n)]
+    succ = [{} for _ in range(n)]
     for i, o in enumerate(ops):
-        for d in o["deps"]:
-            succ[d].append(i)
-    rank = [0.0] * n
+        for d, raw in o["deps"].items():
+            succ[d][i] = raw
+    pri = [0.0] * n
     for i in range(n - 1, -1, -1):
         c = min(a[1] + a[2] for a in ops[i]["alts"].values())
-        rank[i] = c + LAT + max([rank[j] for j in succ[i]] + [0.0])
+        pri[i] = c + LAT + max([pri[j] for j in succ[i]] + [0.0])
     keys = sorted(set(o["key"] for o in ops))
     both = sorted(set(o["key"] for o in ops if len(o["alts"]) > 1 and "V" in o["alts"]))
-    early, spare = {}, {k: 0.3 for k in both}
-    best = deal(ops, succ, rank, early, spare)
+    spare = {k: 0.3 for k in both}
+
+    def forward(p, sp):
+        p = list(p)
+        for i in range(n - 1, -1, -1):
+            for j in succ[i]:
+                if p[j] + 1e-4 > p[i]:
+                    p[i] = p[j] + 1e-4
+        return deal(ops, sorted(range(n), key=lambda k: -p[k]), sp)
+    best = cur = forward(pri, spare)
     z = 12345
-    for _ in range(TRIES):
-        e2, s2 = dict(early), dict(spare)
-        for _k in range(3):
+    for it in range(TRIES):
+        s2, shift = dict(spare), {}
+        for _k in range(2):
             z = (z * 1103515245 + 12345) % 2147483648
             step = (-2.0, -1.0, -0.5, -0.2, 0.2, 0.5, 1.0, 2.0)[(z >> 8) % 8]
             if (z >> 12) % 3 == 0:
                 k = both[(z >> 14) % len(both)]
-                s2[k] = s2.get(k, 0.0) + step / 2
+                s2[k] += step / 2
             else:
-                k = keys[(z >> 14) % len(keys)]
-                e2[k] = e2.get(k, 0.0) + step
-        got = deal(ops, succ, rank, e2, s2)
-        if got[0] <= best[0]:
-            best, early, spare = got, e2, s2
+                shift[keys[(z >> 14) % len(keys)]] = step
+        p2 = [pri[i] + shift.get(ops[i]["key"], 0.0) for i in range(n)]
+        got = forward(p2, s2)
+        if it % 10 == 0:
+            p3 = deal(ops, sorted(range(n), key=lambda k: (-got[2][k], -k)), s2, succ)[2]
+            again = forward(p3, s2)
+            if again[0] < got[0]:
+                got, p2 = again, p3
+        z = (z * 1103515245 + 12345) % 2147483648
+        if got[0] <= cur[0] + 0.15 * (1 - it / TRIES) * ((z >> 8) % 1000) / 1000:
+            cur, pri, spare = got, p2, s2
+            if got[0] < best[0]:
+                best = got
     SPAN[0] = best[0]
-    PLAN.append(best[1])
-    return best[1]
+    PLAN.append(sorted((best[1][i], i, best[3][i]) for i in range(n)))
+    return PLAN[0]
 
 
 def rank_program(g, core, T, topo):
@@ -167,8 +184,9 @@ def rank_program(g, core, T, topo):
         else:
             add({"V": (lambda: V.tensor_scalar(out, in0, s1, s2, o0, o1), vc(w(out), f), 0)}, rd, wr)
 
-    def tt(out, a, b, o, rd, wr, f=2.0):
-        add({"V": (lambda: V.tensor_tensor(out, a, b, o), vc(w(out), f), 0)}, rd, wr)
+    def tt(out, a, b, o, rd, wr, f=2.0, alone=False):
+        add({"V": (lambda: V.tensor_tensor(out, a, b, o), vc(w(out), f) + LAT * alone, -LAT * alone)}, rd, wr)
+        ops[-1]["alone"] = alone
 
     def cp(out, a, rd, wr, f=1.0):
         add({"V": (lambda: V.tensor_copy(out, a), vc(w(out), f), 0)}, rd, wr)
@@ -190,7 +208,7 @@ def rank_program(g, core, T, topo):
     def ms(ap, v, wr, f=1.0, s=True):
         alts = {"V": (lambda: V.memset(ap, v), vc(w(ap), f), 0)}
         if s and w(ap) <= 128:
-            alts["S"] = (lambda: S.activation(ap, T.tj[:, 0:w(ap)], AF.Identity, bias=float(v), scale=0.0), vc(w(ap)), 0)
+            alts["S"] = (lambda: S.activation(ap, T.tj[0:ap.shape[0], 0:w(ap)], AF.Identity, bias=float(v), scale=0.0), vc(w(ap)), 0)
         elif s:
             alts["S"] = (lambda: S.activation(ap, T.kat[0:ap.shape[0], 0:w(ap)], AF.Identity, bias=float(v), scale=0.0), vc(w(ap)), 0)
         add(alts, [] if len(alts) == 1 else ["tj"] if w(ap) <= 128 else ["kat0"], wr)
@@ -242,37 +260,19 @@ def rank_program(g, core, T, topo):
     iota(T.tj[:], [[1, 128]], 0, -1, ["tj"])
     iota(T.k72[:, 0:72], [[-15, 2], [0, 36]], 16, 0, ["k72a"])
     iota(T.kd[:, 0:32], [[0, 4], [-1, 8]], -1, 0, ["kd"])
-    iota(T.th[:, 0:64], [[1, 4], [7, 8], [1, 2]], -7, 0, ["tha"])
-    iota(T.th[:, 64:128], [[1, 4], [-7, 8], [1, 2]], 49, 0, ["thb"])
-    iota(T.kv[:, 0:64], [[16, 4], [1, 8], [128, 2]], -1, 0, ["kva"])
-    iota(T.kv[:, 64:128], [[16, 4], [-1, 8], [128, 2]], 7, 0, ["kvb"])
     iota(T.ios[:], [[16, 12], [0, 2], [1, 16]], 0, 0, ["ios"])
-    for k in range(4):
-        iota(T.ioh[:, 32 * k:32 * k + 32], [[16, 2], [1, 8], [32, 2]], 64 * k - 105, 0, ["ioh%d" % k])
-    iota(T.w1[:, 0:8], [[-1, 2], [16, 4]], 0, 0, ["w1a"])
-    iota(T.w1[:, 8:16], [[16, 8]], 0, 0, ["w1b"])
-    iota(T.idc[:], [[16, 4], [-112, 8]], 784 + 1536, 0, ["idc"])
-    IOH = ["ioh%d" % k for k in range(4)]
     ms(T.kat[:, 0:512], 1.0, ["kat0"], 0.5, False)
-    ms(T.mt[:], 0.0, ["mtp"], 0.5, False)
-    ms(T.xin[:, 1792:2048], 0.0, ["xinp"], 0.5)
-    ms(T.xs[:, 1792:2048], 0.0, ["xsp"], 0.5)
-    ms(T.u1l[:], 1, ["u1l"], s=False)
+    for t, z in ((1, 128), (2, C), (3, 320)):
+        ms(T.mt[:, t:4 * z:4], 0.0, ["mtp%d" % t], 0.5)
     ms(T.ul[:], 1, ["ul"], s=False)
-    ts(T.pi[:, 1:2], T.pi[:, 0:1], 15, A.bitwise_and, ["pi0"], ["pi1"])
-    ts(T.pi[:, 2:3], T.pi[:, 0:1], 7, A.bitwise_and, ["pi0"], ["pi2"])
-    ts(T.pi[:, 3:4], T.pi[:, 0:1], 3, A.arith_shift_right, ["pi0"], ["pi3"])
-    ts(T.pi[:, 4:5], T.pi[:, 0:1], 5, A.arith_shift_right, ["pi0"], ["pi4"], 1, A.bitwise_and)
-    ts(T.pi[:, 5:6], T.pi[:, 0:1], 6, A.arith_shift_right, ["pi0"], ["pi5"])
+    for k, (n, o) in enumerate(((15, A.bitwise_and), (7, A.bitwise_and), (3, A.arith_shift_right), (32, A.bitwise_and), (79, A.bitwise_and))):
+        ts(T.pi[:, k + 1:k + 2], T.pi[:, 0:1], n, o, ["pi0"], ["pi%d" % (k + 1)])
     cp(T.pv[:, 0:5], T.pi[:, 1:6], ["pi1", "pi2", "pi3", "pi4", "pi5"], ["pv"])
-    ts(T.w2[:, 0:1], T.pv[:, 0:1], 8.0, A.is_lt, ["pv"], ["w20"], T.pv[:, 0:1], A.mult)
-    ts(T.w2[:, 1:2], T.pv[:, 0:1], 8.0, A.is_ge, ["pv"], ["w21"])
-    ts(T.ul[:, 0:1], T.w2[:, 0:1], 16.0, A.mult, ["w20", "w21"], ["ul"], T.w2[:, 1:2], A.add)
+    ts(T.pi[:, 6:7], T.pi[:, 0:1], 14, A.bitwise_and, ["pi0"], ["pi6"])
+    ts(T.ul[:, 0:1], T.pi[:, 6:7], 8.0, A.mult, ["pi6"], ["ul"])
     quant("qu", 0, 128, T.ut, ["ut"], ["qu"])
-    pick("qup", "qu", 128, 128, T.ul[:, 0:8], ["qu", "ul"])
-    pick("qu1", "qu", 128, 128, T.u1l[:, 0:8], ["qu", "u1l"])
+    pick("qup", "qu", 144, 128, T.ul[:, 0:9], ["qu", "ul"])
     quant("qv", 0, 128, T.vt, ["vt"], ["qv"])
-    ts(T.ctri[:], T.tj[:], 0.0, A.is_gt, ["tj"], ["ctri"], 2.0 ** -100, A.mult)
     quant("ka", 0, 128, T.kat, ["kat0"], ["ka0"])
     one = T.kat[:, 0:128]
     asel(T.nar[:, 0:128], one, [[1, 128]], A.is_ge, 0.0, 0, -1, ["kat0"], ["tri"])
@@ -281,20 +281,28 @@ def rank_program(g, core, T, topo):
     for t in range(4):
         mv(T.kat[:, 512 + t:1024:4], T.nar[:, 0:128], ["tri"], ["kat1%d" % t], f=0.5)
         mv(T.kat[:, 1024 + t:1536:4], T.nar[:, 256:384], ["del"], ["kat2%d" % t], f=0.5)
-        ms(T.kat[:, 1536 + t:2048:4], 1.0 if t < 2 else 0.5, ["kat3%d" % t], 0.5)
-    quant("ka", 128, 512, T.kat, ["kat%d%d" % (a, t) for a in (1, 2, 3) for t in range(4)], ["ka1"])
-    ms(T.flt[:, 0:512], 0.0, ["flz", "fa3"], 0.5)
-    ms(T.flt[:, 512:1152], 0.0, ["fly", "fb3"], 0.5, False)
-    quant("fl", 128, 256, T.flt, ["fly"], ["flw", "fl1"])
-    ms(T.thr[:], -1.0, ["thr%d" % t for t in range(4)] + ["thc%d" % t for t in range(4)])
-    for t in range(4):
-        ms(T.thr[:, 72 * t:72 * t + 8], float(NF), ["thr%d" % t])
-        if t < 3:
-            ms(T.thr[:, 72 * t + 40:64 * t + 64], float(NF), ["thc%d" % t])
+    quant("ka", 128, 384, T.kat, ["kat%d%d" % (a, t) for a in (1, 2) for t in range(4)], ["ka1"])
+    ms(T.flt[:, 0:512], 0.0, ["flz"], 0.5)
+    ms(T.flt[:, 512:640], 0.0, ["fly"], 0.5)
+    ms(T.flt[0:64, 642:1152:4], 0.0, ["fb2"], 0.5)
+    ms(T.cmt[0:64, 2:1536:4], 0.0, ["cm2"], 0.5)
+    quant("fl", 32, 160, T.flt, ["flz", "fly"], ["flw", "fl0"])
+    ms(T.krt[:, 0:256], 256.0, ["kr0"], 0.5)
+    ms(T.krt[:, 96:128], 1.0, ["kr0"], 0.5)
+    ms(T.krt[:, 256:608], 1.0, ["kr1"], 0.5)
+    quant("kr", 0, 152, T.krt, ["kr0", "kr1"], ["kr"])
+    if GM:
+        iota(T.thr[:], [[192, 2], [128, 2]], NF - C + 1, 1, ["thr"])
+        lin(T.thr[:], T.thr[:], 1.0 / 128, 0.0, ["thr"], ["thr"])
+    else:
+        ts(T.ctri[:], T.tj[:], 0.0, A.is_ge, ["tj"], ["ctri"], 2.0 ** -100, A.mult)
+        for t in range(3):
+            ms(T.thr[:, t:t + 1], (NF + 1 - C + B1[t + 1]) / 128, ["thr"])
+        ms(T.acc[:, 7:8], NF + 1.0, ["bnd3"])
     ms(T.k72[:, 80:152], 0.0, ["k72d"])
     ms(T.k72[:, 88:152:9], -1e29, ["k72d"])
     ms(T.cmx[:, 0:1], -1e29, ["cmx0"])
-    ms(T.kd[:, 32:64], math.exp(-1.0), ["kdr"])
+    ms(T.kd[:, 32:64], math.exp(-1.0), ["kdr"], s=False)
     act(T.kd[:, 32:64:8], T.kat[:, 0:4], ["kat0"], ["kdr"], AF.Ln, 1.3)
     for b in range(4):
         asel(T.eft[:, 512 * b:512 * b + 512], T.kat[:, 0:512], [[-256, 4], [-1, 32], [256, 4]], A.is_equal, 0.0, -32 * b, 1, ["kat0"], ["eft%d" % b])
@@ -304,69 +312,42 @@ def rank_program(g, core, T, topo):
     ts(T.ebl[:], T.ebi[:], T.pv[:, 0:1], A.add, ["ebi0", "ebi1", "pv"], ["ebl"])
     for b in range(4):
         pick("eb", "ef", 256, 512, T.ebl[:, 16 * b:16 * b + 16], ["ef%d" % j for j in range(4)] + ["ebl"], 256 * b, "eb%d" % b)
-    lin(T.w2[:, 8:16], T.w1[:, 0:8], 1.0, T.pv[:, 2:3], ["w1a", "pv"], ["c"])
-    lin(T.w2[:, 16:24], T.w2[:, 8:16], 1.0 / 7.0, -3.0 / 7.0, ["c"], ["mf"])
-    lin(T.w2[:, 72:76], T.w2[:, 8:12], -1.0, -0.5, ["c"], ["c0"])
-    lin(T.w2[:, 76:80], T.w2[:, 8:12], -1.0, 3.5, ["c"], ["c4"])
-    cp(T.wi[:, 0:8], T.w2[:, 16:24], ["mf"], ["mi"])
-    ts(T.w2[:, 56:64], T.wi[:, 0:8], -7.0, A.mult, ["mi"], ["m7"])
-    tt(T.w2[:, 24:32], T.w2[:, 56:64], T.w2[:, 8:16], A.add, ["m7", "c"], ["rho"])
-    ts(T.w2[:, 32:40], T.w2[:, 24:32], 4.0, A.is_ge, ["rho"], ["y128"], -128.0, A.mult)
-    ts(T.cb[:, 0:4], T.w2[:, 32:36], T.pv[:, 1:2], A.subtract, ["y128", "pv"], ["cb0"])
-    ts(T.cb[:, 4:8], T.w2[:, 36:40], T.pv[:, 1:2], A.subtract, ["y128", "pv"], ["cb1"], -8.0, A.add)
-    for a in range(2):
-        for t in range(4):
-            lin(T.io4[:, 256 * t + 128 * a:256 * t + 128 * a + 128], T.ioh[:], 1.0, T.cb[:, 4 * a + t:4 * a + t + 1], IOH + ["cb%d" % a], ["io%d%d" % (a, t)], 0.5)
-    lin(T.w2[:, 40:44], T.w2[:, 24:28], 16.0, 0.0, ["rho"], ["r16a"])
-    lin(T.w2[:, 44:48], T.w2[:, 28:32], 16.0, 128.0, ["rho"], ["r16b"])
-    ts(T.w2[:, 48:56], T.w2[:, 24:32], 4.0, A.is_ge, ["rho"], ["y64"], -64.0, A.mult)
-    tt(T.w2[:, 64:72], T.w2[:, 40:48], T.wi[:, 0:8], A.add, ["r16a", "r16b", "mi"], ["r17"])
-    tt(T.cb[:, 8:16], T.w2[:, 64:72], T.w2[:, 48:56], A.add, ["r17", "y64"], ["rid"])
-    for a in range(2):
-        for t in range(4):
-            ts(T.kbt[:, 512 * a + t:512 * a + 512:4], T.kv[:], T.cb[:, 8 + 4 * a + t:9 + 4 * a + t], A.is_equal,
-               ["kva", "kvb", "rid"], ["kb%d%d" % (a, t)], f=0.5)
-            act(T.kbt[:, 1024 + 512 * a + t:1536 + 512 * a:4], T.th[:], ["tha", "thb", "c0", "c4"], ["kb%d%d" % (2 + a, t)], AF.Sign,
-                bias=T.w2[:, 72 + 4 * a + t:73 + 4 * a + t])
-        for z in range(2):
-            o = T.kbt[:, 1024 + 512 * a + 256 * z:1280 + 512 * a + 256 * z]
-            lin(o, o, 0.5, z - 0.5, ["kb%d%d" % (2 + a, t) for t in range(4)], ["kc%d%d" % (a, z)], 0.5)
-    quant("kb", 0, 256, T.kbt, ["kb%d%d" % (a, t) for a in (0, 1) for t in range(4)], ["kb0"])
-    quant("kb", 256, 512, T.kbt, ["kc00", "kc01", "kc10", "kc11"], ["kb1"])
-    ms(T.kmin[:, 0:128:2], 2 * BIG, ["kmin0"])
-    ms(T.kmin[:, 1:128:2], -BIG, ["kmin1"])
-    ms(T.kmin[:, 128:160:2], 0.0, ["kpk0"])
-    ms(T.kmin[:, 129:160:2], 256.0, ["kpk1"])
-    ms(T.kst[:, 0:32], -float(NF), ["kst0"])
-    ms(T.kst[:, 32:64], float(NF), ["kst1"])
-    ms(T.kst[:, 0:64:8], 2 * BIG, ["kst0", "kst1"])
-    lin(T.w2[:, 2:3], T.pv[:, 3:4], 896.0, T.pv[:, 0:1], ["pv"], ["w22"])
-    lin(T.w2[:, 3:4], T.pv[:, 4:5], 64.0, T.w2[:, 2:3], ["pv", "w22"], ["w23"])
+    for k in range(4):
+        iota(T.ioh[:, 32 * k:32 * k + 32], [[16, 2], [1, 8], [32, 2]], 64 * (k % 2) - 8 * (k // 2) - 105, 0, ["ioh%d" % k])
+    ts(T.ioh[:], T.ioh[:], T.pv[:, 1:2], A.subtract, ["ioh%d" % k for k in range(4)] + ["pv"], ["io"], f=0.5)
+    iota(T.kv[:], [[7, 2], [1, 8], [-7, 8]], 42, 0, ["kv"])
+    iota(T.w1[:, 16:20], [[24, 2], [16, 2]], 0, 0, ["w1c"])
+    lin(T.w2[:, 8:12], T.w1[:, 16:20], 1.0, T.pv[:, 2:3], ["w1c", "pv"], ["c"])
+    for t in range(4):
+        ts(T.kbt[:, t:512:4], T.kv[:], T.w2[:, 8 + t:9 + t], A.is_equal, ["kv", "c"], ["kb0%d" % t], f=0.5)
+        ts(T.kbt[:, 512 + t:1024:4], T.kv[:], T.w2[:, 8 + t:9 + t], A.is_gt, ["kv", "c"], ["kb1%d" % t], f=0.5)
+    lin(T.kbt[:, 512:768], T.kbt[:, 512:768], 1.0, -1.0, ["kb1%d" % t for t in range(4)], ["kc"], 0.5)
+    quant("kb", 0, 256, T.kbt, ["kb0%d" % t for t in range(4)] + ["kc"], ["kb"])
+    iota(T.kpk[:], [[0, 16], [256, 2]], 0, 0, ["kpk"])
+    iota(T.kst[:], [[2 * NF, 2], [0, 32]], -NF, 0, ["kst"])
+    ms(T.kst[:, 0:64:8], 2 * BIG, ["kst"])
+    ms(T.sm[:], 255.0, ["sm00", "sm01", "sm10", "sm11"])
+    iota(T.idc[:], [[16, 4], [-112, 8]], 784 + 1536, 0, ["idc"])
+    lin(T.w2[:, 3:4], T.pv[:, 3:4], 28.0, T.pv[:, 4:5], ["pv"], ["w23"])
     lin(T.idc[:], T.idc[:], 1.0, T.w2[:, 3:4], ["idc", "w23"], ["idc"])
-    n_ = T.w1[:, 16:24]
-    lin(n_, T.w1[:, 8:16], 1.0, T.pv[:, 0:1], ["w1b", "pv"], ["n"])
-    lin(T.w2[:, 4:5], T.pv[:, 1:2], -2.0, 7.0, ["pv"], ["w24"])
-    ts(T.rev[:], T.w1[:, 16:18], T.w2[:, 4:5], A.add, ["n", "w24"], ["rev"])
-    lin(T.w1[:, 40:48], n_, 1.0 / 7.0, -3.0 / 7.0, ["n"], ["mf2"])
-    cp(T.wi[:, 8:16], T.w1[:, 40:48], ["mf2"], ["mi2"])
-    ts(T.w1[:, 64:72], T.wi[:, 8:16], -57.0, A.mult, ["mi2"], ["m72"])
-    lin(T.w2[:, 5:6], T.pv[:, 3:4], 64.0, 7.0, ["pv"], ["w25"])
-    lin(T.w2[:, 6:7], T.pv[:, 3:4], -128.0, 72.0, ["pv"], ["w26"])
-    lin(T.w1[:, 72:80], n_, 8.0, T.w2[:, 5:6], ["n", "w25"], ["r8"])
-    ts(T.w1[:, 80:88], n_, 56.0, A.is_ge, ["n", "w26"], ["b32"], T.w2[:, 6:7], A.mult)
-    tt(T.w1[:, 72:80], T.w1[:, 72:80], T.w1[:, 64:72], A.add, ["r8", "m72"], ["r8"])
-    tt(T.w1[:, 88:96], T.w1[:, 72:80], T.w1[:, 80:88], A.add, ["r8", "b32"], ["o2"])
-    cp(T.ordr[:], T.w1[:, 88:96], ["o2"], ["ordr"])
+    iota(T.w1[:, 0:8], [[0, 2], [16, 4]], -3, 0, ["w1a"])
+    iota(T.w1[:, 8:16], [[64, 2], [128, 4]], 7, 0, ["w1b"])
+    ts(T.wi[:], T.w1[:, 0:8], T.pv[:, 0:1], A.add, ["w1a", "pv"], ["wi"], 1.0 / 7.0, A.mult)
+    lin(T.w2[:, 0:1], T.pv[:, 0:1], 8.0, 0.0, ["pv"], ["w20"])
+    for k in range(2):
+        lin(T.w2[:, 1 + k:2 + k], T.pv[:, 3:4], 2.0 - 4 * k, T.w2[:, 0:1], ["pv", "w20"], ["w2%d" % (k + 1)])
+        ts(T.w1[:, 24 + 4 * k:28 + 4 * k], T.wi[:, 4 * k:4 * k + 4], -57.0, A.mult, ["wi", "w2%d" % (k + 1)], ["o%d" % k], T.w2[:, 1 + k:2 + k], A.add)
+    tt(T.w1[:, 24:32], T.w1[:, 24:32], T.w1[:, 8:16], A.add, ["o0", "o1", "w1b"], ["o2"])
+    cp(T.ordr[:], T.w1[:, 24:32], ["o2"], ["ordr"])
 
     H = len(CUTS) - 1
     SC64 = 1.0 / 64
 
     def quant_x(r, tile, h, rd):
-        last = h == H - 1 and r < R
-        quant("t%d" % r, CUTS[h], 512 if last else CUTS[h + 1], tile, rd, ["t%d_%d" % (r, h)])
+        quant("t%d" % r, CUTS[h], CUTS[h + 1], tile, rd, ["t%d_%d" % (r, h)])
 
     for h in range(H):
-        quant_x(0, T.xin, h, ["xin0", "xinp"] + (["xin1"] if CUTS[h + 1] > 256 else []))
+        quant_x(0, T.xin, h, ["xin0"] + (["xin1"] if CUTS[h + 1] > 256 else []))
 
     for r in range(R):
         t_ = "t%d" % r
@@ -375,36 +356,47 @@ def rank_program(g, core, T, topo):
         def tk(a, b):
             return ["%s_%d" % (t_, h) for h in range(H) if CUTS[h] < b and a < CUTS[h + 1]]
         for t, bk in enumerate((0, 1, 4, 5)):
-            mm(bk, t_, 128 * t, "qup", 0, 128, tk(128 * t, 128 * t + 128) + ["qupc", "qups"])
-            mv(T.sc[:, 9 * t:9 * t + 9], ps(bk, 0, 9), ["#%d" % bk], ["sc%d" % t])
-        for bk, a, z in ((3, 0, 256), (2, 128, C), (7, 256, C)):
-            mm(bk, "qu1", 0, t_, a, z - a, tk(a, z) + ["qu1c", "qu1s"])
-
-        def si(t, p=128):
-            return T.sc[0:p, 9 * t + 8:9 * t + 9]
-
-        def mt(t, a, b, p=128):
-            return T.mt[0:p, 4 * a + t:4 * b:4]
+            mm(bk, t_, B0[t], "qup", 0, 128, tk(B0[t], B0[t] + 128) + ["qupc", "qups"])
+            mv(T.sc[:, 9 * t:9 * t + 9], T.ps[:, 512 * bk:512 * bk + 18:2], ["#%d" % bk], ["sc%d" % t])
+        ROW = ((2, 0, 320), (6, 320, C))
+        for bk, a, z in ROW + ((3, 0, 320), (7, 320, C)) * (not GM):
+            mm(bk, "qup", 16, t_, a, z - a, tk(a, z) + ["qupc", "qups"])
+        MK = ["mtp1", "mtp2", "mtp3"]
         for t in range(4):
-            p, a = (128 if t < 3 else 64), 128 * t
-            act(T.dd[0:p, a:a + p], ps(3 if t < 2 else 7, a % 256, a % 256 + p, p), ["#%d" % (3 if t < 2 else 7), "sc%d" % t], ["d%d" % t],
-                AF.Identity, bias=si(t, p), scale=-1.0)
-            tt(mt(t, a, a + p, p), T.dd[0:p, a:a + p], T.ctri[0:p, 0:p], A.is_lt, ["d%d" % t, "ctri", "mtp"], ["md%d" % t])
-            if t < 3:
-                ts(mt(t, a + 128, C), ps(2, a, C - 128), si(t), A.is_ge, ["#2", "sc%d" % t, "mtp"], ["mu%d" % t])
-                act(T.dd[:, 512:512 + C - 128 - a], mt(t, a + 128, C), ["mu%d" % t], ["acc%d" % t, "junk"], AF.Identity, 0.02,
-                    bias=-1.0, accum_out=T.acc[:, t:t + 1])
-                act(T.th2[:, 64 * t:64 * t + 64], T.thr[:, 64 * t:64 * t + 64], ["acc%d" % t, "thr%d" % t, "thc%d" % t], ["th2%d" % t], AF.Identity,
-                    bias=T.acc[:, t:t + 1])
+            p, a, z = slice(64 * (t == 2), 128), B1[t], B1[t + 1]
+            bias = T.thr[p, t:t + 1]
+            if not GM:
+                bk = 3 if t < 3 else 7
+                act(T.df[p, a:z], T.ps[p, 512 * bk + a % 320:512 * bk + a % 320 + z - a], ["#%d" % bk, "sc%d" % t], ["d%d" % t], AF.Identity,
+                    bias=T.sc[p, 9 * t + 8:9 * t + 9], scale=-1.0)
+                MK.append("md%d%d" % (t, 2 if t < 3 else 6))
+                tt(T.mt[p, 4 * a + t:4 * z:4], T.df[p, a:z], T.ctri[p, p.start:128], A.is_lt, ["d%d" % t, "ctri"] + MK[:3], MK[-1:])
+                a = z
+            for bk, lo, hi in ROW:
+                if max(lo, a) < hi:
+                    k, o = "mu%d%d" % (t, bk), T.mt[p, 4 * max(lo, a) + t:4 * hi:4]
+                    ts(o, T.ps[p, 512 * bk + max(lo, a) - lo:512 * bk + hi - lo], T.sc[p, 9 * t + 8:9 * t + 9], A.is_ge,
+                       ["#%d" % bk, "sc%d" % t] + MK[:3], [k])
+                    if lo <= a and GM:
+                        d = T.mt[:, 4 * a + t:4 * z:4]
+                        asel(d, d, [[1, z - a]], A.is_ge, 0.0, p.start, -1, [k], [k])
+                    MK.append(k)
+                    if hi < C:
+                        act(T.dd[p, a:hi], o, [k], ["acc%d" % t, "junk2"], AF.Identity, 0.02, accum_out=T.acc[p, t:t + 1])
+                        lin(T.th2[p, t:t + 1], T.acc[p, t:t + 1], 1.0 / 128, bias, ["acc%d" % t, "thr"], ["th2%d" % t])
+                        bias = T.th2[p, t:t + 1]
+                    else:
+                        act(T.dd[p, lo:hi], o, [k, "th2%d" % t, "thr"], ["bnd%d" % t, "junk6"], AF.Identity, 0.02, bias=bias, accum_out=T.acc[p, 4 + t:5 + t])
         SC = ["sc0", "sc1", "sc2", "sc3"]
         mv(T.sc[:, 36:72], T.sc[:, 0:36], SC, ["scn"], -1.0)
-        quant("m", 0, 512 if r == 0 else C, T.mt, ["md0", "md1", "md2", "md3", "mu0", "mu1", "mu2", "mtp"], ["m"])
+        for bk, a, z in ROW:
+            quant("m", a, z, T.mt, MK[:3] + [k for k in MK[3:] if k[-1] == str(bk)], ["m%d" % bk])
         for t in range(4):
-            mm(t, "m", 128 * t, "ka", 0, 128, ["m", "ka0"])
+            mm(t, "m", B0[t], "kr", 24 - 8 * t, 128, ["m%d" % (2 if t < 3 else 6), "kr"])
         scan(T.cmx[:, 1:73], T.sc[:, 0:72], T.k72[:, 80:152], -1e29, A.max, A.add, SC + ["scn", "k72d"], ["cmx"])
         tt(T.rr[:, 0:72], T.sc[:, 0:72], T.cmx[:, 0:72], A.is_le, SC + ["scn", "cmx", "cmx0"], ["rr"])
-        scan(T.cm2[:, 0:72], T.k72[:, 0:72], T.rr[:, 0:72], 0.0, A.add, A.mult, ["rr", "k72a"], ["cm2"])
-        tt(T.cde[:, 0:4], T.cm2[:, 43:72:9], T.cm2[:, 7:36:9], A.subtract, ["cm2"], ["cde"])
+        scan(T.cm2[:, 0:72], T.k72[:, 0:72], T.rr[:, 0:72], 0.0, A.add, A.mult, ["rr", "k72a"], ["cm2s"])
+        tt(T.cde[:, 0:4], T.cm2[:, 43:72:9], T.cm2[:, 7:36:9], A.subtract, ["cm2s"], ["cde"])
         for b in range(4):
             mm(6 + b % 2, "ef", 128 * b, t_, 0, C, ["ef%d" % b] + TA)
             o = 3072 + 896 * (b // 2) + b % 2
@@ -412,83 +404,86 @@ def rank_program(g, core, T, topo):
         for k in range(2):
             dma("Y", "dfh%d" % k, T.fh[:, 896 * k:896 * k + 896], T.win[:, 3072 + 896 * k:3968 + 896 * k], ["ft%d" % (2 * k), "ft%d" % (2 * k + 1)], ["fh%d" % k], 2.9)
         for t in range(4):
-            p = 128 if t < 3 else 64
-            th_ = (T.th2 if t < 3 else T.thr)[0:p, 64 * t:64 * t + 64]
-            tt(T.flt[0:p, t:256:4], ps(t, 0, 64, p), th_, A.is_lt, ["#%d" % t, "flz", "th2%d" % t if t < 3 else "thr3"], ["fa%d" % t], 1.0)
-            act(T.flt[0:p, 640 + t:896:4], T.tj[0:p, 0:64], ["fa%d" % t, "tj", "flw"], ["fb%d" % t], AF.Identity, bias=T.flt[0:p, 33 * t:33 * t + 1], scale=0.0)
+            p = slice(64 * (t == 2), 128)
+            ts(T.flt[p, t:256:4], T.ps[p, 512 * t:512 * t + 64], T.acc[p, 4 + t:5 + t], A.is_lt, ["#%d" % t, "flw", "bnd%d" % t], ["fa%d" % t])
+            act(T.flt[p, 640 + t:1152:4], T.tj[p, :], ["fa%d" % t, "tj"], ["fb%d" % t], AF.Identity, bias=T.flt[p, 33 * t:33 * t + 1], scale=0.0)
         quant("fl", 0, 128, T.flt, ["fa%d" % t for t in range(4)], ["fl0"])
         quant("fl", 160, 288, T.flt, ["fb%d" % t for t in range(4)], ["fl1"])
         mm(5, "ka", 128, "fl", 0, 128, ["fl0", "ka1"], True, False)
-        mm(5, "ka", 0, "fl", 32, 128, ["fl0", "flw"], False, True)
+        mm(5, "ka", 0, "fl", 32, 128, ["fl0", "flw", "ka0"], False, True)
         mm(4, "ka", 256, "fl", 0, 128, ["fl0", "ka1"])
         tt(T.eq[:], ps(4, 0, 32), T.kd[:, 0:32], A.is_equal, ["#4", "kd"], ["eq"], 1.0)
         scan(T.wv[:], T.kd[:, 32:64], T.eq[:], 0.0, A.mult, A.add, ["eq", "kdr"], ["wv"])
         for t in range(4):
-            ts(T.sot[:, t:1024:4], T.io4[:, 256 * t:256 * t + 256], T.cde[:, t:t + 1], A.is_equal,
-               ["io0%d" % t, "io1%d" % t, "cde", "wv"], ["so%d" % t], T.wv[:, 8 * t + 7:8 * t + 8], A.mult, 0.5)
-        quant("so", 0, 256, T.sot, ["so%d" % t for t in range(4)], ["so"])
-        mm(0, "fl", 160, "kb", 256, 128, ["fl1", "kb1"], True, False)
-        mm(0, "fl", 96, "kb", 384, 128, ["fl0", "fl1", "flw", "kb1"], False, True)
-        mm(2, "so", 0, "kb", 0, 128, ["so", "kb0"], True, False)
-        mm(2, "so", 128, "kb", 128, 128, ["so", "kb0"], False, True)
-        act(T.ln[:], ps(2, 0, 128), ["#2", "kdr"], ["ln"], AF.Ln, bias=2.0 ** -62, scale=math.exp(-0.2))
-        act(T.nb[:, 64:128], ps(2, 64, 128), ["#2"], ["nb1"], AF.Identity, bias=255.0, scale=-2.0 ** 30)
-        act(T.nb[:, 0:64], ps(2, 0, 64), ["#2"], ["nb0"], AF.Identity, bias=BIG, scale=-2.0 ** 30)
-        tt(T.lev[:], ps(0, 0, 128), T.ln[:], A.subtract, ["#0", "ln"], ["lev"], 1.0)
-        tt(T.cand[:], T.lev[:], T.nb[:], A.max, ["lev", "nb0", "nb1"], ["cand"])
-        scan(T.sm[:], T.kmin[:, 0:128], T.cand[:], 0.0, A.max, A.min, ["cand", "kmin0", "kmin1"], ["sm"])
-        scan(T.pkf[:], T.kmin[:, 128:160], T.sm[:, 65:128:2], 0.0, A.mult, A.add, ["sm", "kpk0", "kpk1"], ["pkf"])
+            ts(T.sot[:, t:512:4], T.ioh[:], T.cde[:, t:t + 1], A.is_equal, ["io", "cde", "wv"], ["so%d" % t], T.wv[:, 8 * t + 7:8 * t + 8], A.mult, 0.5)
+        quant("so", 0, 128, T.sot, ["so%d" % t for t in range(4)], ["so"])
+        mm(0, "fl", 160, "kb", 128, 128, ["fl1", "kb"])
+        mm(2, "so", 0, "kb", 0, 128, ["so", "kb"])
+        for z, none in ((1, 255.0), (0, BIG)):
+            c = slice(64 * z, 64 * z + 64)
+            act(T.ln[:, c], ps(2, c.start, c.stop), ["#2", "kdr"], ["ln%d" % z], AF.Ln, bias=2.0 ** -62, scale=math.exp(-0.2))
+            act(T.nb[:, c], ps(2, c.start, c.stop), ["#2"], ["nb%d" % z], AF.Identity, bias=none, scale=-2.0 ** 30)
+            tt(T.lev[:, c], ps(0, c.start, c.stop), T.ln[:, c], A.subtract, ["#0", "ln%d" % z], ["lev%d" % z], 1.0)
+            tt(T.cand[:, c], T.lev[:, c], T.nb[:, c], A.max, ["lev%d" % z, "nb%d" % z], ["cand%d" % z])
+            for y in range(2):
+                a, n = 64 * z + 32 * y, 32 - 8 * y
+                tt(T.sm[64 * y:64 * y + 64, 32 * z:32 * z + n], T.cand[0:64, a:a + n], T.cand[64:128, a + 8:a + 8 + n], A.min, ["cand%d" % z],
+                   ["sm%d%d" % (z, y)], alone=True)
+        scan(T.pkf[:], T.kpk[:], T.sm[:, 32:64], 0.0, A.mult, A.add, ["sm10", "sm11", "kpk"], ["pkf"])
         cp(T["pk%d" % r][:], T.pkf[:, 1:32:2], ["pkf"], ["pk%d" % r])
         send(T["lst%d" % r][:], T["pk%d" % r][:], "al%d" % r, 1, ["pk%d" % r], ["lst%d" % r], 2.0)
-        act(T.pn[:, 0:2], T.ps[:, 2560 + 16:2560 + 32:8], ["#5"], ["pn"], AF.Identity, bias=0.5, scale=-1.0)
-        for t in (0, 1):
-            ts(T.cmt[:, t:1536:4], T.ios[:], ps(5, 8 * t, 8 * t + 1), A.is_ge, ["#5", "ios"], ["cm%d" % t], f=0.5)
-        for t in (2, 3):
-            act(T.cmt[:, t:1536:4], T.ios[:], ["pn", "ios"], ["cm%d" % t], AF.Sign, bias=T.pn[:, t - 2:t - 1])
+        act(T.pn[:], T.ps[:, 2560:2560 + 32:8], ["#5"], ["pn"], AF.Identity, bias=0.5, scale=-1.0)
+        for t in range(4):
+            p = slice(64 * (t == 2), 128)
+            if t in CMS:
+                act(T.cmt[p, t:1536:4], T.ios[p, :], ["pn", "ios"], ["cm%d" % t], AF.Sign, bias=T.pn[p, t:t + 1])
+            else:
+                ts(T.cmt[p, t:1536:4], T.ios[p, :], T.ps[p, 2560 + 8 * t:2561 + 8 * t], A.is_ge, ["#5", "ios"], ["cm%d" % t], 2.0, A.mult, 0.5)
         quant("cm", 0, 384, T.cmt, ["cm%d" % t for t in range(4)], ["cm"])
-        mm(1, "ka", 384, "cm", 0, 384, ["cm", "ka1"])
+        mm(1, "ka", 0, "cm", 0, 384, ["cm", "ka0"])
         add({"V": (lambda: V.transpose(T.lrow[:], ps(1, 0, 384)), vc(384), 0)}, ["#1"], ["lrow"])
-        ts(T.pl[:], T.lrow[:, 0:384:32], 128.0, A.add, ["lrow"], ["pl"])
+        ts(T.pl[:], T.lrow[:, 0:384:32], 0.5, A.mult, ["lrow"], ["pl"], float(sum(32 if t == 2 else 64 for t in CMS)), A.add)
         sl, ld = "slot%d" % r, "land%d" % r
-        pick(sl, t_, NF, 512, T.pl[:, 0:12], TA + ["pl"])
+        pick(sl, t_, NF, C, T.pl[:, 0:12], TA + ["pl"])
         send(T[ld + "c"][:].bitcast(dt.uint8), T[sl + "c"][:].bitcast(dt.uint8), "ac%d" % r, 2, [sl + "c"], [ld + "c"], 2.3)
         send(T[ld + "s"][:], T[sl + "s"][:], "ac%d" % r, 2, [sl + "s"], [ld + "s"], 2.1)
 
         def unpack(src, base, key, banks, on):
             for k in range(8):
                 bk = banks[k % len(banks)]
-                mm(bk, "eb", 128 * k, src, 0, NF, [src + "c", src + "s", "eb%dc" % (k // 2), "eb%ds" % (k // 2)])
                 o = base + NF * (7 - k)
                 a, z = (0, NF) if r == 0 else (max(0, 136 - 56 * k), NF) if base else (0, min(NF, 399 - 56 * k))
-                mv(T.win[:, o + a:o + z], ps(bk, a, z), ["#%d" % bk], ["%s%d" % (key, k)], SC64, on=on)
-        unpack(sl, 0, "wo", (3, 4, 5), "S")
-        scan(T.kos[:], T.kst[:, 0:32], T.sm[:, 1:64:2], 0.0, A.add, A.min, ["sm", "kst0"], ["kos"])
-        tt(T.own[:], T.kos[:, 0:32].indirect(T.rev[:, 0:2]), T.idc[:], A.min, ["kos", "rev", "idc"], ["own"], 3.0)
+                a0, z0 = min(a, NF - 128), max(z + z % 2, 128)
+                mm(bk, "eb", 128 * k, src, a0, z0 - a0, [src + "c", src + "s", "eb%dc" % (k // 2), "eb%ds" % (k // 2)])
+                mv(T.win[:, o + a:o + z], ps(bk, a - a0, z - a0), ["#%d" % bk], ["%s%d" % (key, k)], SC64, on=on)
+        unpack(sl, 0, "wo", (3, 4, 5), "SV")
+        scan(T.kos[:, 31::-1], T.kst[:, 0:32], T.sm[:, 31::-1], 0.0, A.add, A.min, ["sm00", "sm01", "kst"], ["kos"])
+        tt(T.own[:], T.kos[:], T.idc[:], A.min, ["kos", "idc"], ["own"])
         unpack(ld, 1536, "wa", (6, 7, 1, 2, 0), "SV")
         cp(T.ai[:], T["lst%d" % r][:], ["lst%d" % r], ["ai"])
         ts(T.a2[:, 0:32:2], T.ai[:], 8, A.arith_shift_right, ["ai"], ["a2h"])
         ts(T.a2[:, 1:32:2], T.ai[:], 255, A.bitwise_and, ["ai"], ["a2l"])
         ts(T.kn[:], T.a2[:], float(NF), A.is_ge, ["a2h", "a2l"], ["kn"], BIG, A.mult)
         tt(T.kn[:], T.kn[:], T.a2[:], A.add, ["kn", "a2h", "a2l"], ["kn"])
-        scan(T.kns[:], T.kst[:, 32:64], T.kn[:], 0.0, A.add, A.min, ["kn", "kst1"], ["kns"])
+        scan(T.kns[:], T.kst[:, 32:64], T.kn[:], 0.0, A.add, A.min, ["kn", "kst"], ["kns"])
         for k in range(2):
             tt(T.rep[0:64, 32 * k:32 * k + 32], T.kns[64 * k:64 * k + 64, :], T.own[64 * k:64 * k + 64, :], A.min, ["kns", "own"], ["rep%d" % k])
         for k in range(2):
             mv(T.rep[32 * k:32 * k + 32, 64:128], T.rep[32 - 32 * k:64 - 32 * k, 0:64], ["rep0", "rep1"], ["rp%d" % k])
         mv(T.rep[64:128, :], T.rep[0:64, :], ["rep0", "rep1", "rp0", "rp1"], ["rp2"])
-        ts(T.off[:], T.rep[:, 0:128].indirect(T.ordr[:, 0:7]), 1536.0, A.add, ["rep0", "rep1", "rp0", "rp1", "rp2", "ordr"], ["off"], f=2.0)
+        ts(T.off[:], T.rep[:, 0:128].indirect(T.ordr[:, 0:8]), 1536.0, A.add, ["rep0", "rep1", "rp0", "rp1", "rp2", "ordr"], ["off"], f=2.0)
         WIN = ["ft%d" % b for b in range(4)] + ["%s%d" % (a, k) for a in ("wo", "wa") for k in range(8)]
         for h in range(H):
             a, z = CUTS[h], CUTS[h + 1]
             for b1 in range(2):
                 lo, hi = 896 * b1 + 2 * a, 896 * b1 + 2 * z
-                tt(T.yt[:, lo:hi], T.win[:, 0:4864].indirect(T.off[:, lo // 16:hi // 16]), T.fh[:, lo:hi],
+                tt(T.yt[:, lo:hi], T.win[:, 0:4864].indirect(T.off[:, 64 * b1 + a // 8:64 * b1 + z // 8]), T.fh[:, lo:hi],
                    A.add, WIN + ["off", "fh%d" % b1], ["yt%d%d" % (b1, h)], 1.6)
             for be in range(4):
                 for b in range(4):
                     o = 896 * (be // 2)
                     mv(T.yy[32 * be:32 * be + 32, 4 * a + b:4 * z:4], T.yt[32 * b:32 * b + 32, o + 2 * a + be % 2:o + 2 * z:2],
-                       ["yt%d%d" % (be // 2, h)], ["yy%d%d%d" % (be, b, h)], f=0.5, on="VSG")
+                       ["yt%d%d" % (be // 2, h)], ["yy%d%d%d" % (be, b, h)], f=0.5, on=GC)
             quant("qy", a, z, T.yy, ["yy%d%d%d" % (i, b, h) for i in range(4) for b in range(4)], ["qy%d" % h])
             for b in range(4):
                 bk = (4 * h + b) % 8
@@ -496,7 +491,7 @@ def rank_program(g, core, T, topo):
                 mm(bk, "qw", 128 * b, "qy", a, z - a, ["qy%d" % h, "qwc", "qws"])
                 mv(T.y1[:, pl], T.yy[:, 4 * a + b:4 * z:4], ["yy%d%d%d" % (i, b, h) for i in range(4)], ["y1%d%d" % (b, h)], 32.0, 0.5)
                 tt(T.xs[:, 4 * a + b:4 * z:4], ps(bk, 0, z - a), T.y1[:, pl], A.add, ["#%d" % bk, "y1%d%d" % (b, h)], ["xs%d%d" % (b, h)], 1.0)
-            quant_x(r + 1, T.xs, h, ["xs%d%d" % (b, h) for b in range(4)] + ["xsp"])
+            quant_x(r + 1, T.xs, h, ["xs%d%d" % (b, h) for b in range(4)])
 
     t_ = "t%d" % R
     for h in range(H):
@@ -510,7 +505,7 @@ def rank_program(g, core, T, topo):
         dma("YS", "outs", T.osc[4 * k:4 * k + 4, :], T[t_ + "s"][32 * k:32 * k + 4, 0:C], ["%s_%d" % (t_, h) for h in range(H)], [], 2.0)
 
     Q = {"V": V, "S": S, "P": g.tensor, "G": g, "Y": g.sync}
-    cnt, seen, tok, eng, knew, sent = {}, {e: {} for e in Q}, {}, {}, {}, 0
+    cnt, seen, tok, eng, knew, sent, moved, alone = {}, {e: {} for e in Q}, {}, {}, {}, 0, False, False
     for _, i, e in schedule(ops):
         o = ops[i]
         for d, raw in sorted(o["deps"].items(), reverse=True):
@@ -522,9 +517,17 @@ def rank_program(g, core, T, topo):
                     if not ops[d]["arrive"]:
                         for s2, v2 in knew[d].items():
                             seen[e][s2] = max(seen[e].get(s2, 0), v2)
-        if e == "G" and not o["arrive"] and len(o["alts"]) > 1 and seen[e].get(e, 0) < cnt.get(e, 0):
-            g.wait_ge(T.sem.G, cnt[e])
-            seen[e][e] = cnt[e]
+        if e == "G" and not o["arrive"]:
+            moves = len(o["alts"]) > 1
+            if (moves or moved) and seen[e].get(e, 0) < cnt.get(e, 0):
+                g.wait_ge(T.sem.G, cnt[e])
+                seen[e][e] = cnt[e]
+            moved = moves
+        if e == "V":
+            if alone and seen[e].get(e, 0) < cnt[e]:
+                V.wait_ge(T.sem.V, cnt[e])
+                seen[e][e] = cnt[e]
+            alone = o.get("alone")
         ins = o["alts"][e][0]()
         eng[i] = e
         knew[i] = dict(seen[e])

@@ -6,9 +6,14 @@ BIG = 8192.0
 CUTS = (0, 320, 448)
 B0 = (0, 128, 192, 320)
 B1 = (0, 128, 256, 320, 448)
-CMS = (1, 2, 3)
-GM = False
-GC = "VS"
+WA, WS, NH = 8 * NF, NF + 224, 3
+WF = WA + 7 * WS + NF
+FW = 2 * C - 112 * NH
+FD = "Y"
+UPS = ((0, 3), (3, 4))
+YP = 2
+GAT = ((288, 448), (0, 288))
+GC = "VSG"
 Q4, U8, BF, F32, I32, U16 = "float8_e4m3fn_x4", "uint8", "bfloat16", "float32", "int32", "uint16"
 SCRATCH = {}
 
@@ -30,25 +35,28 @@ for _r in range(R):
     _sb("pk%d" % _r, 16, U16)
     _sb("lst%d" % _r, 16, U16)
 for _n, _w in (("qu", 128), ("qup", 144), ("qv", 128), ("qw", 512), ("ef", 512), ("eb", 1024), ("ka", 384),
-               ("kb", 256), ("kr", 152), ("m", C), ("fl", 288), ("cm", 384), ("so", 128), ("qy", C)):
+               ("kb", 256), ("kr", 152), ("m", C), ("fl", 288), ("cm", NF), ("so", 128), ("qy", C)):
     _q(_n, _w)
 for _n, _w in (("xin", 4 * C), ("xs", 4 * C), ("ut", 512), ("vt", 512), ("eft", 2048), ("kat", 1536), ("kbt", 1024), ("mt", 4 * C),
-               ("flt", 1152), ("cmt", 1536), ("sot", 512), ("krt", 608), ("ios", 384), ("ioh", 128), ("kv", 128), ("win", 4864),
-               ("yt", 4 * C), ("fh", 4 * C), ("yy", 4 * C), ("y1", 4 * C), ("nar", 384), ("df", C), ("ctri", 128)):
+               ("flt", 1152), ("cmt", 4 * NF), ("sot", 512), ("krt", 608), ("ios", NF), ("k16", NF), ("ioh", 128), ("kv", 128),
+               ("win", WF + 2 * FW), ("yt", 4 * C), ("fh", 4 * C), ("yy", 4 * C), ("y1", 4 * C), ("nar", 384), ("ctri", 128), ("tj", 128)):
     _sb(_n, _w, BF)
-for _n, _w in (("sc", 80), ("cmx", 80), ("cm2", 80), ("rr", 80), ("cde", 16), ("k72", 160), ("thr", 4), ("th2", 4), ("dd", C), ("ebi", 64), ("kd", 64),
-               ("eq", 32), ("wv", 32), ("lrow", 384), ("ln", 128), ("nb", 128), ("cand", 128), ("sm", 64), ("kpk", 32),
-               ("pkf", 32), ("kos", 32), ("own", 32), ("kn", 32), ("kns", 32), ("rep", 128), ("kst", 64), ("idc", 32),
-               ("w1", 32), ("w2", 16), ("pv", 8), ("yo", C), ("tj", 128), ("acc", 8), ("pn", 4)):
+for _n, _w in (("sc", 80), ("cmx", 80), ("cm2", 80), ("rr", 80), ("cde", 16), ("k72", 160), ("thr", 4), ("th2", 4), ("dd", C), ("ebi", 8), ("kd", 64),
+               ("eq", 32), ("wv", 32), ("lrow", NF), ("ln", 128), ("nb", 128), ("cand", 128), ("sm", 64), ("kpk", 32),
+               ("pkf", 32), ("kos", 32), ("own", 32), ("kn", 32), ("kns", 32), ("rep", 128), ("df", C), ("up", 4), ("kst", 64), ("idc", 32),
+               ("w1", 32), ("w2", 16), ("pv", 8), ("yo", C), ("acc", 8)):
     _sb(_n, _w, F32)
 for _n, _w in (("lev", 128), ("ai", 16), ("a2", 32), ("pi", 8), ("wi", 8)):
     _sb(_n, _w, I32)
-for _n, _w in (("ul", 10), ("pl", 12), ("ordr", 8), ("off", 128), ("ebl", 64)):
+for _n, _w in (("ul", 10), ("pl", 12), ("ordr", 8), ("off", 128), ("ebl", 16)):
     _sb(_n, _w, U16)
 SCRATCH["ps"] = ("psum", [128, 4096], F32)
-SEMAPHORES = ["V", "S", "P", "G", "dx0", "dx1", "du", "dv", "dwc", "dws", "outs", "sent", "dfh0", "dfh1"] + \
+SEMAPHORES = ["V", "S", "P", "G", "dx0", "dx1", "du", "dv", "dwc", "dws", "outs", "sent", "dw", "dfh0", "dfh1"] + ["d%s%d" % (k, b) for k in "ef" for b in (1, 2, 3)] + \
              ["%s%d" % (k, r) for k in ("ac", "al") for r in range(R)]
-CY, OV, LAT, PE = 0.00087, 0.05, 0.12, 0.0008
+CY, OV, LAT, LATG, PE, RI, DL = 0.00085, 0.005, 0.2, 0.22, 0.0006, 0.4, -1.0
+MORE = {"S": 0.008, "G": 0.02}
+CASES = ((1.0, 0.005, 0.0, 0.0, 0.19, 0.23, 0.2, 0.0, -0.3, 1.0, 0.4, 0.0), (1.0, 0.0, 0.0, 0.0, 0.21, 0.21, 0.1, -0.3, 0.0, 0.85, 0.6, 0.0),
+         (1.0, 0.015, 0.01, 0.03, 0.16, 0.19, 0.4, 0.5, -0.8, 1.2, 0.15, 0.015), (1.35, 0.005, 0.0, 0.0, 0.22, 0.25, 0.3, 0.5, 0.2, 1.4, 0.6, 0.0))
 TRIES = 6000
 SPAN, PLAN = [0.0], []
 
@@ -66,7 +74,7 @@ def deal(ops, order, spare, back=None):
         for e, (fn, hold, tail) in ops[i]["alts"].items():
             t = 0.0
             for d, raw in (back[i] if back else ops[i]["deps"]).items():
-                u = done[d] + LAT if raw or eng[d] != e else (done[d] if back else start[d] + 1e-6)
+                u = done[d] + (LATG if (eng[d] if back else e) == "G" else LAT) if raw or eng[d] != e else (done[d] if back else start[d] + 1e-6)
                 if u > t:
                     t = u
             if back:
@@ -113,7 +121,31 @@ def schedule(ops):
                 if p[j] + 1e-4 > p[i]:
                     p[i] = p[j] + 1e-4
         return deal(ops, sorted(range(n), key=lambda k: -p[k]), sp)
-    best = cur = forward(pri, spare)
+    deps = [list(o["deps"].items()) for o in ops]
+    cases = []
+    for f, ov, ovs, ovg, lat, own, latg, dl, dr, pe, ri, px in CASES:
+        cost = [{e: (ri, h + t + dr - ri) if o["arrive"] else (h, t + dl) if o["sem"] else (h * pe, 0.0) if e == "P"
+                 else ((h + t - OV) * f + ov + ovs * (e == "S") + ovg * (e == "G") + px * o["psum"], 0.0) for e, (fn, h, t) in o["alts"].items()} for o in ops]
+        cases.append((cost, lat, own, latg))
+
+    def score(got):
+        order, eng, total = sorted(range(n), key=lambda k: (got[1][k], k)), got[3], 0.0
+        waits = [[(d, eng[d] == eng[i]) for d, raw in deps[i] if raw or eng[d] != eng[i]] for i in range(n)]
+        for cost, lat, own, latg in cases:
+            free, done = {}, [0.0] * n
+            for i in order:
+                e = eng[i]
+                t = free.get(e, 0.0)
+                for d, same in waits[i]:
+                    u = done[d] + (latg if e == "G" else own if same else lat)
+                    if u > t:
+                        t = u
+                c = cost[i][e]
+                free[e] = t + c[0] + (own if ops[i].get("alone") else 0.0)
+                done[i] = t + c[0] + c[1]
+            total += max(done)
+        return (total / len(cases) if cases else got[0],) + got
+    best = cur = score(forward(pri, spare))
     z = 12345
     for it in range(TRIES):
         s2, shift = dict(spare), {}
@@ -133,12 +165,15 @@ def schedule(ops):
             if again[0] < got[0]:
                 got, p2 = again, p3
         z = (z * 1103515245 + 12345) % 2147483648
+        if got[0] > cur[1] + 0.6:
+            continue
+        got = score(got)
         if got[0] <= cur[0] + 0.15 * (1 - it / TRIES) * ((z >> 8) % 1000) / 1000:
             cur, pri, spare = got, p2, s2
             if got[0] < best[0]:
                 best = got
-    SPAN[0] = best[0]
-    PLAN.append(sorted((best[1][i], i, best[3][i]) for i in range(n)))
+    SPAN[:] = best[:2]
+    PLAN.append(sorted((best[2][i], i, best[4][i]) for i in range(n)))
     return PLAN[0]
 
 
@@ -170,7 +205,9 @@ def rank_program(g, core, T, topo):
         for k in wr:
             lastw[k] = len(ops)
             readers[k] = []
-        ops.append({"alts": alts, "deps": deps, "sem": sem, "arrive": arrive, "key": name(wr[0] if wr[:1] and wr[0][0] != "#" else rd[0])})
+        if not sem and not arrive:
+            alts = {e: (a[0], a[1] + MORE.get(e, 0.0), a[2]) for e, a in alts.items()}
+        ops.append({"alts": alts, "deps": deps, "sem": sem, "arrive": arrive, "psum": any(k[0] == "#" for k in rd), "key": name(wr[0] if wr[:1] and wr[0][0] != "#" else rd[0])})
 
     def w(ap):
         return ap.shape[1]
@@ -198,8 +235,9 @@ def rank_program(g, core, T, topo):
         if "S" in on:
             alts["S"] = ((lambda: S.activation(out, a, AF.Copy)) if scale is None else (lambda: S.activation(out, a, AF.Copy, scale=scale)), vc(n), 0)
         if "G" in on:
-            alts["G"] = (lambda: g.affine_select(out, a, [[0, n]], A.is_ge, 0.0, 0, 0), 0.24 + 2 * n * CY + OV, 0)
+            alts["G"] = (lambda: g.affine_select(out, a, [[0, n]], A.is_ge, 0.0, 0, 0), 0.17 + 2 * n * CY + OV, 0)
         add(alts, rd, wr)
+        ops[-1]["moves"] = out.shape[0] < 128
 
     def lin(out, a, k, c, rd, wr, f=1.0):
         add({"V": (lambda: V.tensor_scalar(out, a, k, c, A.mult, A.add), vc(w(out), f), 0),
@@ -211,7 +249,10 @@ def rank_program(g, core, T, topo):
             alts["S"] = (lambda: S.activation(ap, T.tj[0:ap.shape[0], 0:w(ap)], AF.Identity, bias=float(v), scale=0.0), vc(w(ap)), 0)
         elif s:
             alts["S"] = (lambda: S.activation(ap, T.kat[0:ap.shape[0], 0:w(ap)], AF.Identity, bias=float(v), scale=0.0), vc(w(ap)), 0)
-        add(alts, [] if len(alts) == 1 else ["tj"] if w(ap) <= 128 else ["kat0"], wr)
+        rd = [] if len(alts) == 1 else ["tj"] if w(ap) <= 128 else ["kat0"]
+        if s and ap.shape[0] == 128 and v == int(v) and abs(v) < 2 ** 20:
+            alts["G"] = (lambda: g.iota(ap, [[0, w(ap)]], int(v), 0, allow_small_or_imprecise_dtypes=True), 0.13 + 2 * w(ap) * CY + OV, 0)
+        add(alts, rd, wr)
 
     def scan(out, d0, d1, init, o0, o1, rd, wr):
         add({"V": (lambda: V.tensor_tensor_scan(out, d0, d1, init, o0, o1), vc(w(out)), 0)}, rd, wr)
@@ -244,14 +285,14 @@ def rank_program(g, core, T, topo):
 
     def dma(on, sem, out, in_, rd, wr, t=2.2):
         qs = {"Y": g.sync, "S": S}
-        add({e: (lambda e=e: qs[e].dma_start(out, in_), 0.08, t) for e in on}, rd, wr, sem)
+        add({e: (lambda e=e: qs[e].dma_start(out, in_), 0.12, t + DL) for e in on}, rd, wr, sem)
 
     def send(out, in_, sem, n, rd, wr, t):
-        add({"G": (lambda: g.remote_dma(out, in_, T.sem[sem], T.sem.sent, pid, rid, mask), 0.4, t)}, rd, wr, None, (sem, n * neng))
+        add({"G": (lambda: g.remote_dma(out, in_, T.sem[sem], T.sem.sent, pid, rid, mask), RI, t - RI)}, rd, wr, None, (sem, n * neng))
 
     dma("Y", "du", T.ut[:], T.u[:], [], ["ut"], 2.5)
-    dma("Y", "dx0", T.xin[:, 0:1024], T.x[:, 0:1024], [], ["xin0"], 3.0)
-    dma("S", "dx1", T.xin[:, 1024:1792], T.x[:, 1024:1792], [], ["xin1"], 2.8)
+    dma("Y", "dx0", T.xin[:, 0:4 * CUTS[1]], T.x[:, 0:4 * CUTS[1]], [], ["xin0"], 3.2)
+    dma("S", "dx1", T.xin[:, 4 * CUTS[1]:4 * C], T.x[:, 4 * CUTS[1]:4 * C], [], ["xin1"], 2.6)
     dma("Y", "dwc", T.qwc[:].bitcast(dt.uint8), T.wc[:], ["xin0"], ["qwc"], 3.0)
     dma("Y", "dws", T.qws[:], T.ws[:], ["xin0"], ["qws"])
     dma("Y", "dv", T.vt[:], T.v[:], ["xin0"], ["vt"])
@@ -260,7 +301,8 @@ def rank_program(g, core, T, topo):
     iota(T.tj[:], [[1, 128]], 0, -1, ["tj"])
     iota(T.k72[:, 0:72], [[-15, 2], [0, 36]], 16, 0, ["k72a"])
     iota(T.kd[:, 0:32], [[0, 4], [-1, 8]], -1, 0, ["kd"])
-    iota(T.ios[:], [[16, 12], [0, 2], [1, 16]], 0, 0, ["ios"])
+    iota(T.ios[:], [[1, NF]], 0, 0, ["ios"])
+    iota(T.k16[:], [[0, NF // 16], [1, 16]], 0, 0, ["k16"])
     ms(T.kat[:, 0:512], 1.0, ["kat0"], 0.5, False)
     for t, z in ((1, 128), (2, C), (3, 320)):
         ms(T.mt[:, t:4 * z:4], 0.0, ["mtp%d" % t], 0.5)
@@ -268,53 +310,55 @@ def rank_program(g, core, T, topo):
     for k, (n, o) in enumerate(((15, A.bitwise_and), (7, A.bitwise_and), (3, A.arith_shift_right), (32, A.bitwise_and), (79, A.bitwise_and))):
         ts(T.pi[:, k + 1:k + 2], T.pi[:, 0:1], n, o, ["pi0"], ["pi%d" % (k + 1)])
     cp(T.pv[:, 0:5], T.pi[:, 1:6], ["pi1", "pi2", "pi3", "pi4", "pi5"], ["pv"])
+    ts(T.k16[:], T.k16[:], T.pv[:, 0:1], A.is_equal, ["k16", "pv"], ["k16"], BIG, A.mult, 0.5)
     ts(T.pi[:, 6:7], T.pi[:, 0:1], 14, A.bitwise_and, ["pi0"], ["pi6"])
     ts(T.ul[:, 0:1], T.pi[:, 6:7], 8.0, A.mult, ["pi6"], ["ul"])
     quant("qu", 0, 128, T.ut, ["ut"], ["qu"])
     pick("qup", "qu", 144, 128, T.ul[:, 0:9], ["qu", "ul"])
     quant("qv", 0, 128, T.vt, ["vt"], ["qv"])
     quant("ka", 0, 128, T.kat, ["kat0"], ["ka0"])
-    one = T.kat[:, 0:128]
-    asel(T.nar[:, 0:128], one, [[1, 128]], A.is_ge, 0.0, 0, -1, ["kat0"], ["tri"])
-    asel(T.nar[:, 128:256], T.nar[:, 0:128], [[-8, 16], [0, 8]], A.is_ge, 0.0, 0, 1, ["tri"], ["blk"])
+    for t in range(4):
+        ts(T.kat[:, 512 + t:1024:4], T.tj[:], 0.0, A.is_ge, ["tj"], ["tri%d" % t], f=0.5)
+    asel(T.nar[:, 128:256], T.kat[:, 512:1024:4], [[-8, 16], [0, 8]], A.is_ge, 0.0, 0, 1, ["tri0"], ["blk"])
     asel(T.nar[:, 256:384], T.nar[:, 128:256], [[1, 128]], A.not_equal, -8.0, 0, -1, ["blk"], ["del"])
     for t in range(4):
-        mv(T.kat[:, 512 + t:1024:4], T.nar[:, 0:128], ["tri"], ["kat1%d" % t], f=0.5)
-        mv(T.kat[:, 1024 + t:1536:4], T.nar[:, 256:384], ["del"], ["kat2%d" % t], f=0.5)
-    quant("ka", 128, 384, T.kat, ["kat%d%d" % (a, t) for a in (1, 2) for t in range(4)], ["ka1"])
+        mv(T.kat[:, 1024 + t:1536:4], T.nar[:, 256:384], ["del"], ["kat2%d" % t], f=0.5, on="VSG")
+    quant("ka", 128, 384, T.kat, ["tri%d" % t for t in range(4)] + ["kat2%d" % t for t in range(4)], ["ka1"])
     ms(T.flt[:, 0:512], 0.0, ["flz"], 0.5)
     ms(T.flt[:, 512:640], 0.0, ["fly"], 0.5)
     ms(T.flt[0:64, 642:1152:4], 0.0, ["fb2"], 0.5)
-    ms(T.cmt[0:64, 2:1536:4], 0.0, ["cm2"], 0.5)
+    ms(T.cmt[0:64, 2:4 * NF:4], 0.0, ["cm2"], 0.5)
+    ms(T.cmt[:, 3:256:4], 0.0, ["cm3"], 0.5)
     quant("fl", 32, 160, T.flt, ["flz", "fly"], ["flw", "fl0"])
-    ms(T.krt[:, 0:256], 256.0, ["kr0"], 0.5)
+    ms(T.krt[:, 0:256], -256.0, ["kr0"], 0.5)
     ms(T.krt[:, 96:128], 1.0, ["kr0"], 0.5)
     ms(T.krt[:, 256:608], 1.0, ["kr1"], 0.5)
     quant("kr", 0, 152, T.krt, ["kr0", "kr1"], ["kr"])
-    if GM:
-        iota(T.thr[:], [[192, 2], [128, 2]], NF - C + 1, 1, ["thr"])
-        lin(T.thr[:], T.thr[:], 1.0 / 128, 0.0, ["thr"], ["thr"])
-    else:
-        ts(T.ctri[:], T.tj[:], 0.0, A.is_ge, ["tj"], ["ctri"], 2.0 ** -100, A.mult)
-        for t in range(3):
-            ms(T.thr[:, t:t + 1], (NF + 1 - C + B1[t + 1]) / 128, ["thr"])
-        ms(T.acc[:, 7:8], NF + 1.0, ["bnd3"])
+    ts(T.ctri[:], T.tj[:], 0.0, A.is_le, ["tj"], ["ctri"], f=0.5)
+    iota(T.acc[:, 4:8], [[192, 2], [128, 2]], 128 - NF, 0, ["bnd0", "bnd1", "bnd2", "bnd3"])
+    lin(T.thr[:], T.acc[:, 4:8], 1.0 / 128, 0.0, ["bnd0", "bnd1", "bnd2"], ["thr"])
     ms(T.k72[:, 80:152], 0.0, ["k72d"])
     ms(T.k72[:, 88:152:9], -1e29, ["k72d"])
     ms(T.cmx[:, 0:1], -1e29, ["cmx0"])
     ms(T.kd[:, 32:64], math.exp(-1.0), ["kdr"], s=False)
     act(T.kd[:, 32:64:8], T.kat[:, 0:4], ["kat0"], ["kdr"], AF.Ln, 1.3)
+    asel(T.eft[:, 0:512], T.kat[:, 0:512], [[-256, 4], [-1, 32], [256, 4]], A.is_equal, 0.0, 0, 1, ["kat0"], ["eft0", "efu0"])
     for b in range(4):
-        asel(T.eft[:, 512 * b:512 * b + 512], T.kat[:, 0:512], [[-256, 4], [-1, 32], [256, 4]], A.is_equal, 0.0, -32 * b, 1, ["kat0"], ["eft%d" % b])
-        quant("ef", 128 * b, 128 * b + 128, T.eft, ["eft%d" % b], ["ef%d" % b])
+        if b:
+            dma("Y", "de%d" % b, T.eft[32 * b:128, 512 * b:512 * b + 512], T.eft[0:128 - 32 * b, 0:512], ["eft0"], ["eft%d" % b], 2.2)
+            dma("Y", "df%d" % b, T.eft[0:32 * b, 512 * b:512 * b + 512], T.eft[128 - 32 * b:128, 0:512], ["eft0"], ["efu%d" % b], 2.2)
+        quant("ef", 128 * b, 128 * b + 128, T.eft, ["eft%d" % b, "efu%d" % b], ["ef%d" % b])
+    iota(T.ebi[:], [[16, 2], [32, 4]], 0, 0, ["ebi"])
     for e in range(2):
-        iota(T.ebi[:, e:64:2], [[128, 4], [16, 2], [32, 4]], 0, 0, ["ebi%d" % e])
-    ts(T.ebl[:], T.ebi[:], T.pv[:, 0:1], A.add, ["ebi0", "ebi1", "pv"], ["ebl"])
+        ts(T.ebl[:, e:16:2], T.ebi[:], T.pv[:, 0:1], A.add, ["ebi", "pv"], ["ebl%d" % e])
     for b in range(4):
-        pick("eb", "ef", 256, 512, T.ebl[:, 16 * b:16 * b + 16], ["ef%d" % j for j in range(4)] + ["ebl"], 256 * b, "eb%d" % b)
+        add({"V": (lambda b=b: V.tensor_copy(T.ebc[:, 256 * b:256 * b + 256].bitcast(dt.uint32), T.efc[:, 128 * b:128 * b + 128].bitcast(dt.uint32).indirect(T.ebl[:])),
+                   0.08 + 400 * CY, 0)}, ["ef%d" % b, "ebl0", "ebl1"], ["eb%dc" % b])
+        add({"S": (lambda b=b: S.activation(T.ebs[:, 256 * b:256 * b + 256], T.efs[:, 128 * b:128 * b + 128].indirect(T.ebl[:]), AF.Copy), 0.09 + 400 * CY, 0)},
+            ["ef%d" % b, "ebl0", "ebl1"], ["eb%ds" % b])
+    iota(T.nar[:, 0:32], [[16, 2], [1, 8], [32, 2]], -105, 0, ["ioi"])
     for k in range(4):
-        iota(T.ioh[:, 32 * k:32 * k + 32], [[16, 2], [1, 8], [32, 2]], 64 * (k % 2) - 8 * (k // 2) - 105, 0, ["ioh%d" % k])
-    ts(T.ioh[:], T.ioh[:], T.pv[:, 1:2], A.subtract, ["ioh%d" % k for k in range(4)] + ["pv"], ["io"], f=0.5)
+        ts(T.ioh[:, 32 * k:32 * k + 32], T.nar[:, 0:32], T.pv[:, 1:2], A.subtract, ["ioi", "pv"], ["io%d" % k], 64.0 * (k % 2) - 8 * (k // 2), A.add)
     iota(T.kv[:], [[7, 2], [1, 8], [-7, 8]], 42, 0, ["kv"])
     iota(T.w1[:, 16:20], [[24, 2], [16, 2]], 0, 0, ["w1c"])
     lin(T.w2[:, 8:12], T.w1[:, 16:20], 1.0, T.pv[:, 2:3], ["w1c", "pv"], ["c"])
@@ -323,13 +367,19 @@ def rank_program(g, core, T, topo):
         ts(T.kbt[:, 512 + t:1024:4], T.kv[:], T.w2[:, 8 + t:9 + t], A.is_gt, ["kv", "c"], ["kb1%d" % t], f=0.5)
     lin(T.kbt[:, 512:768], T.kbt[:, 512:768], 1.0, -1.0, ["kb1%d" % t for t in range(4)], ["kc"], 0.5)
     quant("kb", 0, 256, T.kbt, ["kb0%d" % t for t in range(4)] + ["kc"], ["kb"])
-    iota(T.kpk[:], [[0, 16], [256, 2]], 0, 0, ["kpk"])
-    iota(T.kst[:], [[2 * NF, 2], [0, 32]], -NF, 0, ["kst"])
-    ms(T.kst[:, 0:64:8], 2 * BIG, ["kst"])
+    for k in range(2):
+        ms(T.kpk[:, k:32:2], 256.0 * k, ["kpk%d" % k])
+        ms(T.kst[:, 32 * k:32 * k + 32], float(WS if k else -NF), ["kst%d" % k])
+    ms(T.kst[:, 0:64:8], 2 * BIG, ["kst0", "kst1", "kst"])
     ms(T.sm[:], 255.0, ["sm00", "sm01", "sm10", "sm11"])
-    iota(T.idc[:], [[16, 4], [-112, 8]], 784 + 1536, 0, ["idc"])
-    lin(T.w2[:, 3:4], T.pv[:, 3:4], 28.0, T.pv[:, 4:5], ["pv"], ["w23"])
+    iota(T.idc[:], [[16, 4], [-112, 8]], 784 + WF - WA, 0, ["idc"])
+    iota(T.kn[:], [[16, 4], [WS, 8]], NF, 0, ["kn"])
+    lin(T.w2[:, 3:4], T.pv[:, 3:4], FW / 32, T.pv[:, 4:5], ["pv"], ["w23"])
+    lin(T.w2[:, 4:5], T.pv[:, 3:4], 3.5, T.pv[:, 4:5], ["pv"], ["w24"])
     lin(T.idc[:], T.idc[:], 1.0, T.w2[:, 3:4], ["idc", "w23"], ["idc"])
+    for q in range(NH):
+        lin(T.idc[:, q:32:8], T.kn[:, q:32:8], 1.0, T.w2[:, 4:5], ["kn", "w24"], ["idc"])
+    dma("Y", "dw", T.win[:, WA + NH * WS + NF:WF], T.x[:, 0:WF - WA - NH * WS - NF], ["xin0"], ["wa%d" % k for k in range(7 - NH)])
     iota(T.w1[:, 0:8], [[0, 2], [16, 4]], -3, 0, ["w1a"])
     iota(T.w1[:, 8:16], [[64, 2], [128, 4]], 7, 0, ["w1b"])
     ts(T.wi[:], T.w1[:, 0:8], T.pv[:, 0:1], A.add, ["w1a", "pv"], ["wi"], 1.0 / 7.0, A.mult)
@@ -347,7 +397,7 @@ def rank_program(g, core, T, topo):
         quant("t%d" % r, CUTS[h], CUTS[h + 1], tile, rd, ["t%d_%d" % (r, h)])
 
     for h in range(H):
-        quant_x(0, T.xin, h, ["xin0"] + (["xin1"] if CUTS[h + 1] > 256 else []))
+        quant_x(0, T.xin, h, ["xin%d" % min(h, 1)])
 
     for r in range(R):
         t_ = "t%d" % r
@@ -358,31 +408,32 @@ def rank_program(g, core, T, topo):
         for t, bk in enumerate((0, 1, 4, 5)):
             mm(bk, t_, B0[t], "qup", 0, 128, tk(B0[t], B0[t] + 128) + ["qupc", "qups"])
             mv(T.sc[:, 9 * t:9 * t + 9], T.ps[:, 512 * bk:512 * bk + 18:2], ["#%d" % bk], ["sc%d" % t])
+        for a, z in UPS:
+            act(T.up[:, a:z], T.sc[:, 9 * a + 8:9 * z:9], ["sc%d" % t for t in range(a, z)], ["up%d" % t for t in range(a, z)], AF.Abs,
+                bias=2.0 ** -125, scale=0.6 * 2.0 ** -23)
         ROW = ((2, 0, 320), (6, 320, C))
-        for bk, a, z in ROW + ((3, 0, 320), (7, 320, C)) * (not GM):
+        for bk, a, z in ((2, 0, 320), (3, 128, 320), (6, 320, C)):
             mm(bk, "qup", 16, t_, a, z - a, tk(a, z) + ["qupc", "qups"])
         MK = ["mtp1", "mtp2", "mtp3"]
         for t in range(4):
             p, a, z = slice(64 * (t == 2), 128), B1[t], B1[t + 1]
             bias = T.thr[p, t:t + 1]
-            if not GM:
-                bk = 3 if t < 3 else 7
-                act(T.df[p, a:z], T.ps[p, 512 * bk + a % 320:512 * bk + a % 320 + z - a], ["#%d" % bk, "sc%d" % t], ["d%d" % t], AF.Identity,
-                    bias=T.sc[p, 9 * t + 8:9 * t + 9], scale=-1.0)
-                MK.append("md%d%d" % (t, 2 if t < 3 else 6))
-                tt(T.mt[p, 4 * a + t:4 * z:4], T.df[p, a:z], T.ctri[p, p.start:128], A.is_lt, ["d%d" % t, "ctri"] + MK[:3], MK[-1:])
-                a = z
+            bk = 2 if t < 3 else 6
+            act(T.df[p, a:z], T.ctri[p, p.start:128], ["ctri", "sc%d" % t, "up%d" % t], ["d%d" % t], AF.Identity,
+                bias=T.sc[p, 9 * t + 8:9 * t + 9], scale=T.up[p, t:t + 1])
+            MK.append("md%d%d" % (t, bk))
+            tt(T.mt[p, 4 * a + t:4 * z:4], T.ps[p, 512 * bk + a % 320:512 * bk + a % 320 + z - a], T.df[p, a:z], A.is_lt, ["#%d" % bk, "d%d" % t] + MK[:3], MK[-1:], 1.0)
+            a = z
             for bk, lo, hi in ROW:
                 if max(lo, a) < hi:
                     k, o = "mu%d%d" % (t, bk), T.mt[p, 4 * max(lo, a) + t:4 * hi:4]
-                    ts(o, T.ps[p, 512 * bk + max(lo, a) - lo:512 * bk + hi - lo], T.sc[p, 9 * t + 8:9 * t + 9], A.is_ge,
-                       ["#%d" % bk, "sc%d" % t] + MK[:3], [k])
-                    if lo <= a and GM:
-                        d = T.mt[:, 4 * a + t:4 * z:4]
-                        asel(d, d, [[1, z - a]], A.is_ge, 0.0, p.start, -1, [k], [k])
                     MK.append(k)
+                    if hi == C:
+                        ts(o, T.ps[p, 512 * bk:512 * bk + hi - lo], T.sc[p, 9 * t + 8:9 * t + 9], A.is_lt, ["#%d" % bk, "sc%d" % t] + MK[:3], [k])
                     if hi < C:
-                        act(T.dd[p, a:hi], o, [k], ["acc%d" % t, "junk2"], AF.Identity, 0.02, accum_out=T.acc[p, t:t + 1])
+                        act(T.dd[p, a:hi], T.ps[p, 512 * 3 + a - 128:512 * 3 + hi - 128], ["#3", "sc%d" % t], ["sg%d" % t, "junk2"], AF.Sign,
+                            bias=T.sc[p, 9 * t + 8:9 * t + 9], scale=-1.0)
+                        act(o, T.dd[p, a:hi], ["sg%d" % t, "junk2"] + MK[:3], [k, "acc%d" % t], AF.Relu, 0.02, accum_out=T.acc[p, t:t + 1])
                         lin(T.th2[p, t:t + 1], T.acc[p, t:t + 1], 1.0 / 128, bias, ["acc%d" % t, "thr"], ["th2%d" % t])
                         bias = T.th2[p, t:t + 1]
                     else:
@@ -399,14 +450,23 @@ def rank_program(g, core, T, topo):
         tt(T.cde[:, 0:4], T.cm2[:, 43:72:9], T.cm2[:, 7:36:9], A.subtract, ["cm2s"], ["cde"])
         for b in range(4):
             mm(6 + b % 2, "ef", 128 * b, t_, 0, C, ["ef%d" % b] + TA)
-            o = 3072 + 896 * (b // 2) + b % 2
-            mv(T.win[:, o:3072 + 896 * (b // 2 + 1):2], ps(6 + b % 2, 0, C), ["#%d" % (6 + b % 2)], ["ft%d" % b], SC64, on="S")
+            o = 896 * (b // 2) + b % 2
+            mv(T.fh[:, o:896 * (b // 2 + 1):2], ps(6 + b % 2, 0, C), ["#%d" % (6 + b % 2)], ["ft%d" % b], SC64, on="SV")
         for k in range(2):
-            dma("Y", "dfh%d" % k, T.fh[:, 896 * k:896 * k + 896], T.win[:, 3072 + 896 * k:3968 + 896 * k], ["ft%d" % (2 * k), "ft%d" % (2 * k + 1)], ["fh%d" % k], 2.9)
+            ft = ["ft%d" % (2 * k), "ft%d" % (2 * k + 1)]
+            if FD:
+                dma(FD, "dfh%d" % k, T.win[:, WF + FW * k:WF + FW * k + FW], T.fh[:, 896 * k:896 * k + FW], ft, ["fh%d" % k], 2.5)
+            else:
+                mv(T.win[:, WF + FW * k:WF + FW * k + FW], T.fh[:, 896 * k:896 * k + FW], ft, ["fh%d" % k], f=0.5, on=GC)
+            for q in range(NH):
+                o = WA + WS * q + NF + 112 * k
+                mv(T.win[:, o:o + 112], T.fh[:, 896 * k + 112 * (7 - q):896 * k + 112 * (8 - q)], ft, ["fg%d%d" % (k, q)], f=0.5, on=GC)
         for t in range(4):
             p = slice(64 * (t == 2), 128)
-            ts(T.flt[p, t:256:4], T.ps[p, 512 * t:512 * t + 64], T.acc[p, 4 + t:5 + t], A.is_lt, ["#%d" % t, "flw", "bnd%d" % t], ["fa%d" % t])
-            act(T.flt[p, 640 + t:1152:4], T.tj[p, :], ["fa%d" % t, "tj"], ["fb%d" % t], AF.Identity, bias=T.flt[p, 33 * t:33 * t + 1], scale=0.0)
+            ts(T.flt[p, t:256:4], T.ps[p, 512 * t:512 * t + 64], T.acc[p, 4 + t:5 + t], A.is_gt, ["#%d" % t, "flw", "bnd%d" % t], ["fa%d" % t])
+            o, c = T.flt[p, 640 + t:1152:4], T.flt[p, 33 * t:33 * t + 1]
+            add({"V": (lambda o=o, c=c, p=p: V.tensor_scalar(o, T.kat[p, 0:128], c, None, A.mult), vc(96), 0),
+                 "S": (lambda o=o, c=c, p=p: S.activation(o, T.kat[p, 0:128], AF.Identity, bias=c, scale=0.0), vc(128), 0)}, ["fa%d" % t, "kat0"], ["fb%d" % t])
         quant("fl", 0, 128, T.flt, ["fa%d" % t for t in range(4)], ["fl0"])
         quant("fl", 160, 288, T.flt, ["fb%d" % t for t in range(4)], ["fl1"])
         mm(5, "ka", 128, "fl", 0, 128, ["fl0", "ka1"], True, False)
@@ -415,7 +475,7 @@ def rank_program(g, core, T, topo):
         tt(T.eq[:], ps(4, 0, 32), T.kd[:, 0:32], A.is_equal, ["#4", "kd"], ["eq"], 1.0)
         scan(T.wv[:], T.kd[:, 32:64], T.eq[:], 0.0, A.mult, A.add, ["eq", "kdr"], ["wv"])
         for t in range(4):
-            ts(T.sot[:, t:512:4], T.ioh[:], T.cde[:, t:t + 1], A.is_equal, ["io", "cde", "wv"], ["so%d" % t], T.wv[:, 8 * t + 7:8 * t + 8], A.mult, 0.5)
+            ts(T.sot[:, t:512:4], T.ioh[:], T.cde[:, t:t + 1], A.is_equal, ["io0", "io1", "io2", "io3", "cde", "wv"], ["so%d" % t], T.wv[:, 8 * t + 7:8 * t + 8], A.mult, 0.5)
         quant("so", 0, 128, T.sot, ["so%d" % t for t in range(4)], ["so"])
         mm(0, "fl", 160, "kb", 128, 128, ["fl1", "kb"])
         mm(2, "so", 0, "kb", 0, 128, ["so", "kb"])
@@ -429,37 +489,33 @@ def rank_program(g, core, T, topo):
                 a, n = 64 * z + 32 * y, 32 - 8 * y
                 tt(T.sm[64 * y:64 * y + 64, 32 * z:32 * z + n], T.cand[0:64, a:a + n], T.cand[64:128, a + 8:a + 8 + n], A.min, ["cand%d" % z],
                    ["sm%d%d" % (z, y)], alone=True)
-        scan(T.pkf[:], T.kpk[:], T.sm[:, 32:64], 0.0, A.mult, A.add, ["sm10", "sm11", "kpk"], ["pkf"])
+        scan(T.pkf[:], T.kpk[:], T.sm[:, 32:64], 0.0, A.mult, A.add, ["sm10", "sm11", "kpk0", "kpk1"], ["pkf"])
         cp(T["pk%d" % r][:], T.pkf[:, 1:32:2], ["pkf"], ["pk%d" % r])
         send(T["lst%d" % r][:], T["pk%d" % r][:], "al%d" % r, 1, ["pk%d" % r], ["lst%d" % r], 2.0)
-        act(T.pn[:], T.ps[:, 2560:2560 + 32:8], ["#5"], ["pn"], AF.Identity, bias=0.5, scale=-1.0)
         for t in range(4):
-            p = slice(64 * (t == 2), 128)
-            if t in CMS:
-                act(T.cmt[p, t:1536:4], T.ios[p, :], ["pn", "ios"], ["cm%d" % t], AF.Sign, bias=T.pn[p, t:t + 1])
-            else:
-                ts(T.cmt[p, t:1536:4], T.ios[p, :], T.ps[p, 2560 + 8 * t:2561 + 8 * t], A.is_ge, ["#5", "ios"], ["cm%d" % t], 2.0, A.mult, 0.5)
-        quant("cm", 0, 384, T.cmt, ["cm%d" % t for t in range(4)], ["cm"])
-        mm(1, "ka", 0, "cm", 0, 384, ["cm", "ka0"])
-        add({"V": (lambda: V.transpose(T.lrow[:], ps(1, 0, 384)), vc(384), 0)}, ["#1"], ["lrow"])
-        ts(T.pl[:], T.lrow[:, 0:384:32], 0.5, A.mult, ["lrow"], ["pl"], float(sum(32 if t == 2 else 64 for t in CMS)), A.add)
+            p, a = slice(64 * (t == 2), 128), 64 * (t == 3)
+            ts(T.cmt[p, 4 * a + t:4 * NF:4], T.ios[p, a:NF], T.ps[p, 2560 + 8 * t:2561 + 8 * t], A.is_ge, ["#5", "ios"], ["cm%d" % t], f=0.5)
+        quant("cm", 0, NF, T.cmt, ["cm%d" % t for t in range(4)], ["cm"])
+        mm(1, "ka", 0, "cm", 0, NF, ["cm", "ka0"])
+        scan(T.lrow[:], T.k16[:], ps(1, 0, NF), 0.0, A.add, A.min, ["#1", "k16"], ["lrow"])
+        cp(T.pl[:], T.lrow[:, 15:NF:16], ["lrow"], ["pl"])
         sl, ld = "slot%d" % r, "land%d" % r
         pick(sl, t_, NF, C, T.pl[:, 0:12], TA + ["pl"])
         send(T[ld + "c"][:].bitcast(dt.uint8), T[sl + "c"][:].bitcast(dt.uint8), "ac%d" % r, 2, [sl + "c"], [ld + "c"], 2.3)
         send(T[ld + "s"][:], T[sl + "s"][:], "ac%d" % r, 2, [sl + "s"], [ld + "s"], 2.1)
 
         def unpack(src, base, key, banks, on):
-            for k in range(8):
+            for k in range(7, -1, -1):
                 bk = banks[k % len(banks)]
-                o = base + NF * (7 - k)
-                a, z = (0, NF) if r == 0 else (max(0, 136 - 56 * k), NF) if base else (0, min(NF, 399 - 56 * k))
+                o = base + (WS if base else NF) * (7 - k)
+                a, z = (max(0, 136 - 56 * k), NF) if base else (0, NF if r == 0 else min(NF, 399 - 56 * k))
                 a0, z0 = min(a, NF - 128), max(z + z % 2, 128)
                 mm(bk, "eb", 128 * k, src, a0, z0 - a0, [src + "c", src + "s", "eb%dc" % (k // 2), "eb%ds" % (k // 2)])
                 mv(T.win[:, o + a:o + z], ps(bk, a - a0, z - a0), ["#%d" % bk], ["%s%d" % (key, k)], SC64, on=on)
         unpack(sl, 0, "wo", (3, 4, 5), "SV")
         scan(T.kos[:, 31::-1], T.kst[:, 0:32], T.sm[:, 31::-1], 0.0, A.add, A.min, ["sm00", "sm01", "kst"], ["kos"])
         tt(T.own[:], T.kos[:], T.idc[:], A.min, ["kos", "idc"], ["own"])
-        unpack(ld, 1536, "wa", (6, 7, 1, 2, 0), "SV")
+        unpack(ld, WA, "wa", (6, 7, 1, 2, 0), "SV")
         cp(T.ai[:], T["lst%d" % r][:], ["lst%d" % r], ["ai"])
         ts(T.a2[:, 0:32:2], T.ai[:], 8, A.arith_shift_right, ["ai"], ["a2h"])
         ts(T.a2[:, 1:32:2], T.ai[:], 255, A.bitwise_and, ["ai"], ["a2l"])
@@ -471,26 +527,30 @@ def rank_program(g, core, T, topo):
         for k in range(2):
             mv(T.rep[32 * k:32 * k + 32, 64:128], T.rep[32 - 32 * k:64 - 32 * k, 0:64], ["rep0", "rep1"], ["rp%d" % k])
         mv(T.rep[64:128, :], T.rep[0:64, :], ["rep0", "rep1", "rp0", "rp1"], ["rp2"])
-        ts(T.off[:], T.rep[:, 0:128].indirect(T.ordr[:, 0:8]), 1536.0, A.add, ["rep0", "rep1", "rp0", "rp1", "rp2", "ordr"], ["off"], f=2.0)
-        WIN = ["ft%d" % b for b in range(4)] + ["%s%d" % (a, k) for a in ("wo", "wa") for k in range(8)]
-        for h in range(H):
-            a, z = CUTS[h], CUTS[h + 1]
+        ts(T.off[:], T.rep[:, 0:128].indirect(T.ordr[:, 0:8]), float(WA), A.add, ["rep0", "rep1", "rp0", "rp1", "rp2", "ordr"], ["off"], f=2.0)
+        WIN = ["ft%d" % b for b in range(4)] + ["wo%d" % k for k in range(8)] + ["fg%d%d" % (k, q) for k in range(2) for q in range(NH)] + ["off"]
+        for i, (a, z) in enumerate(GAT):
+            n = NH if a >= C - 56 * NH else 8
             for b1 in range(2):
                 lo, hi = 896 * b1 + 2 * a, 896 * b1 + 2 * z
-                tt(T.yt[:, lo:hi], T.win[:, 0:4864].indirect(T.off[:, 64 * b1 + a // 8:64 * b1 + z // 8]), T.fh[:, lo:hi],
-                   A.add, WIN + ["off", "fh%d" % b1], ["yt%d%d" % (b1, h)], 1.6)
+                tt(T.yt[:, lo:hi], T.win[:, 0:WA + NH * WS if n < 8 else WF + 2 * FW].indirect(T.off[:, 64 * b1 + a // 8:64 * b1 + z // 8]), T.fh[:, lo:hi],
+                   A.add, WIN + ["wa%d" % (7 - k) for k in range(n)] + ["fh0", "fh1"] * (n == 8), ["yt%d%d" % (b1, i)], 1.6)
+        for h in range(H):
+            a, z = CUTS[h], CUTS[h + 1]
             for be in range(4):
                 for b in range(4):
                     o = 896 * (be // 2)
                     mv(T.yy[32 * be:32 * be + 32, 4 * a + b:4 * z:4], T.yt[32 * b:32 * b + 32, o + 2 * a + be % 2:o + 2 * z:2],
-                       ["yt%d%d" % (be // 2, h)], ["yy%d%d%d" % (be, b, h)], f=0.5, on=GC)
+                       ["yt%d%d" % (be // 2, i) for i, (c, d) in enumerate(GAT) if c < z and a < d], ["yy%d%d%d" % (be, b, h)], f=0.5, on=GC)
             quant("qy", a, z, T.yy, ["yy%d%d%d" % (i, b, h) for i in range(4) for b in range(4)], ["qy%d" % h])
             for b in range(4):
                 bk = (4 * h + b) % 8
-                pl = slice(C * b + a, C * b + z)
                 mm(bk, "qw", 128 * b, "qy", a, z - a, ["qy%d" % h, "qwc", "qws"])
-                mv(T.y1[:, pl], T.yy[:, 4 * a + b:4 * z:4], ["yy%d%d%d" % (i, b, h) for i in range(4)], ["y1%d%d" % (b, h)], 32.0, 0.5)
-                tt(T.xs[:, 4 * a + b:4 * z:4], ps(bk, 0, z - a), T.y1[:, pl], A.add, ["#%d" % bk, "y1%d%d" % (b, h)], ["xs%d%d" % (b, h)], 1.0)
+                if b < YP:
+                    c = slice(4 * a + b, 4 * z, YP)
+                    mv(T.y1[:, c], T.yy[:, c], ["yy%d%d%d" % (i, j, h) for i in range(4) for j in range(b, 4, YP)], ["y1%d%d" % (b, h)], 32.0, 0.5)
+                c = slice(4 * a + b, 4 * z, 4)
+                tt(T.xs[:, c], ps(bk, 0, z - a), T.y1[:, c], A.add, ["#%d" % bk, "y1%d%d" % (b % YP, h)], ["xs%d%d" % (b, h)], 1.0)
             quant_x(r + 1, T.xs, h, ["xs%d%d" % (b, h) for b in range(4)])
 
     t_ = "t%d" % R
@@ -518,8 +578,8 @@ def rank_program(g, core, T, topo):
                         for s2, v2 in knew[d].items():
                             seen[e][s2] = max(seen[e].get(s2, 0), v2)
         if e == "G" and not o["arrive"]:
-            moves = len(o["alts"]) > 1
-            if (moves or moved) and seen[e].get(e, 0) < cnt.get(e, 0):
+            moves = o.get("moves", False)
+            if moves != moved and seen[e].get(e, 0) < cnt.get(e, 0):
                 g.wait_ge(T.sem.G, cnt[e])
                 seen[e][e] = cnt[e]
             moved = moves

@@ -8,9 +8,12 @@ B0 = (0, 128, 192, 320)
 B1 = (0, 128, 256, 320, 448)
 WA, WS, NH = 8 * NF, NF + 224, 3
 WF = WA + 7 * WS + NF
+KEY = 194
+TOP = WA + KEY + int(BIG)
 FW = 2 * C - 112 * NH
 FD = "Y"
 UPS = ((0, 3), (3, 4))
+REP2 = True
 YP = 2
 GAT = ((288, 448), (0, 288))
 GC = "VSG"
@@ -34,31 +37,31 @@ for _r in range(R):
     _q("land%d" % _r, NF)
     _sb("pk%d" % _r, 16, U16)
     _sb("lst%d" % _r, 16, U16)
-for _n, _w in (("qu", 128), ("qup", 144), ("qv", 128), ("qw", 512), ("ef", 512), ("eb", 1024), ("ka", 384),
-               ("kb", 256), ("kr", 152), ("m", C), ("fl", 288), ("cm", NF), ("so", 128), ("qy", C)):
+for _n, _w in (("qu", 128), ("qup", 144), ("qv", 128), ("qw", 512), ("ef", 512), ("eb", 1024), ("ka", 256),
+               ("kb", 512), ("kr", 216), ("m", C), ("fl", 192), ("cm", NF), ("so", 128), ("qy", C)):
     _q(_n, _w)
-for _n, _w in (("xin", 4 * C), ("xs", 4 * C), ("ut", 512), ("vt", 512), ("eft", 2048), ("kat", 1536), ("kbt", 1024), ("mt", 4 * C),
-               ("flt", 1152), ("cmt", 4 * NF), ("sot", 512), ("krt", 608), ("ios", NF), ("k16", NF), ("ioh", 128), ("kv", 128),
+for _n, _w in (("xin", 4 * C), ("xs", 4 * C), ("ut", 512), ("vt", 512), ("eft", 2048), ("kat", 1024), ("kbt", 2048), ("mt", 4 * C),
+               ("flt", 768), ("cmt", 4 * NF), ("sot", 512), ("krt", 864), ("ios", NF), ("k16", NF), ("ioh", 128), ("k8", 512),
                ("win", WF + 2 * FW), ("yt", 4 * C), ("fh", 4 * C), ("yy", 4 * C), ("y1", 4 * C), ("nar", 384), ("ctri", 128), ("tj", 128)):
     _sb(_n, _w, BF)
-for _n, _w in (("sc", 80), ("cmx", 80), ("cm2", 80), ("rr", 80), ("cde", 16), ("k72", 160), ("thr", 4), ("th2", 4), ("dd", C), ("ebi", 8), ("kd", 64),
-               ("eq", 32), ("wv", 32), ("lrow", NF), ("ln", 128), ("nb", 128), ("cand", 128), ("sm", 64), ("kpk", 32),
+for _n, _w in (("sc", 80), ("cmx", 80), ("cm2", 80), ("rr", 80), ("k72", 160), ("thr", 4), ("dd", 640), ("ebi", 8), ("cv", 32),
+               ("eq", 32), ("lrow", NF), ("ln", 512), ("cand", 128), ("cb", 64), ("sm", 64), ("kpk", 32),
                ("pkf", 32), ("kos", 32), ("own", 32), ("kn", 32), ("kns", 32), ("rep", 128), ("df", C), ("up", 4), ("kst", 64), ("idc", 32),
                ("w1", 32), ("w2", 16), ("pv", 8), ("yo", C), ("acc", 8)):
     _sb(_n, _w, F32)
-for _n, _w in (("lev", 128), ("ai", 16), ("a2", 32), ("pi", 8), ("wi", 8)):
+for _n, _w in (("ci", 32), ("ai", 16), ("a2", 32), ("pi", 8), ("wi", 8)):
     _sb(_n, _w, I32)
-for _n, _w in (("ul", 10), ("pl", 12), ("ordr", 8), ("off", 128), ("ebl", 16)):
+for _n, _w in (("ul", 10), ("pl", 12), ("ordr", 8), ("cl", 8), ("off", 128), ("ebl", 16)):
     _sb(_n, _w, U16)
 SCRATCH["ps"] = ("psum", [128, 4096], F32)
-SEMAPHORES = ["V", "S", "P", "G", "dx0", "dx1", "du", "dv", "dwc", "dws", "outs", "sent", "dw", "dfh0", "dfh1"] + ["d%s%d" % (k, b) for k in "ef" for b in (1, 2, 3)] + \
+SEMAPHORES = ["V", "S", "P", "G", "dx0", "dx1", "du", "dv", "dwc", "dws", "outs", "sent", "dw", "dfh0", "dfh1"] + ["d%s%d" % (k, b) for k in "ef" for b in (1, 2, 3)] + ["dk%d" % k for k in range(7)] + \
              ["%s%d" % (k, r) for k in ("ac", "al") for r in range(R)]
 CY, OV, LAT, LATG, PE, RI, DL = 0.00085, 0.005, 0.2, 0.22, 0.0006, 0.4, -1.0
 MORE = {"S": 0.008, "G": 0.02}
 CASES = ((1.0, 0.005, 0.0, 0.0, 0.19, 0.23, 0.2, 0.0, -0.3, 1.0, 0.4, 0.0), (1.0, 0.0, 0.0, 0.0, 0.21, 0.21, 0.1, -0.3, 0.0, 0.85, 0.6, 0.0),
          (1.0, 0.015, 0.01, 0.03, 0.16, 0.19, 0.4, 0.5, -0.8, 1.2, 0.15, 0.015), (1.35, 0.005, 0.0, 0.0, 0.22, 0.25, 0.3, 0.5, 0.2, 1.4, 0.6, 0.0))
-TRIES = 6000
-SPAN, PLAN = [0.0], []
+TRIES, MOVES = 2500, 25000
+SPAN, PLAN, STEP = [0.0], [], [0, 0, 0]
 
 
 def name(k):
@@ -172,9 +175,103 @@ def schedule(ops):
             cur, pri, spare = got, p2, s2
             if got[0] < best[0]:
                 best = got
-    SPAN[:] = best[:2]
-    PLAN.append(sorted((best[2][i], i, best[4][i]) for i in range(n)))
+    order, eng, SPAN[:] = polish(ops, deps, succ, cases, sorted(range(n), key=lambda k: (best[2][k], k)), list(best[4]))
+    PLAN.append([(p, i, eng[i]) for p, i in enumerate(order)])
     return PLAN[0]
+
+
+def polish(ops, deps, succ, cases, order, eng):
+    n = len(ops)
+    twin = [[j for j in (i - STEP[0], i + STEP[0], i - 2 * STEP[0], i + 2 * STEP[0]) if STEP[1] <= i < STEP[2] and STEP[1] <= j < STEP[2]] for i in range(n)]
+
+    def run(order, eng, first, old):
+        out, total = [], 0.0
+        for c, (cost, lat, own, latg) in enumerate(cases):
+            done, hold, why = (list(x) for x in old[c]) if old else ([0.0] * n, [0.0] * n, [-1] * n)
+            free, last = {}, {}
+            p = first - 1
+            while p >= 0 and len(free) < 5:
+                i = order[p]
+                if eng[i] not in free:
+                    free[eng[i]], last[eng[i]] = hold[i], i
+                p -= 1
+            for p in range(first, n):
+                i = order[p]
+                e = eng[i]
+                t, by = free.get(e, 0.0), -2 - last.get(e, -1)
+                for d, raw in deps[i]:
+                    if eng[d] != e:
+                        u = done[d] + (latg if e == "G" else lat)
+                    elif raw:
+                        u = done[d] + (latg if e == "G" else own)
+                    else:
+                        continue
+                    if u > t:
+                        t, by = u, d
+                k = cost[i][e]
+                free[e] = hold[i] = t + k[0]
+                done[i] = t + k[0] + k[1]
+                why[i], last[e] = by, i
+            total += max(done)
+            out.append((done, hold, why))
+        return total / len(cases), out
+
+    def ahead(order, i, j):
+        a, b = order.index(j), order.index(i)
+        if a >= b:
+            return None
+        need, move = {d for d, raw in deps[i]}, [i]
+        for k in order[b - 1:a - 1 if a else None:-1]:
+            if k in need:
+                if k == j or len(move) > 6:
+                    return None
+                move.append(k)
+                need.update(d for d, raw in deps[k])
+        gone = set(move)
+        order[a:b + 1] = move[::-1] + [k for k in order[a:b + 1] if k not in gone]
+        return a
+    cur, state = run(order, eng, 0, None)
+    start, best, z = cur, (cur, list(order), list(eng)), 4321
+    for it in range(MOVES):
+        z = (z * 1103515245 + 12345) % 2147483648
+        done, hold, why = state[(z >> 8) % len(cases)]
+        i, pairs = done.index(max(done)), []
+        while why[i] != -1:
+            j = why[i] if why[i] >= 0 else -2 - why[i]
+            if why[i] < 0:
+                pairs.append((i, j))
+            i = j
+        z = (z * 1103515245 + 12345) % 2147483648
+        i, j = pairs[(z >> 8) % len(pairs)]
+        z = (z * 1103515245 + 12345) % 2147483648
+        kind, every, o2, e2, first = (z >> 8) % 8, (z >> 12) % 4 > 0, list(order), list(eng), n
+        if kind < 5:
+            p = order.index(j)
+            for _k in range((0, 0, 0, 1, 3)[kind]):
+                q = p - 1
+                while q >= 0 and eng[order[q]] != eng[i]:
+                    q -= 1
+                p = q if q >= 0 else p
+            j = order[p]
+            for k in [i] + (twin[i] if every else []):
+                if 0 <= j + k - i < n:
+                    a = ahead(o2, k, j + k - i)
+                    first = first if a is None else min(first, a)
+        else:
+            i = j if kind < 7 else i
+            other = [e for e in ops[i]["alts"] if e != eng[i]]
+            if other:
+                for k in [i] + (twin[i] if every else []):
+                    e2[k] = other[(z >> 16) % len(other)]
+                    first = min(first, o2.index(k))
+        if first < n:
+            got, s2 = run(o2, e2, first, state)
+            z = (z * 1103515245 + 12345) % 2147483648
+            if got <= cur + 0.12 * (1 - it / MOVES) * ((z >> 8) % 1000) / 1000:
+                cur, state, order, eng = got, s2, o2, e2
+                if got < best[0]:
+                    best = (got, list(order), list(eng))
+    return best[1], best[2], (start, best[0])
 
 
 def rank_program(g, core, T, topo):
@@ -300,14 +397,13 @@ def rank_program(g, core, T, topo):
     iota(T.pi[:, 0:1], [[0, 1]], 0, 1, ["pi0"], False)
     iota(T.tj[:], [[1, 128]], 0, -1, ["tj"])
     iota(T.k72[:, 0:72], [[-15, 2], [0, 36]], 16, 0, ["k72a"])
-    iota(T.kd[:, 0:32], [[0, 4], [-1, 8]], -1, 0, ["kd"])
     iota(T.ios[:], [[1, NF]], 0, 0, ["ios"])
     iota(T.k16[:], [[0, NF // 16], [1, 16]], 0, 0, ["k16"])
     ms(T.kat[:, 0:512], 1.0, ["kat0"], 0.5, False)
     for t, z in ((1, 128), (2, C), (3, 320)):
         ms(T.mt[:, t:4 * z:4], 0.0, ["mtp%d" % t], 0.5)
     ms(T.ul[:], 1, ["ul"], s=False)
-    for k, (n, o) in enumerate(((15, A.bitwise_and), (7, A.bitwise_and), (3, A.arith_shift_right), (32, A.bitwise_and), (79, A.bitwise_and))):
+    for k, (n, o) in enumerate(((15, A.bitwise_and), (7, A.bitwise_and), (6, A.arith_shift_right), (32, A.bitwise_and), (79, A.bitwise_and))):
         ts(T.pi[:, k + 1:k + 2], T.pi[:, 0:1], n, o, ["pi0"], ["pi%d" % (k + 1)])
     cp(T.pv[:, 0:5], T.pi[:, 1:6], ["pi1", "pi2", "pi3", "pi4", "pi5"], ["pv"])
     ts(T.k16[:], T.k16[:], T.pv[:, 0:1], A.is_equal, ["k16", "pv"], ["k16"], BIG, A.mult, 0.5)
@@ -316,32 +412,26 @@ def rank_program(g, core, T, topo):
     quant("qu", 0, 128, T.ut, ["ut"], ["qu"])
     pick("qup", "qu", 144, 128, T.ul[:, 0:9], ["qu", "ul"])
     quant("qv", 0, 128, T.vt, ["vt"], ["qv"])
-    quant("ka", 0, 128, T.kat, ["kat0"], ["ka0"])
     for t in range(4):
         ts(T.kat[:, 512 + t:1024:4], T.tj[:], 0.0, A.is_ge, ["tj"], ["tri%d" % t], f=0.5)
-    asel(T.nar[:, 128:256], T.kat[:, 512:1024:4], [[-8, 16], [0, 8]], A.is_ge, 0.0, 0, 1, ["tri0"], ["blk"])
-    asel(T.nar[:, 256:384], T.nar[:, 128:256], [[1, 128]], A.not_equal, -8.0, 0, -1, ["blk"], ["del"])
-    for t in range(4):
-        mv(T.kat[:, 1024 + t:1536:4], T.nar[:, 256:384], ["del"], ["kat2%d" % t], f=0.5, on="VSG")
-    quant("ka", 128, 384, T.kat, ["tri%d" % t for t in range(4)] + ["kat2%d" % t for t in range(4)], ["ka1"])
-    ms(T.flt[:, 0:512], 0.0, ["flz"], 0.5)
-    ms(T.flt[:, 512:640], 0.0, ["fly"], 0.5)
-    ms(T.flt[0:64, 642:1152:4], 0.0, ["fb2"], 0.5)
+    quant("ka", 0, 256, T.kat, ["kat0"] + ["tri%d" % t for t in range(4)], ["ka0", "ka1"])
+    ms(T.flt[0:64, 2:576:4], 0.0, ["fa2"], 0.5)
+    ms(T.sot[0:64, 2:512:4], 0.0, ["so2"], 0.5)
     ms(T.cmt[0:64, 2:4 * NF:4], 0.0, ["cm2"], 0.5)
     ms(T.cmt[:, 3:256:4], 0.0, ["cm3"], 0.5)
-    quant("fl", 32, 160, T.flt, ["flz", "fly"], ["flw", "fl0"])
-    ms(T.krt[:, 0:256], -256.0, ["kr0"], 0.5)
-    ms(T.krt[:, 96:128], 1.0, ["kr0"], 0.5)
-    ms(T.krt[:, 256:608], 1.0, ["kr1"], 0.5)
-    quant("kr", 0, 152, T.krt, ["kr0", "kr1"], ["kr"])
+    ms(T.krt[:, 0:64], -256.0, ["kr0"], 0.5)
+    ms(T.krt[:, 24:32], 1.0, ["kr0"], 0.5)
+    ms(T.krt[:, 64:332], 1.0, ["kr1"], 0.5)
+    ms(T.krt[:, 332:600], 1.0, ["kr2"], 0.5)
+    quant("kr", 0, 150, T.krt, ["kr0", "kr1", "kr2"], ["kr"])
     ts(T.ctri[:], T.tj[:], 0.0, A.is_le, ["tj"], ["ctri"], f=0.5)
     iota(T.acc[:, 4:8], [[192, 2], [128, 2]], 128 - NF, 0, ["bnd0", "bnd1", "bnd2", "bnd3"])
     lin(T.thr[:], T.acc[:, 4:8], 1.0 / 128, 0.0, ["bnd0", "bnd1", "bnd2"], ["thr"])
     ms(T.k72[:, 80:152], 0.0, ["k72d"])
     ms(T.k72[:, 88:152:9], -1e29, ["k72d"])
     ms(T.cmx[:, 0:1], -1e29, ["cmx0"])
-    ms(T.kd[:, 32:64], math.exp(-1.0), ["kdr"], s=False)
-    act(T.kd[:, 32:64:8], T.kat[:, 0:4], ["kat0"], ["kdr"], AF.Ln, 1.3)
+    ms(T.k8[:], 1.0, ["k8"], 0.5)
+    ms(T.k8[:, 0:512:8], 0.0, ["k8"], 0.5)
     asel(T.eft[:, 0:512], T.kat[:, 0:512], [[-256, 4], [-1, 32], [256, 4]], A.is_equal, 0.0, 0, 1, ["kat0"], ["eft0", "efu0"])
     for b in range(4):
         if b:
@@ -359,23 +449,38 @@ def rank_program(g, core, T, topo):
     iota(T.nar[:, 0:32], [[16, 2], [1, 8], [32, 2]], -105, 0, ["ioi"])
     for k in range(4):
         ts(T.ioh[:, 32 * k:32 * k + 32], T.nar[:, 0:32], T.pv[:, 1:2], A.subtract, ["ioi", "pv"], ["io%d" % k], 64.0 * (k % 2) - 8 * (k // 2), A.add)
-    iota(T.kv[:], [[7, 2], [1, 8], [-7, 8]], 42, 0, ["kv"])
-    iota(T.w1[:, 16:20], [[24, 2], [16, 2]], 0, 0, ["w1c"])
-    lin(T.w2[:, 8:12], T.w1[:, 16:20], 1.0, T.pv[:, 2:3], ["w1c", "pv"], ["c"])
-    for t in range(4):
-        ts(T.kbt[:, t:512:4], T.kv[:], T.w2[:, 8 + t:9 + t], A.is_equal, ["kv", "c"], ["kb0%d" % t], f=0.5)
-        ts(T.kbt[:, 512 + t:1024:4], T.kv[:], T.w2[:, 8 + t:9 + t], A.is_gt, ["kv", "c"], ["kb1%d" % t], f=0.5)
-    lin(T.kbt[:, 512:768], T.kbt[:, 512:768], 1.0, -1.0, ["kb1%d" % t for t in range(4)], ["kc"], 0.5)
-    quant("kb", 0, 256, T.kbt, ["kb0%d" % t for t in range(4)] + ["kc"], ["kb"])
+    ms(T.kbt[:, 512:1024], -2.0 / 256, ["kb1"], 0.5)
+    asel(T.kbt[:, 512:1024], T.kbt[:, 512:1024], [[-256, 4], [-1, 32], [256, 4]], A.is_gt, -3.0 / 256, -32, 1, ["kb1"], ["kb1"])
+    asel(T.kbt[:, 512:1024], T.kbt[:, 512:1024], [[-256, 4], [-1, 32], [256, 4]], A.not_equal, 320.0 / 256, -32, 1, ["kb1"], ["kb1"])
+    for k, (q, o, a, n) in enumerate(((0, 0, 32, 96), (0, 96, 96, 32), (2, 32, 0, 96), (2, 0, 0, 32), (3, 64, 0, 64), (3, 0, 0, 32), (3, 32, 0, 32))):
+        dma("Y", "dk%d" % k, T.kbt[o:o + n, 512 * q:512 * q + 512], T.kbt[a:a + n, 512:1024], ["kb1"], ["kbd%d" % k], 2.2)
+    quant("kb", 0, 256, T.kbt, ["kb1", "kbd0", "kbd1"], ["kba"])
+    quant("kb", 256, 512, T.kbt, ["kbd%d" % k for k in range(2, 7)], ["kbb"])
+    lin(T.w2[:, 5:6], T.pv[:, 2:3], 8.0, T.pv[:, 0:1], ["pv"], ["w25"])
+    lin(T.w2[:, 6:7], T.pv[:, 1:2], -57.0, T.w2[:, 5:6], ["pv", "w25"], ["w26"])
+    iota(T.cv[:, 0:8], [[56, 2], [16, 4]], 336, 0, ["cv0"])
+    iota(T.cv[:, 8:16], [[0, 2], [-64, 2], [0, 2]], 32, 0, ["cv1"])
+    lin(T.cv[:, 8:16], T.cv[:, 8:16], T.pv[:, 2:3], T.w2[:, 6:7], ["cv1", "pv", "w26"], ["cv1"])
+    tt(T.cv[:, 0:8], T.cv[:, 0:8], T.cv[:, 8:16], A.add, ["cv0", "cv1"], ["cv0"])
+    for k, (n, o, v) in enumerate(((256.0, A.is_ge, 64.0), (448.0, A.is_ge, -256.0), (0.0, A.is_lt, 320.0))):
+        ts(T.cv[:, 8 * k + 8:8 * k + 16], T.cv[:, 0:8], n, o, ["cv0"], ["cv%d" % (k + 1)], v, A.mult)
+    tt(T.cv[:, 0:16], T.cv[:, 0:16], T.cv[:, 16:32], A.add, ["cv0", "cv1", "cv2", "cv3"], ["cv0", "cv1"])
+    tt(T.ci[:, 0:8], T.cv[:, 0:8], T.cv[:, 8:16], A.add, ["cv0", "cv1"], ["ci0"])
+    ts(T.ci[:, 8:16], T.ci[:, 0:8], 96, A.bitwise_and, ["ci0"], ["ci1"])
+    ts(T.ci[:, 16:24], T.ci[:, 0:8], 2, A.arith_shift_right, ["ci0"], ["ci2"], 96, A.bitwise_and)
+    ts(T.ci[:, 24:32], T.ci[:, 0:8], 31, A.bitwise_and, ["ci0"], ["ci3"])
+    ts(T.ci[:, 8:16], T.ci[:, 8:16], 4.0, A.mult, ["ci1"], ["ci1"], 7.0, A.add)
+    tt(T.ci[:, 16:24], T.ci[:, 16:24], T.ci[:, 24:32], A.add, ["ci2", "ci3"], ["ci2"])
+    tt(T.ci[:, 0:8], T.ci[:, 8:16], T.ci[:, 16:24], A.add, ["ci1", "ci2"], ["ci0"])
+    cp(T.cl[:], T.ci[:, 0:8], ["ci0"], ["cl"])
     for k in range(2):
         ms(T.kpk[:, k:32:2], 256.0 * k, ["kpk%d" % k])
-        ms(T.kst[:, 32 * k:32 * k + 32], float(WS if k else -NF), ["kst%d" % k])
-    ms(T.kst[:, 0:64:8], 2 * BIG, ["kst0", "kst1", "kst"])
-    ms(T.sm[:], 255.0, ["sm00", "sm01", "sm10", "sm11"])
-    iota(T.idc[:], [[16, 4], [-112, 8]], 784 + WF - WA, 0, ["idc"])
-    iota(T.kn[:], [[16, 4], [WS, 8]], NF, 0, ["kn"])
-    lin(T.w2[:, 3:4], T.pv[:, 3:4], FW / 32, T.pv[:, 4:5], ["pv"], ["w23"])
-    lin(T.w2[:, 4:5], T.pv[:, 3:4], 3.5, T.pv[:, 4:5], ["pv"], ["w24"])
+        ms(T.kst[:, 32 * k:32 * k + 32], float(-WS if k else NF), ["kst%d" % k])
+    ms(T.kst[:, 0:64:8], -2 * BIG, ["kst0", "kst1", "kst"])
+    iota(T.idc[:], [[-16, 4], [112, 8]], TOP - 784 - WF, 0, ["idc"])
+    iota(T.kn[:], [[-16, 4], [-WS, 8]], TOP - WA - NF, 0, ["kn"])
+    ts(T.w2[:, 3:4], T.pv[:, 3:4], -FW / 32, A.mult, ["pv"], ["w23"], T.pv[:, 4:5], A.subtract)
+    ts(T.w2[:, 4:5], T.pv[:, 3:4], -3.5, A.mult, ["pv"], ["w24"], T.pv[:, 4:5], A.subtract)
     lin(T.idc[:], T.idc[:], 1.0, T.w2[:, 3:4], ["idc", "w23"], ["idc"])
     for q in range(NH):
         lin(T.idc[:, q:32:8], T.kn[:, q:32:8], 1.0, T.w2[:, 4:5], ["kn", "w24"], ["idc"])
@@ -399,6 +504,7 @@ def rank_program(g, core, T, topo):
     for h in range(H):
         quant_x(0, T.xin, h, ["xin%d" % min(h, 1)])
 
+    STEP[1] = len(ops)
     for r in range(R):
         t_ = "t%d" % r
         TA = ["%s_%d" % (t_, h) for h in range(H)]
@@ -408,9 +514,13 @@ def rank_program(g, core, T, topo):
         for t, bk in enumerate((0, 1, 4, 5)):
             mm(bk, t_, B0[t], "qup", 0, 128, tk(B0[t], B0[t] + 128) + ["qupc", "qups"])
             mv(T.sc[:, 9 * t:9 * t + 9], T.ps[:, 512 * bk:512 * bk + 18:2], ["#%d" % bk], ["sc%d" % t])
+        mm(7, t_, B0[3], "qup", 0, 128, tk(B0[3], C) + ["qupc", "qups"])
         for a, z in UPS:
-            act(T.up[:, a:z], T.sc[:, 9 * a + 8:9 * z:9], ["sc%d" % t for t in range(a, z)], ["up%d" % t for t in range(a, z)], AF.Abs,
-                bias=2.0 ** -125, scale=0.6 * 2.0 ** -23)
+            if a < 3:
+                act(T.up[:, a:z], T.sc[:, 9 * a + 8:9 * z:9], ["sc%d" % t for t in range(a, z)], ["up%d" % t for t in range(a, z)], AF.Abs,
+                    bias=2.0 ** -125, scale=0.6 * 2.0 ** -23)
+            else:
+                act(T.up[:, 3:4], ps(7, 16, 17), ["#7"], ["up3"], AF.Abs, bias=2.0 ** -125, scale=0.6 * 2.0 ** -23)
         ROW = ((2, 0, 320), (6, 320, C))
         for bk, a, z in ((2, 0, 320), (3, 128, 320), (6, 320, C)):
             mm(bk, "qup", 16, t_, a, z - a, tk(a, z) + ["qupc", "qups"])
@@ -431,23 +541,22 @@ def rank_program(g, core, T, topo):
                     if hi == C:
                         ts(o, T.ps[p, 512 * bk:512 * bk + hi - lo], T.sc[p, 9 * t + 8:9 * t + 9], A.is_lt, ["#%d" % bk, "sc%d" % t] + MK[:3], [k])
                     if hi < C:
-                        act(T.dd[p, a:hi], T.ps[p, 512 * 3 + a - 128:512 * 3 + hi - 128], ["#3", "sc%d" % t], ["sg%d" % t, "junk2"], AF.Sign,
+                        d = T.dd[p, 192 * t:192 * t + hi - a]
+                        act(d, T.ps[p, 512 * 3 + a - 128:512 * 3 + hi - 128], ["#3", "sc%d" % t], ["sg%d" % t], AF.Sign,
                             bias=T.sc[p, 9 * t + 8:9 * t + 9], scale=-1.0)
-                        act(o, T.dd[p, a:hi], ["sg%d" % t, "junk2"] + MK[:3], [k, "acc%d" % t], AF.Relu, 0.02, accum_out=T.acc[p, t:t + 1])
-                        lin(T.th2[p, t:t + 1], T.acc[p, t:t + 1], 1.0 / 128, bias, ["acc%d" % t, "thr"], ["th2%d" % t])
-                        bias = T.th2[p, t:t + 1]
+                        act(o, d, ["sg%d" % t] + MK[:3], [k, "acc%d" % t], AF.Relu, 0.02, accum_out=T.acc[p, t:t + 1])
                     else:
-                        act(T.dd[p, lo:hi], o, [k, "th2%d" % t, "thr"], ["bnd%d" % t, "junk6"], AF.Identity, 0.02, bias=bias, accum_out=T.acc[p, 4 + t:5 + t])
-        SC = ["sc0", "sc1", "sc2", "sc3"]
-        mv(T.sc[:, 36:72], T.sc[:, 0:36], SC, ["scn"], -1.0)
+                        act(T.dd[p, 256 + 128 * t:384 + 128 * t], o, [k, "thr"], ["bnd%d" % t], AF.Identity, 0.02, bias=bias, accum_out=T.acc[p, 4 + t:5 + t])
+        SC = ["sc0", "sc1", "sc2", "sc3", "scn", "sn3"]
+        mv(T.sc[:, 36:63], T.sc[:, 0:27], SC[0:3], ["scn"], -1.0)
+        mv(T.sc[:, 63:72], T.ps[:, 512 * 7:512 * 7 + 18:2], ["#7"], ["sn3"], -1.0)
         for bk, a, z in ROW:
             quant("m", a, z, T.mt, MK[:3] + [k for k in MK[3:] if k[-1] == str(bk)], ["m%d" % bk])
         for t in range(4):
-            mm(t, "m", B0[t], "kr", 24 - 8 * t, 128, ["m%d" % (2 if t < 3 else 6), "kr"])
-        scan(T.cmx[:, 1:73], T.sc[:, 0:72], T.k72[:, 80:152], -1e29, A.max, A.add, SC + ["scn", "k72d"], ["cmx"])
-        tt(T.rr[:, 0:72], T.sc[:, 0:72], T.cmx[:, 0:72], A.is_le, SC + ["scn", "cmx", "cmx0"], ["rr"])
+            mm(t, "m", B0[t], "kr", 6 - 2 * t, 144, ["m%d" % (2 if t < 3 else 6), "kr"])
+        scan(T.cmx[:, 1:73], T.sc[:, 0:72], T.k72[:, 80:152], -1e29, A.max, A.add, SC + ["k72d"], ["cmx"])
+        tt(T.rr[:, 0:72], T.sc[:, 0:72], T.cmx[:, 0:72], A.is_le, SC + ["cmx", "cmx0"], ["rr"])
         scan(T.cm2[:, 0:72], T.k72[:, 0:72], T.rr[:, 0:72], 0.0, A.add, A.mult, ["rr", "k72a"], ["cm2s"])
-        tt(T.cde[:, 0:4], T.cm2[:, 43:72:9], T.cm2[:, 7:36:9], A.subtract, ["cm2s"], ["cde"])
         for b in range(4):
             mm(6 + b % 2, "ef", 128 * b, t_, 0, C, ["ef%d" % b] + TA)
             o = 896 * (b // 2) + b % 2
@@ -463,38 +572,36 @@ def rank_program(g, core, T, topo):
                 mv(T.win[:, o:o + 112], T.fh[:, 896 * k + 112 * (7 - q):896 * k + 112 * (8 - q)], ft, ["fg%d%d" % (k, q)], f=0.5, on=GC)
         for t in range(4):
             p = slice(64 * (t == 2), 128)
-            ts(T.flt[p, t:256:4], T.ps[p, 512 * t:512 * t + 64], T.acc[p, 4 + t:5 + t], A.is_gt, ["#%d" % t, "flw", "bnd%d" % t], ["fa%d" % t])
-            o, c = T.flt[p, 640 + t:1152:4], T.flt[p, 33 * t:33 * t + 1]
-            add({"V": (lambda o=o, c=c, p=p: V.tensor_scalar(o, T.kat[p, 0:128], c, None, A.mult), vc(96), 0),
-                 "S": (lambda o=o, c=c, p=p: S.activation(o, T.kat[p, 0:128], AF.Identity, bias=c, scale=0.0), vc(128), 0)}, ["fa%d" % t, "kat0"], ["fb%d" % t])
-        quant("fl", 0, 128, T.flt, ["fa%d" % t for t in range(4)], ["fl0"])
-        quant("fl", 160, 288, T.flt, ["fb%d" % t for t in range(4)], ["fl1"])
+            o, c = T.flt[p, t:576:4], T.ps[p, 512 * t:512 * t + 144]
+            if t < 2:
+                ts(o, c, T.acc[p, t:t + 1], A.subtract, ["#%d" % t, "bnd%d" % t, "acc%d" % t], ["fa%d" % t], T.acc[p, 4 + t:5 + t], A.is_gt)
+            else:
+                ts(o, c, T.acc[p, 4 + t:5 + t], A.is_gt, ["#%d" % t, "bnd%d" % t], ["fa%d" % t])
+        quant("fl", 0, 144, T.flt, ["fa%d" % t for t in range(4)], ["fl0"])
         mm(5, "ka", 128, "fl", 0, 128, ["fl0", "ka1"], True, False)
-        mm(5, "ka", 0, "fl", 32, 128, ["fl0", "flw", "ka0"], False, True)
-        mm(4, "ka", 256, "fl", 0, 128, ["fl0", "ka1"])
-        tt(T.eq[:], ps(4, 0, 32), T.kd[:, 0:32], A.is_equal, ["#4", "kd"], ["eq"], 1.0)
-        scan(T.wv[:], T.kd[:, 32:64], T.eq[:], 0.0, A.mult, A.add, ["eq", "kdr"], ["wv"])
+        mm(5, "ka", 0, "fl", 8, 128, ["fl0", "ka0"], False, True)
         for t in range(4):
-            ts(T.sot[:, t:512:4], T.ioh[:], T.cde[:, t:t + 1], A.is_equal, ["io0", "io1", "io2", "io3", "cde", "wv"], ["so%d" % t], T.wv[:, 8 * t + 7:8 * t + 8], A.mult, 0.5)
+            p = slice(64 * (t == 2), 128)
+            ts(T.sot[p, t:512:4], T.ioh[p, :], T.cm2[p, 9 * t + 7:9 * t + 8], A.add, ["io0", "io1", "io2", "io3", "cm2s"], ["so%d" % t],
+               T.cm2[p, 9 * t + 43:9 * t + 44], A.is_equal, 0.5)
         quant("so", 0, 128, T.sot, ["so%d" % t for t in range(4)], ["so"])
-        mm(0, "fl", 160, "kb", 128, 128, ["fl1", "kb"])
-        mm(2, "so", 0, "kb", 0, 128, ["so", "kb"])
-        for z, none in ((1, 255.0), (0, BIG)):
-            c = slice(64 * z, 64 * z + 64)
-            act(T.ln[:, c], ps(2, c.start, c.stop), ["#2", "kdr"], ["ln%d" % z], AF.Ln, bias=2.0 ** -62, scale=math.exp(-0.2))
-            act(T.nb[:, c], ps(2, c.start, c.stop), ["#2"], ["nb%d" % z], AF.Identity, bias=none, scale=-2.0 ** 30)
-            tt(T.lev[:, c], ps(0, c.start, c.stop), T.ln[:, c], A.subtract, ["#0", "ln%d" % z], ["lev%d" % z], 1.0)
-            tt(T.cand[:, c], T.lev[:, c], T.nb[:, c], A.max, ["lev%d" % z, "nb%d" % z], ["cand%d" % z])
+        mm(4, "so", 0, "ef", 0, 512, ["so"] + ["ef%d" % b for b in range(4)], True, False)
+        mm(4, "fl", 16, "kb", 0, 512, ["fl0", "kba", "kbb"], False, True)
+        scan(T.ln[:], T.k8[:], ps(4, 0, 512), 0.0, A.mult, A.max, ["#4", "k8"], ["ln"])
+        for z in (1, 0):
+            o, c = T.cand[:, 64 * z:64 * z + 64], T.ln[:].indirect(T.cl[:, 4 * z:4 * z + 4])
+            add({"V": (lambda o=o, c=c: V.tensor_scalar(o, c, 256.0, None, A.mult), 0.05 + 100 * CY, 0),
+                 "S": (lambda o=o, c=c: S.activation(o, c, AF.Copy, scale=256.0), 0.065 + 100 * CY, 0)}, ["ln", "cl"], ["cand%d" % z])
             for y in range(2):
-                a, n = 64 * z + 32 * y, 32 - 8 * y
-                tt(T.sm[64 * y:64 * y + 64, 32 * z:32 * z + n], T.cand[0:64, a:a + n], T.cand[64:128, a + 8:a + 8 + n], A.min, ["cand%d" % z],
-                   ["sm%d%d" % (z, y)], alone=True)
+                mv(T.cb[64 * y:64 * y + 64, 32 * z:32 * z + 32], T.cand[64 - 64 * y:128 - 64 * y, 64 * z + 32:64 * z + 64], ["cand%d" % z], ["cb%d%d" % (z, y)])
+            tt(T.sm[:, 32 * z:32 * z + 32], T.cand[:, 64 * z:64 * z + 32], T.cb[:, 32 * z:32 * z + 32], A.max, ["cand%d" % z, "cb%d0" % z, "cb%d1" % z],
+               ["sm%d0" % z, "sm%d1" % z])
         scan(T.pkf[:], T.kpk[:], T.sm[:, 32:64], 0.0, A.mult, A.add, ["sm10", "sm11", "kpk0", "kpk1"], ["pkf"])
         cp(T["pk%d" % r][:], T.pkf[:, 1:32:2], ["pkf"], ["pk%d" % r])
         send(T["lst%d" % r][:], T["pk%d" % r][:], "al%d" % r, 1, ["pk%d" % r], ["lst%d" % r], 2.0)
         for t in range(4):
             p, a = slice(64 * (t == 2), 128), 64 * (t == 3)
-            ts(T.cmt[p, 4 * a + t:4 * NF:4], T.ios[p, a:NF], T.ps[p, 2560 + 8 * t:2561 + 8 * t], A.is_ge, ["#5", "ios"], ["cm%d" % t], f=0.5)
+            ts(T.cmt[p, 4 * a + t:4 * NF:4], T.ios[p, a:NF], T.ps[p, 2560 + 2 * t:2561 + 2 * t], A.is_ge, ["#5", "ios"], ["cm%d" % t], f=0.5)
         quant("cm", 0, NF, T.cmt, ["cm%d" % t for t in range(4)], ["cm"])
         mm(1, "ka", 0, "cm", 0, NF, ["cm", "ka0"])
         scan(T.lrow[:], T.k16[:], ps(1, 0, NF), 0.0, A.add, A.min, ["#1", "k16"], ["lrow"])
@@ -513,21 +620,26 @@ def rank_program(g, core, T, topo):
                 mm(bk, "eb", 128 * k, src, a0, z0 - a0, [src + "c", src + "s", "eb%dc" % (k // 2), "eb%ds" % (k // 2)])
                 mv(T.win[:, o + a:o + z], ps(bk, a - a0, z - a0), ["#%d" % bk], ["%s%d" % (key, k)], SC64, on=on)
         unpack(sl, 0, "wo", (3, 4, 5), "SV")
-        scan(T.kos[:, 31::-1], T.kst[:, 0:32], T.sm[:, 31::-1], 0.0, A.add, A.min, ["sm00", "sm01", "kst"], ["kos"])
-        tt(T.own[:], T.kos[:], T.idc[:], A.min, ["kos", "idc"], ["own"])
+        ts(T.eq[:], T.sm[:, 0:32], 0.0, A.is_gt, ["sm00", "sm01"], ["eq"], BIG + NF, A.mult)
+        tt(T.eq[:], T.eq[:], T.sm[:, 0:32], A.add, ["eq", "sm00", "sm01"], ["eq"])
+        scan(T.kos[:, 31::-1], T.kst[:, 0:32], T.eq[:, 31::-1], 0.0, A.add, A.max, ["eq", "kst"], ["kos"])
+        tt(T.own[:], T.kos[:], T.idc[:], A.max, ["kos", "idc"], ["own"])
         unpack(ld, WA, "wa", (6, 7, 1, 2, 0), "SV")
         cp(T.ai[:], T["lst%d" % r][:], ["lst%d" % r], ["ai"])
         ts(T.a2[:, 0:32:2], T.ai[:], 8, A.arith_shift_right, ["ai"], ["a2h"])
         ts(T.a2[:, 1:32:2], T.ai[:], 255, A.bitwise_and, ["ai"], ["a2l"])
-        ts(T.kn[:], T.a2[:], float(NF), A.is_ge, ["a2h", "a2l"], ["kn"], BIG, A.mult)
+        ts(T.kn[:], T.a2[:], 0.0, A.is_gt, ["a2h", "a2l"], ["kn"], BIG, A.mult)
         tt(T.kn[:], T.kn[:], T.a2[:], A.add, ["kn", "a2h", "a2l"], ["kn"])
-        scan(T.kns[:], T.kst[:, 32:64], T.kn[:], 0.0, A.add, A.min, ["kn", "kst"], ["kns"])
-        for k in range(2):
-            tt(T.rep[0:64, 32 * k:32 * k + 32], T.kns[64 * k:64 * k + 64, :], T.own[64 * k:64 * k + 64, :], A.min, ["kns", "own"], ["rep%d" % k])
-        for k in range(2):
-            mv(T.rep[32 * k:32 * k + 32, 64:128], T.rep[32 - 32 * k:64 - 32 * k, 0:64], ["rep0", "rep1"], ["rp%d" % k])
-        mv(T.rep[64:128, :], T.rep[0:64, :], ["rep0", "rep1", "rp0", "rp1"], ["rp2"])
-        ts(T.off[:], T.rep[:, 0:128].indirect(T.ordr[:, 0:8]), float(WA), A.add, ["rep0", "rep1", "rp0", "rp1", "rp2", "ordr"], ["off"], f=2.0)
+        scan(T.kns[:], T.kst[:, 32:64], T.kn[:], 0.0, A.add, A.max, ["kn", "kst"], ["kns"])
+        for k in range(4 if REP2 else 2):
+            y, o = 64 * (k % 2), 64 * (k // 2)
+            tt(T.rep[o:o + 64, y // 2:y // 2 + 32], T.kns[y:y + 64, :], T.own[y:y + 64, :], A.max, ["kns", "own"], ["rep%d" % k])
+        for k in range(4 if REP2 else 2):
+            mv(T.rep[32 * k:32 * k + 32, 64:128], T.rep[32 - 32 * (k % 2):64 - 32 * (k % 2), 0:64], ["rep0", "rep1"], ["rp%d" % k])
+        if not REP2:
+            mv(T.rep[64:128, :], T.rep[0:64, :], ["rep0", "rep1", "rp0", "rp1"], ["rp2", "rp3", "rep2", "rep3"])
+        ts(T.off[:], T.rep[:, 0:128].indirect(T.ordr[:, 0:8]), -1.0, A.mult, ["%s%d" % (s, k) for s in ("rep", "rp") for k in range(4)] + ["ordr"], ["off"],
+           float(TOP), A.add, f=2.0)
         WIN = ["ft%d" % b for b in range(4)] + ["wo%d" % k for k in range(8)] + ["fg%d%d" % (k, q) for k in range(2) for q in range(NH)] + ["off"]
         for i, (a, z) in enumerate(GAT):
             n = NH if a >= C - 56 * NH else 8
@@ -553,6 +665,7 @@ def rank_program(g, core, T, topo):
                 tt(T.xs[:, c], ps(bk, 0, z - a), T.y1[:, c], A.add, ["#%d" % bk, "y1%d%d" % (b % YP, h)], ["xs%d%d" % (b, h)], 1.0)
             quant_x(r + 1, T.xs, h, ["xs%d%d" % (b, h) for b in range(4)])
 
+    STEP[0], STEP[2] = (len(ops) - STEP[1]) // R, len(ops)
     t_ = "t%d" % R
     for h in range(H):
         a, z = CUTS[h], CUTS[h + 1]

@@ -3,19 +3,29 @@ from concourse.mybir import dt, AluOpType as A, ActivationFunctionType as AF
 
 C, NF, R = 448, 192, 3
 BIG = 8192.0
-CUTS = (0, 320, 448)
+CUTS = (0, 128, 288, 448)
 B0 = (0, 128, 192, 320)
-B1 = (0, 128, 256, 320, 448)
-WA, WS, NH = 8 * NF, NF + 224, 3
-WF = WA + 7 * WS + NF
+B1 = B0 + (C,)
+HALF = (slice(0, 128), slice(0, 64), slice(0, 128), slice(0, 128))
+MQ = ((128, 448), (0, 128))
+FA = "VS"
+OFF = ((32, 64), (64, 128), (0, 32))
+ZP, ZT = (), 2.2
+QUIET = True
+MF = 1
+BK = {"c3": 4, "r3": 5, "c2": 7, "c1": 6, "r1": 0, "s1": 1, "c0": 2, "d0": 3, "r0": 4, "k3": 1, "k2": 7, "k1": 6, "k0": 5,
+      "p": 0, "c": 4, "l": 1, "f": (2, 3), "o": (5, 6, 7), "a": (2, 3, 0, 1, 4), "w": (0, 1, 2, 3, 4, 5, 6, 7)}
+WA, WS, NH = 9 * NF, NF + 224, 3
+WF = WA + 8 * WS + NF
 KEY = 194
-TOP = WA + KEY + int(BIG)
+TOP = WA + KEY - WS
+NC = 480
+OWN = float(2 * NF - WS)
 FW = 2 * C - 112 * NH
-FD = "Y"
-UPS = ((0, 3), (3, 4))
-REP2 = True
+MN = True
+UPS = ((3, 4), (1, 3))
 YP = 2
-GAT = ((288, 448), (0, 288))
+GAT = ((288, 448), (128, 288), (0, 128))
 GC = "VSG"
 Q4, U8, BF, F32, I32, U16 = "float8_e4m3fn_x4", "uint8", "bfloat16", "float32", "int32", "uint16"
 SCRATCH = {}
@@ -35,32 +45,32 @@ for _r in range(R + 1):
 for _r in range(R):
     _q("slot%d" % _r, NF)
     _q("land%d" % _r, NF)
-    _sb("pk%d" % _r, 16, U16)
-    _sb("lst%d" % _r, 16, U16)
-for _n, _w in (("qu", 128), ("qup", 144), ("qv", 128), ("qw", 512), ("ef", 512), ("eb", 1024), ("ka", 256),
-               ("kb", 512), ("kr", 216), ("m", C), ("fl", 192), ("cm", NF), ("so", 128), ("qy", C)):
+    _sb("pk%d" % _r, 15, U16)
+    _sb("lst%d" % _r, 15, U16)
+for _n, _w in (("qu", 128), ("qup", 144), ("qv", 128), ("qw", 512), ("ef", 1024), ("ka", 128),
+               ("kb", NC), ("pm", NC), ("kr", 216), ("m", C), ("fl", 192), ("cm", NF), ("so", 128), ("qy", C)):
     _q(_n, _w)
-for _n, _w in (("xin", 4 * C), ("xs", 4 * C), ("ut", 512), ("vt", 512), ("eft", 2048), ("kat", 1024), ("kbt", 2048), ("mt", 4 * C),
-               ("flt", 768), ("cmt", 4 * NF), ("sot", 512), ("krt", 864), ("ios", NF), ("k16", NF), ("ioh", 128), ("k8", 512),
-               ("win", WF + 2 * FW), ("yt", 4 * C), ("fh", 4 * C), ("yy", 4 * C), ("y1", 4 * C), ("nar", 384), ("ctri", 128), ("tj", 128)):
+for _n, _w in (("xin", 4 * C), ("xs", 4 * C), ("ut", 512), ("vt", 512), ("eft", 4096), ("kat", 512), ("trt", 512), ("kbt", 4 * NC), ("pmt", 4 * NC),
+               ("dw", 128 + C), ("mt", 4 * C), ("flt", 768), ("cmt", 4 * NF), ("sot", 512), ("krt", 864), ("ios", NF), ("k16", NF), ("ioh", 128), ("k8", NC),
+               ("win", WF + 2 * FW), ("yt", 4 * C), ("fh", 4 * C), ("yy", 4 * C), ("y1", 4 * C), ("nar", 384), ("ctri", 128), ("tj", 128), ("cm2", 80), ("pc", 4), ("zz", 1600)):
     _sb(_n, _w, BF)
-for _n, _w in (("sc", 80), ("cmx", 80), ("cm2", 80), ("rr", 80), ("k72", 160), ("thr", 4), ("dd", 640), ("ebi", 8), ("cv", 32),
-               ("eq", 32), ("lrow", NF), ("ln", 512), ("cand", 128), ("cb", 64), ("sm", 64), ("kpk", 32),
-               ("pkf", 32), ("kos", 32), ("own", 32), ("kn", 32), ("kns", 32), ("rep", 128), ("df", C), ("up", 4), ("kst", 64), ("idc", 32),
+for _n, _w in (("sc", 80), ("cmx", 80), ("rr", 80), ("k72", 160), ("thr", 4), ("dd", 640), ("ebi", 8), ("cv", 32),
+               ("eq", 64), ("eo", 64), ("lrow", NF), ("ln", NC), ("sm", 64), ("kpk", 32), ("ke", 64), ("idn", 72),
+               ("pkf", 32), ("kos", 64), ("own", 64), ("kn", 64), ("kns", 64), ("rep", 128), ("df", C), ("up", 4), ("kst", 128), ("idc", 72),
                ("w1", 32), ("w2", 16), ("pv", 8), ("yo", C), ("acc", 8)):
     _sb(_n, _w, F32)
-for _n, _w in (("ci", 32), ("ai", 16), ("a2", 32), ("pi", 8), ("wi", 8)):
+for _n, _w in (("ci", 32), ("ai", 30), ("a2", 60), ("pi", 8), ("wi", 8)):
     _sb(_n, _w, I32)
 for _n, _w in (("ul", 10), ("pl", 12), ("ordr", 8), ("cl", 8), ("off", 128), ("ebl", 16)):
     _sb(_n, _w, U16)
 SCRATCH["ps"] = ("psum", [128, 4096], F32)
-SEMAPHORES = ["V", "S", "P", "G", "dx0", "dx1", "du", "dv", "dwc", "dws", "outs", "sent", "dw", "dfh0", "dfh1"] + ["d%s%d" % (k, b) for k in "ef" for b in (1, 2, 3)] + ["dk%d" % k for k in range(7)] + \
+SEMAPHORES = ["V", "S", "P", "G", "dx0", "dx1", "dx2", "dz0", "dz1", "dz2", "dz3", "du", "dv", "dwc", "dws", "outs", "sent", "dw", "dg", "dfh0", "dfh1"] + ["de%d" % k for k in range(1, 8)] + \
              ["%s%d" % (k, r) for k in ("ac", "al") for r in range(R)]
 CY, OV, LAT, LATG, PE, RI, DL = 0.00085, 0.005, 0.2, 0.22, 0.0006, 0.4, -1.0
 MORE = {"S": 0.008, "G": 0.02}
 CASES = ((1.0, 0.005, 0.0, 0.0, 0.19, 0.23, 0.2, 0.0, -0.3, 1.0, 0.4, 0.0), (1.0, 0.0, 0.0, 0.0, 0.21, 0.21, 0.1, -0.3, 0.0, 0.85, 0.6, 0.0),
          (1.0, 0.015, 0.01, 0.03, 0.16, 0.19, 0.4, 0.5, -0.8, 1.2, 0.15, 0.015), (1.35, 0.005, 0.0, 0.0, 0.22, 0.25, 0.3, 0.5, 0.2, 1.4, 0.6, 0.0))
-TRIES, MOVES = 2500, 25000
+TRIES, MOVES, SEED, KINDS, HEAT = 400, 45000, 4321, 10, 0.03
 SPAN, PLAN, STEP = [0.0], [], [0, 0, 0]
 
 
@@ -105,6 +115,18 @@ def schedule(ops):
     if PLAN:
         return PLAN[0]
     n = len(ops)
+    anc, short = [0] * n, []
+    for i, o in enumerate(ops):
+        far = 0
+        for d, raw in o["deps"].items():
+            if raw:
+                far |= anc[d]
+        short.append(dict(o, deps={d: raw for d, raw in o["deps"].items() if not far >> d & 1}))
+        anc[i] = far
+        for d, raw in o["deps"].items():
+            if raw:
+                anc[i] |= 1 << d
+    ops = short
     succ = [{} for _ in range(n)]
     for i, o in enumerate(ops):
         for d, raw in o["deps"].items():
@@ -185,36 +207,62 @@ def polish(ops, deps, succ, cases, order, eng):
     twin = [[j for j in (i - STEP[0], i + STEP[0], i - 2 * STEP[0], i + 2 * STEP[0]) if STEP[1] <= i < STEP[2] and STEP[1] <= j < STEP[2]] for i in range(n)]
 
     def run(order, eng, first, old):
-        out, total = [], 0.0
+        last, p = {}, first - 1
+        while p >= 0 and len(last) < 5:
+            last.setdefault(eng[order[p]], order[p])
+            p -= 1
+        rest = []
+        for i in order[first:]:
+            e = eng[i]
+            rest.append((i, e, [d for d, raw in deps[i] if eng[d] != e], [d for d, raw in deps[i] if raw and eng[d] == e]))
+        out, total, was = [], 0.0, 0.0
         for c, (cost, lat, own, latg) in enumerate(cases):
-            done, hold, why = (list(x) for x in old[c]) if old else ([0.0] * n, [0.0] * n, [-1] * n)
-            free, last = {}, {}
-            p = first - 1
-            while p >= 0 and len(free) < 5:
-                i = order[p]
-                if eng[i] not in free:
-                    free[eng[i]], last[eng[i]] = hold[i], i
-                p -= 1
-            for p in range(first, n):
-                i = order[p]
-                e = eng[i]
-                t, by = free.get(e, 0.0), -2 - last.get(e, -1)
-                for d, raw in deps[i]:
-                    if eng[d] != e:
-                        u = done[d] + (latg if e == "G" else lat)
-                    elif raw:
-                        u = done[d] + (latg if e == "G" else own)
-                    else:
-                        continue
-                    if u > t:
-                        t, by = u, d
+            done, hold = (list(old[c][0]), list(old[c][1])) if old else ([0.0] * n, [0.0] * n)
+            free = {e: hold[last[e]] if e in last else 0.0 for e in "VSPGY"}
+            for i, e, far, near in rest:
+                t = free[e]
+                if far:
+                    x = latg if e == "G" else lat
+                    for d in far:
+                        if done[d] + x > t:
+                            t = done[d] + x
+                if near:
+                    x = latg if e == "G" else own
+                    for d in near:
+                        if done[d] + x > t:
+                            t = done[d] + x
                 k = cost[i][e]
-                free[e] = hold[i] = t + k[0]
-                done[i] = t + k[0] + k[1]
-                why[i], last[e] = by, i
-            total += max(done)
-            out.append((done, hold, why))
+                free[e] = hold[i] = t = t + k[0]
+                done[i] = t + k[1]
+            end = max(done)
+            total += end
+            out.append((done, hold, end))
+            if old:
+                was += old[c][2]
+                if total > was + 0.45:
+                    return 1e9, None
         return total / len(cases), out
+
+    def chain(order, eng, c, state):
+        cost, lat, own, latg = cases[c]
+        done, hold, end = state[c]
+        before, last = [-1] * n, {}
+        for i in order:
+            before[i] = last.get(eng[i], -1)
+            last[eng[i]] = i
+        i, pairs = done.index(end), []
+        while i >= 0:
+            e, j = eng[i], before[i]
+            t = hold[j] if j >= 0 else 0.0
+            for d, raw in deps[i]:
+                if raw or eng[d] != e:
+                    u = done[d] + (latg if e == "G" else own if eng[d] == e else lat)
+                    if u > t:
+                        t, j = u, -2 - d
+            if j >= 0:
+                pairs.append((i, j))
+            i = j if j > -2 else -2 - j
+        return pairs
 
     def ahead(order, i, j):
         a, b = order.index(j), order.index(i)
@@ -230,22 +278,60 @@ def polish(ops, deps, succ, cases, order, eng):
         gone = set(move)
         order[a:b + 1] = move[::-1] + [k for k in order[a:b + 1] if k not in gone]
         return a
+    def behind(order, j, i):
+        a, b = order.index(j), order.index(i)
+        if a >= b:
+            return None
+        after, move = set(succ[j]), [j]
+        for k in order[a + 1:b + 1]:
+            if k in after:
+                if k == i or len(move) > 6:
+                    return None
+                move.append(k)
+                after.update(succ[k])
+        gone = set(move)
+        order[a:b + 1] = [k for k in order[a:b + 1] if k not in gone] + move
+        return a
+
+    def alike(order, eng, a, b):
+        at, e2 = [0] * n, list(eng)
+        for p, i in enumerate(order):
+            at[i] = p
+        ra, rb = (range(STEP[1] + k * STEP[0], STEP[1] + (k + 1) * STEP[0]) for k in (a, b))
+        for p, i in zip(sorted(at[i] for i in rb), sorted(ra, key=lambda i: at[i])):
+            at[i + (b - a) * STEP[0]] = p
+            e2[i + (b - a) * STEP[0]] = eng[i]
+        for i in range(n):
+            for d, raw in deps[i]:
+                if at[i] <= at[d]:
+                    at[i] = at[d] + 1e-3
+        return sorted(range(n), key=lambda i: (at[i], i)), e2
     cur, state = run(order, eng, 0, None)
-    start, best, z = cur, (cur, list(order), list(eng)), 4321
+    start, best, z, known = cur, (cur, list(order), list(eng)), SEED, {}
     for it in range(MOVES):
+        if it % 1000 == 999:
+            for a, b in ((1, 2), (2, 1), (1, 0), (0, 1)):
+                o2, e2 = alike(order, eng, a, b)
+                got, s2 = run(o2, e2, 0, None)
+                if got < cur:
+                    cur, state, order, eng, known = got, s2, o2, e2, {}
+                    if got < best[0]:
+                        best = (got, list(order), list(eng))
         z = (z * 1103515245 + 12345) % 2147483648
-        done, hold, why = state[(z >> 8) % len(cases)]
-        i, pairs = done.index(max(done)), []
-        while why[i] != -1:
-            j = why[i] if why[i] >= 0 else -2 - why[i]
-            if why[i] < 0:
-                pairs.append((i, j))
-            i = j
+        c = (z >> 8) % len(cases)
+        if c not in known:
+            known[c] = chain(order, eng, c, state)
+        pairs = known[c]
         z = (z * 1103515245 + 12345) % 2147483648
         i, j = pairs[(z >> 8) % len(pairs)]
         z = (z * 1103515245 + 12345) % 2147483648
-        kind, every, o2, e2, first = (z >> 8) % 8, (z >> 12) % 4 > 0, list(order), list(eng), n
-        if kind < 5:
+        kind, every, o2, e2, first = (z >> 8) % KINDS, (z >> 12) % 4 > 0, list(order), list(eng), n
+        if kind > 7:
+            for k in [j] + (twin[j] if every else []):
+                if 0 <= i + k - j < n:
+                    a = behind(o2, k, i + k - j)
+                    first = first if a is None else min(first, a)
+        elif kind < 5:
             p = order.index(j)
             for _k in range((0, 0, 0, 1, 3)[kind]):
                 q = p - 1
@@ -267,8 +353,8 @@ def polish(ops, deps, succ, cases, order, eng):
         if first < n:
             got, s2 = run(o2, e2, first, state)
             z = (z * 1103515245 + 12345) % 2147483648
-            if got <= cur + 0.12 * (1 - it / MOVES) * ((z >> 8) % 1000) / 1000:
-                cur, state, order, eng = got, s2, o2, e2
+            if got <= cur + HEAT * (1 - it / MOVES) * ((z >> 8) % 1000) / 1000:
+                cur, state, order, eng, known = got, s2, o2, e2, {}
                 if got < best[0]:
                     best = (got, list(order), list(eng))
     return best[1], best[2], (start, best[0])
@@ -345,8 +431,8 @@ def rank_program(g, core, T, topo):
         if s and w(ap) <= 128:
             alts["S"] = (lambda: S.activation(ap, T.tj[0:ap.shape[0], 0:w(ap)], AF.Identity, bias=float(v), scale=0.0), vc(w(ap)), 0)
         elif s:
-            alts["S"] = (lambda: S.activation(ap, T.kat[0:ap.shape[0], 0:w(ap)], AF.Identity, bias=float(v), scale=0.0), vc(w(ap)), 0)
-        rd = [] if len(alts) == 1 else ["tj"] if w(ap) <= 128 else ["kat0"]
+            alts["S"] = (lambda: S.activation(ap, T.dw[0:ap.shape[0], 128:128 + w(ap)], AF.Identity, bias=float(v), scale=0.0), vc(w(ap)), 0)
+        rd = [] if len(alts) == 1 else ["tj"] if w(ap) <= 128 else ["dw0"]
         if s and ap.shape[0] == 128 and v == int(v) and abs(v) < 2 ** 20:
             alts["G"] = (lambda: g.iota(ap, [[0, w(ap)]], int(v), 0, allow_small_or_imprecise_dtypes=True), 0.13 + 2 * w(ap) * CY + OV, 0)
         add(alts, rd, wr)
@@ -380,118 +466,126 @@ def rank_program(g, core, T, topo):
         add({"S": (lambda: S.activation(T[dst + "s"][:, a:a + n], T[src + "s"][:, 0:wd].indirect(off), AF.Copy), 0.09 + 1.56 * n * CY, 0)},
             rd, [(key or dst) + "s"])
 
-    def dma(on, sem, out, in_, rd, wr, t=2.2):
+    def dma(on, sem, out, in_, rd, wr, t=2.2, hold=0.12):
         qs = {"Y": g.sync, "S": S}
-        add({e: (lambda e=e: qs[e].dma_start(out, in_), 0.12, t + DL) for e in on}, rd, wr, sem)
+        add({e: (lambda e=e: qs[e].dma_start(out, in_), hold, t + DL) for e in on}, rd, wr, sem)
 
     def send(out, in_, sem, n, rd, wr, t):
         add({"G": (lambda: g.remote_dma(out, in_, T.sem[sem], T.sem.sent, pid, rid, mask), RI, t - RI)}, rd, wr, None, (sem, n * neng))
 
     dma("Y", "du", T.ut[:], T.u[:], [], ["ut"], 2.5)
-    dma("Y", "dx0", T.xin[:, 0:4 * CUTS[1]], T.x[:, 0:4 * CUTS[1]], [], ["xin0"], 3.2)
-    dma("S", "dx1", T.xin[:, 4 * CUTS[1]:4 * C], T.x[:, 4 * CUTS[1]:4 * C], [], ["xin1"], 2.6)
-    dma("Y", "dwc", T.qwc[:].bitcast(dt.uint8), T.wc[:], ["xin0"], ["qwc"], 3.0)
-    dma("Y", "dws", T.qws[:], T.ws[:], ["xin0"], ["qws"])
-    dma("Y", "dv", T.vt[:], T.v[:], ["xin0"], ["vt"])
+    for h in range(len(CUTS) - 2, -1, -1):
+        dma("SY"[h % 2], "dx%d" % h, T.xin[:, 4 * CUTS[h]:4 * CUTS[h + 1]], T.x[:, 4 * CUTS[h]:4 * CUTS[h + 1]], [], ["xin%d" % h], 3.2 - 0.3 * h)
 
-    iota(T.pi[:, 0:1], [[0, 1]], 0, 1, ["pi0"], False)
+    iota(T.pi[:, 0:2], [[8, 2]], 0, 1, ["pi0"], False)
     iota(T.tj[:], [[1, 128]], 0, -1, ["tj"])
+    act(T.ctri[:], T.tj[:], ["tj"], ["ctri"], AF.Sigmoid, 1.5, bias=-128.0, scale=-256.0)
     iota(T.k72[:, 0:72], [[-15, 2], [0, 36]], 16, 0, ["k72a"])
     iota(T.ios[:], [[1, NF]], 0, 0, ["ios"])
     iota(T.k16[:], [[0, NF // 16], [1, 16]], 0, 0, ["k16"])
-    ms(T.kat[:, 0:512], 1.0, ["kat0"], 0.5, False)
-    for t, z in ((1, 128), (2, C), (3, 320)):
-        ms(T.mt[:, t:4 * z:4], 0.0, ["mtp%d" % t], 0.5)
+    ms(T.dw[:], -3.0 / 256, ["dw0", "dw"], 0.5, False)
+    ms(T.kat[:, 0:448], 1.0, ["kat0"], 0.5)
+    ms(T.kat[:, 448:512], 1.0, ["kat1"], 0.5)
+    for t, a in ((0, 128), (1, 0), (2, 320)):
+        ms(T.mt[:, 4 * a + t:4 * C:4], 0.0, ["mtp%d" % t], 0.5)
     ms(T.ul[:], 1, ["ul"], s=False)
-    for k, (n, o) in enumerate(((15, A.bitwise_and), (7, A.bitwise_and), (6, A.arith_shift_right), (32, A.bitwise_and), (79, A.bitwise_and))):
-        ts(T.pi[:, k + 1:k + 2], T.pi[:, 0:1], n, o, ["pi0"], ["pi%d" % (k + 1)])
-    cp(T.pv[:, 0:5], T.pi[:, 1:6], ["pi1", "pi2", "pi3", "pi4", "pi5"], ["pv"])
-    ts(T.k16[:], T.k16[:], T.pv[:, 0:1], A.is_equal, ["k16", "pv"], ["k16"], BIG, A.mult, 0.5)
-    ts(T.pi[:, 6:7], T.pi[:, 0:1], 14, A.bitwise_and, ["pi0"], ["pi6"])
-    ts(T.ul[:, 0:1], T.pi[:, 6:7], 8.0, A.mult, ["pi6"], ["ul"])
+    ts(T.pi[:, 2:4], T.pi[:, 0:2], 15, A.bitwise_and, ["pi0"], ["pi2"])
+    ts(T.pi[:, 4:5], T.pi[:, 0:1], 6, A.arith_shift_right, ["pi0"], ["pi4"])
+    ts(T.pi[:, 5:6], T.pi[:, 0:1], 32, A.bitwise_and, ["pi0"], ["pi5"])
+    ts(T.pi[:, 6:7], T.pi[:, 0:1], 16, A.bitwise_and, ["pi0"], ["pi6"])
+    cp(T.pv[:, 0:5], T.pi[:, 2:7], ["pi2", "pi4", "pi5", "pi6"], ["pv"])
+    ts(T.k16[:], T.k16[:], T.pv[:, 0:1], A.is_equal, ["k16", "pv"], ["k16"], BIG, A.mult)
+    ts(T.pi[:, 7:8], T.pi[:, 0:1], 14, A.bitwise_and, ["pi0"], ["pi7"])
+    ts(T.ul[:, 0:1], T.pi[:, 7:8], 8.0, A.mult, ["pi7"], ["ul"])
     quant("qu", 0, 128, T.ut, ["ut"], ["qu"])
     pick("qup", "qu", 144, 128, T.ul[:, 0:9], ["qu", "ul"])
-    quant("qv", 0, 128, T.vt, ["vt"], ["qv"])
     for t in range(4):
-        ts(T.kat[:, 512 + t:1024:4], T.tj[:], 0.0, A.is_ge, ["tj"], ["tri%d" % t], f=0.5)
-    quant("ka", 0, 256, T.kat, ["kat0"] + ["tri%d" % t for t in range(4)], ["ka0", "ka1"])
-    ms(T.flt[0:64, 2:576:4], 0.0, ["fa2"], 0.5)
-    ms(T.sot[0:64, 2:512:4], 0.0, ["so2"], 0.5)
-    ms(T.cmt[0:64, 2:4 * NF:4], 0.0, ["cm2"], 0.5)
+        add({"V": (lambda t=t: V.tensor_scalar(T.trt[:, t:512:4], T.tj[:], 0.0, None, A.is_ge), vc(64), 0),
+             "S": (lambda t=t: S.activation(T.trt[:, t:512:4], T.tj[:], AF.Sigmoid, bias=128.0, scale=256.0), vc(128), 0)}, ["tj", "ctri"], ["tri%d" % t])
+    quant("ka", 0, 128, T.trt, ["tri%d" % t for t in range(4)], ["ka1"])
+    ms(T.flt[64:128, 1:576:4], 0.0, ["fa1"], 0.5)
+    ms(T.sot[64:128, 1:512:4], 0.0, ["so1"], 0.5)
+    ms(T.cmt[64:128, 1:4 * NF:4], 0.0, ["cm1"], 0.5)
     ms(T.cmt[:, 3:256:4], 0.0, ["cm3"], 0.5)
-    ms(T.krt[:, 0:64], -256.0, ["kr0"], 0.5)
+    ms(T.krt[:, 0:64], 256.0, ["kr0"], 0.5)
     ms(T.krt[:, 24:32], 1.0, ["kr0"], 0.5)
     ms(T.krt[:, 64:332], 1.0, ["kr1"], 0.5)
     ms(T.krt[:, 332:600], 1.0, ["kr2"], 0.5)
     quant("kr", 0, 150, T.krt, ["kr0", "kr1", "kr2"], ["kr"])
-    ts(T.ctri[:], T.tj[:], 0.0, A.is_le, ["tj"], ["ctri"], f=0.5)
-    iota(T.acc[:, 4:8], [[192, 2], [128, 2]], 128 - NF, 0, ["bnd0", "bnd1", "bnd2", "bnd3"])
-    lin(T.thr[:], T.acc[:, 4:8], 1.0 / 128, 0.0, ["bnd0", "bnd1", "bnd2"], ["thr"])
     ms(T.k72[:, 80:152], 0.0, ["k72d"])
     ms(T.k72[:, 88:152:9], -1e29, ["k72d"])
     ms(T.cmx[:, 0:1], -1e29, ["cmx0"])
-    ms(T.k8[:], 1.0, ["k8"], 0.5)
-    ms(T.k8[:, 0:512:8], 0.0, ["k8"], 0.5)
-    asel(T.eft[:, 0:512], T.kat[:, 0:512], [[-256, 4], [-1, 32], [256, 4]], A.is_equal, 0.0, 0, 1, ["kat0"], ["eft0", "efu0"])
-    for b in range(4):
-        if b:
-            dma("Y", "de%d" % b, T.eft[32 * b:128, 512 * b:512 * b + 512], T.eft[0:128 - 32 * b, 0:512], ["eft0"], ["eft%d" % b], 2.2)
-            dma("Y", "df%d" % b, T.eft[0:32 * b, 512 * b:512 * b + 512], T.eft[128 - 32 * b:128, 0:512], ["eft0"], ["efu%d" % b], 2.2)
-        quant("ef", 128 * b, 128 * b + 128, T.eft, ["eft%d" % b, "efu%d" % b], ["ef%d" % b])
-    iota(T.ebi[:], [[16, 2], [32, 4]], 0, 0, ["ebi"])
-    for e in range(2):
-        ts(T.ebl[:, e:16:2], T.ebi[:], T.pv[:, 0:1], A.add, ["ebi", "pv"], ["ebl%d" % e])
-    for b in range(4):
-        add({"V": (lambda b=b: V.tensor_copy(T.ebc[:, 256 * b:256 * b + 256].bitcast(dt.uint32), T.efc[:, 128 * b:128 * b + 128].bitcast(dt.uint32).indirect(T.ebl[:])),
-                   0.08 + 400 * CY, 0)}, ["ef%d" % b, "ebl0", "ebl1"], ["eb%dc" % b])
-        add({"S": (lambda b=b: S.activation(T.ebs[:, 256 * b:256 * b + 256], T.efs[:, 128 * b:128 * b + 128].indirect(T.ebl[:]), AF.Copy), 0.09 + 400 * CY, 0)},
-            ["ef%d" % b, "ebl0", "ebl1"], ["eb%ds" % b])
+    if MN:
+        ms(T.cmx[:, 40:41], 1e29, ["cmx1"])
+    asel(T.eft[:, 0:512], T.kat[:, 0:512], [[-256, 4], [-1, 32], [256, 4]], A.is_equal, 0.0, 0, 1, ["kat0", "kat1"], ["eft0", "efu0"])
+    for k in (0, 2, 4, 6, 7, 5, 3, 1):
+        if k:
+            dma("Y", "de%d" % k, T.eft[16 * k:128, 512 * k:512 * k + 512], T.eft[0:128 - 16 * k, 0:512], ["eft0", "xin0"], ["eft%d" % k], 2.4, 0.2)
+            dma("Y", "de%d" % k, T.eft[0:16 * k, 512 * k:512 * k + 512], T.eft[128 - 16 * k:128, 0:512], ["eft0", "xin0"], ["efu%d" % k], 2.4, 0.2)
+        quant("ef", 128 * k, 128 * k + 128, T.eft, ["eft%d" % k, "efu%d" % k], ["ef%d" % k])
+    for y in range(2):
+        ms(T.kat[64 * y:64 * y + 64, 8 - 8 * y:NC:16], 0.0, ["kat0"], 0.5)
     iota(T.nar[:, 0:32], [[16, 2], [1, 8], [32, 2]], -105, 0, ["ioi"])
     for k in range(4):
-        ts(T.ioh[:, 32 * k:32 * k + 32], T.nar[:, 0:32], T.pv[:, 1:2], A.subtract, ["ioi", "pv"], ["io%d" % k], 64.0 * (k % 2) - 8 * (k // 2), A.add)
-    ms(T.kbt[:, 512:1024], -2.0 / 256, ["kb1"], 0.5)
-    asel(T.kbt[:, 512:1024], T.kbt[:, 512:1024], [[-256, 4], [-1, 32], [256, 4]], A.is_gt, -3.0 / 256, -32, 1, ["kb1"], ["kb1"])
-    asel(T.kbt[:, 512:1024], T.kbt[:, 512:1024], [[-256, 4], [-1, 32], [256, 4]], A.not_equal, 320.0 / 256, -32, 1, ["kb1"], ["kb1"])
-    for k, (q, o, a, n) in enumerate(((0, 0, 32, 96), (0, 96, 96, 32), (2, 32, 0, 96), (2, 0, 0, 32), (3, 64, 0, 64), (3, 0, 0, 32), (3, 32, 0, 32))):
-        dma("Y", "dk%d" % k, T.kbt[o:o + n, 512 * q:512 * q + 512], T.kbt[a:a + n, 512:1024], ["kb1"], ["kbd%d" % k], 2.2)
-    quant("kb", 0, 256, T.kbt, ["kb1", "kbd0", "kbd1"], ["kba"])
-    quant("kb", 256, 512, T.kbt, ["kbd%d" % k for k in range(2, 7)], ["kbb"])
-    lin(T.w2[:, 5:6], T.pv[:, 2:3], 8.0, T.pv[:, 0:1], ["pv"], ["w25"])
-    lin(T.w2[:, 6:7], T.pv[:, 1:2], -57.0, T.w2[:, 5:6], ["pv", "w25"], ["w26"])
-    iota(T.cv[:, 0:8], [[56, 2], [16, 4]], 336, 0, ["cv0"])
-    iota(T.cv[:, 8:16], [[0, 2], [-64, 2], [0, 2]], 32, 0, ["cv1"])
-    lin(T.cv[:, 8:16], T.cv[:, 8:16], T.pv[:, 2:3], T.w2[:, 6:7], ["cv1", "pv", "w26"], ["cv1"])
+        ts(T.ioh[:, 32 * k:32 * k + 32], T.nar[:, 0:32], T.pv[:, k // 2:k // 2 + 1], A.subtract, ["ioi", "pv"], ["io%d" % k], 64.0 * (k % 2), A.add)
+    asel(T.dw[:, 0:128], T.dw[:, 0:128], [[1, 128]], A.is_gt, -2.0 / 256, 0, -1, ["dw"], ["dw"])
+    asel(T.dw[:, 0:128], T.dw[:, 0:128], [[1, 128]], A.not_equal, 320.0 / 256, 0, -1, ["dw"], ["dw"])
+    for t in range(4):
+        a = 8 + B0[t]
+        ms(T.kbt[:, t:4 * a:4], -2.0 / 256, ["kb%d" % t], 0.5)
+        mv(T.kbt[:, 4 * a + t:4 * NC:4], T.dw[:, 0:NC - a], ["dw", "dw0"], ["kc%d" % t], f=0.5, on=GC)
+    KB = ["k%s%d" % (k, t) for k in "bc" for t in range(4)]
+    for k in range(2):
+        o, a = T.pmt[:, 2 * NC * k:2 * NC * (k + 1)], T.kbt[:, 2 * NC * k:2 * NC * (k + 1)]
+        add({"V": (lambda o=o, a=a: V.tensor_scalar(o, a, 0.0, None, A.is_gt), vc(2 * NC, 0.5), 0),
+             "S": (lambda o=o, a=a: S.activation(o, a, AF.Relu, scale=0.8), vc(2 * NC), 0)}, KB, ["pmt%d" % k])
+        quant("kb", NC // 2 * k, NC // 2 * (k + 1), T.kbt, KB, ["kb" + "ab"[k]])
+        quant("pm", NC // 2 * k, NC // 2 * (k + 1), T.pmt, ["pmt%d" % k], ["pm%d" % k])
+    iota(T.cv[:, 0:8], [[0, 2], [16, 4]], -4, 0, ["cv0"])
+    iota(T.cv[:, 8:16], [[-7, 2], [-112, 4]], 58, 0, ["cv1"])
+    ts(T.ci[:, 0:8], T.cv[:, 0:8], T.pv[:, 0:1], A.add, ["cv0", "pv"], ["ci0"], 1.0 / 9.0, A.mult)
+    lin(T.w2[:, 5:6], T.pv[:, 0:1], -7.0, 0.0, ["pv"], ["w25"])
+    ts(T.cv[:, 0:8], T.ci[:, 0:8], 64.0, A.mult, ["ci0", "w25"], ["cv0"], T.w2[:, 5:6], A.add)
     tt(T.cv[:, 0:8], T.cv[:, 0:8], T.cv[:, 8:16], A.add, ["cv0", "cv1"], ["cv0"])
-    for k, (n, o, v) in enumerate(((256.0, A.is_ge, 64.0), (448.0, A.is_ge, -256.0), (0.0, A.is_lt, 320.0))):
-        ts(T.cv[:, 8 * k + 8:8 * k + 16], T.cv[:, 0:8], n, o, ["cv0"], ["cv%d" % (k + 1)], v, A.mult)
-    tt(T.cv[:, 0:16], T.cv[:, 0:16], T.cv[:, 16:32], A.add, ["cv0", "cv1", "cv2", "cv3"], ["cv0", "cv1"])
-    tt(T.ci[:, 0:8], T.cv[:, 0:8], T.cv[:, 8:16], A.add, ["cv0", "cv1"], ["ci0"])
-    ts(T.ci[:, 8:16], T.ci[:, 0:8], 96, A.bitwise_and, ["ci0"], ["ci1"])
-    ts(T.ci[:, 16:24], T.ci[:, 0:8], 2, A.arith_shift_right, ["ci0"], ["ci2"], 96, A.bitwise_and)
-    ts(T.ci[:, 24:32], T.ci[:, 0:8], 31, A.bitwise_and, ["ci0"], ["ci3"])
-    ts(T.ci[:, 8:16], T.ci[:, 8:16], 4.0, A.mult, ["ci1"], ["ci1"], 7.0, A.add)
-    tt(T.ci[:, 16:24], T.ci[:, 16:24], T.ci[:, 24:32], A.add, ["ci2", "ci3"], ["ci2"])
+    ts(T.ci[:, 0:8], T.cv[:, 0:8], 0.0, A.max, ["cv0"], ["ci0"], 58.0, A.min)
+    ts(T.ci[:, 8:16], T.ci[:, 0:8], T.pv[:, 2:3], A.add, ["ci0", "pv"], ["ci1"])
+    ts(T.ci[:, 16:24], T.ci[:, 0:8], 1, A.arith_shift_right, ["ci0"], ["ci2"])
+    ts(T.ci[:, 8:16], T.ci[:, 8:16], 1, A.bitwise_and, ["ci1"], ["ci1"])
+    ts(T.ci[:, 8:16], T.ci[:, 8:16], 30.0, A.mult, ["ci1"], ["ci1"])
     tt(T.ci[:, 0:8], T.ci[:, 8:16], T.ci[:, 16:24], A.add, ["ci1", "ci2"], ["ci0"])
     cp(T.cl[:], T.ci[:, 0:8], ["ci0"], ["cl"])
     for k in range(2):
         ms(T.kpk[:, k:32:2], 256.0 * k, ["kpk%d" % k])
-        ms(T.kst[:, 32 * k:32 * k + 32], float(-WS if k else NF), ["kst%d" % k])
-    ms(T.kst[:, 0:64:8], -2 * BIG, ["kst0", "kst1", "kst"])
-    iota(T.idc[:], [[-16, 4], [112, 8]], TOP - 784 - WF, 0, ["idc"])
-    iota(T.kn[:], [[-16, 4], [-WS, 8]], TOP - WA - NF, 0, ["kn"])
-    ts(T.w2[:, 3:4], T.pv[:, 3:4], -FW / 32, A.mult, ["pv"], ["w23"], T.pv[:, 4:5], A.subtract)
-    ts(T.w2[:, 4:5], T.pv[:, 3:4], -3.5, A.mult, ["pv"], ["w24"], T.pv[:, 4:5], A.subtract)
+        ms(T.kst[:, 64 * k:64 * k + 64], float(-WS if k else NF), ["kst%d" % k])
+    ms(T.kst[:, 8:64:9], -2 * BIG, ["kst0"])
+    ms(T.kst[:, 64:128:9], -BIG, ["kst1"])
+    iota(T.idc[:], [[-16, 8], [112, 9]], TOP - 896 - WF, 0, ["idc"])
+    iota(T.idn[:], [[-16, 8], [-WS, 9]], TOP - WA - NF, 0, ["idn"])
+    lin(T.w2[:, 6:7], T.pv[:, 4:5], WS / 16, float(TOP), ["pv"], ["top"])
+    lin(T.w2[:, 7:8], T.pv[:, 4:5], (WS - NF) / 16, OWN, ["pv"], ["ow"])
+    ts(T.w2[:, 8:9], T.pv[:, 4:5], WS / 16, A.mult, ["pv"], ["w28"], T.pv[:, 0:1], A.subtract)
+    lin(T.w2[:, 3:4], T.pv[:, 3:4], -FW / 32, T.w2[:, 8:9], ["pv", "w28"], ["w23"])
+    lin(T.w2[:, 4:5], T.pv[:, 3:4], -3.5, T.w2[:, 8:9], ["pv", "w28"], ["w24"])
     lin(T.idc[:], T.idc[:], 1.0, T.w2[:, 3:4], ["idc", "w23"], ["idc"])
     for q in range(NH):
-        lin(T.idc[:, q:32:8], T.kn[:, q:32:8], 1.0, T.w2[:, 4:5], ["kn", "w24"], ["idc"])
-    dma("Y", "dw", T.win[:, WA + NH * WS + NF:WF], T.x[:, 0:WF - WA - NH * WS - NF], ["xin0"], ["wa%d" % k for k in range(7 - NH)])
+        lin(T.idc[:, q + 1:72:9], T.idn[:, q + 1:72:9], 1.0, T.w2[:, 4:5], ["idn", "w24"], ["idc"])
+    a = WA + (NH + 1) * WS + NF
+    dma("Y", "dw", T.win[:, a:WF], T.x[:, 0:WF - a], ["xin0"], ["wa%d" % k for k in range(NH + 2, 9)], 2.2, 1.3)
+    dma("Y", "dg", T.win[:, WA + NF:WA + WS], T.x[:, 0:WS - NF], ["xin0"], ["gap"], 2.2, 0.2)
+    late = ["eft%d" % k for k in range(1, 8)] + ["efu%d" % k for k in range(1, 8)]
+    dma("Y", "dwc", T.qwc[:].bitcast(dt.uint8), T.wc[:], late, ["qwc"], 2.2, 0.8)
+    dma("Y", "dws", T.qws[:], T.ws[:], late, ["qws"], 2.2, 0.2)
+    dma("Y", "dv", T.vt[:], T.v[:], late, ["vt"], 2.2, 0.4)
+    quant("qv", 0, 128, T.vt, ["vt"], ["qv"])
+    if QUIET:
+        add({"Y": (None, 0.0, 0.0)}, ["qwc", "qws", "vt", "gap", "wa8"], ["quiet"], "none")
     iota(T.w1[:, 0:8], [[0, 2], [16, 4]], -3, 0, ["w1a"])
-    iota(T.w1[:, 8:16], [[64, 2], [128, 4]], 7, 0, ["w1b"])
+    iota(T.w1[:, 8:16], [[64, 2], [144, 4]], 8, 0, ["w1b"])
     ts(T.wi[:], T.w1[:, 0:8], T.pv[:, 0:1], A.add, ["w1a", "pv"], ["wi"], 1.0 / 7.0, A.mult)
-    lin(T.w2[:, 0:1], T.pv[:, 0:1], 8.0, 0.0, ["pv"], ["w20"])
+    lin(T.w2[:, 0:1], T.pv[:, 0:1], 9.0, 0.0, ["pv"], ["w20"])
     for k in range(2):
         lin(T.w2[:, 1 + k:2 + k], T.pv[:, 3:4], 2.0 - 4 * k, T.w2[:, 0:1], ["pv", "w20"], ["w2%d" % (k + 1)])
-        ts(T.w1[:, 24 + 4 * k:28 + 4 * k], T.wi[:, 4 * k:4 * k + 4], -57.0, A.mult, ["wi", "w2%d" % (k + 1)], ["o%d" % k], T.w2[:, 1 + k:2 + k], A.add)
+        ts(T.w1[:, 24 + 4 * k:28 + 4 * k], T.wi[:, 4 * k:4 * k + 4], -64.0, A.mult, ["wi", "w2%d" % (k + 1)], ["o%d" % k], T.w2[:, 1 + k:2 + k], A.add)
     tt(T.w1[:, 24:32], T.w1[:, 24:32], T.w1[:, 8:16], A.add, ["o0", "o1", "w1b"], ["o2"])
     cp(T.ordr[:], T.w1[:, 24:32], ["o2"], ["ordr"])
 
@@ -502,7 +596,7 @@ def rank_program(g, core, T, topo):
         quant("t%d" % r, CUTS[h], CUTS[h + 1], tile, rd, ["t%d_%d" % (r, h)])
 
     for h in range(H):
-        quant_x(0, T.xin, h, ["xin%d" % min(h, 1)])
+        quant_x(0, T.xin, h, ["xin%d" % h])
 
     STEP[1] = len(ops)
     for r in range(R):
@@ -511,100 +605,107 @@ def rank_program(g, core, T, topo):
 
         def tk(a, b):
             return ["%s_%d" % (t_, h) for h in range(H) if CUTS[h] < b and a < CUTS[h + 1]]
-        for t, bk in enumerate((0, 1, 4, 5)):
-            mm(bk, t_, B0[t], "qup", 0, 128, tk(B0[t], B0[t] + 128) + ["qupc", "qups"])
+        QU = ["qupc", "qups"]
+        row = {3: (BK["r3"], 320), 2: (BK["r1"], 128), 1: (BK["r1"], 128), 0: (BK["r0"], 0)}
+        for t in (3, 2, 1, 0):
+            bk = BK["c%d" % t]
+            mm(bk, t_, B0[t], "qup", 0, 128, tk(B0[t], B0[t] + 128) + QU)
             mv(T.sc[:, 9 * t:9 * t + 9], T.ps[:, 512 * bk:512 * bk + 18:2], ["#%d" % bk], ["sc%d" % t])
-        mm(7, t_, B0[3], "qup", 0, 128, tk(B0[3], C) + ["qupc", "qups"])
+            if t != 2:
+                a, z = B1[t], B1[t + 1 + (t == 1)]
+                for k in ("r%d" % t, "s1")[:1 + (t == 1)]:
+                    mm(BK[k], "qup", 16, t_, a, z - a, tk(a, z) + QU)
+        bd = BK["d0"]
+        mm(bd, t_, 0, "qup", 0, 128, tk(0, 128) + QU)
         for a, z in UPS:
-            if a < 3:
-                act(T.up[:, a:z], T.sc[:, 9 * a + 8:9 * z:9], ["sc%d" % t for t in range(a, z)], ["up%d" % t for t in range(a, z)], AF.Abs,
-                    bias=2.0 ** -125, scale=0.6 * 2.0 ** -23)
-            else:
-                act(T.up[:, 3:4], ps(7, 16, 17), ["#7"], ["up3"], AF.Abs, bias=2.0 ** -125, scale=0.6 * 2.0 ** -23)
-        ROW = ((2, 0, 320), (6, 320, C))
-        for bk, a, z in ((2, 0, 320), (3, 128, 320), (6, 320, C)):
-            mm(bk, "qup", 16, t_, a, z - a, tk(a, z) + ["qupc", "qups"])
-        MK = ["mtp1", "mtp2", "mtp3"]
+            act(T.up[:, a:z], T.sc[:, 9 * a + 8:9 * z:9], ["sc%d" % t for t in range(a, z)], ["up%d" % t for t in range(a, z)], AF.Abs,
+                bias=2.0 ** -125, scale=0.6 * 2.0 ** -23)
         for t in range(4):
-            p, a, z = slice(64 * (t == 2), 128), B1[t], B1[t + 1]
-            bias = T.thr[p, t:t + 1]
-            bk = 2 if t < 3 else 6
-            act(T.df[p, a:z], T.ctri[p, p.start:128], ["ctri", "sc%d" % t, "up%d" % t], ["d%d" % t], AF.Identity,
-                bias=T.sc[p, 9 * t + 8:9 * t + 9], scale=T.up[p, t:t + 1])
-            MK.append("md%d%d" % (t, bk))
-            tt(T.mt[p, 4 * a + t:4 * z:4], T.ps[p, 512 * bk + a % 320:512 * bk + a % 320 + z - a], T.df[p, a:z], A.is_lt, ["#%d" % bk, "d%d" % t] + MK[:3], MK[-1:], 1.0)
-            a = z
-            for bk, lo, hi in ROW:
-                if max(lo, a) < hi:
-                    k, o = "mu%d%d" % (t, bk), T.mt[p, 4 * max(lo, a) + t:4 * hi:4]
-                    MK.append(k)
-                    if hi == C:
-                        ts(o, T.ps[p, 512 * bk:512 * bk + hi - lo], T.sc[p, 9 * t + 8:9 * t + 9], A.is_lt, ["#%d" % bk, "sc%d" % t] + MK[:3], [k])
-                    if hi < C:
-                        d = T.dd[p, 192 * t:192 * t + hi - a]
-                        act(d, T.ps[p, 512 * 3 + a - 128:512 * 3 + hi - 128], ["#3", "sc%d" % t], ["sg%d" % t], AF.Sign,
-                            bias=T.sc[p, 9 * t + 8:9 * t + 9], scale=-1.0)
-                        act(o, d, ["sg%d" % t] + MK[:3], [k, "acc%d" % t], AF.Relu, 0.02, accum_out=T.acc[p, t:t + 1])
-                    else:
-                        act(T.dd[p, 256 + 128 * t:384 + 128 * t], o, [k, "thr"], ["bnd%d" % t], AF.Identity, 0.02, bias=bias, accum_out=T.acc[p, 4 + t:5 + t])
-        SC = ["sc0", "sc1", "sc2", "sc3", "scn", "sn3"]
-        mv(T.sc[:, 36:63], T.sc[:, 0:27], SC[0:3], ["scn"], -1.0)
-        mv(T.sc[:, 63:72], T.ps[:, 512 * 7:512 * 7 + 18:2], ["#7"], ["sn3"], -1.0)
-        for bk, a, z in ROW:
-            quant("m", a, z, T.mt, MK[:3] + [k for k in MK[3:] if k[-1] == str(bk)], ["m%d" % bk])
-        for t in range(4):
-            mm(t, "m", B0[t], "kr", 6 - 2 * t, 144, ["m%d" % (2 if t < 3 else 6), "kr"])
-        scan(T.cmx[:, 1:73], T.sc[:, 0:72], T.k72[:, 80:152], -1e29, A.max, A.add, SC + ["k72d"], ["cmx"])
-        tt(T.rr[:, 0:72], T.sc[:, 0:72], T.cmx[:, 0:72], A.is_le, SC + ["cmx", "cmx0"], ["rr"])
-        scan(T.cm2[:, 0:72], T.k72[:, 0:72], T.rr[:, 0:72], 0.0, A.add, A.mult, ["rr", "k72a"], ["cm2s"])
+            if not any(a <= t < z for a, z in UPS):
+                bk = BK["c%d" % t] if t else bd
+                act(T.up[:, t:t + 1], ps(bk, 16, 17), ["#%d" % bk], ["up%d" % t], AF.Abs, bias=2.0 ** -125, scale=0.6 * 2.0 ** -23)
+        MK = ["mtp0", "mtp1", "mtp2"]
+        for t in (3, 2, 1, 0):
+            p, a, z = HALF[t], B1[t], B1[t + 1]
+            s = T.sc[p, 9 * t + 8:9 * t + 9]
+            bk, o = row[t]
+            lin(T.df[p, a:z], T.ctri[p, 0:z - a], T.up[p, t:t + 1], s, ["ctri", "sc%d" % t, "up%d" % t], ["d%d" % t])
+            tt(T.mt[p, 4 * a + t:4 * z:4], T.ps[p, 512 * bk + a - o:512 * bk + z - o], T.df[p, a:z], A.is_ge, ["#%d" % bk, "d%d" % t] + MK, ["md%d" % t], 1.0)
+            if t > 1:
+                d = T.dd[:, 64 * t - 128:64 * t + a - 256]
+                act(d, ps(BK["s1"], 0, a - 128), ["#%d" % BK["s1"], "sc%d" % t], ["sg%d" % t], AF.Sign, bias=s, scale=-1.0)
+                act(T.mt[:, 512 + t:4 * a:4], d, ["sg%d" % t] + MK, ["mv%d" % t, "acc%d" % t], AF.Relu, 0.02, scale=-1.0, accum_out=T.acc[:, t:t + 1])
+                lin(T.thr[:, t:t + 1], T.acc[:, t:t + 1], 2.0, 2.0 * (NF - a) + 1, ["acc%d" % t], ["thr%d" % t])
+            if t:
+                o = T.mt[p, t:512:4]
+                ts(o, T.ps[p, 512 * BK["r0"]:512 * BK["r0"] + 128], s, A.is_gt, ["#%d" % BK["r0"], "sc%d" % t] + MK, ["mu%d" % t])
+                act(T.dd[p, 128 + 128 * t:256 + 128 * t], o, ["mu%d" % t] + ["thr%d" % t] * (t > 1), ["bnd%d" % t], AF.Identity, 0.02, scale=256.0,
+                    bias=T.thr[p, t:t + 1] if t > 1 else 2.0 * (NF - a) + 1, accum_out=T.acc[p, 4 + t:5 + t])
+        SC = ["sc0", "sc1", "sc2", "sc3", "scn", "sn0"]
+        if not MN:
+            mv(T.sc[:, 45:72], T.sc[:, 9:36], SC[1:4], ["scn"], -1.0)
+            mv(T.sc[:, 36:45], T.ps[:, 512 * bd:512 * bd + 18:2], ["#%d" % bd], ["sn0"], -1.0)
+        for a, z in MQ:
+            quant("m", a, z, T.mt, MK + (["md0", "mu1", "mu2", "mu3"] if a == 0 else ["md1", "md2", "mv2", "mv3"] * (a < 320) + ["md3"] * (z > 320)), ["m%d" % a])
+        for t in (3, 2, 1, 0):
+            mm(BK["k%d" % t], "m", B0[t], "kr", 6 - 2 * t, 144, ["m%d" % a for a, z in MQ if a <= B0[t] < z] + ["kr"])
+        if MN:
+            scan(T.cmx[:, 1:37], T.sc[:, 0:36], T.k72[:, 80:116], -1e29, A.max, A.add, SC[0:4] + ["k72d"], ["cmx"])
+            scan(T.cmx[:, 41:77], T.sc[:, 0:36], T.k72[:, 80:116], 1e29, A.min, A.subtract, SC[0:4] + ["k72d"], ["cmn"])
+            tt(T.rr[:, 0:36], T.sc[:, 0:36], T.cmx[:, 0:36], A.is_le, SC[0:4] + ["cmx", "cmx0"], ["rr"])
+            tt(T.rr[:, 36:72], T.sc[:, 0:36], T.cmx[:, 40:76], A.is_ge, SC[0:4] + ["cmn", "cmx1"], ["rn"])
+        else:
+            scan(T.cmx[:, 1:73], T.sc[:, 0:72], T.k72[:, 80:152], -1e29, A.max, A.add, SC + ["k72d"], ["cmx"])
+            tt(T.rr[:, 0:72], T.sc[:, 0:72], T.cmx[:, 0:72], A.is_le, SC + ["cmx", "cmx0"], ["rr"])
+        scan(T.cm2[:, 0:72], T.k72[:, 0:72], T.rr[:, 0:72], 0.0, A.add, A.mult, ["rr", "k72a"] + ["rn"] * MN, ["cm2s"])
         for b in range(4):
-            mm(6 + b % 2, "ef", 128 * b, t_, 0, C, ["ef%d" % b] + TA)
-            o = 896 * (b // 2) + b % 2
-            mv(T.fh[:, o:896 * (b // 2 + 1):2], ps(6 + b % 2, 0, C), ["#%d" % (6 + b % 2)], ["ft%d" % b], SC64, on="SV")
+            bk = BK["f"][b % len(BK["f"])]
+            mm(bk, "ef", 256 * b, t_, 0, C, ["ef%d" % (2 * b)] + TA)
+            o = 896 * (b // 2)
+            mv(T.fh[:, o + b % 2:o + 896:2], ps(bk, 0, C), ["#%d" % bk], ["ft%d" % b], SC64, on="SV")
         for k in range(2):
             ft = ["ft%d" % (2 * k), "ft%d" % (2 * k + 1)]
-            if FD:
-                dma(FD, "dfh%d" % k, T.win[:, WF + FW * k:WF + FW * k + FW], T.fh[:, 896 * k:896 * k + FW], ft, ["fh%d" % k], 2.5)
-            else:
-                mv(T.win[:, WF + FW * k:WF + FW * k + FW], T.fh[:, 896 * k:896 * k + FW], ft, ["fh%d" % k], f=0.5, on=GC)
+            for q in range(2):
+                o = FW // 2 * q
+                mv(T.win[:, WF + FW * k + o:WF + FW * k + o + FW // 2], T.fh[:, 896 * k + o:896 * k + o + FW // 2], ft, ["fh%d%d" % (k, q)], f=0.5, on=GC)
             for q in range(NH):
-                o = WA + WS * q + NF + 112 * k
-                mv(T.win[:, o:o + 112], T.fh[:, 896 * k + 112 * (7 - q):896 * k + 112 * (8 - q)], ft, ["fg%d%d" % (k, q)], f=0.5, on=GC)
+                o, c = WA + WS * (q + 1) + NF + 112 * k, 896 * k + 112 * (7 - q)
+                mv(T.win[:, o:o + 112], T.fh[:, c:c + 112], ft, ["fg%d%d" % (k, q)], f=0.5, on=GC)
         for t in range(4):
-            p = slice(64 * (t == 2), 128)
-            o, c = T.flt[p, t:576:4], T.ps[p, 512 * t:512 * t + 144]
-            if t < 2:
-                ts(o, c, T.acc[p, t:t + 1], A.subtract, ["#%d" % t, "bnd%d" % t, "acc%d" % t], ["fa%d" % t], T.acc[p, 4 + t:5 + t], A.is_gt)
-            else:
-                ts(o, c, T.acc[p, 4 + t:5 + t], A.is_gt, ["#%d" % t, "bnd%d" % t], ["fa%d" % t])
+            p, bk = HALF[t], BK["k%d" % t]
+            o, c, b = T.flt[p, t:576:4], T.ps[p, 512 * bk:512 * bk + 144], T.acc[p, 4 + t:5 + t] if t else 256.0 * NF + 128
+            alts = {"V": (lambda o=o, c=c, b=b: V.tensor_scalar(o, c, 256.0, b, A.mult, A.is_lt), vc(144), 0),
+                    "S": (lambda o=o, c=c, b=b: S.activation(o, c, AF.Sigmoid, bias=b, scale=-256.0), vc(144), 0)}
+            add({e: alts[e] for e in FA}, ["#%d" % bk, "ctri"] + ["bnd%d" % t] * (t > 0), ["fa%d" % t])
         quant("fl", 0, 144, T.flt, ["fa%d" % t for t in range(4)], ["fl0"])
-        mm(5, "ka", 128, "fl", 0, 128, ["fl0", "ka1"], True, False)
-        mm(5, "ka", 0, "fl", 8, 128, ["fl0", "ka0"], False, True)
+        bp, bc, bl = BK["p"], BK["c"], BK["l"]
+        mm(bp, "ka", 0, "fl", 0, 128, ["fl0", "ka1"], True, False)
+        mm(bp, "kr", 16, "fl", 8, 128, ["fl0", "kr"], False, True)
         for t in range(4):
-            p = slice(64 * (t == 2), 128)
+            p = HALF[t]
             ts(T.sot[p, t:512:4], T.ioh[p, :], T.cm2[p, 9 * t + 7:9 * t + 8], A.add, ["io0", "io1", "io2", "io3", "cm2s"], ["so%d" % t],
                T.cm2[p, 9 * t + 43:9 * t + 44], A.is_equal, 0.5)
         quant("so", 0, 128, T.sot, ["so%d" % t for t in range(4)], ["so"])
-        mm(4, "so", 0, "ef", 0, 512, ["so"] + ["ef%d" % b for b in range(4)], True, False)
-        mm(4, "fl", 16, "kb", 0, 512, ["fl0", "kba", "kbb"], False, True)
-        scan(T.ln[:], T.k8[:], ps(4, 0, 512), 0.0, A.mult, A.max, ["#4", "k8"], ["ln"])
-        for z in (1, 0):
-            o, c = T.cand[:, 64 * z:64 * z + 64], T.ln[:].indirect(T.cl[:, 4 * z:4 * z + 4])
-            add({"V": (lambda o=o, c=c: V.tensor_scalar(o, c, 256.0, None, A.mult), 0.05 + 100 * CY, 0),
-                 "S": (lambda o=o, c=c: S.activation(o, c, AF.Copy, scale=256.0), 0.065 + 100 * CY, 0)}, ["ln", "cl"], ["cand%d" % z])
-            for y in range(2):
-                mv(T.cb[64 * y:64 * y + 64, 32 * z:32 * z + 32], T.cand[64 - 64 * y:128 - 64 * y, 64 * z + 32:64 * z + 64], ["cand%d" % z], ["cb%d%d" % (z, y)])
-            tt(T.sm[:, 32 * z:32 * z + 32], T.cand[:, 64 * z:64 * z + 32], T.cb[:, 32 * z:32 * z + 32], A.max, ["cand%d" % z, "cb%d0" % z, "cb%d1" % z],
-               ["sm%d0" % z, "sm%d1" % z])
-        scan(T.pkf[:], T.kpk[:], T.sm[:, 32:64], 0.0, A.mult, A.add, ["sm10", "sm11", "kpk0", "kpk1"], ["pkf"])
-        cp(T["pk%d" % r][:], T.pkf[:, 1:32:2], ["pkf"], ["pk%d" % r])
-        send(T["lst%d" % r][:], T["pk%d" % r][:], "al%d" % r, 1, ["pk%d" % r], ["lst%d" % r], 2.0)
+        for k in range(2):
+            if k == MF:
+                mm(bc, "so", 0, "pm", 0, NC, ["so", "pm0", "pm1"], k == 0, k == 1)
+            else:
+                mm(bc, "fl", 16, "kb", 0, NC, ["fl0", "kba", "kbb"], k == 0, k == 1)
+        scan(T.ln[:], T.kat[:, 0:NC], ps(bc, 0, NC), 0.0, A.mult, A.max, ["#%d" % bc, "kat0"], ["ln"])
+        for y in range(2):
+            p = slice(64 * y, 64 * y + 64)
+            scan(T.pkf[p, 0:30], T.kpk[p, 0:30], T.ln[p, 7 + 8 * y:NC:16], 0.0, A.mult, A.add, ["ln", "kpk0", "kpk1"], ["pkf%d" % y])
+            for o in range(2):
+                lin(T.sm[64 * o:64 * o + 64, 30 * (o ^ y):30 * (o ^ y) + 30], T.ln[p, 7 + 8 * y:NC:16], 256.0, T.w2[p, 7:8], ["ln", "ow"], ["sm%d%d" % (y, o)])
+        ts(T["pk%d" % r][:], T.pkf[:, 1:30:2], 256.0, A.mult, ["pkf0", "pkf1"], ["pk%d" % r])
+        send(T["lst%d" % r][:], T["pk%d" % r][:], "al%d" % r, 1, ["pk%d" % r] + ["quiet"] * QUIET, ["lst%d" % r], 2.0)
+        mv(T.pc[:], T.ps[:, 512 * bp:512 * bp + 8:2], ["#%d" % bp], ["pc"])
         for t in range(4):
-            p, a = slice(64 * (t == 2), 128), 64 * (t == 3)
-            ts(T.cmt[p, 4 * a + t:4 * NF:4], T.ios[p, a:NF], T.ps[p, 2560 + 2 * t:2561 + 2 * t], A.is_ge, ["#5", "ios"], ["cm%d" % t], f=0.5)
+            p, a = HALF[t], 64 * (t == 3)
+            ts(T.cmt[p, 4 * a + t:4 * NF:4], T.ios[p, a:NF], T.pc[p, t:t + 1], A.is_ge, ["pc", "ios"], ["cm%d" % t], f=0.5)
         quant("cm", 0, NF, T.cmt, ["cm%d" % t for t in range(4)], ["cm"])
-        mm(1, "ka", 0, "cm", 0, NF, ["cm", "ka0"])
-        scan(T.lrow[:], T.k16[:], ps(1, 0, NF), 0.0, A.add, A.min, ["#1", "k16"], ["lrow"])
+        mm(bl, "kr", 16, "cm", 0, NF, ["cm", "kr"])
+        scan(T.lrow[:], T.k16[:], ps(bl, 0, NF), 0.0, A.add, A.min, ["#%d" % bl, "k16"], ["lrow"])
         cp(T.pl[:], T.lrow[:, 15:NF:16], ["lrow"], ["pl"])
         sl, ld = "slot%d" % r, "land%d" % r
         pick(sl, t_, NF, C, T.pl[:, 0:12], TA + ["pl"])
@@ -612,51 +713,62 @@ def rank_program(g, core, T, topo):
         send(T[ld + "s"][:], T[sl + "s"][:], "ac%d" % r, 2, [sl + "s"], [ld + "s"], 2.1)
 
         def unpack(src, base, key, banks, on):
-            for k in range(7, -1, -1):
-                bk = banks[k % len(banks)]
-                o = base + (WS if base else NF) * (7 - k)
-                a, z = (max(0, 136 - 56 * k), NF) if base else (0, NF if r == 0 else min(NF, 399 - 56 * k))
+            for i in range(9):
+                k = 7 - i
+                bk = banks[i % len(banks)]
+                o = base + (WS if base else NF) * i
+                a, z = (max(0, 80 - 56 * k), NF) if base else (0, NF if r == 0 else min(NF, 399 - 56 * k))
                 a0, z0 = min(a, NF - 128), max(z + z % 2, 128)
-                mm(bk, "eb", 128 * k, src, a0, z0 - a0, [src + "c", src + "s", "eb%dc" % (k // 2), "eb%ds" % (k // 2)])
-                mv(T.win[:, o + a:o + z], ps(bk, a - a0, z - a0), ["#%d" % bk], ["%s%d" % (key, k)], SC64, on=on)
-        unpack(sl, 0, "wo", (3, 4, 5), "SV")
-        ts(T.eq[:], T.sm[:, 0:32], 0.0, A.is_gt, ["sm00", "sm01"], ["eq"], BIG + NF, A.mult)
-        tt(T.eq[:], T.eq[:], T.sm[:, 0:32], A.add, ["eq", "sm00", "sm01"], ["eq"])
-        scan(T.kos[:, 31::-1], T.kst[:, 0:32], T.eq[:, 31::-1], 0.0, A.add, A.max, ["eq", "kst"], ["kos"])
-        tt(T.own[:], T.kos[:], T.idc[:], A.max, ["kos", "idc"], ["own"])
-        unpack(ld, WA, "wa", (6, 7, 1, 2, 0), "SV")
-        cp(T.ai[:], T["lst%d" % r][:], ["lst%d" % r], ["ai"])
-        ts(T.a2[:, 0:32:2], T.ai[:], 8, A.arith_shift_right, ["ai"], ["a2h"])
-        ts(T.a2[:, 1:32:2], T.ai[:], 255, A.bitwise_and, ["ai"], ["a2l"])
-        ts(T.kn[:], T.a2[:], 0.0, A.is_gt, ["a2h", "a2l"], ["kn"], BIG, A.mult)
-        tt(T.kn[:], T.kn[:], T.a2[:], A.add, ["kn", "a2h", "a2l"], ["kn"])
-        scan(T.kns[:], T.kst[:, 32:64], T.kn[:], 0.0, A.add, A.max, ["kn", "kst"], ["kns"])
-        for k in range(4 if REP2 else 2):
-            y, o = 64 * (k % 2), 64 * (k // 2)
-            tt(T.rep[o:o + 64, y // 2:y // 2 + 32], T.kns[y:y + 64, :], T.own[y:y + 64, :], A.max, ["kns", "own"], ["rep%d" % k])
-        for k in range(4 if REP2 else 2):
-            mv(T.rep[32 * k:32 * k + 32, 64:128], T.rep[32 - 32 * (k % 2):64 - 32 * (k % 2), 0:64], ["rep0", "rep1"], ["rp%d" % k])
-        if not REP2:
-            mv(T.rep[64:128, :], T.rep[0:64, :], ["rep0", "rep1", "rp0", "rp1"], ["rp2", "rp3", "rep2", "rep3"])
-        ts(T.off[:], T.rep[:, 0:128].indirect(T.ordr[:, 0:8]), -1.0, A.mult, ["%s%d" % (s, k) for s in ("rep", "rp") for k in range(4)] + ["ordr"], ["off"],
-           float(TOP), A.add, f=2.0)
-        WIN = ["ft%d" % b for b in range(4)] + ["wo%d" % k for k in range(8)] + ["fg%d%d" % (k, q) for k in range(2) for q in range(NH)] + ["off"]
+                mm(bk, "ef", 128 * (k % 8), src, a0, z0 - a0, [src + "c", src + "s", "ef%d" % (k % 8)])
+                mv(T.win[:, o + a:o + z], ps(bk, a - a0, z - a0), ["#%d" % bk], ["%s%d" % (key, i)], SC64, on=on)
+        unpack(sl, 0, "wo", BK["o"], "SV")
+        SM = ["sm00", "sm01", "sm10", "sm11", "cl"]
+        ts(T.eo[:], T.sm[:, 0:60].indirect(T.cl[:, 4:8]), T.w2[:, 7:8], A.is_equal, SM, ["eo"], -2 * BIG, A.mult, 2.5)
+        tt(T.eq[:], T.sm[:, 0:60].indirect(T.cl[:, 4:8]), T.eo[:], A.add, SM + ["eo"], ["eq"], 2.5)
+        scan(T.kos[:, 63::-1], T.kst[:, 63::-1], T.eq[:, 63::-1], 0.0, A.add, A.max, ["eq", "kst0"], ["kos"])
+        tt(T.own[:], T.kos[:], T.idc[:, 0:64], A.max, ["kos", "idc"], ["own"])
+        unpack(ld, WA, "wa", BK["a"], "SV")
+        cp(T.ai[:, 0:15], T["lst%d" % r][:], ["lst%d" % r], ["ai"])
+        for y in range(2):
+            cp(T.ai[64 * y:64 * y + 64, 15:30], T["lst%d" % r][64 - 64 * y:128 - 64 * y, :], ["lst%d" % r], ["ai%d" % y])
+        ts(T.a2[:, 0:60:2], T.ai[:], 8, A.arith_shift_right, ["ai", "ai0", "ai1"], ["a2h"])
+        ts(T.a2[:, 1:60:2], T.ai[:], 255, A.bitwise_and, ["ai", "ai0", "ai1"], ["a2l"])
+        ts(T.ke[:], T.a2[:].indirect(T.cl[:, 0:4]), 0.0, A.is_equal, ["a2h", "a2l", "cl"], ["ke"], f=2.5)
+        tt(T.kn[:], T.a2[:].indirect(T.cl[:, 0:4]), T.kst[:, 64:128], A.add, ["a2h", "a2l", "cl", "kst1"], ["kn"], 2.5)
+        scan(T.kns[:], T.ke[:], T.kn[:], 0.0, A.mult, A.add, ["kn", "ke"], ["kns"])
+        tt(T.rep[:, 0:64], T.kns[:], T.own[:], A.max, ["kns", "own"], ["rep"])
+        for k in range(4):
+            mv(T.rep[32 * k:32 * k + 32, 64:128], T.rep[32 * (k ^ 1):32 * (k ^ 1) + 32, 0:64], ["rep"], ["rp%d" % k])
+        for a, z in OFF:
+            ts(T.off[:, a:z], T.rep[:, 0:128].indirect(T.ordr[:, a // 16:z // 16]), -1.0, A.mult, ["rep"] + ["rp%d" % k for k in range(4)] + ["ordr", "top"],
+               ["off%d" % a], T.w2[:, 6:7], A.add, f=1.6 + 60 / (z - a))
+        WIN = ["ft%d" % b for b in range(4)] + ["wo%d" % k for k in range(9)] + ["fg%d%d" % (k, q) for k in range(2) for q in range(NH)] + ["gap"]
         for i, (a, z) in enumerate(GAT):
-            n = NH if a >= C - 56 * NH else 8
+            n = NH + 1 if a >= C - 56 * NH else 9
             for b1 in range(2):
                 lo, hi = 896 * b1 + 2 * a, 896 * b1 + 2 * z
-                tt(T.yt[:, lo:hi], T.win[:, 0:WA + NH * WS if n < 8 else WF + 2 * FW].indirect(T.off[:, 64 * b1 + a // 8:64 * b1 + z // 8]), T.fh[:, lo:hi],
-                   A.add, WIN + ["wa%d" % (7 - k) for k in range(n)] + ["fh0", "fh1"] * (n == 8), ["yt%d%d" % (b1, i)], 1.6)
-        for h in range(H):
+                tt(T.yt[:, lo:hi], T.win[:, 0:WA + n * WS if n < 9 else WF + 2 * FW].indirect(T.off[:, 64 * b1 + a // 8:64 * b1 + z // 8]),
+                   T.fh[:, lo:hi], A.add, WIN + ["wa%d" % k for k in range(n)] + ["fh00", "fh01", "fh10", "fh11"] * (n == 9)
+                   + ["off%d" % c for c, d in OFF if c < 64 * b1 + z // 8 and 64 * b1 + a // 8 < d], ["yt%d%d" % (b1, i)], 1.56 + 30 / (z - a))
+        for h in range(H - 1, -1, -1):
             a, z = CUTS[h], CUTS[h + 1]
-            for be in range(4):
+            if h in ZP:
+                n = 2 * (z - a)
+                for b in range(4):
+                    o = (n + 16) * b + 8
+                    for be in range(4):
+                        c = 896 * (be // 2) + 2 * a
+                        dma("Y", "dz%d" % b, T.zz[32 * be:32 * be + 32, o - be % 2:o - be % 2 + n], T.yt[32 * b:32 * b + 32, c:c + n],
+                            ["yt%d%d" % (be // 2, i) for i, (c, d) in enumerate(GAT) if c < z and a < d], ["zz%d%d" % (be, b)], ZT)
+                    mv(T.yy[:, 4 * a + b:4 * z:4], T.zz[:, o:o + n:2], ["zz%d%d" % (be, b) for be in range(4)], ["yy%d%d%d" % (be, b, h) for be in range(4)], f=0.5, on=GC)
+            for be in range(4 * (h not in ZP)):
                 for b in range(4):
                     o = 896 * (be // 2)
                     mv(T.yy[32 * be:32 * be + 32, 4 * a + b:4 * z:4], T.yt[32 * b:32 * b + 32, o + 2 * a + be % 2:o + 2 * z:2],
                        ["yt%d%d" % (be // 2, i) for i, (c, d) in enumerate(GAT) if c < z and a < d], ["yy%d%d%d" % (be, b, h)], f=0.5, on=GC)
             quant("qy", a, z, T.yy, ["yy%d%d%d" % (i, b, h) for i in range(4) for b in range(4)], ["qy%d" % h])
             for b in range(4):
-                bk = (4 * h + b) % 8
+                bk = BK["w"][(4 * h + b) % 8]
                 mm(bk, "qw", 128 * b, "qy", a, z - a, ["qy%d" % h, "qwc", "qws"])
                 if b < YP:
                     c = slice(4 * a + b, 4 * z, YP)
@@ -679,9 +791,14 @@ def rank_program(g, core, T, topo):
 
     Q = {"V": V, "S": S, "P": g.tensor, "G": g, "Y": g.sync}
     cnt, seen, tok, eng, knew, sent, moved, alone = {}, {e: {} for e in Q}, {}, {}, {}, 0, False, False
+    at = {i: p for p, i, e in schedule(ops)}
     for _, i, e in schedule(ops):
         o = ops[i]
-        for d, raw in sorted(o["deps"].items(), reverse=True):
+        if o["sem"] == "none":
+            continue
+        for d, raw in sorted(o["deps"].items(), key=lambda x: -at[x[0]]):
+            if ops[d]["sem"] == "none":
+                continue
             if raw or eng[d] != e or ops[d]["sem"] or ops[d]["arrive"]:
                 s, v = tok[d]
                 if seen[e].get(s, 0) < v:

import math
from concourse.mybir import dt, AluOpType as A, ActivationFunctionType as AF

C, NF, R = 448, 192, 3
BIG = 8192.0
CUTS = (0, 128, 288, 448)
B0 = (0, 128, 192, 320)
B1 = B0 + (C,)
HALF = (slice(0, 128), slice(0, 64), slice(0, 128), slice(0, 128))
MQ = ((128, 448), (0, 128))
FA = "VS"
OFF = ((32, 64), (64, 128), (0, 32))
ZP, ZT = (), 2.2
QUIET = True
MF = 1
BK = {"c3": 4, "r3": 5, "c2": 7, "c1": 6, "r1": 0, "s1": 1, "c0": 2, "d0": 3, "r0": 4, "k3": 1, "k2": 7, "k1": 6, "k0": 5,
      "p": 0, "c": 4, "l": 1, "f": (2, 3), "o": (5, 6, 7), "a": (2, 3, 0, 1, 4), "w": (0, 1, 2, 3, 4, 5, 6, 7)}
WA, WS, NH = 9 * NF, NF + 224, 3
WF = WA + 8 * WS + NF
KEY = 194
TOP = WA + KEY - WS
NC = 480
OWN = float(2 * NF - WS)
FW = 2 * C - 112 * NH
MN = True
UPS = ((3, 4), (1, 3))
YP = 2
GAT = ((288, 448), (128, 288), (0, 128))
GC = "VSG"
Q4, U8, BF, F32, I32, U16 = "float8_e4m3fn_x4", "uint8", "bfloat16", "float32", "int32", "uint16"
SCRATCH = {}


def _sb(name, n, d):
    SCRATCH[name] = ("sbuf", [128, n], d)


def _q(name, n):
    _sb(name + "c", n, Q4)
    _sb(name + "s", n, U8)


for _r in range(R + 1):
    _q("t%d" % _r, C)
for _r in range(R):
    _q("slot%d" % _r, NF)
    _q("land%d" % _r, NF)
    _sb("pk%d" % _r, 15, U16)
    _sb("lst%d" % _r, 15, U16)
for _n, _w in (("qu", 128), ("qup", 144), ("qv", 128), ("qw", 512), ("ef", 1024), ("ka", 128),
               ("kb", NC), ("pm", NC), ("kr", 216), ("m", C), ("fl", 192), ("cm", NF), ("so", 128), ("qy", C)):
    _q(_n, _w)
for _n, _w in (("xin", 4 * C), ("xs", 4 * C), ("ut", 512), ("vt", 512), ("eft", 4096), ("kat", 512), ("trt", 512), ("kbt", 4 * NC), ("pmt", 4 * NC),
               ("dw", 128 + C), ("mt", 4 * C), ("flt", 768), ("cmt", 4 * NF), ("sot", 512), ("krt", 864), ("ios", NF), ("k16", NF), ("ioh", 128), ("k8", NC),
               ("win", WF + 2 * FW), ("yt", 4 * C), ("fh", 4 * C), ("yy", 4 * C), ("y1", 4 * C), ("nar", 384), ("ctri", 128), ("tj", 128), ("cm2", 80), ("pc", 4), ("zz", 1600)):
    _sb(_n, _w, BF)
for _n, _w in (("sc", 80), ("cmx", 80), ("rr", 80), ("k72", 160), ("thr", 4), ("dd", 640), ("ebi", 8), ("cv", 32),
               ("eq", 64), ("eo", 64), ("lrow", NF), ("ln", NC), ("sm", 64), ("kpk", 32), ("ke", 64), ("idn", 72),
               ("pkf", 32), ("kos", 64), ("own", 64), ("kn", 64), ("kns", 64), ("rep", 128), ("df", C), ("up", 4), ("kst", 128), ("idc", 72),
               ("w1", 32), ("w2", 16), ("pv", 8), ("yo", C), ("acc", 8)):
    _sb(_n, _w, F32)
for _n, _w in (("ci", 32), ("ai", 30), ("a2", 60), ("pi", 8), ("wi", 8)):
    _sb(_n, _w, I32)
for _n, _w in (("ul", 10), ("pl", 12), ("ordr", 8), ("cl", 8), ("off", 128), ("ebl", 16)):
    _sb(_n, _w, U16)
SCRATCH["ps"] = ("psum", [128, 4096], F32)
SEMAPHORES = ["V", "S", "P", "G", "dx0", "dx1", "dx2", "dz0", "dz1", "dz2", "dz3", "du", "dv", "dwc", "dws", "outs", "sent", "dw", "dg", "dfh0", "dfh1"] + ["de%d" % k for k in range(1, 8)] + \
             ["%s%d" % (k, r) for k in ("ac", "al") for r in range(R)]
CY, OV, LAT, LATG, PE, RI, DL = 0.00085, 0.005, 0.2, 0.22, 0.0006, 0.4, -1.0
MORE = {"S": 0.008, "G": 0.02}
CASES = ((1.0, 0.005, 0.0, 0.0, 0.19, 0.23, 0.2, 0.0, -0.3, 1.0, 0.4, 0.0), (1.0, 0.0, 0.0, 0.0, 0.21, 0.21, 0.1, -0.3, 0.0, 0.85, 0.6, 0.0),
         (1.0, 0.015, 0.01, 0.03, 0.16, 0.19, 0.4, 0.5, -0.8, 1.2, 0.15, 0.015), (1.35, 0.005, 0.0, 0.0, 0.22, 0.25, 0.3, 0.5, 0.2, 1.4, 0.6, 0.0))
TRIES, MOVES, SEED, KINDS, HEAT = 400, 45000, 4321, 10, 0.03
SPAN, PLAN, STEP = [0.0], [], [0, 0, 0]


def name(k):
    return k[0] + k[2:] if k[0] == "t" and k[2:3] == "_" else k[:4] + k[5:] if k[:4] in ("slot", "land") else k[:2] if k[:2] in ("pk", "ls") else k


def deal(ops, order, spare, back=None):
    n = len(ops)
    busy = {}
    done, eng, start = [0.0] * n, [None] * n, [0.0] * n
    for i in order:
        best = None
        for e, (fn, hold, tail) in ops[i]["alts"].items():
            t = 0.0
            for d, raw in (back[i] if back else ops[i]["deps"]).items():
                u = done[d] + (LATG if (eng[d] if back else e) == "G" else LAT) if raw or eng[d] != e else (done[d] if back else start[d] + 1e-6)
                if u > t:
                    t = u
            if back:
                t, tail = t + tail, 0.0
            line = busy.setdefault(e, [])
            lo, hi = 0, len(line)
            while lo < hi:
                mid = (lo + hi) // 2
                if line[mid][1] <= t:
                    lo = mid + 1
                else:
                    hi = mid
            while lo < len(line) and t + hold > line[lo][0]:
                t = max(t, line[lo][1])
                lo += 1
            val = t + hold + tail + (spare.get(ops[i]["key"], 0.0) if e == "V" else 0.0)
            if best is None or val < best[4]:
                best = (t + hold + tail, t, e, hold, val, lo)
        done[i], start[i], eng[i] = best[0], best[1], best[2]
        busy[best[2]].insert(best[5], (best[1], best[1] + best[3]))
    return max(done), start, done, eng


def schedule(ops):
    if PLAN:
        return PLAN[0]
    n = len(ops)
    anc, short = [0] * n, []
    for i, o in enumerate(ops):
        far = 0
        for d, raw in o["deps"].items():
            if raw:
                far |= anc[d]
        short.append(dict(o, deps={d: raw for d, raw in o["deps"].items() if not far >> d & 1}))
        anc[i] = far
        for d, raw in o["deps"].items():
            if raw:
                anc[i] |= 1 << d
    ops = short
    succ = [{} for _ in range(n)]
    for i, o in enumerate(ops):
        for d, raw in o["deps"].items():
            succ[d][i] = raw
    pri = [0.0] * n
    for i in range(n - 1, -1, -1):
        c = min(a[1] + a[2] for a in ops[i]["alts"].values())
        pri[i] = c + LAT + max([pri[j] for j in succ[i]] + [0.0])
    keys = sorted(set(o["key"] for o in ops))
    both = sorted(set(o["key"] for o in ops if len(o["alts"]) > 1 and "V" in o["alts"]))
    spare = {k: 0.3 for k in both}

    def forward(p, sp):
        p = list(p)
        for i in range(n - 1, -1, -1):
            for j in succ[i]:
                if p[j] + 1e-4 > p[i]:
                    p[i] = p[j] + 1e-4
        return deal(ops, sorted(range(n), key=lambda k: -p[k]), sp)
    deps = [list(o["deps"].items()) for o in ops]
    cases = []
    for f, ov, ovs, ovg, lat, own, latg, dl, dr, pe, ri, px in CASES:
        cost = [{e: (ri, h + t + dr - ri) if o["arrive"] else (h, t + dl) if o["sem"] else (h * pe, 0.0) if e == "P"
                 else ((h + t - OV) * f + ov + ovs * (e == "S") + ovg * (e == "G") + px * o["psum"], 0.0) for e, (fn, h, t) in o["alts"].items()} for o in ops]
        cases.append((cost, lat, own, latg))

    def score(got):
        order, eng, total = sorted(range(n), key=lambda k: (got[1][k], k)), got[3], 0.0
        waits = [[(d, eng[d] == eng[i]) for d, raw in deps[i] if raw or eng[d] != eng[i]] for i in range(n)]
        for cost, lat, own, latg in cases:
            free, done = {}, [0.0] * n
            for i in order:
                e = eng[i]
                t = free.get(e, 0.0)
                for d, same in waits[i]:
                    u = done[d] + (latg if e == "G" else own if same else lat)
                    if u > t:
                        t = u
                c = cost[i][e]
                free[e] = t + c[0] + (own if ops[i].get("alone") else 0.0)
                done[i] = t + c[0] + c[1]
            total += max(done)
        return (total / len(cases) if cases else got[0],) + got
    best = cur = score(forward(pri, spare))
    z = 12345
    for it in range(TRIES):
        s2, shift = dict(spare), {}
        for _k in range(2):
            z = (z * 1103515245 + 12345) % 2147483648
            step = (-2.0, -1.0, -0.5, -0.2, 0.2, 0.5, 1.0, 2.0)[(z >> 8) % 8]
            if (z >> 12) % 3 == 0:
                k = both[(z >> 14) % len(both)]
                s2[k] += step / 2
            else:
                shift[keys[(z >> 14) % len(keys)]] = step
        p2 = [pri[i] + shift.get(ops[i]["key"], 0.0) for i in range(n)]
        got = forward(p2, s2)
        if it % 10 == 0:
            p3 = deal(ops, sorted(range(n), key=lambda k: (-got[2][k], -k)), s2, succ)[2]
            again = forward(p3, s2)
            if again[0] < got[0]:
                got, p2 = again, p3
        z = (z * 1103515245 + 12345) % 2147483648
        if got[0] > cur[1] + 0.6:
            continue
        got = score(got)
        if got[0] <= cur[0] + 0.15 * (1 - it / TRIES) * ((z >> 8) % 1000) / 1000:
            cur, pri, spare = got, p2, s2
            if got[0] < best[0]:
                best = got
    order, eng, SPAN[:] = polish(ops, deps, succ, cases, sorted(range(n), key=lambda k: (best[2][k], k)), list(best[4]))
    PLAN.append([(p, i, eng[i]) for p, i in enumerate(order)])
    return PLAN[0]


def polish(ops, deps, succ, cases, order, eng):
    n = len(ops)
    twin = [[j for j in (i - STEP[0], i + STEP[0], i - 2 * STEP[0], i + 2 * STEP[0]) if STEP[1] <= i < STEP[2] and STEP[1] <= j < STEP[2]] for i in range(n)]

    def run(order, eng, first, old):
        last, p = {}, first - 1
        while p >= 0 and len(last) < 5:
            last.setdefault(eng[order[p]], order[p])
            p -= 1
        rest = []
        for i in order[first:]:
            e = eng[i]
            rest.append((i, e, [d for d, raw in deps[i] if eng[d] != e], [d for d, raw in deps[i] if raw and eng[d] == e]))
        out, total, was = [], 0.0, 0.0
        for c, (cost, lat, own, latg) in enumerate(cases):
            done, hold = (list(old[c][0]), list(old[c][1])) if old else ([0.0] * n, [0.0] * n)
            free = {e: hold[last[e]] if e in last else 0.0 for e in "VSPGY"}
            for i, e, far, near in rest:
                t = free[e]
                if far:
                    x = latg if e == "G" else lat
                    for d in far:
                        if done[d] + x > t:
                            t = done[d] + x
                if near:
                    x = latg if e == "G" else own
                    for d in near:
                        if done[d] + x > t:
                            t = done[d] + x
                k = cost[i][e]
                free[e] = hold[i] = t = t + k[0]
                done[i] = t + k[1]
            end = max(done)
            total += end
            out.append((done, hold, end))
            if old:
                was += old[c][2]
                if total > was + 0.45:
                    return 1e9, None
        return total / len(cases), out

    def chain(order, eng, c, state):
        cost, lat, own, latg = cases[c]
        done, hold, end = state[c]
        before, last = [-1] * n, {}
        for i in order:
            before[i] = last.get(eng[i], -1)
            last[eng[i]] = i
        i, pairs = done.index(end), []
        while i >= 0:
            e, j = eng[i], before[i]
            t = hold[j] if j >= 0 else 0.0
            for d, raw in deps[i]:
                if raw or eng[d] != e:
                    u = done[d] + (latg if e == "G" else own if eng[d] == e else lat)
                    if u > t:
                        t, j = u, -2 - d
            if j >= 0:
                pairs.append((i, j))
            i = j if j > -2 else -2 - j
        return pairs

    def ahead(order, i, j):
        a, b = order.index(j), order.index(i)
        if a >= b:
            return None
        need, move = {d for d, raw in deps[i]}, [i]
        for k in order[b - 1:a - 1 if a else None:-1]:
            if k in need:
                if k == j or len(move) > 6:
                    return None
                move.append(k)
                need.update(d for d, raw in deps[k])
        gone = set(move)
        order[a:b + 1] = move[::-1] + [k for k in order[a:b + 1] if k not in gone]
        return a
    def behind(order, j, i):
        a, b = order.index(j), order.index(i)
        if a >= b:
            return None
        after, move = set(succ[j]), [j]
        for k in order[a + 1:b + 1]:
            if k in after:
                if k == i or len(move) > 6:
                    return None
                move.append(k)
                after.update(succ[k])
        gone = set(move)
        order[a:b + 1] = [k for k in order[a:b + 1] if k not in gone] + move
        return a

    def alike(order, eng, a, b):
        at, e2 = [0] * n, list(eng)
        for p, i in enumerate(order):
            at[i] = p
        ra, rb = (range(STEP[1] + k * STEP[0], STEP[1] + (k + 1) * STEP[0]) for k in (a, b))
        for p, i in zip(sorted(at[i] for i in rb), sorted(ra, key=lambda i: at[i])):
            at[i + (b - a) * STEP[0]] = p
            e2[i + (b - a) * STEP[0]] = eng[i]
        for i in range(n):
            for d, raw in deps[i]:
                if at[i] <= at[d]:
                    at[i] = at[d] + 1e-3
        return sorted(range(n), key=lambda i: (at[i], i)), e2
    cur, state = run(order, eng, 0, None)
    start, best, z, known = cur, (cur, list(order), list(eng)), SEED, {}
    for it in range(MOVES):
        if it % 1000 == 999:
            for a, b in ((1, 2), (2, 1), (1, 0), (0, 1)):
                o2, e2 = alike(order, eng, a, b)
                got, s2 = run(o2, e2, 0, None)
                if got < cur:
                    cur, state, order, eng, known = got, s2, o2, e2, {}
                    if got < best[0]:
                        best = (got, list(order), list(eng))
        z = (z * 1103515245 + 12345) % 2147483648
        c = (z >> 8) % len(cases)
        if c not in known:
            known[c] = chain(order, eng, c, state)
        pairs = known[c]
        z = (z * 1103515245 + 12345) % 2147483648
        i, j = pairs[(z >> 8) % len(pairs)]
        z = (z * 1103515245 + 12345) % 2147483648
        kind, every, o2, e2, first = (z >> 8) % KINDS, (z >> 12) % 4 > 0, list(order), list(eng), n
        if kind > 7:
            for k in [j] + (twin[j] if every else []):
                if 0 <= i + k - j < n:
                    a = behind(o2, k, i + k - j)
                    first = first if a is None else min(first, a)
        elif kind < 5:
            p = order.index(j)
            for _k in range((0, 0, 0, 1, 3)[kind]):
                q = p - 1
                while q >= 0 and eng[order[q]] != eng[i]:
                    q -= 1
                p = q if q >= 0 else p
            j = order[p]
            for k in [i] + (twin[i] if every else []):
                if 0 <= j + k - i < n:
                    a = ahead(o2, k, j + k - i)
                    first = first if a is None else min(first, a)
        else:
            i = j if kind < 7 else i
            other = [e for e in ops[i]["alts"] if e != eng[i]]
            if other:
                for k in [i] + (twin[i] if every else []):
                    e2[k] = other[(z >> 16) % len(other)]
                    first = min(first, o2.index(k))
        if first < n:
            got, s2 = run(o2, e2, first, state)
            z = (z * 1103515245 + 12345) % 2147483648
            if got <= cur + HEAT * (1 - it / MOVES) * ((z >> 8) % 1000) / 1000:
                cur, state, order, eng, known = got, s2, o2, e2, {}
                if got < best[0]:
                    best = (got, list(order), list(eng))
    return best[1], best[2], (start, best[0])


def rank_program(g, core, T, topo):
    rank = T.rank_of(core)
    if rank is None:
        return
    nxt = T.cores[(rank + 1) % len(T.cores)]
    rid, pid, _ = topo.addr(nxt)
    mask = topo.mask(core, nxt)
    neng = len(topo.engines(core, nxt))
    V, S = g.vector, g.scalar
    ops, lastw, readers = [], {}, {}

    def add(alts, rd, wr, sem=None, arrive=None):
        deps = {}
        for k in wr:
            for d in ([lastw[k]] if k in lastw else []) + readers.get(k, []):
                deps[d] = k[0] != "#"
        for k in rd:
            if k[0] == "#":
                for d in readers.get(k, [])[-1:]:
                    deps.setdefault(d, False)
        for k in rd:
            if k in lastw:
                deps[lastw[k]] = True
        for k in rd:
            readers.setdefault(k, []).append(len(ops))
        for k in wr:
            lastw[k] = len(ops)
            readers[k] = []
        if not sem and not arrive:
            alts = {e: (a[0], a[1] + MORE.get(e, 0.0), a[2]) for e, a in alts.items()}
        ops.append({"alts": alts, "deps": deps, "sem": sem, "arrive": arrive, "psum": any(k[0] == "#" for k in rd), "key": name(wr[0] if wr[:1] and wr[0][0] != "#" else rd[0])})

    def w(ap):
        return ap.shape[1]

    def vc(n, f=1.0):
        return max(64, n * f) * CY + OV

    def ts(out, in0, s1, o0, rd, wr, s2=None, o1=None, f=1.0):
        if o1 is None:
            add({"V": (lambda: V.tensor_scalar(out, in0, s1, None, o0), vc(w(out), f), 0)}, rd, wr)
        else:
            add({"V": (lambda: V.tensor_scalar(out, in0, s1, s2, o0, o1), vc(w(out), f), 0)}, rd, wr)

    def tt(out, a, b, o, rd, wr, f=2.0, alone=False):
        add({"V": (lambda: V.tensor_tensor(out, a, b, o), vc(w(out), f) + LAT * alone, -LAT * alone)}, rd, wr)
        ops[-1]["alone"] = alone

    def cp(out, a, rd, wr, f=1.0):
        add({"V": (lambda: V.tensor_copy(out, a), vc(w(out), f), 0)}, rd, wr)

    def mv(out, a, rd, wr, scale=None, f=1.0, on="VS"):
        n, alts = w(out), {}
        if "V" in on:
            alts["V"] = ((lambda: V.tensor_copy(out, a)) if scale is None else (lambda: V.tensor_scalar(out, a, scale, None, A.mult)), vc(n, f), 0)
        if "S" in on:
            alts["S"] = ((lambda: S.activation(out, a, AF.Copy)) if scale is None else (lambda: S.activation(out, a, AF.Copy, scale=scale)), vc(n), 0)
        if "G" in on:
            alts["G"] = (lambda: g.affine_select(out, a, [[0, n]], A.is_ge, 0.0, 0, 0), 0.17 + 2 * n * CY + OV, 0)
        add(alts, rd, wr)
        ops[-1]["moves"] = out.shape[0] < 128

    def lin(out, a, k, c, rd, wr, f=1.0):
        add({"V": (lambda: V.tensor_scalar(out, a, k, c, A.mult, A.add), vc(w(out), f), 0),
             "S": (lambda: S.activation(out, a, AF.Identity, bias=c, scale=k), vc(w(out)), 0)}, rd, wr)

    def ms(ap, v, wr, f=1.0, s=True):
        alts = {"V": (lambda: V.memset(ap, v), vc(w(ap), f), 0)}
        if s and w(ap) <= 128:
            alts["S"] = (lambda: S.activation(ap, T.tj[0:ap.shape[0], 0:w(ap)], AF.Identity, bias=float(v), scale=0.0), vc(w(ap)), 0)
        elif s:
            alts["S"] = (lambda: S.activation(ap, T.dw[0:ap.shape[0], 128:128 + w(ap)], AF.Identity, bias=float(v), scale=0.0), vc(w(ap)), 0)
        rd = [] if len(alts) == 1 else ["tj"] if w(ap) <= 128 else ["dw0"]
        if s and ap.shape[0] == 128 and v == int(v) and abs(v) < 2 ** 20:
            alts["G"] = (lambda: g.iota(ap, [[0, w(ap)]], int(v), 0, allow_small_or_imprecise_dtypes=True), 0.13 + 2 * w(ap) * CY + OV, 0)
        add(alts, rd, wr)

    def scan(out, d0, d1, init, o0, o1, rd, wr):
        add({"V": (lambda: V.tensor_tensor_scan(out, d0, d1, init, o0, o1), vc(w(out)), 0)}, rd, wr)

    def act(out, a, rd, wr, fn, extra=0.0, **kw):
        add({"S": (lambda: S.activation(out, a, fn, **kw), vc(w(out)) + extra, 0)}, rd, wr)

    def iota(out, pat, base, ch, wr, flag=True):
        fn = (lambda: g.iota(out, pat, base, ch, allow_small_or_imprecise_dtypes=True)) if flag else (lambda: g.iota(out, pat, base, ch))
        add({"G": (fn, 0.13 + 2 * w(out) * CY + OV, 0)}, [], wr)

    def asel(out, a, pat, cmp, fill, base, ch, rd, wr):
        add({"G": (lambda: g.affine_select(out, a, pat, cmp, fill, base, ch), 0.17 + 2 * w(out) * CY + OV, 0)}, rd, wr)

    def quant(nm, a, b, tile, rd, wr):
        add({"V": (lambda: V.quantize_mx(T[nm + "c"][:, a:b], T[nm + "s"][:, a:b], tile[:, 4 * a:4 * b]), 0.012 + 0.00092 * (b - a) + OV, 0)}, rd, wr)

    def mm(bank, st, sa, mo, ma, n, rd, start=True, stop=True):
        add({"P": (lambda: g.tensor.matmul_mx(T.ps[:, 512 * bank:512 * bank + n], T[st + "c"][:, sa:sa + 128], T[st + "s"][:, sa:sa + 128],
                                              T[mo + "c"][:, ma:ma + n], T[mo + "s"][:, ma:ma + n], start, stop), (n + 16) * PE, 0)}, rd, ["#%d" % bank])

    def ps(bank, a, b, p=128):
        return T.ps[0:p, 512 * bank + a:512 * bank + b]

    def pick(dst, src, n, wd, off, rd, a=0, key=None):
        add({"V": (lambda: V.tensor_copy(T[dst + "c"][:, a:a + n].bitcast(dt.uint32), T[src + "c"][:, 0:wd].bitcast(dt.uint32).indirect(off)),
                   0.08 + 1.56 * n * CY, 0)}, rd, [(key or dst) + "c"])
        add({"S": (lambda: S.activation(T[dst + "s"][:, a:a + n], T[src + "s"][:, 0:wd].indirect(off), AF.Copy), 0.09 + 1.56 * n * CY, 0)},
            rd, [(key or dst) + "s"])

    def dma(on, sem, out, in_, rd, wr, t=2.2, hold=0.12):
        qs = {"Y": g.sync, "S": S}
        add({e: (lambda e=e: qs[e].dma_start(out, in_), hold, t + DL) for e in on}, rd, wr, sem)

    def send(out, in_, sem, n, rd, wr, t):
        add({"G": (lambda: g.remote_dma(out, in_, T.sem[sem], T.sem.sent, pid, rid, mask), RI, t - RI)}, rd, wr, None, (sem, n * neng))

    dma("Y", "du", T.ut[:], T.u[:], [], ["ut"], 2.5)
    for h in range(len(CUTS) - 2, -1, -1):
        dma("SY"[h % 2], "dx%d" % h, T.xin[:, 4 * CUTS[h]:4 * CUTS[h + 1]], T.x[:, 4 * CUTS[h]:4 * CUTS[h + 1]], [], ["xin%d" % h], 3.2 - 0.3 * h)

    iota(T.pi[:, 0:2], [[8, 2]], 0, 1, ["pi0"], False)
    iota(T.tj[:], [[1, 128]], 0, -1, ["tj"])
    act(T.ctri[:], T.tj[:], ["tj"], ["ctri"], AF.Sigmoid, 1.5, bias=-128.0, scale=-256.0)
    iota(T.k72[:, 0:72], [[-15, 2], [0, 36]], 16, 0, ["k72a"])
    iota(T.ios[:], [[1, NF]], 0, 0, ["ios"])
    iota(T.k16[:], [[0, NF // 16], [1, 16]], 0, 0, ["k16"])
    ms(T.dw[:], -3.0 / 256, ["dw0", "dw"], 0.5, False)
    ms(T.kat[:, 0:448], 1.0, ["kat0"], 0.5)
    ms(T.kat[:, 448:512], 1.0, ["kat1"], 0.5)
    for t, a in ((0, 128), (1, 0), (2, 320)):
        ms(T.mt[:, 4 * a + t:4 * C:4], 0.0, ["mtp%d" % t], 0.5)
    ms(T.ul[:], 1, ["ul"], s=False)
    ts(T.pi[:, 2:4], T.pi[:, 0:2], 15, A.bitwise_and, ["pi0"], ["pi2"])
    ts(T.pi[:, 4:5], T.pi[:, 0:1], 6, A.arith_shift_right, ["pi0"], ["pi4"])
    ts(T.pi[:, 5:6], T.pi[:, 0:1], 32, A.bitwise_and, ["pi0"], ["pi5"])
    ts(T.pi[:, 6:7], T.pi[:, 0:1], 16, A.bitwise_and, ["pi0"], ["pi6"])
    cp(T.pv[:, 0:5], T.pi[:, 2:7], ["pi2", "pi4", "pi5", "pi6"], ["pv"])
    ts(T.k16[:], T.k16[:], T.pv[:, 0:1], A.is_equal, ["k16", "pv"], ["k16"], BIG, A.mult)
    ts(T.pi[:, 7:8], T.pi[:, 0:1], 14, A.bitwise_and, ["pi0"], ["pi7"])
    ts(T.ul[:, 0:1], T.pi[:, 7:8], 8.0, A.mult, ["pi7"], ["ul"])
    quant("qu", 0, 128, T.ut, ["ut"], ["qu"])
    pick("qup", "qu", 144, 128, T.ul[:, 0:9], ["qu", "ul"])
    for t in range(4):
        add({"V": (lambda t=t: V.tensor_scalar(T.trt[:, t:512:4], T.tj[:], 0.0, None, A.is_ge), vc(64), 0),
             "S": (lambda t=t: S.activation(T.trt[:, t:512:4], T.tj[:], AF.Sigmoid, bias=128.0, scale=256.0), vc(128), 0)}, ["tj", "ctri"], ["tri%d" % t])
    quant("ka", 0, 128, T.trt, ["tri%d" % t for t in range(4)], ["ka1"])
    ms(T.flt[64:128, 1:576:4], 0.0, ["fa1"], 0.5)
    ms(T.sot[64:128, 1:512:4], 0.0, ["so1"], 0.5)
    ms(T.cmt[64:128, 1:4 * NF:4], 0.0, ["cm1"], 0.5)
    ms(T.cmt[:, 3:256:4], 0.0, ["cm3"], 0.5)
    ms(T.krt[:, 0:64], 256.0, ["kr0"], 0.5)
    ms(T.krt[:, 24:32], 1.0, ["kr0"], 0.5)
    ms(T.krt[:, 64:332], 1.0, ["kr1"], 0.5)
    ms(T.krt[:, 332:600], 1.0, ["kr2"], 0.5)
    quant("kr", 0, 150, T.krt, ["kr0", "kr1", "kr2"], ["kr"])
    ms(T.k72[:, 80:152], 0.0, ["k72d"])
    ms(T.k72[:, 88:152:9], -1e29, ["k72d"])
    ms(T.cmx[:, 0:1], -1e29, ["cmx0"])
    if MN:
        ms(T.cmx[:, 40:41], 1e29, ["cmx1"])
    asel(T.eft[:, 0:512], T.kat[:, 0:512], [[-256, 4], [-1, 32], [256, 4]], A.is_equal, 0.0, 0, 1, ["kat0", "kat1"], ["eft0", "efu0"])
    for k in (0, 2, 4, 6, 7, 5, 3, 1):
        if k:
            dma("Y", "de%d" % k, T.eft[16 * k:128, 512 * k:512 * k + 512], T.eft[0:128 - 16 * k, 0:512], ["eft0", "xin0"], ["eft%d" % k], 2.4, 0.2)
            dma("Y", "de%d" % k, T.eft[0:16 * k, 512 * k:512 * k + 512], T.eft[128 - 16 * k:128, 0:512], ["eft0", "xin0"], ["efu%d" % k], 2.4, 0.2)
        quant("ef", 128 * k, 128 * k + 128, T.eft, ["eft%d" % k, "efu%d" % k], ["ef%d" % k])
    for y in range(2):
        ms(T.kat[64 * y:64 * y + 64, 8 - 8 * y:NC:16], 0.0, ["kat0"], 0.5)
    iota(T.nar[:, 0:32], [[16, 2], [1, 8], [32, 2]], -105, 0, ["ioi"])
    for k in range(4):
        ts(T.ioh[:, 32 * k:32 * k + 32], T.nar[:, 0:32], T.pv[:, k // 2:k // 2 + 1], A.subtract, ["ioi", "pv"], ["io%d" % k], 64.0 * (k % 2), A.add)
    asel(T.dw[:, 0:128], T.dw[:, 0:128], [[1, 128]], A.is_gt, -2.0 / 256, 0, -1, ["dw"], ["dw"])
    asel(T.dw[:, 0:128], T.dw[:, 0:128], [[1, 128]], A.not_equal, 320.0 / 256, 0, -1, ["dw"], ["dw"])
    for t in range(4):
        a = 8 + B0[t]
        ms(T.kbt[:, t:4 * a:4], -2.0 / 256, ["kb%d" % t], 0.5)
        mv(T.kbt[:, 4 * a + t:4 * NC:4], T.dw[:, 0:NC - a], ["dw", "dw0"], ["kc%d" % t], f=0.5, on=GC)
    KB = ["k%s%d" % (k, t) for k in "bc" for t in range(4)]
    for k in range(2):
        o, a = T.pmt[:, 2 * NC * k:2 * NC * (k + 1)], T.kbt[:, 2 * NC * k:2 * NC * (k + 1)]
        add({"V": (lambda o=o, a=a: V.tensor_scalar(o, a, 0.0, None, A.is_gt), vc(2 * NC, 0.5), 0),
             "S": (lambda o=o, a=a: S.activation(o, a, AF.Relu, scale=0.8), vc(2 * NC), 0)}, KB, ["pmt%d" % k])
        quant("kb", NC // 2 * k, NC // 2 * (k + 1), T.kbt, KB, ["kb" + "ab"[k]])
        quant("pm", NC // 2 * k, NC // 2 * (k + 1), T.pmt, ["pmt%d" % k], ["pm%d" % k])
    iota(T.cv[:, 0:8], [[0, 2], [16, 4]], -4, 0, ["cv0"])
    iota(T.cv[:, 8:16], [[-7, 2], [-112, 4]], 58, 0, ["cv1"])
    ts(T.ci[:, 0:8], T.cv[:, 0:8], T.pv[:, 0:1], A.add, ["cv0", "pv"], ["ci0"], 1.0 / 9.0, A.mult)
    lin(T.w2[:, 5:6], T.pv[:, 0:1], -7.0, 0.0, ["pv"], ["w25"])
    ts(T.cv[:, 0:8], T.ci[:, 0:8], 64.0, A.mult, ["ci0", "w25"], ["cv0"], T.w2[:, 5:6], A.add)
    tt(T.cv[:, 0:8], T.cv[:, 0:8], T.cv[:, 8:16], A.add, ["cv0", "cv1"], ["cv0"])
    ts(T.ci[:, 0:8], T.cv[:, 0:8], 0.0, A.max, ["cv0"], ["ci0"], 58.0, A.min)
    ts(T.ci[:, 8:16], T.ci[:, 0:8], T.pv[:, 2:3], A.add, ["ci0", "pv"], ["ci1"])
    ts(T.ci[:, 16:24], T.ci[:, 0:8], 1, A.arith_shift_right, ["ci0"], ["ci2"])
    ts(T.ci[:, 8:16], T.ci[:, 8:16], 1, A.bitwise_and, ["ci1"], ["ci1"])
    ts(T.ci[:, 8:16], T.ci[:, 8:16], 30.0, A.mult, ["ci1"], ["ci1"])
    tt(T.ci[:, 0:8], T.ci[:, 8:16], T.ci[:, 16:24], A.add, ["ci1", "ci2"], ["ci0"])
    cp(T.cl[:], T.ci[:, 0:8], ["ci0"], ["cl"])
    for k in range(2):
        ms(T.kpk[:, k:32:2], 256.0 * k, ["kpk%d" % k])
        ms(T.kst[:, 64 * k:64 * k + 64], float(-WS if k else NF), ["kst%d" % k])
    ms(T.kst[:, 8:64:9], -2 * BIG, ["kst0"])
    ms(T.kst[:, 64:128:9], -BIG, ["kst1"])
    iota(T.idc[:], [[-16, 8], [112, 9]], TOP - 896 - WF, 0, ["idc"])
    iota(T.idn[:], [[-16, 8], [-WS, 9]], TOP - WA - NF, 0, ["idn"])
    lin(T.w2[:, 6:7], T.pv[:, 4:5], WS / 16, float(TOP), ["pv"], ["top"])
    lin(T.w2[:, 7:8], T.pv[:, 4:5], (WS - NF) / 16, OWN, ["pv"], ["ow"])
    ts(T.w2[:, 8:9], T.pv[:, 4:5], WS / 16, A.mult, ["pv"], ["w28"], T.pv[:, 0:1], A.subtract)
    lin(T.w2[:, 3:4], T.pv[:, 3:4], -FW / 32, T.w2[:, 8:9], ["pv", "w28"], ["w23"])
    lin(T.w2[:, 4:5], T.pv[:, 3:4], -3.5, T.w2[:, 8:9], ["pv", "w28"], ["w24"])
    lin(T.idc[:], T.idc[:], 1.0, T.w2[:, 3:4], ["idc", "w23"], ["idc"])
    for q in range(NH):
        lin(T.idc[:, q + 1:72:9], T.idn[:, q + 1:72:9], 1.0, T.w2[:, 4:5], ["idn", "w24"], ["idc"])
    a = WA + (NH + 1) * WS + NF
    dma("Y", "dw", T.win[:, a:WF], T.x[:, 0:WF - a], ["xin0"], ["wa%d" % k for k in range(NH + 2, 9)], 2.2, 1.3)
    dma("Y", "dg", T.win[:, WA + NF:WA + WS], T.x[:, 0:WS - NF], ["xin0"], ["gap"], 2.2, 0.2)
    late = ["eft%d" % k for k in range(1, 8)] + ["efu%d" % k for k in range(1, 8)]
    dma("Y", "dwc", T.qwc[:].bitcast(dt.uint8), T.wc[:], late, ["qwc"], 2.2, 0.8)
    dma("Y", "dws", T.qws[:], T.ws[:], late, ["qws"], 2.2, 0.2)
    dma("Y", "dv", T.vt[:], T.v[:], late, ["vt"], 2.2, 0.4)
    quant("qv", 0, 128, T.vt, ["vt"], ["qv"])
    if QUIET:
        add({"Y": (None, 0.0, 0.0)}, ["qwc", "qws", "vt", "gap", "wa8"], ["quiet"], "none")
    iota(T.w1[:, 0:8], [[0, 2], [16, 4]], -3, 0, ["w1a"])
    iota(T.w1[:, 8:16], [[64, 2], [144, 4]], 8, 0, ["w1b"])
    ts(T.wi[:], T.w1[:, 0:8], T.pv[:, 0:1], A.add, ["w1a", "pv"], ["wi"], 1.0 / 7.0, A.mult)
    lin(T.w2[:, 0:1], T.pv[:, 0:1], 9.0, 0.0, ["pv"], ["w20"])
    for k in range(2):
        lin(T.w2[:, 1 + k:2 + k], T.pv[:, 3:4], 2.0 - 4 * k, T.w2[:, 0:1], ["pv", "w20"], ["w2%d" % (k + 1)])
        ts(T.w1[:, 24 + 4 * k:28 + 4 * k], T.wi[:, 4 * k:4 * k + 4], -64.0, A.mult, ["wi", "w2%d" % (k + 1)], ["o%d" % k], T.w2[:, 1 + k:2 + k], A.add)
    tt(T.w1[:, 24:32], T.w1[:, 24:32], T.w1[:, 8:16], A.add, ["o0", "o1", "w1b"], ["o2"])
    cp(T.ordr[:], T.w1[:, 24:32], ["o2"], ["ordr"])

    H = len(CUTS) - 1
    SC64 = 1.0 / 64

    def quant_x(r, tile, h, rd):
        quant("t%d" % r, CUTS[h], CUTS[h + 1], tile, rd, ["t%d_%d" % (r, h)])

    for h in range(H):
        quant_x(0, T.xin, h, ["xin%d" % h])

    STEP[1] = len(ops)
    for r in range(R):
        t_ = "t%d" % r
        TA = ["%s_%d" % (t_, h) for h in range(H)]

        def tk(a, b):
            return ["%s_%d" % (t_, h) for h in range(H) if CUTS[h] < b and a < CUTS[h + 1]]
        QU = ["qupc", "qups"]
        row = {3: (BK["r3"], 320), 2: (BK["r1"], 128), 1: (BK["r1"], 128), 0: (BK["r0"], 0)}
        for t in (3, 2, 1, 0):
            bk = BK["c%d" % t]
            mm(bk, t_, B0[t], "qup", 0, 128, tk(B0[t], B0[t] + 128) + QU)
            mv(T.sc[:, 9 * t:9 * t + 9], T.ps[:, 512 * bk:512 * bk + 18:2], ["#%d" % bk], ["sc%d" % t])
            if t != 2:
                a, z = B1[t], B1[t + 1 + (t == 1)]
                for k in ("r%d" % t, "s1")[:1 + (t == 1)]:
                    mm(BK[k], "qup", 16, t_, a, z - a, tk(a, z) + QU)
        bd = BK["d0"]
        mm(bd, t_, 0, "qup", 0, 128, tk(0, 128) + QU)
        for a, z in UPS:
            act(T.up[:, a:z], T.sc[:, 9 * a + 8:9 * z:9], ["sc%d" % t for t in range(a, z)], ["up%d" % t for t in range(a, z)], AF.Abs,
                bias=2.0 ** -125, scale=0.6 * 2.0 ** -23)
        for t in range(4):
            if not any(a <= t < z for a, z in UPS):
                bk = BK["c%d" % t] if t else bd
                act(T.up[:, t:t + 1], ps(bk, 16, 17), ["#%d" % bk], ["up%d" % t], AF.Abs, bias=2.0 ** -125, scale=0.6 * 2.0 ** -23)
        MK = ["mtp0", "mtp1", "mtp2"]
        for t in (3, 2, 1, 0):
            p, a, z = HALF[t], B1[t], B1[t + 1]
            s = T.sc[p, 9 * t + 8:9 * t + 9]
            bk, o = row[t]
            lin(T.df[p, a:z], T.ctri[p, 0:z - a], T.up[p, t:t + 1], s, ["ctri", "sc%d" % t, "up%d" % t], ["d%d" % t])
            tt(T.mt[p, 4 * a + t:4 * z:4], T.ps[p, 512 * bk + a - o:512 * bk + z - o], T.df[p, a:z], A.is_ge, ["#%d" % bk, "d%d" % t] + MK, ["md%d" % t], 1.0)
            if t > 1:
                d = T.dd[:, 64 * t - 128:64 * t + a - 256]
                act(d, ps(BK["s1"], 0, a - 128), ["#%d" % BK["s1"], "sc%d" % t], ["sg%d" % t], AF.Sign, bias=s, scale=-1.0)
                act(T.mt[:, 512 + t:4 * a:4], d, ["sg%d" % t] + MK, ["mv%d" % t, "acc%d" % t], AF.Relu, 0.02, scale=-1.0, accum_out=T.acc[:, t:t + 1])
                lin(T.thr[:, t:t + 1], T.acc[:, t:t + 1], 2.0, 2.0 * (NF - a) + 1, ["acc%d" % t], ["thr%d" % t])
            if t:
                o = T.mt[p, t:512:4]
                ts(o, T.ps[p, 512 * BK["r0"]:512 * BK["r0"] + 128], s, A.is_gt, ["#%d" % BK["r0"], "sc%d" % t] + MK, ["mu%d" % t])
                act(T.dd[p, 128 + 128 * t:256 + 128 * t], o, ["mu%d" % t] + ["thr%d" % t] * (t > 1), ["bnd%d" % t], AF.Identity, 0.02, scale=256.0,
                    bias=T.thr[p, t:t + 1] if t > 1 else 2.0 * (NF - a) + 1, accum_out=T.acc[p, 4 + t:5 + t])
        SC = ["sc0", "sc1", "sc2", "sc3", "scn", "sn0"]
        if not MN:
            mv(T.sc[:, 45:72], T.sc[:, 9:36], SC[1:4], ["scn"], -1.0)
            mv(T.sc[:, 36:45], T.ps[:, 512 * bd:512 * bd + 18:2], ["#%d" % bd], ["sn0"], -1.0)
        for a, z in MQ:
            quant("m", a, z, T.mt, MK + (["md0", "mu1", "mu2", "mu3"] if a == 0 else ["md1", "md2", "mv2", "mv3"] * (a < 320) + ["md3"] * (z > 320)), ["m%d" % a])
        for t in (3, 2, 1, 0):
            mm(BK["k%d" % t], "m", B0[t], "kr", 6 - 2 * t, 144, ["m%d" % a for a, z in MQ if a <= B0[t] < z] + ["kr"])
        if MN:
            scan(T.cmx[:, 1:37], T.sc[:, 0:36], T.k72[:, 80:116], -1e29, A.max, A.add, SC[0:4] + ["k72d"], ["cmx"])
            scan(T.cmx[:, 41:77], T.sc[:, 0:36], T.k72[:, 80:116], 1e29, A.min, A.subtract, SC[0:4] + ["k72d"], ["cmn"])
            tt(T.rr[:, 0:36], T.sc[:, 0:36], T.cmx[:, 0:36], A.is_le, SC[0:4] + ["cmx", "cmx0"], ["rr"])
            tt(T.rr[:, 36:72], T.sc[:, 0:36], T.cmx[:, 40:76], A.is_ge, SC[0:4] + ["cmn", "cmx1"], ["rn"])
        else:
            scan(T.cmx[:, 1:73], T.sc[:, 0:72], T.k72[:, 80:152], -1e29, A.max, A.add, SC + ["k72d"], ["cmx"])
            tt(T.rr[:, 0:72], T.sc[:, 0:72], T.cmx[:, 0:72], A.is_le, SC + ["cmx", "cmx0"], ["rr"])
        scan(T.cm2[:, 0:72], T.k72[:, 0:72], T.rr[:, 0:72], 0.0, A.add, A.mult, ["rr", "k72a"] + ["rn"] * MN, ["cm2s"])
        for b in range(4):
            bk = BK["f"][b % len(BK["f"])]
            mm(bk, "ef", 256 * b, t_, 0, C, ["ef%d" % (2 * b)] + TA)
            o = 896 * (b // 2)
            mv(T.fh[:, o + b % 2:o + 896:2], ps(bk, 0, C), ["#%d" % bk], ["ft%d" % b], SC64, on="SV")
        for k in range(2):
            ft = ["ft%d" % (2 * k), "ft%d" % (2 * k + 1)]
            for q in range(2):
                o = FW // 2 * q
                mv(T.win[:, WF + FW * k + o:WF + FW * k + o + FW // 2], T.fh[:, 896 * k + o:896 * k + o + FW // 2], ft, ["fh%d%d" % (k, q)], f=0.5, on=GC)
            for q in range(NH):
                o, c = WA + WS * (q + 1) + NF + 112 * k, 896 * k + 112 * (7 - q)
                mv(T.win[:, o:o + 112], T.fh[:, c:c + 112], ft, ["fg%d%d" % (k, q)], f=0.5, on=GC)
        for t in range(4):
            p, bk = HALF[t], BK["k%d" % t]
            o, c, b = T.flt[p, t:576:4], T.ps[p, 512 * bk:512 * bk + 144], T.acc[p, 4 + t:5 + t] if t else 256.0 * NF + 128
            alts = {"V": (lambda o=o, c=c, b=b: V.tensor_scalar(o, c, 256.0, b, A.mult, A.is_lt), vc(144), 0),
                    "S": (lambda o=o, c=c, b=b: S.activation(o, c, AF.Sigmoid, bias=b, scale=-256.0), vc(144), 0)}
            add({e: alts[e] for e in FA}, ["#%d" % bk, "ctri"] + ["bnd%d" % t] * (t > 0), ["fa%d" % t])
        quant("fl", 0, 144, T.flt, ["fa%d" % t for t in range(4)], ["fl0"])
        bp, bc, bl = BK["p"], BK["c"], BK["l"]
        mm(bp, "ka", 0, "fl", 0, 128, ["fl0", "ka1"], True, False)
        mm(bp, "kr", 16, "fl", 8, 128, ["fl0", "kr"], False, True)
        for t in range(4):
            p = HALF[t]
            ts(T.sot[p, t:512:4], T.ioh[p, :], T.cm2[p, 9 * t + 7:9 * t + 8], A.add, ["io0", "io1", "io2", "io3", "cm2s"], ["so%d" % t],
               T.cm2[p, 9 * t + 43:9 * t + 44], A.is_equal, 0.5)
        quant("so", 0, 128, T.sot, ["so%d" % t for t in range(4)], ["so"])
        for k in range(2):
            if k == MF:
                mm(bc, "so", 0, "pm", 0, NC, ["so", "pm0", "pm1"], k == 0, k == 1)
            else:
                mm(bc, "fl", 16, "kb", 0, NC, ["fl0", "kba", "kbb"], k == 0, k == 1)
        scan(T.ln[:], T.kat[:, 0:NC], ps(bc, 0, NC), 0.0, A.mult, A.max, ["#%d" % bc, "kat0"], ["ln"])
        for y in range(2):
            p = slice(64 * y, 64 * y + 64)
            scan(T.pkf[p, 0:30], T.kpk[p, 0:30], T.ln[p, 7 + 8 * y:NC:16], 0.0, A.mult, A.add, ["ln", "kpk0", "kpk1"], ["pkf%d" % y])
            for o in range(2):
                lin(T.sm[64 * o:64 * o + 64, 30 * (o ^ y):30 * (o ^ y) + 30], T.ln[p, 7 + 8 * y:NC:16], 256.0, T.w2[p, 7:8], ["ln", "ow"], ["sm%d%d" % (y, o)])
        ts(T["pk%d" % r][:], T.pkf[:, 1:30:2], 256.0, A.mult, ["pkf0", "pkf1"], ["pk%d" % r])
        send(T["lst%d" % r][:], T["pk%d" % r][:], "al%d" % r, 1, ["pk%d" % r] + ["quiet"] * QUIET, ["lst%d" % r], 2.0)
        mv(T.pc[:], T.ps[:, 512 * bp:512 * bp + 8:2], ["#%d" % bp], ["pc"])
        for t in range(4):
            p, a = HALF[t], 64 * (t == 3)
            ts(T.cmt[p, 4 * a + t:4 * NF:4], T.ios[p, a:NF], T.pc[p, t:t + 1], A.is_ge, ["pc", "ios"], ["cm%d" % t], f=0.5)
        quant("cm", 0, NF, T.cmt, ["cm%d" % t for t in range(4)], ["cm"])
        mm(bl, "kr", 16, "cm", 0, NF, ["cm", "kr"])
        scan(T.lrow[:], T.k16[:], ps(bl, 0, NF), 0.0, A.add, A.min, ["#%d" % bl, "k16"], ["lrow"])
        cp(T.pl[:], T.lrow[:, 15:NF:16], ["lrow"], ["pl"])
        sl, ld = "slot%d" % r, "land%d" % r
        pick(sl, t_, NF, C, T.pl[:, 0:12], TA + ["pl"])
        send(T[ld + "c"][:].bitcast(dt.uint8), T[sl + "c"][:].bitcast(dt.uint8), "ac%d" % r, 2, [sl + "c"], [ld + "c"], 2.3)
        send(T[ld + "s"][:], T[sl + "s"][:], "ac%d" % r, 2, [sl + "s"], [ld + "s"], 2.1)

        def unpack(src, base, key, banks, on):
            for i in range(9):
                k = 7 - i
                bk = banks[i % len(banks)]
                o = base + (WS if base else NF) * i
                a, z = (max(0, 80 - 56 * k), NF) if base else (0, NF if r == 0 else min(NF, 399 - 56 * k))
                a0, z0 = min(a, NF - 128), max(z + z % 2, 128)
                mm(bk, "ef", 128 * (k % 8), src, a0, z0 - a0, [src + "c", src + "s", "ef%d" % (k % 8)])
                mv(T.win[:, o + a:o + z], ps(bk, a - a0, z - a0), ["#%d" % bk], ["%s%d" % (key, i)], SC64, on=on)
        unpack(sl, 0, "wo", BK["o"], "SV")
        SM = ["sm00", "sm01", "sm10", "sm11", "cl"]
        ts(T.eo[:], T.sm[:, 0:60].indirect(T.cl[:, 4:8]), T.w2[:, 7:8], A.is_equal, SM, ["eo"], -2 * BIG, A.mult, 2.5)
        tt(T.eq[:], T.sm[:, 0:60].indirect(T.cl[:, 4:8]), T.eo[:], A.add, SM + ["eo"], ["eq"], 2.5)
        scan(T.kos[:, 63::-1], T.kst[:, 63::-1], T.eq[:, 63::-1], 0.0, A.add, A.max, ["eq", "kst0"], ["kos"])
        tt(T.own[:], T.kos[:], T.idc[:, 0:64], A.max, ["kos", "idc"], ["own"])
        unpack(ld, WA, "wa", BK["a"], "SV")
        cp(T.ai[:, 0:15], T["lst%d" % r][:], ["lst%d" % r], ["ai"])
        for y in range(2):
            cp(T.ai[64 * y:64 * y + 64, 15:30], T["lst%d" % r][64 - 64 * y:128 - 64 * y, :], ["lst%d" % r], ["ai%d" % y])
        ts(T.a2[:, 0:60:2], T.ai[:], 8, A.arith_shift_right, ["ai", "ai0", "ai1"], ["a2h"])
        ts(T.a2[:, 1:60:2], T.ai[:], 255, A.bitwise_and, ["ai", "ai0", "ai1"], ["a2l"])
        ts(T.ke[:], T.a2[:].indirect(T.cl[:, 0:4]), 0.0, A.is_equal, ["a2h", "a2l", "cl"], ["ke"], f=2.5)
        tt(T.kn[:], T.a2[:].indirect(T.cl[:, 0:4]), T.kst[:, 64:128], A.add, ["a2h", "a2l", "cl", "kst1"], ["kn"], 2.5)
        scan(T.kns[:], T.ke[:], T.kn[:], 0.0, A.mult, A.add, ["kn", "ke"], ["kns"])
        tt(T.rep[:, 0:64], T.kns[:], T.own[:], A.max, ["kns", "own"], ["rep"])
        for k in range(4):
            mv(T.rep[32 * k:32 * k + 32, 64:128], T.rep[32 * (k ^ 1):32 * (k ^ 1) + 32, 0:64], ["rep"], ["rp%d" % k])
        for a, z in OFF:
            ts(T.off[:, a:z], T.rep[:, 0:128].indirect(T.ordr[:, a // 16:z // 16]), -1.0, A.mult, ["rep"] + ["rp%d" % k for k in range(4)] + ["ordr", "top"],
               ["off%d" % a], T.w2[:, 6:7], A.add, f=1.6 + 60 / (z - a))
        WIN = ["ft%d" % b for b in range(4)] + ["wo%d" % k for k in range(9)] + ["fg%d%d" % (k, q) for k in range(2) for q in range(NH)] + ["gap"]
        for i, (a, z) in enumerate(GAT):
            n = NH + 1 if a >= C - 56 * NH else 9
            for b1 in range(2):
                lo, hi = 896 * b1 + 2 * a, 896 * b1 + 2 * z
                tt(T.yt[:, lo:hi], T.win[:, 0:WA + n * WS if n < 9 else WF + 2 * FW].indirect(T.off[:, 64 * b1 + a // 8:64 * b1 + z // 8]),
                   T.fh[:, lo:hi], A.add, WIN + ["wa%d" % k for k in range(n)] + ["fh00", "fh01", "fh10", "fh11"] * (n == 9)
                   + ["off%d" % c for c, d in OFF if c < 64 * b1 + z // 8 and 64 * b1 + a // 8 < d], ["yt%d%d" % (b1, i)], 1.56 + 30 / (z - a))
        for h in range(H - 1, -1, -1):
            a, z = CUTS[h], CUTS[h + 1]
            if h in ZP:
                n = 2 * (z - a)
                for b in range(4):
                    o = (n + 16) * b + 8
                    for be in range(4):
                        c = 896 * (be // 2) + 2 * a
                        dma("Y", "dz%d" % b, T.zz[32 * be:32 * be + 32, o - be % 2:o - be % 2 + n], T.yt[32 * b:32 * b + 32, c:c + n],
                            ["yt%d%d" % (be // 2, i) for i, (c, d) in enumerate(GAT) if c < z and a < d], ["zz%d%d" % (be, b)], ZT)
                    mv(T.yy[:, 4 * a + b:4 * z:4], T.zz[:, o:o + n:2], ["zz%d%d" % (be, b) for be in range(4)], ["yy%d%d%d" % (be, b, h) for be in range(4)], f=0.5, on=GC)
            for be in range(4 * (h not in ZP)):
                for b in range(4):
                    o = 896 * (be // 2)
                    mv(T.yy[32 * be:32 * be + 32, 4 * a + b:4 * z:4], T.yt[32 * b:32 * b + 32, o + 2 * a + be % 2:o + 2 * z:2],
                       ["yt%d%d" % (be // 2, i) for i, (c, d) in enumerate(GAT) if c < z and a < d], ["yy%d%d%d" % (be, b, h)], f=0.5, on=GC)
            quant("qy", a, z, T.yy, ["yy%d%d%d" % (i, b, h) for i in range(4) for b in range(4)], ["qy%d" % h])
            for b in range(4):
                bk = BK["w"][(4 * h + b) % 8]
                mm(bk, "qw", 128 * b, "qy", a, z - a, ["qy%d" % h, "qwc", "qws"])
                if b < YP:
                    c = slice(4 * a + b, 4 * z, YP)
                    mv(T.y1[:, c], T.yy[:, c], ["yy%d%d%d" % (i, j, h) for i in range(4) for j in range(b, 4, YP)], ["y1%d%d" % (b, h)], 32.0, 0.5)
                c = slice(4 * a + b, 4 * z, 4)
                tt(T.xs[:, c], ps(bk, 0, z - a), T.y1[:, c], A.add, ["#%d" % bk, "y1%d%d" % (b % YP, h)], ["xs%d%d" % (b, h)], 1.0)
            quant_x(r + 1, T.xs, h, ["xs%d%d" % (b, h) for b in range(4)])

    STEP[0], STEP[2] = (len(ops) - STEP[1]) // R, len(ops)
    t_ = "t%d" % R
    for h in range(H):
        a, z = CUTS[h], CUTS[h + 1]
        k_ = ["%s_%d" % (t_, h)]
        mm(h, "qv", 0, t_, a, z - a, ["qv"] + k_)
        dma("Y", "outs", T.oc[:, 4 * a:4 * z], T[t_ + "c"][:, a:z].bitcast(dt.uint8), k_, [], 2.5)
        mv(T.yo[:, a:z], ps(h, 0, z - a), ["#%d" % h], ["yo%d" % h])
        dma("Y", "outs", T.y[:, a:z], T.yo[:, a:z], ["yo%d" % h], [], 2.5)
    for k in range(4):
        dma("YS", "outs", T.osc[4 * k:4 * k + 4, :], T[t_ + "s"][32 * k:32 * k + 4, 0:C], ["%s_%d" % (t_, h) for h in range(H)], [], 2.0)

    Q = {"V": V, "S": S, "P": g.tensor, "G": g, "Y": g.sync}
    cnt, seen, tok, eng, knew, sent, moved, alone = {}, {e: {} for e in Q}, {}, {}, {}, 0, False, False
    at = {i: p for p, i, e in schedule(ops)}
    for _, i, e in schedule(ops):
        o = ops[i]
        if o["sem"] == "none":
            continue
        for d, raw in sorted(o["deps"].items(), key=lambda x: -at[x[0]]):
            if ops[d]["sem"] == "none":
                continue
            if raw or eng[d] != e or ops[d]["sem"] or ops[d]["arrive"]:
                s, v = tok[d]
                if seen[e].get(s, 0) < v:
                    Q[e].wait_ge(T.sem[s], v)
                    seen[e][s] = v
                    if not ops[d]["arrive"]:
                        for s2, v2 in knew[d].items():
                            seen[e][s2] = max(seen[e].get(s2, 0), v2)
        if e == "G" and not o["arrive"]:
            moves = o.get("moves", False)
            if moves != moved and seen[e].get(e, 0) < cnt.get(e, 0):
                g.wait_ge(T.sem.G, cnt[e])
                seen[e][e] = cnt[e]
            moved = moves
        if e == "V":
            if alone and seen[e].get(e, 0) < cnt[e]:
                V.wait_ge(T.sem.V, cnt[e])
                seen[e][e] = cnt[e]
            alone = o.get("alone")
        ins = o["alts"][e][0]()
        eng[i] = e
        knew[i] = dict(seen[e])
        if o["arrive"]:
            tok[i] = o["arrive"]
            sent += neng
        else:
            s, n = (o["sem"], 16) if o["sem"] else (e, 1)
            cnt[s] = cnt.get(s, 0) + n
            ins.then_inc(T.sem[s], n)
            tok[i] = (s, cnt[s])
    for s in cnt:
        g.sync.wait_ge(T.sem[s], cnt[s])
    g.wait_ge(T.sem.sent, sent)
